import numpy as np, ml_dtypes
CORES = [5,29,101,125,133,157,229,253]
N = 8
import mx_ref
BF = ml_dtypes.bfloat16
def gentries(a):
    return np.ascontiguousarray(a.reshape(8, 16, -1).transpose(0, 2, 1)).reshape(8, -1)
def gtable(e):
    e = np.asarray(e); return np.ascontiguousarray(e.reshape(8, -1, 16).transpose(0, 2, 1)).reshape(128, -1).astype(np.int32)
def gcols(t, e):
    v = np.concatenate([t.reshape(8, 16, -1, 4), np.zeros((8, 16, 1, 4), BF)], axis=2)
    return np.ascontiguousarray(np.stack([v[g][:, e[g]] for g in range(8)])).reshape(128, -1)
def tile(rs):
    return np.stack(rs, axis=2).reshape(128, -1).astype(BF)
def pick(q, e):
    c = np.concatenate([q[0].reshape(128, -1, 4), np.zeros((128, 1, 4), np.uint8)], axis=1); s = np.concatenate([q[1], np.ones((16, 1), np.uint8)], axis=1)
    return (np.ascontiguousarray(c[:, e].reshape(128, -1)), np.ascontiguousarray(s[:, e]))
def join(*qs):
    return (np.concatenate([q[0] for q in qs], axis=1), np.concatenate([q[1] for q in qs], axis=1))
def put(q, e, v):
    c, s = q[0].reshape(128, -1, 4).copy(), q[1].copy(); c[:, e] = v[0].reshape(128, -1, 4); s[:, e] = v[1]
    return (c.reshape(128, -1), s)
def pk(c, s):
    return (np.ascontiguousarray(c), mx_ref.live(s))
def emit(q):
    return q[0], q[1]
def packed(v, rng):
    q = [mx_ref.quantize(np.ascontiguousarray(v[r])) for r in range(N)]
    return np.stack([a for a, b in q]), np.stack([mx_ref.plane(b, rng) for a, b in q])
def values_of_codes():
    e, c = np.zeros((128, 128, 4), np.float32), np.zeros((128, 2, 4), np.uint8)
    e[np.arange(128), np.arange(128), 0] = 1
    c[:127, :, 0] = np.arange(256).reshape(2, 128).T[:127]
    return mx_ref.matmul(mx_ref.quantize(e.reshape(128, 512).astype(BF)), (c.reshape(128, 8), np.full((16, 2), 127, np.uint8))).T.reshape(-1).astype(np.float64)
CODE_VALUE, SCALE_VALUE = values_of_codes(), 2.0 ** (np.arange(256) - 127.0)
def decode(q):
    return (CODE_VALUE[q[0]].reshape(16, 8, -1, 4) * SCALE_VALUE[q[1]][:, None, :, None] + 0.0).reshape(128, -1).astype(np.float32)
def f(rng, *shape):
    return mx_ref.flush((rng.standard_normal(shape, dtype=np.float32) * np.exp2(rng.integers(-2, 3, shape[:-1] + (1,)))).astype(BF))
def wide(rng, *shape, cols=0):
    v = rng.standard_normal(shape, dtype=np.float32) * np.exp2(rng.integers(-12, 13, shape)).astype(np.float32)
    if cols: v *= np.repeat(np.exp2(rng.integers(-cols, cols + 1, shape[:-2] + (1, shape[-1] // 4))) * (rng.random(shape[:-2] + (1, shape[-1] // 4)) > 0.0625), 4, axis=-1).astype(np.float32)
    return mx_ref.flush(v.astype(BF))
C = 320
STEP = [4, 1, 2]
def numbers_of(rng):
    return {"x": np.array(f(rng, N, 128, 4 * C)), "u": np.array(f(rng, N, 128, 512)), "v": np.array(f(rng, N, 128, 512))}
def stored(a, b):
    return {"lam": np.stack([gtable(a[r]) for r in range(N)]), "rho": np.stack([gtable(b[r]) for r in range(N)])}
def dealt(rng):
    e = np.tile(np.arange(C), (N, 8, 1))
    return np.stack([rng.permuted(e, axis=2), rng.permuted(e, axis=2)], axis=3).reshape(N, 8, 2 * C)
def lists(rng):
    a = dealt(rng)
    return stored(a, dealt(rng))
def layers(rng):
    return np.array(f(rng, N, 128, 2048)).reshape(N, 8, 16, 4, 8, 16, 4)
def weights(rng, w):
    c, p = packed(np.ascontiguousarray(w).reshape(N, 128, 2048), rng)
    return {"wc": c, "ws": p}
def unread(u):
    u = u.reshape(N, 128, 128, 4)
    u[:, :, ::16] = 0
    u[:, :, 1::16] = 0
    return u
def setup_inputs(rng):
    return {**numbers_of(rng), **lists(rng), **weights(rng, layers(rng))}
def setup_inputs_ties(rng):
    d = numbers_of(rng)
    o = rng.permutation(N)
    s = rng.integers(-1, 2, (N, 8, 2, C)).astype(np.float32)
    s[o[1]] = 1
    s[o[2]] = -1
    x = d["x"].reshape(N, 8, 16, C, 4)
    x[:, :, :2] = 0
    x[:, :, :2, :, 0] = s.astype(BF)
    c = np.ones(N, np.float32)
    c[o[0]] = 0
    u = unread(d["u"])
    for h in range(0, 128, 16):
        for i in range(2): u[:, h + i, h + i, 0] = c.astype(BF)
    w = layers(rng)
    w[:, :, :, :, :, :8] = 0
    for g in range(8): w[:, g, 15, 0, g, 15, 0] = 2.0 ** 8
    return {"x": x.reshape(N, 128, 4 * C), "u": u.reshape(N, 128, 512), "v": d["v"], **lists(rng), **weights(rng, w)}
def setup_inputs_near(rng):
    d = numbers_of(rng)
    lo = np.unique(np.minimum(np.arange(N), np.arange(N) ^ STEP[0]))
    o = np.zeros(N, np.int64)
    o[lo] = rng.permutation(N // 2) % 2
    o[lo ^ STEP[0]] = o[lo]
    k = np.where(o == 0, 2.0 ** -30, 1.0).astype(np.float32)
    some = rng.permutation(8)[:4]
    x = d["x"].astype(np.float32).reshape(N, 8, 16, C, 4)
    x[:, :, :8] = 0
    x[:, some, 8:] = 0
    for g in some: x[:, g, 15, :, 0] = k[:, None]
    for i in range(2):
        s = rng.integers(-1, 2, (N, 8, C)) * k[:, None, None]
        x[:, :, 2 * i, :, 0] = 1.125 * s
        x[:, :, 2 * i + 1, :, 0] = -1.25 * s
        x[:, :, 6, :, i] = rng.choice([-1.0, 1.0], (N, 8, C)) * k[:, None, None]
        x[:, :, 6, :, 2 + i] = rng.choice([-1.0, 1.0], (N, 8, C)) * k[:, None, None]
    x[:, :, 7, :, 0] = k[:, None, None]
    for r in range(N):
        for g in rng.permutation(8)[:4]: x[r, g, 2 * rng.integers(2), rng.integers(C), 0] = 2.0 ** 30 * rng.choice([-1.0, 1.0])
    u = unread(d["u"])
    for h in range(0, 128, 16):
        for i in range(2):
            u[:, h + 2 * i, h + i, 0] = (1.125 * k).astype(BF)
            u[:, h + 2 * i + 1, h + i, 0] = k.astype(BF)
            u[:, h + 4 + i, h + i, 0] = k.astype(BF)
    w = layers(rng)
    w[:, :, :8] = 0
    w[:, :, :, :, :, :8] = 0
    w[:, :8] = 0
    for g in range(8):
        for i in range(2): w[:, g, 6, 0, g, 4 + i, i] = 2.0 ** -8
        w[:, g, 7, 0, g, 7, 0] = 32.0
    for g in some:
        for i in range(2):
            u[:, 16 * g + 8 + 2 * i, 16 * g + i, 0] = (1.125 * k).astype(BF)
            u[:, 16 * g + 9 + 2 * i, 16 * g + i, 0] = k.astype(BF)
            w[:, g, 6, 0, g, 8 + 2 * i, 2 + i] = 1.125 * 2.0 ** -8
            w[:, g, 6, 0, g, 9 + 2 * i, 2 + i] = -1.25 * 2.0 ** -8
        w[:, g, 7, 0, g, 14, 0] = 32.0
    return {"x": x.reshape(N, 128, 4 * C).astype(BF), "u": u.reshape(N, 128, 512), "v": d["v"], **lists(rng), **weights(rng, w)}
def setup_inputs_odd(rng):
    d = numbers_of(rng)
    x = d["x"].astype(np.float32).reshape(N, 8, 16, C, 4)
    x[:, :, 8:] = 0
    x[:, :, 0, :, 0] = 1.96875 * 2.0 ** 8
    for i in range(2):
        x[:, :, 1 + 2 * i, :, 0] = 2.0 ** -5
        x[:, :, 2 + 2 * i, :, 0] = (7 + 2 * rng.integers(0, 2, (N, 8, C))) * 2.0 ** -8
    x[:, :, 8, :, 0] = -1.125
    x[:, :, 10, :, 0] = 0.0703125 * rng.choice([-1.0, 1.0], (N, 8, C))
    u = unread(d["u"])
    for h in range(0, 128, 16):
        for i in range(2):
            c = rng.choice([-1.0, 1.0], N).astype(np.float32)
            u[:, h + 1 + 2 * i, h + i, 0] = c.astype(BF)
            u[:, h + 2 + 2 * i, h + i, 0] = (-1.125 * c).astype(BF)
    w = np.zeros((N, 8, 16, 4, 8, 16, 4), np.float32)
    for g in range(8):
        w[:, g, 8, 0, g, 8, 0] = -28.0
        w[:, g, 2, 0, g, 12, 0] = 32.0
        for b in range(4): w[:, g, 10, b, g, 9, 0] = -2.0 ** (b - 5)
    return {"x": x.reshape(N, 128, 4 * C).astype(BF), "u": u.reshape(N, 128, 512), "v": d["v"], **lists(rng), **weights(rng, w.astype(BF))}
def setup_inputs_ends(rng):
    d = numbers_of(rng)
    o, e = rng.permutation(N) % 4, rng.permutation(N) % 4
    s = rng.choice([-1.0, 1.0], (N, 128, C, 4))
    s[o == 0] = -1
    s[o == 1] = rng.choice([-1.0, 1.0], (N, 1, C, 1))[o == 1]
    x = s * (0.93 + 0.02 * rng.random((N, 128, C, 4))) * 2.0 ** 30
    x[o == 3] = 2.0 ** -30
    size = np.where(o == 3, 2.0 ** -30, 2.0 ** 30)
    u = unread(d["u"])
    for r in range(N):
        h = rng.permutation(8)
        for i in range(2):
            c = np.where(h < 2, 0.0, ((h >> i) % 2) * 2.0 - 1.0) * size[r]
            u[r, :, i::16] = c.astype(np.float32).astype(BF)[None, :, None]
    v = rng.choice([-1.0, 1.0], (N, 128, 512)) * np.where(o < 2, 2.0 ** 30, 2.0 ** -30)[:, None, None]
    t = rng.integers(0, C, (2, N, 8, 2 * C))
    t[:, e == 0] = C - 1
    t[:, e == 1] = 0
    t[:, e == 2] = np.arange(2 * C) % 2 * (C - 1)
    w = np.zeros((N, 128, 4, 128, 4), np.float32)
    j = np.arange(127)
    for b in range(4): w[:, j, b, j, b] = np.array([-0.25, -0.25, -2.0 ** -8, 32.0])[o][:, None]
    return {"x": x.astype(np.float32).reshape(N, 128, 4 * C).astype(BF), "u": u.reshape(N, 128, 512), "v": v.astype(np.float32).astype(BF), **stored(t[0], t[1]), **weights(rng, w.astype(BF))}
def setup_inputs_spread(rng):
    d = setup_inputs(rng)
    d["x"] = wide(rng, N, 128, 4 * C, cols=6)
    return d
def check_inputs(d):
    b = []
    for k in ("x", "u", "v"):
        a = np.abs(d[k].astype(np.float32))
        if not (np.isfinite(a).all() and ((a == 0) | (a >= 2.0 ** -30) & (a <= 2.0 ** 30)).all()): b.append("a value of " + k)
    for k in ("lam", "rho"):
        if not ((d[k] >= 0) & (d[k] < C)).all(): b.append("an entry of " + k)
    none, least, most = [emit(mx_ref.quantize(np.full((128, 16), k, np.float32).astype(BF)))[1][0, 0] for k in (0.0, 2.0 ** -8, 2.0 ** 8)]
    for r in range(N):
        if ((d["wc"][r] == 0x7F) | (d["wc"][r] == 0xFF)).any(): b.append("wc: a code that is no number")
        s = mx_ref.live(d["ws"][r])
        if ((s != none) & ((s < least) | (s > most))).any(): b.append("ws: a scale out of range")
        if (((d["wc"][r].reshape(16, 8, 512, 4) & 0x7F) != 0) & (s == none)[:, None, :, None]).any(): b.append("wc: a code other than zero under the scale of zeros")
    return b
def swapped(t, where):
    a = t.reshape(8, C, 2)
    return np.where(where[:, :, None], a[:, :, ::-1], a).reshape(8, 2 * C)
def reference(x, u, v, lam, rho, wc, ws):
    qu = [mx_ref.quantize(u[r]) for r in range(N)]
    lay = [pk(wc[r], ws[r]) for r in range(N)]
    left, right = [gentries(lam[r]) for r in range(N)], [gentries(rho[r]) for r in range(N)]
    now = [x[r] for r in range(N)]
    q = [mx_ref.quantize(now[r]) for r in range(N)]
    s = [mx_ref.matmul(qu[r], q[r]) for r in range(N)]
    for step in STEP:
        at, mid, sent = [], [], []
        for r in range(N):
            bit = (s[r][::16] > 0).astype(np.int64)
            up, down = np.zeros((8, C), np.int64), np.zeros((8, C), np.int64)
            up[0] = np.arange(C)
            down[7] = np.arange(C)
            for g in range(7):
                up[g + 1] = left[r][g][2 * up[g] + bit[g]]
            for g in range(7, 0, -1):
                down[g - 1] = right[r][g][2 * down[g] + bit[g]]
            at.append(np.take_along_axis(up, down, axis=1))
            mid.append(((now[r].astype(np.float32) + gcols(now[r], at[r]).astype(np.float32)) * np.float32(0.5)).astype(BF))
            z = mx_ref.quantize(mid[r])
            sent.append(mx_ref.quantize(tile([mx_ref.matmul(pick(lay[r], np.arange(128 * b, 128 * b + 128)), z) * np.float32(0.03125) for b in range(4)])))
        for r in range(N):
            p = r ^ step
            far = gcols(decode(sent[p]).astype(BF), np.take_along_axis(at[p], at[r], axis=1))
            now[r] = (mid[r].astype(np.float32) + far.astype(np.float32)).astype(BF)
            q[r] = mx_ref.quantize(now[r])
            s[r] = mx_ref.matmul(qu[r], q[r])
            left[r], right[r] = swapped(left[r], s[r][1::16] < 0), swapped(right[r], s[r][1::16] > 0)
    y, lr = np.zeros((N, 128, C), np.float32), np.zeros((N, 8, 4 * C), np.float32)
    oc, osc = np.zeros((N, 128, 4 * C), np.uint8), np.zeros((N, 16, C), np.uint8)
    for r in range(N):
        y[r] = mx_ref.matmul(mx_ref.quantize(v[r]), q[r])
        lr[r] = np.concatenate([left[r], right[r]], axis=1)
        oc[r], osc[r] = emit(q[r])
    return {"y": y, "lr": lr, "oc": oc, "osc": osc}

@@ -1,0 +1,713 @@
+from concourse.bass import DstId, RemoteDMATransfer
+from concourse.mybir import dt, AluOpType, ActivationFunctionType
+import comms_topo
+
+OP = AluOpType
+AF = ActivationFunctionType
+STEP = [4, 1, 2]
+BIG = 1.0e6
+WAKE, SPARE, LOOK = 0.07, 0.5, 0.3
+EPS = 2.0 ** -93
+
+F, B, I, U, C4, S8 = "float32", "bfloat16", "int32", "uint16", "float8_e4m3fn_x4", "uint8"
+SCRATCH = {"ps": ("psum", [128, 4096], F)}
+for _n, _w, _d in [
+    ("x0", 1280, B), ("x1", 1280, B), ("x2", 1280, B), ("x3", 1280, B), ("xh", 1280, B), ("xg", 1280, B), ("vt", 1280, B), ("ht", 1280, B), ("dd", 1280, B),
+    ("ub", 512, B), ("vb", 512, B), ("et", 2048, B), ("ones", 512, B),
+    ("uq", 128, C4), ("us", 128, S8), ("vq", 128, C4), ("vs", 128, S8), ("wq", 512, C4), ("wsp", 512, S8),
+    ("utq", 128, C4), ("uts", 128, S8), ("ufq", 768, C4), ("ufs", 768, S8), ("eq", 512, C4), ("es", 512, S8),
+    ("qx0", 320, C4), ("sx0", 320, S8), ("qx1", 320, C4), ("sx1", 320, S8), ("qx2", 320, C4), ("sx2", 320, S8), ("qx3", 320, C4), ("sx3", 320, S8),
+    ("qv", 320, C4), ("qvs", 320, S8),
+    ("qh1", 320, C4), ("sh1", 320, S8), ("qh2", 320, C4), ("sh2", 320, S8), ("qh3", 320, C4), ("sh3", 320, S8),
+    ("lq1", 320, C4), ("ls1", 320, S8), ("lq2", 320, C4), ("ls2", 320, S8), ("lq3", 320, C4), ("ls3", 320, S8), ("rlq", 320, C4), ("rls", 320, S8),
+    ("nl", 320, I), ("nlu", 320, U), ("tw", 5120, F), ("tx", 3840, F), ("nw", 3840, B), ("w4", 320, F),
+    ("cw", 120, F), ("cx", 120, F), ("fb", 60, F), ("fx", 120, F), ("fl", 240, F), ("flu", 256, U), ("lz", 64, F),
+    ("jj", 320, I), ("jk", 320, I), ("mask", 320, F), ("rs", 320, F), ("rb", 800, F), ("st", 320, F),
+    ("cid", 16, F), ("dva", 16, F), ("dvb", 16, F), ("ea", 16, F), ("da", 16, F), ("eb", 16, F), ("db", 16, F), ("tmp", 256, F),
+    ("y1", 160, F), ("y1s", 160, F), ("y2i", 160, F), ("y2b", 160, F), ("y2", 960, F), ("y2s", 960, F), ("ye", 640, F), ("yes", 640, F),
+    ("lu", 128, U), ("nu", 128, U), ("lt0", 16, F), ("lt1", 16, F), ("bc0", 320, B), ("bc1", 320, B), ("lw", 640, B), ("km", 320, B), ("kt", 320, B),
+    ("mlu", 32, U), ("ld", 64, F), ("kl1", 20, U), ("kl2", 20, U), ("kl3", 20, U), ("kr1", 20, U), ("kr2", 20, U), ("kr3", 20, U), ("rlk", 20, U),
+    ("kw", 320, F), ("ky", 320, F), ("kys", 320, F), ("mo", 128, U),
+    ("sn", 320, F), ("fn", 20, F), ("ltb", 40, F), ("rtb", 40, F), ("lrow", 640, F), ("rrow", 640, F), ("lni", 80, I), ("lnu", 80, U), ("lout", 80, F), ("lt2", 64, F),
+    ("yb", 320, F), ("sgc", 8, F), ("sgn", 8, F), ("cli", 64, I), ("clu", 64, U), ("ui", 64, I), ("uf", 64, F), ("uoff", 64, U), ("qi", 16, I), ("qf", 128, F),
+]:
+    SCRATCH[_n] = ("sbuf", [128, _w], _d)
+
+SEMAPHORES = (["sv", "sa", "st", "sg", "dx0", "dx1", "du", "dv", "dw", "dl", "dt0", "dt1", "fn1", "fn2", "fn3", "oy", "ol", "oq0", "oq1", "dfx", "lsem", "ry0", "ry1", "rz0", "rz1", "rk"]
+              + ["dn%d" % s for s in range(8)] + ["ar%d%d" % (r, h) for r in (1, 2, 3) for h in (0, 1)] + ["kr%d" % r for r in (1, 2, 3)])
+
+
+AT, WID = (0, 160), (160, 160)
+
+
+def cols(h):
+    return slice(AT[h], AT[h] + WID[h])
+
+
+def quad(h, t=0, step=1):
+    return slice(4 * AT[h] + t, 4 * (AT[h] + WID[h]), step)
+
+
+def part(h):
+    return slice(AT[h] // 16, (AT[h] + WID[h]) // 16)
+
+
+def bits_of(engines):
+    m = 0
+    for e in engines:
+        m |= 1 << e
+    return m
+
+
+def relays_of(core, dst, topo):
+    c = [k for k in topo.cores_of(core) if k != core and topo.may_write(k, dst)]
+    return [[k for k in c if topo.die(k) == topo.die(core)][0], [k for k in c if topo.die(k) != topo.die(core)][0]]
+
+
+def relay_program(g, core, T, topo):
+    for r, src in enumerate(T.cores):
+        dst = T.cores[r ^ STEP[1]]
+        if core not in topo.cores_of(src) or core == src:
+            continue
+        rel = relays_of(src, dst, topo)
+        if core not in rel:
+            continue
+        k = rel.index(core)
+        rid, pid = topo.addr(dst, core)
+        m, n = topo.mask(core, dst), len(topo.engines(core, dst))
+        half = len(topo.engines(src, core)) // 2
+        sent = 0
+        if k == 0:
+            g.wait_ge(T.sem.rk, half)
+            g.remote_dma(T.kr2[:], T.rlk[:], T.sem.kr2, T.sem.lsem, pid, rid, m)
+            sent += n
+        for h in (0, 1):
+            w = WID[h] // 2
+            a = AT[h] + w * k
+            g.wait_ge(T.sem["ry%d" % h], half)
+            g.remote_dma(T.lq2[:, a:a + w].bitcast(dt.uint8), T.rlq[:, a:a + w].bitcast(dt.uint8), T.sem["ar2%d" % h], T.sem.lsem, pid, rid, m)
+            g.wait_ge(T.sem["rz%d" % h], half)
+            g.remote_dma(T.ls2[:, a:a + w], T.rls[:, a:a + w], T.sem["ar2%d" % h], T.sem.lsem, pid, rid, m)
+            sent += 2 * n
+        g.wait_ge(T.sem.lsem, sent)
+
+
+def table_of(a, s):
+    if s < 6:
+        return ("l", s + 1) if s < 2 * a else ("r", 6 - s + 2 * a)
+    return ("r", 7) if (s == 6) == (a == 0) else ("l", 0)
+
+
+def rank_program(g, core, T, topo):
+    rank = T.rank_of(core)
+    if rank is None:
+        relay_program(g, core, T, topo)
+        return
+    Q = {"g": g, "v": g.vector, "a": g.scalar, "t": g.tensor, "s": g.sync}
+    SEM = {"g": "sg", "v": "sv", "a": "sa", "t": "st"}
+    nodes, writer, readers = [], {}, {}
+
+    def node(fns, cost, late, r, w, sem, inc):
+        pre, after = set(), set()
+        for k in list(r) + list(w):
+            if k in writer:
+                (after if k[0] == "@" else pre).add(writer[k])
+        for k in w:
+            if k[0] != "@":
+                pre.update(readers.get(k, ()))
+        i = len(nodes)
+        nodes.append({"fns": fns, "cost": cost, "late": late, "pre": sorted(pre), "order": sorted(pre | after), "sem": sem, "inc": inc})
+        for k in r:
+            readers.setdefault(k, set()).add(i)
+        for k in w:
+            writer[k] = i
+            readers[k] = set()
+
+    def op(q, fn, r, w, us):
+        node({q: fn}, {q: us}, 0.0, r, list(w) + (["gpsimd"] if q == "g" else []), None, 1)
+
+    def dma(q, pairs, r, w, sem):
+        def go(e):
+            for o, i in pairs:
+                e.dma_start(o, i).then_inc(T.sem[sem], 16)
+        node({q: go}, {q: 0.06 * len(pairs)}, 2.0, r, w, sem, 16 * len(pairs))
+
+    def us(n, cycles, gather):
+        return 0.05 + n * 0.0015 if gather else max(64, n * cycles) * 0.001
+
+    def tt(o, a, b, f, r, w, n=10, x=False, c=2):
+        op("v", lambda e: e.tensor_tensor(o, a, b, f), r, w, us(n, c, x))
+
+    def ts(o, a, s1, s2, f1, f2, r, w, n=10, x=False, c=1):
+        if f2 is None:
+            op("v", lambda e: e.tensor_scalar(o, a, s1, None, f1), r, w, us(n, c, x))
+        else:
+            op("v", lambda e: e.tensor_scalar(o, a, s1, s2, f1, f2), r, w, us(n, c, x))
+
+    def lin(o, a, m, b, r, w, n=10, x=False):
+        ts(o, a, float(m), float(b), OP.mult, OP.add, r, w, n, x)
+
+    def cp(o, a, r, w, q="v", n=10, x=False, c=1):
+        fns = {"v": lambda e: e.tensor_copy(o, a), "a": lambda e: e.activation(o, a, AF.Copy)}
+        node({k: fns[k] for k in q}, {k: us(n, c if k == "v" else 1, x) for k in q}, 0.0, r, w, None, 1)
+
+    def scaled(o, a, m, r, w, q, n, c=1):
+        fns = {"v": lambda e: e.tensor_scalar(o, a, m, None, OP.mult), "a": lambda e: e.activation(o, a, AF.Copy, scale=m)}
+        node({k: fns[k] for k in q}, {k: us(n, c if k == "v" else 1, False) for k in q}, 0.0, r, w, None, 1)
+
+    def tr(o, a, r, w, n, c=1):
+        op("v", lambda e: e.transpose(o, a), r, w, us(n, c, False))
+
+    def scan(o, d0, d1, f0, f1, r, w, n=160):
+        op("v", lambda e: e.tensor_tensor_scan(o, d0, d1, BIG, f0, f1), r, w, us(n, 1, False))
+
+    def mm(bank, n, lq, lsc, rq, rsc, r):
+        op("t", lambda e: e.matmul_mx(T.ps[:, 512 * bank:512 * bank + n], lq, lsc, rq, rsc, True, True), r, ["b%d" % bank], (n + 16) * 0.0011)
+
+    def fill(o, c, w, n=10):
+        op("v", lambda e: e.memset(o, c), [], w, us(n, 1, False))
+
+    def quant(q, s, t, r, w, n=640):
+        op("v", lambda e: e.quantize_mx(q, s, t), r, w, 0.012 + n * 0.00028)
+
+    def arrange():
+        n = len(nodes)
+        tail = [0.0] * n
+        out = [[] for _ in range(n)]
+        for i, d in enumerate(nodes):
+            for p in d["order"]:
+                out[p].append(i)
+        for i in range(n - 1, -1, -1):
+            d = nodes[i]
+            tail[i] = min(d["cost"].values()) + d["late"] + max([tail[k] + WAKE for k in out[i]] + [0.0])
+        left = [len(d["order"]) for d in nodes]
+        ready = [0.0] * n
+        open_ = [i for i in range(n) if left[i] == 0]
+        free, order = {}, []
+        while open_:
+            cand = []
+            for i in open_:
+                d = nodes[i]
+                for q in d["cost"]:
+                    s = max(free.get(q, 0.0), ready[i])
+                    extra = SPARE if q == "v" and len(d["cost"]) > 1 else 0.0
+                    cand.append((s, i, q, extra))
+            best = {}
+            for s, i, q, extra in cand:
+                e = s + nodes[i]["cost"][q] + extra
+                if i not in best or e < best[i][0]:
+                    best[i] = (e, s, q)
+            s0, i0 = min((v[1], i) for i, v in best.items())
+            q0 = best[i0][2]
+            same = [(i, v[1]) for i, v in best.items() if v[2] == q0]
+            i = max([k for k in same if k[1] <= s0 + 1e-9], key=lambda k: tail[k[0]])[0]
+            c = nodes[i]["cost"][q0]
+            soon = [k for k in same if k[1] < s0 + LOOK * c and tail[k[0]] > tail[i]]
+            if soon:
+                i = max(soon, key=lambda k: tail[k[0]])[0]
+            e, s, q = best[i]
+            open_.remove(i)
+            free[q] = s + nodes[i]["cost"][q]
+            order.append((s, len(order), i, q))
+            for k in out[i]:
+                left[k] -= 1
+                ready[k] = max(ready[k], free[q] + nodes[i]["late"] + WAKE)
+                if left[k] == 0:
+                    open_.append(k)
+        return [(i, q) for s, m, i, q in order]
+
+    total, waited = {}, {}
+
+    def need(q, deps):
+        for sem in sorted(deps):
+            if waited.get((q, sem), 0) < deps[sem]:
+                waited[(q, sem)] = deps[sem]
+                Q[q].wait_ge(T.sem[sem], deps[sem])
+
+    def issue():
+        done = {}
+        for i, q in arrange():
+            d = nodes[i]
+            deps = {}
+            for p in d["pre"]:
+                sem, v = done[p]
+                deps[sem] = max(deps.get(sem, 0), v)
+            need(q, deps)
+            inst = d["fns"][q](Q[q])
+            sem = d["sem"] or SEM[q]
+            if d["sem"] is None:
+                inst.then_inc(T.sem[sem], 1)
+            total[sem] = total.get(sem, 0) + d["inc"]
+            done[i] = (sem, total[sem])
+
+    def bank(b, n):
+        return T.ps[:, 512 * b:512 * b + n]
+
+    mask1, rst1 = T.mask[:, 0:160], T.rs[:, 0:160]
+
+    for h in (0, 1):
+        dma("s", [(T.x0[:, quad(h)], T.x[:, quad(h)])], [], ["x0%d" % h], "dx%d" % h)
+    dma("a", [(T.ub[:], T.u[:])], [], ["ub"], "du")
+    for k, s in enumerate((6, 0, 7, 1, 2, 3, 4, 5)):
+        pairs = []
+        for a in range(4):
+            side, gr = table_of(a, s)
+            src = (T.lam if side == "l" else T.rho)[16 * gr:16 * gr + 16, :]
+            for b in (0, 1):
+                p = 16 * (2 * a + b)
+                pairs.append((T.nl[p:p + 16, 40 * s:40 * s + 40], src))
+        dma("s" if k % 2 == 0 else "a", pairs, [], ["nl%d" % s], "dn%d" % s)
+    dma("s", [(T.wq[:].bitcast(dt.uint8), T.wc[:]), (T.wsp[:], T.ws[:])], [], ["wq"], "dw")
+    dma("s", [(T.lni[:, 0:40], T.lam[:]), (T.lni[:, 40:80], T.rho[:])], [], ["lni"], "dl")
+    dma("s", [(T.vb[:], T.v[:])], [], ["vb"], "dv")
+
+    def iota(o, pattern, base, cm, w, fl=False):
+        n = 1
+        for step, count in pattern:
+            n *= count
+        if fl:
+            op("g", lambda e: e.iota(o, pattern, base, cm, allow_small_or_imprecise_dtypes=True), [], w, 0.15 + 0.002 * n)
+        else:
+            op("g", lambda e: e.iota(o, pattern, base, cm), [], w, 0.15 + 0.002 * n)
+
+    iota(T.qi[:, 0:4], [[0, 4]], 0, 1, ["qi"])
+    iota(T.uf[:, 0:4], [[2, 4]], 0, 0, ["ufa"], True)
+    iota(T.uf[:, 4:8], [[32, 4]], 96, 0, ["ufb"], True)
+    iota(T.ui[:, 0:48], [[-16, 6], [32, 4], [0, 2]], 97, 0, ["ui"])
+    iota(T.w4[:], [[4, 320]], 1280, 0, ["w4"], True)
+    iota(T.jj[:], [[1, 320]], 128, -1, ["jj"])
+    iota(T.jk[:], [[1, 320]], 0, 0, ["jk"])
+    for a in range(4):
+        iota(T.cid[32 * a:32 * a + 32, 0:10], [[128, 10]], 1280, 4, ["cid%d" % a], True)
+    CID = ["cid%d" % a for a in range(4)]
+    iota(T.cli[:, 0:10], [[1, 10]], 0, 0, ["cl16"])
+    iota(T.cli[:, 32:52], [[1, 10], [0, 2]], 0, 0, ["cl32"])
+
+    ts(T.qi[:, 4:8], T.qi[:, 0:4], 15, None, OP.bitwise_and, None, ["qi"], ["qa"])
+    q4 = T.qf[:, 0:4]
+    cp(q4, T.qi[:, 4:8], ["qa"], ["q4"])
+    qe = T.qf[:, 20:24]
+    ts(T.qf[:, 24:28], q4, 10.0, -10.0, OP.is_ge, OP.mult, ["q4"], ["q_t"])
+    tt(qe, q4, T.qf[:, 24:28], OP.add, ["q4", "q_t"], ["qe"])
+    tt(T.qf[:, 4:8], qe, T.uf[:, 0:4], OP.is_lt, ["qe", "ufa"], ["q_m"])
+    ts(T.qf[:, 8:12], qe, -16.0, None, OP.mult, None, ["qe"], ["q_r"])
+    tt(T.qf[:, 8:12], T.qf[:, 8:12], T.uf[:, 4:8], OP.add, ["q_r", "ufb"], ["q_r"])
+    lin(T.qf[:, 12:16], qe, 16, 16, ["qe"], ["q_l"])
+    tt(T.qf[:, 12:16], T.qf[:, 12:16], T.qf[:, 8:12], OP.subtract, ["q_l", "q_r"], ["q_l"])
+    tt(T.qf[:, 12:16], T.qf[:, 12:16], T.qf[:, 4:8], OP.mult, ["q_l", "q_m"], ["q_l"])
+    tt(T.qf[:, 8:12], T.qf[:, 8:12], T.qf[:, 12:16], OP.add, ["q_r", "q_l"], ["q_r"])
+    ts(T.qf[:, 16:20], qe, 6.0, None, OP.is_lt, None, ["qe"], ["q_6"])
+    tt(T.qf[:, 8:12], T.qf[:, 8:12], T.qf[:, 16:20], OP.mult, ["q_r", "q_6"], ["q_r"])
+    ts(T.qf[:, 28:32], q4, 10.0, None, OP.is_ge, None, ["q4"], ["q_10"])
+    tt(T.qf[:, 8:12], T.qf[:, 8:12], T.qf[:, 28:32], OP.add, ["q_r", "q_10"], ["q_r"])
+    for k, (c, spec) in enumerate(((4, ((7, 112.0), (8, 1.0), (9, 113.0))), (1, ((6, 112.0), (8, 113.0), (9, 1.0))))):
+        o = 32 + 32 * k
+        for j, (q, val) in enumerate(spec):
+            ts(T.qf[:, o + 4 * j:o + 4 * j + c], T.qf[:, 0:c], float(q), val, OP.is_equal, OP.mult, ["q4"], ["qs%d%d" % (k, j)])
+        tt(T.qf[:, o:o + c], T.qf[:, o:o + c], T.qf[:, o + 4:o + 4 + c], OP.add, ["qs%d0" % k, "qs%d1" % k], ["qs%d0" % k])
+        tt(T.qf[:, o:o + c], T.qf[:, o:o + c], T.qf[:, o + 8:o + 8 + c], OP.add, ["qs%d0" % k, "qs%d2" % k], ["qs%d0" % k])
+    cp(T.qf[:, 32:33], T.qf[:, 64:65], ["qs10", "qs00"], ["qs00"])
+    tt(T.qf[:, 8:12], T.qf[:, 8:12], T.qf[:, 32:36], OP.add, ["q_r", "qs00"], ["q_r"])
+    cp(T.uoff[:, 0:8:2], T.qf[:, 8:12], ["q_r"], ["uoff0"])
+    cp(T.uoff[:, 1:8:2], T.qf[:, 8:12], ["q_r"], ["uoff1"])
+    quant(T.uq[:, 0:128], T.us[:, 0:128], T.ub[:, 0:512], ["ub"], ["uq"])
+    cp(T.utq[:, 0:128].bitcast(dt.uint32), T.uq[:, 0:128].bitcast(dt.uint32).indirect(T.uoff[:, 0:8]), ["uq", "uoff0", "uoff1"], ["utq"], n=128, x=True)
+    cp(T.uts[:, 0:128], T.us[:, 0:128].indirect(T.uoff[:, 0:8]), ["uq", "uoff0", "uoff1"], ["uts"], "av", n=128, x=True)
+
+    ts(T.jj[:], T.jj[:], 15, None, OP.bitwise_and, None, ["jj"], ["jj"], n=320)
+    ts(T.mask[:], T.jj[:], 0.0, None, OP.is_equal, None, ["jj"], ["mask"], n=320)
+    ts(T.jk[:], T.jk[:], 15, None, OP.bitwise_and, None, ["jk"], ["jk"], n=320)
+    ts(T.rs[:], T.jk[:], 0.0, BIG, OP.is_gt, OP.mult, ["jk"], ["rs"], n=320)
+
+    def list_of(s):
+        cp(T.nlu[:, 40 * s:40 * s + 40], T.nl[:, 40 * s:40 * s + 40], ["nl%d" % s], ["nlu%d" % s])
+
+    def window(s):
+        cp(T.tw[:, 640 * s:640 * s + 640], T.w4[:].indirect(T.nlu[:, 40 * s:40 * s + 40]), ["w4", "nlu%d" % s], ["tw%d" % s], "av", n=640, x=True)
+
+    for s in (6, 0, 7, 1, 2, 3, 4, 5):
+        list_of(s)
+        window(s)
+    iota(T.cw[:], [[0, 6], [32, 20]], 0, 0, ["cw"], True)
+    ts(T.qf[:, 96:97], T.qf[:, 0:1], 2.0, None, OP.mult, None, ["q4"], ["q2"])
+    ts(T.cw[:], T.cw[:], T.qf[:, 96:97], None, OP.add, None, ["cw", "q2"], ["cw"], n=120)
+    lin(T.cx[:], T.cw[:], 1, 1, ["cw"], ["cx"], n=120)
+    for h in (0, 1):
+        quant(T.qx0[:, cols(h)], T.sx0[:, cols(h)], T.x0[:, quad(h)], ["x0%d" % h], ["qx0%d" % h], 4 * WID[h])
+    for k in range(3):
+        w = 320 if k < 2 else 160
+        cp(T.rb[:, 320 * k:320 * k + w], T.rs[:, 0:w], ["rs"], ["rb%d" % s for s in ((1, 2), (3, 4), (5,))[k]], "av", n=w)
+    cp(T.clu[:, 0:10], T.cli[:, 0:10], ["cl16"], ["c16"])
+    cp(T.clu[:, 32:52], T.cli[:, 32:52], ["cl32"], ["c32"])
+    cp(T.lt0[0:32, 0:10], T.cid[0:32, 0:10], CID, ["lt0_0"])
+    cp(T.lt1[96:128, 0:10], T.cid[96:128, 0:10], CID, ["lt1_3"])
+    fill(T.ones[:], 1.0, ["ones"], n=256)
+
+    def one_in(b):
+        op("g", lambda e: e.affine_select(T.et[:, 512 * b:512 * b + 512], T.ones[:], [[1, 512]], OP.is_equal, 0.0, -b, -4), ["ones"], ["et%d" % b], 1.2)
+
+    for b in range(4):
+        one_in(b)
+
+    def half_x(k, h):
+        x = T["x%d" % k]
+        for t in range(4):
+            scaled(T.xh[:, 320 * t + AT[h]:320 * t + AT[h] + WID[h]], x[:, quad(h, t, 4)], 0.5, state_parts(k, h)[t % len(state_parts(k, h)):][:1],
+                   ["xh%d%d" % (h, t)], "av", WID[h], 0.5)
+        scaled(T.xg[:, quad(h)], x[:, quad(h)], 0.5, state_parts(k, h), ["xg%d" % h], "av", 4 * WID[h], 0.5)
+
+    def state_parts(k, h):
+        return ["x0%d" % h] if k == 0 else ["xn%d%d%d" % (k, h, t) for t in range(4)]
+
+    half_x(0, 0)
+    half_x(0, 1)
+
+    def scores(k, h):
+        mm(h, WID[h], T.utq[:], T.uts[:], T["qx%d" % k][:, cols(h)], T["sx%d" % k][:, cols(h)], ["utq", "uts", "qx%d%d" % (k, h)])
+        tr(T.st[:, cols(h)], bank(h, WID[h]), ["b%d" % h], ["st%d" % h], WID[h])
+
+    ST = ["st0", "st1"]
+
+    def row(q):
+        return T.st[:, q:320:32]
+
+    def tmp(k):
+        return T.tmp[:, 16 * k:16 * k + 10]
+
+    def rstart(s):
+        return T.rb[:, 160 * (s - 1):160 * s:16]
+
+    def sign(s, j):
+        o, i, sg = T.nw[:, 640 * s + 320 * j:640 * s + 320 * j + 320], bank(2 + s, 320), (T.sgn, T.sgc)[j][:, s:s + 1]
+        eps = EPS if j else -EPS
+        op("a", lambda e: e.activation(o, i, AF.Sign, bias=eps, scale=sg), ["b%d" % (2 + s), "sgc"], ["nw%d%d" % (s, j)], 0.33)
+
+    def flips(k):
+        for s in range(6):
+            mm(2 + s, 320, T.ufq[:, 128 * s:128 * s + 128], T.ufs[:, 128 * s:128 * s + 128], T["qx%d" % k][:], T["sx%d" % k][:], ["ufq", "ufs", "qx%d0" % k, "qx%d1" % k])
+        for s in range(6):
+            sign(s, 0)
+            sign(s, 1)
+
+    def turn_windows():
+        for s in range(6):
+            ts(T.fb[:, 10 * s:10 * s + 10], row(10 + s), T.sgc[:, s:s + 1], 0.0, OP.mult, OP.is_lt, ST + ["sgc"], ["fb%d" % s])
+        pairs = []
+        for a in range(4):
+            for b in (0, 1):
+                for c in (0, 1):
+                    p, q = 32 * a + 16 * b, 32 * a + 16 * c
+                    pairs.append((T.fx[q:q + 16, 60 * b:60 * b + 60], T.fb[p:p + 16, :]))
+        dma("s", pairs, ["fb%d" % s for s in range(6)], ["fx"], "dfx")
+        for k, (base, f) in enumerate(((T.cw, OP.add), (T.cx, OP.subtract))):
+            for b in (0, 1):
+                tt(T.fl[:, 120 * k + b:120 * k + 120:2], base[:, b:120:2], T.fx[:, 60 * b:60 * b + 60], f, ["fx", "cw", "cx"], ["fl%d%d" % (k, b)], n=60)
+            cp(T.flu[:, 128 * k:128 * k + 120], T.fl[:, 120 * k:120 * k + 120], ["fl%d0" % k, "fl%d1" % k], ["flu%d" % k], n=120)
+        for s in range(6):
+            for k in (0, 1):
+                cp(T.tx[:, 640 * s + k:640 * s + 640:2], T.tw[:, 640 * s:640 * s + 640].indirect(T.flu[:, 128 * k + 20 * s:128 * k + 20 * s + 20]),
+                   ["flu%d" % k, "tw%d" % s], ["tx%d%d" % (s, k)], "av", n=320, x=True)
+
+    def direct(n, rd):
+        dv = (T.dva, T.dvb)[n][:, 0:10]
+        name = ("dva", "dvb")[n]
+        o = 5 * n
+        if rd == 1:
+            ts(tmp(o), row(6 + n), 0.0, 2.0, OP.is_gt, OP.mult, ST, ["t%d" % o])
+            tt(tmp(o), tmp(o), T.cid[:, 0:10], OP.add, ["t%d" % o] + CID, ["t%d" % o])
+            lin(T.nu[:, 96 + 16 * n:106 + 16 * n], tmp(o), 0.5, -640, ["t%d" % o], ["nu%d" % (6 + n)])
+            tt(T.ye[:, 160 * n:160 * n + 160], T.tw[:, 640 * (6 + n):640 * (7 + n)].indirect(T.nu[:, 96 + 16 * n:106 + 16 * n]), mask1, OP.mult,
+               ["tw%d" % (6 + n), "nu%d" % (6 + n), "mask"], ["ye%d" % n], n=160, x=True)
+            scan(T.yes[:, 160 * n:160 * n + 160], rst1, T.ye[:, 160 * n:160 * n + 160], OP.min, OP.add, ["rs", "ye%d" % n], ["yes%d" % n])
+            cp(dv, T.yes[:, 160 * n + 15:160 * n + 160:16], ["yes%d" % n], [name])
+        else:
+            e, d = (T.ea, T.eb)[n][:, 0:10], (T.da, T.db)[n][:, 0:10]
+            ts(tmp(o), row(6 + n), 0.0, None, OP.is_gt, None, ST, ["t%d" % o])
+            ts(tmp(o + 1), row(8 + n), T.sgc[:, 6 + n:7 + n], 0.0, OP.mult, OP.is_lt, ST + ["sgc"], ["t%d" % (o + 1)])
+            tt(tmp(o + 2), tmp(o), tmp(o + 1), OP.not_equal, ["t%d" % o, "t%d" % (o + 1)], ["t%d" % (o + 2)])
+            tt(tmp(o + 2), tmp(o + 2), d, OP.mult, ["t%d" % (o + 2), "d%d" % n], ["t%d" % (o + 2)])
+            tt(dv, e, tmp(o + 2), OP.add, ["e%d" % n, "t%d" % (o + 2)], [name])
+
+    def turn_direct(n):
+        o = 5 * n
+        e, d = (T.ea, T.eb)[n][:, 0:10], (T.da, T.db)[n][:, 0:10]
+        tt(tmp(o + 3), tmp(o + 1), d, OP.mult, ["t%d" % (o + 1), "d%d" % n], ["t%d" % (o + 3)])
+        tt(e, e, tmp(o + 3), OP.add, ["e%d" % n, "t%d" % (o + 3)], ["e%d" % n])
+        tt(d, d, tmp(o + 3), OP.subtract, ["d%d" % n, "t%d" % (o + 3)], ["d%d" % n])
+        tt(d, d, tmp(o + 3), OP.subtract, ["d%d" % n, "t%d" % (o + 3)], ["d%d" % n])
+
+    def spread(j):
+        o, win, lst = (T.bc0, T.bc1)[j][:], (T.lt0, T.lt1)[j][:, 0:10], T.clu[:, 32:52]
+        node({"v": lambda e: e.tensor_scalar(o, win.indirect(lst), 0.25, -480.0, OP.mult, OP.add),
+              "a": lambda e: e.activation(o, win.indirect(lst), AF.Copy, bias=-480.0, scale=0.25)},
+             {"v": us(320, 1, True), "a": us(320, 1, True)}, 0.0, ["c32"] + ["lt%d_%d" % (j, a) for a in range(4)], ["bc%d" % j], None, 1)
+        tr(T.lw[:, 320 * j:320 * j + 320], o, ["bc%d" % j], ["lw%d" % j], 320, 0.5)
+
+    def lu(s):
+        return T.lu[:, 16 * s:16 * s + 10]
+
+    def walk(rd):
+        fl = rd > 1
+        rsc, cm, cb = (1280.0, 0.25, -320) if fl else (2.0, 0.5, -640)
+
+        def bits(s):
+            ts(rstart(s), row(s), 0.0, rsc, OP.is_gt, OP.mult, ST, ["rb%d" % s])
+
+        direct(0, rd)
+        ts(tmp(10), row(0), 0.0, rsc, OP.is_gt, OP.mult, ST, ["t10"])
+        tt(tmp(10), tmp(10), T.dva[:, 0:10], OP.add, ["t10", "dva"], ["t10"])
+        lin(lu(0), tmp(10), cm, cb, ["t10"], ["lu0a"])
+        if fl:
+            tt(T.y2i[:], T.dva[:, 0:10].indirect(T.clu[:, 0:10]), mask1, OP.mult, ["dva", "c16", "mask"], ["y2i"], n=160, x=True)
+        tabs = T.tx if rd == 3 else T.tw
+        for s in range(6):
+            L = ["lu%d%s" % (s, c) for c in "abc"]
+            prev = "y2i" if s == 0 else "y2%d" % (s - 1)
+            if fl:
+                pv = T.y2i[:] if s == 0 else T.y2[:, 160 * (s - 1):160 * s]
+                tt(T.y1[:], T.nw[:, 640 * s:640 * s + 640].indirect(lu(s)), pv, OP.add, L + ["nw%d0" % s, "nw%d1" % s, prev, prev + "x"], ["y1"], n=160, x=True)
+            if s < 5:
+                bits(s + 1)
+            if fl:
+                scan(T.y1s[:], rst1, T.y1[:], OP.min, OP.max, ["rs", "y1"], ["y1s"])
+                nu = T.nu[:, 16 * s:16 * s + 10]
+                lin(nu, T.y1s[:, 15:160:16], 0.5, -639.5, ["y1s"], ["nu%d" % s])
+                L, lst = ["nu%d" % s], nu
+            else:
+                lst = lu(s)
+            y2, y2s = T.y2[:, 160 * s:160 * s + 160], T.y2s[:, 160 * s:160 * s + 160]
+            tt(y2, tabs[:, 640 * s:640 * s + 640].indirect(lst), mask1, OP.mult, L + (["tx%d0" % s, "tx%d1" % s] if rd == 3 else ["tw%d" % s]) + ["mask"],
+               ["y2%d" % s, "y2%dx" % s], n=160, x=True)
+            rs = T.rb[:, 160 * s:160 * s + 160] if s < 5 else rst1
+            scan(y2s, rs, y2, OP.min, OP.add, ["y2%d" % s, "y2%dx" % s, "rb%d" % (s + 1), "rs"], ["y2s%d" % s])
+
+            def last(lo, hi):
+                return T.y2s[lo:hi, 160 * s + 15:160 * s + 160:16]
+
+            def rst(lo, hi):
+                return T.rb[lo:hi, 160 * s:160 * s + 160:16]
+
+            if s < 5:
+                n = 16 * (s + 1)
+                for k, (lo, hi) in enumerate({1: ((0, 32), (64, 128)), 3: ((0, 64), (96, 128))}.get(s, ((0, 128),))):
+                    lin(T.lu[lo:hi, n:n + 10], last(lo, hi), cm, cb, ["y2s%d" % s], ["lu%d%s" % (s + 1, "ab"[k])])
+            if s in (1, 3) and fl:
+                lo = 32 if s == 1 else 64
+                cp(T.y2[lo:lo + 32, 160 * s:160 * s + 160], T.y2b[lo:lo + 32, :], ["y2b", "y2%d" % s], ["y2%dx" % s], n=160)
+            lo = 32 * (1 + s // 2)
+            lt = (T.lt0, T.lt1)[s % 2]
+            if s < 5:
+                tt(lt[lo:lo + 32, 0:10], last(lo, lo + 32), rst(lo, lo + 32), OP.subtract, ["y2s%d" % s, "rb%d" % (s + 1)], ["lt%d_%d" % (s % 2, lo // 32)])
+            if s == 0:
+                direct(1, rd)
+                cp(T.lt1[0:32, 0:10], T.dvb[0:32, 0:10], ["dvb"], ["lt1_0"])
+                lin(T.mlu[96:128, 0:20:2], T.dvb[96:128, 0:10], 0.25, -320, ["dvb"], ["ml_e3"])
+                if fl:
+                    tt(T.y2b[:], T.dvb[:, 0:10].indirect(T.clu[:, 0:10]), mask1, OP.mult, ["dvb", "c16", "mask"], ["y2b"], n=160, x=True)
+            if s in (0, 2):
+                k = s + 2
+                lo = 16 * k
+                if k == 2:
+                    ts(tmp(11), row(2), 0.0, rsc, OP.is_gt, OP.mult, ST, ["t11"])
+                else:
+                    ts(tmp(11), row(4), 0.0, rsc, OP.is_gt, OP.mult, ST, ["t11"])
+                tt(tmp(11), tmp(11), T.dvb[:, 0:10], OP.add, ["t11", "dvb"], ["t11"])
+                lin(T.lu[lo:lo + 32, 16 * k:16 * k + 10], T.tmp[lo:lo + 32, 176:186], cm, cb, ["t11"], ["lu%dc" % k])
+            if s == 4:
+                tt(T.tmp[0:96, 192:202], last(0, 96), rst(0, 96), OP.subtract, ["y2s4", "rb5"], ["t12"])
+                ts(T.mlu[0:96, 1:20:2], T.tmp[0:96, 192:202], 0.25, None, OP.mult, None, ["t12"], ["ml_o"])
+            if s in (3, 4):
+                spread(4 - s)
+            if s == 5:
+                ts(T.mlu[96:128, 1:20:2], last(96, 128), 0.25, None, OP.mult, None, ["y2s5"], ["ml_o3"])
+                lin(T.mlu[0:96, 0:20:2], last(0, 96), 0.25, -320, ["y2s5"], ["ml_e"])
+        cp(T.km[:], T.lw[:].indirect(T.mlu[:, 0:20]), ["lw0", "lw1", "ml_e", "ml_o", "ml_e3", "ml_o3"], ["km"], n=320, x=True)
+        tr(T.kt[:], T.km[:], ["km"], ["kt"], 320, 0.5)
+        lin(T["kl%d" % rd][:], T.kt[:, 0:320:16], 1, 160, ["kt"], ["kl%d" % rd])
+
+    sent = [0]
+
+    def send(rd, what, h):
+        dst = T.cores[rank ^ STEP[rd - 1]]
+        def put(fn, cost, late, land, sem, inc, own):
+            sent[0] += own
+            node({"g": fn}, {"g": cost}, late, ["kl%d" % rd if what == "k" else "qh%d%d" % (rd, h)], [land], sem, inc)
+
+        q, s, lq, ls = T["qh%d" % rd], T["sh%d" % rd], T["lq%d" % rd], T["ls%d" % rd]
+        if topo.may_write(core, dst):
+            rid, pid = topo.addr(dst, core)
+            m, n = topo.mask(core, dst), len(topo.engines(core, dst))
+            if what == "k":
+                put(lambda e: e.remote_dma(T["kr%d" % rd][:], T["kl%d" % rd][:], T.sem["kr%d" % rd], T.sem.lsem, pid, rid, m), 1.0, 2.5, "kr%d" % rd, "kr%d" % rd, n, n)
+                return
+            c = cols(h)
+            sem = T.sem["ar%d%d" % (rd, h)]
+
+            def go(e):
+                e.remote_dma(lq[:, c].bitcast(dt.uint8), q[:, c].bitcast(dt.uint8), sem, T.sem.lsem, pid, rid, m)
+                e.remote_dma(ls[:, c], s[:, c], sem, T.sem.lsem, pid, rid, m)
+
+            put(go, 2.0, 4.0, "lq%d%d" % (rd, h), "ar%d%d" % (rd, h), 2 * n, 2 * n)
+            return
+        rel = relays_of(core, dst, topo)
+        ways = [topo.addr(k, core) for k in rel]
+        eng = topo.engines(core, rel[0])
+        n = len(eng) // 2
+        masks = [bits_of(eng[:n]), bits_of(eng[n:])]
+        far = len(topo.engines(rel[0], dst))
+        if what == "k":
+            put(lambda e: e.remote_dma(T.rlk[:], T["kl%d" % rd][:], T.sem.rk, T.sem.lsem, ways[0][1], ways[0][0], masks[0]), 1.0, 5.0, "kr%d" % rd, "kr%d" % rd, far, n)
+            return
+
+        w = WID[h] // 2
+
+        def both_ways(e, view, land, sem):
+            tr_ = []
+            for k in (0, 1):
+                a = AT[h] + w * k
+                tr_.append(RemoteDMATransfer(dst_ids=[DstId(rid=ways[k][0], pnc=ways[k][1])], dma_engine_mask=masks[k], remote_sem=sem,
+                                             src=view(a), dst=land(a)))
+            e.remote_dma_fused(tr_, local_sem=T.sem.lsem)
+
+        def go2(e):
+            both_ways(e, lambda a: q[:, a:a + w].bitcast(dt.uint8), lambda a: T.rlq[:, a:a + w].bitcast(dt.uint8), T.sem["ry%d" % h])
+            both_ways(e, lambda a: s[:, a:a + w], lambda a: T.rls[:, a:a + w], T.sem["rz%d" % h])
+
+        put(go2, 2.0, 6.0, "lq%d%d" % (rd, h), "ar%d%d" % (rd, h), 4 * far, 4 * n)
+
+    def meet(rd, h):
+        for t in range(4):
+            tt(T.vt[:, quad(h, t, 4)], T.xh[:, 320 * t:320 * t + 320].indirect(T["kl%d" % rd][:, part(h)]), T.xg[:, quad(h, t, 4)], OP.add,
+               ["xh0%d" % t, "xh1%d" % t, "xg%d" % h, "kl%d" % rd] + ["@v"] * h, ["vt%d%d" % (h, t)], n=WID[h], x=True)
+
+    def layer(h):
+        c = cols(h)
+        for b in range(4):
+            mm(4 * h + b, WID[h], T.wq[:, 128 * b:128 * b + 128], T.wsp[:, 128 * b:128 * b + 128], T.qv[:, c], T.qvs[:, c], ["wq", "qv%d" % h])
+
+    def layer_out(h, b, q):
+        scaled(T.ht[:, quad(h, b, 4)], bank(4 * h + b, WID[h]), 0.03125, ["b%d" % (4 * h + b)], ["ht%d%d" % (h, b)], q, WID[h])
+
+    def quant_v(h):
+        quant(T.qv[:, cols(h)], T.qvs[:, cols(h)], T.vt[:, quad(h)], ["vt%d%d" % (h, t) for t in range(4)], ["qv%d" % h] + ["@v"] * (1 - h), 4 * WID[h])
+
+    def quant_h(rd, h):
+        quant(T["qh%d" % rd][:, cols(h)], T["sh%d" % rd][:, cols(h)], T.ht[:, quad(h)], ["ht%d%d" % (h, b) for b in range(4)], ["qh%d%d" % (rd, h)], 4 * WID[h])
+
+    def natural(k, rd):
+        mm(0, 320, T.uq[:], T.us[:], T["qx%d" % k][:], T["sx%d" % k][:], ["uq", "qx%d0" % k, "qx%d1" % k])
+        cp(T.sn[:], bank(0, 320), ["b0"], ["sn"], "av", n=320)
+        dma("s", [(T.fn[:], T.sn[1:128:16, :])], ["sn"], ["fn"], "fn%d" % rd)
+
+    def turn_tables(final=False):
+        for k, (tab, f) in enumerate(((T.ltb, OP.is_lt), (T.rtb, OP.is_gt))):
+            n = "lr%d" % k
+            a, d, z = T.lt2[:, 32 * k:32 * k + 20], T.ld[:, 32 * k:32 * k + 20], T.lz[:, 32 * k:32 * k + 20]
+            e0, e1 = tab[:, 0:40:2], tab[:, 1:40:2]
+            o = T.lout[:, 40 * k:40 * k + 40] if final else tab
+            tt(d, e1, e0, OP.subtract, [n + "a", n + "b"], [n + "d"])
+            ts(a, T.fn[:], 0.0, None, f, None, ["fn"], [n + "t"])
+            tt(z, d, a, OP.mult, [n + "d", n + "t"], [n + "z"])
+            tt(o[:, 0:40:2], e0, z, OP.add, [n + "a", n + "z"], [("lo%da" % k) if final else n + "a"])
+            tt(o[:, 1:40:2], e1, z, OP.subtract, [n + "b", n + "z"], [("lo%db" % k) if final else n + "b"])
+
+    for h in (0, 1):
+        scores(0, h)
+    for rd in (1, 2, 3):
+        walk(rd)
+        send(rd, "k", 0)
+        meet(rd, 0)
+        quant_v(0)
+        layer(0)
+        for b in range(4):
+            layer_out(0, b, "av")
+        meet(rd, 1)
+        quant_v(1)
+        layer(1)
+        quant_h(rd, 0)
+        send(rd, "h", 0)
+        for b in range(4):
+            layer_out(1, b, "av")
+        quant_h(rd, 1)
+        send(rd, "h", 1)
+        if rd == 1:
+            quant(T.eq[:], T.es[:], T.et[:], ["et%d" % b for b in range(4)], ["eq"], n=2048)
+            for s in range(6):
+                fill(T.ui[:, 8 * s + 2 * (s // 2 + 1):8 * s + 8], 16 * (s + 1) + 1, ["ui"])
+            cp(T.uoff[:, 8:56], T.ui[:, 0:48], ["ui"], ["uoff2"])
+            fill(T.sgc[:], 1.0, ["sgc"])
+            for hi, lo in ((32, 0), (64, 2), (96, 4)):
+                fill(T.sgc[0:hi, lo:6], -1.0, ["sgc"])
+            fill(T.sgc[0:32, 6:7], -1.0, ["sgc"])
+            fill(T.sgc[32:64, 7:8], -1.0, ["sgc"])
+            fill(T.sgc[64:128, 7:8], -1.0, ["sgc"])
+            ts(T.sgn[:], T.sgc[:], -1.0, None, OP.mult, None, ["sgc"], ["sgc"])
+            cp(T.ufq[:].bitcast(dt.uint32), T.uq[:, 0:128].bitcast(dt.uint32).indirect(T.uoff[:, 8:56]), ["uq", "uoff2"], ["ufq"], n=768, x=True)
+            cp(T.ufs[:], T.us[:, 0:128].indirect(T.uoff[:, 8:56]), ["uq", "uoff2"], ["ufs"], "av", n=768, x=True)
+            for n in (0, 1):
+                for c in (0, 1):
+                    k = 2 * n + c
+                    if n == 0:
+                        lin(T.lu[:, 96 + 16 * c:106 + 16 * c], T.cid[:, 0:10], 0.5, -640 + c, CID, ["lc%d" % c])
+                    tt(T.ye[:, 160 * k:160 * k + 160], T.tw[:, 640 * (6 + n):640 * (7 + n)].indirect(T.lu[:, 96 + 16 * c:106 + 16 * c]), mask1, OP.mult,
+                       ["tw%d" % (6 + n), "lc%d" % c, "mask"], ["ye%d" % k], n=160, x=True)
+                    scan(T.yes[:, 160 * k:160 * k + 160], rst1, T.ye[:, 160 * k:160 * k + 160], OP.min, OP.add, ["rs", "ye%d" % k], ["yes%d" % k])
+                e, d = (T.ea, T.eb)[n][:, 0:10], (T.da, T.db)[n][:, 0:10]
+                first, second = T.yes[:, 320 * n + 15:320 * n + 160:16], T.yes[:, 320 * n + 175:320 * n + 320:16]
+                cp(e, first, ["yes%d" % (2 * n)], ["e%d" % n])
+                tt(d, second, first, OP.subtract, ["yes%d" % (2 * n), "yes%d" % (2 * n + 1)], ["d%d" % n])
+            cp(T.lnu[:], T.lni[:], ["lni"], ["lnu"], n=80)
+        elif rd == 2:
+            turn_direct(0)
+            turn_direct(1)
+        kl, kr = T["kl%d" % rd], T["kr%d" % rd]
+        cp(T.kw[:], T.w4[:].indirect(kr[:]), ["w4", "kr%d" % rd], ["kw"], "av", n=320, x=True)
+        tt(T.ky[:], T.kw[:].indirect(kl[:]), T.mask[:], OP.mult, ["kw", "kl%d" % rd, "mask"], ["ky"], n=320, x=True)
+        scan(T.kys[:], T.rs[:], T.ky[:], OP.min, OP.add, ["ky", "rs"], ["kys"], n=320)
+        lin(T.mo[:, 0:20], T.kys[:, 15:320:16], 0.25, -320, ["kys"], ["mo"])
+        if rd == 1:
+            for k, tgt in ((0, T.lrow), (1, T.rrow)):
+                cp(tgt[:], T.w4[:].indirect(T.lnu[:, 40 * k:40 * k + 40]), ["w4", "lnu"], ["row%d" % k], "av", n=640, x=True)
+                dma("s", [((T.ltb, T.rtb)[k][:], tgt[0:128:16, :])], ["row%d" % k], ["lr%d" % k], "dt%d" % k)
+                tab = (T.ltb, T.rtb)[k]
+                for c in (0, 1):
+                    lin(tab[:, c:40:2], tab[:, c:40:2], 0.25, -320, ["lr%d" % k], ["lr%d%s" % (k, "ab"[c])])
+        if rd == 3:
+            quant(T.vq[:], T.vs[:], T.vb[:], ["vb"], ["vq"])
+        for h in (0, 1):
+            lq, ls = T["lq%d" % rd], T["ls%d" % rd]
+            for b in range(4):
+                mm(4 * h + b, WID[h], T.eq[:, 128 * b:128 * b + 128], T.es[:, 128 * b:128 * b + 128], lq[:, cols(h)], ls[:, cols(h)],
+                   ["eq", "lq%d%d" % (rd, h)])
+            for b in range(4):
+                cp(T.dd[:, 320 * b + AT[h]:320 * b + AT[h] + WID[h]], bank(4 * h + b, WID[h]), ["b%d" % (4 * h + b)], ["dd%d%d" % (h, b)], "av", n=WID[h])
+        xn, qn, sn = T["x%d" % rd], T["qx%d" % rd], T["sx%d" % rd]
+        for h in (0, 1):
+            for t in range(4):
+                tt(xn[:, quad(h, t, 4)], T.dd[:, 320 * t:320 * t + 320].indirect(T.mo[:, part(h)]), T.vt[:, quad(h, t, 4)], OP.add,
+                   ["mo", "vt%d%d" % (h, t), "dd0%d" % t, "dd1%d" % t] + ["@x"] * h, ["xn%d%d%d" % (rd, h, t)], n=WID[h], x=True)
+            quant(qn[:, cols(h)], sn[:, cols(h)], xn[:, quad(h)], state_parts(rd, h), ["qx%d%d" % (rd, h)] + ["@x"] * (1 - h), 4 * WID[h])
+            if rd == 3:
+                c = cols(h)
+                dma("s", [(T.oc[:, quad(h)], qn[:, c].bitcast(dt.uint8))] + [(T.osc[4 * k:4 * k + 4, c], sn[32 * k:32 * k + 4, c]) for k in range(4)],
+                    ["qx3%d" % h], [], "oq%d" % h)
+            else:
+                scores(rd, h)
+        if rd < 3:
+            flips(rd)
+            half_x(rd, 0)
+            half_x(rd, 1)
+            natural(rd, rd)
+            turn_tables()
+            if rd == 1:
+                turn_windows()
+    natural(3, 3)
+    mm(1, 320, T.vq[:], T.vs[:], T.qx3[:], T.sx3[:], ["vq", "qx30", "qx31"])
+    cp(T.yb[:], bank(1, 320), ["b1"], ["yb"], "av", n=320)
+    dma("s", [(T.y[:], T.yb[:])], ["yb"], [], "oy")
+    turn_tables(True)
+    for k in (0, 1):
+        dma("s", [(T.lr[:, 640 * k:640 * k + 640], T.lout[:, 40 * k:40 * k + 40])], ["lo%da" % k, "lo%db" % k], [], "ol")
+    issue()
+    need("g", dict(total))
+    g.wait_ge(T.sem.lsem, sent[0])

@@ -8,36 +8,34 @@ STEP = [4, 1, 2]
 BIG = 1.0e6
 WAKE, SPARE, LOOK = 0.07, 0.5, 0.3
 EPS = 2.0 ** -93
+EVEN = 1.5 * 2.0 ** 24
 
-F, B, I, U, C4, S8 = "float32", "bfloat16", "int32", "uint16", "float8_e4m3fn_x4", "uint8"
+F, B, H, I, U, C4, S8 = "float32", "bfloat16", "float16", "int32", "uint16", "float8_e4m3fn_x4", "uint8"
 SCRATCH = {"ps": ("psum", [128, 4096], F)}
 for _n, _w, _d in [
     ("x0", 1280, B), ("x1", 1280, B), ("x2", 1280, B), ("x3", 1280, B), ("xh", 1280, B), ("xg", 1280, B), ("vt", 1280, B), ("ht", 1280, B), ("dd", 1280, B),
     ("ub", 512, B), ("vb", 512, B), ("et", 2048, B), ("ones", 512, B),
     ("uq", 128, C4), ("us", 128, S8), ("vq", 128, C4), ("vs", 128, S8), ("wq", 512, C4), ("wsp", 512, S8),
-    ("utq", 128, C4), ("uts", 128, S8), ("ufq", 768, C4), ("ufs", 768, S8), ("eq", 512, C4), ("es", 512, S8),
+    ("upq", 384, C4), ("ups", 384, S8), ("eq", 512, C4), ("es", 512, S8),
     ("qx0", 320, C4), ("sx0", 320, S8), ("qx1", 320, C4), ("sx1", 320, S8), ("qx2", 320, C4), ("sx2", 320, S8), ("qx3", 320, C4), ("sx3", 320, S8),
     ("qv", 320, C4), ("qvs", 320, S8),
     ("qh1", 320, C4), ("sh1", 320, S8), ("qh2", 320, C4), ("sh2", 320, S8), ("qh3", 320, C4), ("sh3", 320, S8),
     ("lq1", 320, C4), ("ls1", 320, S8), ("lq2", 320, C4), ("ls2", 320, S8), ("lq3", 320, C4), ("ls3", 320, S8), ("rlq", 320, C4), ("rls", 320, S8),
-    ("nl", 320, I), ("nlu", 320, U), ("tw", 5120, F), ("tx", 3840, F), ("nw", 3840, B), ("w4", 320, F),
-    ("cw", 120, F), ("cx", 120, F), ("fb", 60, F), ("fx", 120, F), ("fl", 240, F), ("flu", 256, U), ("lz", 64, F),
-    ("jj", 320, I), ("jk", 320, I), ("mask", 320, F), ("rs", 320, F), ("rb", 800, F), ("st", 320, F),
-    ("cid", 16, F), ("dva", 16, F), ("dvb", 16, F), ("ea", 16, F), ("da", 16, F), ("eb", 16, F), ("db", 16, F), ("tmp", 256, F),
-    ("y1", 160, F), ("y1s", 160, F), ("y2i", 160, F), ("y2b", 160, F), ("y2", 960, F), ("y2s", 960, F), ("ye", 640, F), ("yes", 640, F),
-    ("lu", 128, U), ("nu", 128, U), ("lt0", 16, F), ("lt1", 16, F), ("bc0", 320, B), ("bc1", 320, B), ("lw", 640, B), ("km", 320, B), ("kt", 320, B),
-    ("mlu", 32, U), ("ld", 64, F), ("kl1", 20, U), ("kl2", 20, U), ("kl3", 20, U), ("kr1", 20, U), ("kr2", 20, U), ("kr3", 20, U), ("rlk", 20, U),
-    ("kw", 320, F), ("ky", 320, F), ("kys", 320, F), ("mo", 128, U),
-    ("sn", 320, F), ("fn", 20, F), ("ltb", 40, F), ("rtb", 40, F), ("lrow", 640, F), ("rrow", 640, F), ("lni", 80, I), ("lnu", 80, U), ("lout", 80, F), ("lt2", 64, F),
-    ("yb", 320, F), ("sgc", 8, F), ("sgn", 8, F), ("cli", 64, I), ("clu", 64, U), ("ui", 64, I), ("uf", 64, F), ("uoff", 64, U), ("qi", 16, I), ("qf", 128, F),
+    ("raw", 640, I), ("oa", 320, F), ("ob", 320, F), ("d0", 1280, B), ("d1", 1280, H), ("win", 1280, B), ("nr", 320, B), ("by", 160, F), ("bx", 160, F),
+    ("go", 160, F), ("tt", 1280, F), ("lu", 192, U), ("ue", 512, B), ("uo", 512, B), ("lp", 320, B), ("lw", 640, B), ("mlu", 32, U), ("km", 320, B), ("kt", 320, B),
+    ("kl1", 32, U), ("kl2", 32, U), ("kl3", 32, U), ("kr1", 20, U), ("kr2", 20, U), ("kr3", 20, U), ("rlk", 20, U),
+    ("w4", 320, F), ("jj", 320, I), ("jk", 320, I), ("mask", 320, F), ("rs", 320, F), ("kw", 320, F), ("ky", 320, F), ("kys", 320, F), ("mo", 32, U),
+    ("lout", 640, F), ("yb", 320, F),
+    ("pi", 16, I), ("pc", 48, F), ("kk", 32, F), ("zz", 8, F), ("sel", 16, F), ("pat", 32, F), ("tmp", 64, F),
+    ("uoff", 24, U), ("cl", 24, U), ("dl", 16, U), ("yl", 16, U), ("xl", 16, U), ("el", 48, U), ("ul", 32, U), ("sl", 16, U),
 ]:
     SCRATCH[_n] = ("sbuf", [128, _w], _d)
 
-SEMAPHORES = (["sv", "sa", "st", "sg", "dx0", "dx1", "du", "dv", "dw", "dl", "dt0", "dt1", "fn1", "fn2", "fn3", "oy", "ol", "oq0", "oq1", "dfx", "lsem", "ry0", "ry1", "rz0", "rz1", "rk"]
-              + ["dn%d" % s for s in range(8)] + ["ar%d%d" % (r, h) for r in (1, 2, 3) for h in (0, 1)] + ["kr%d" % r for r in (1, 2, 3)])
+SEMAPHORES = (["sv", "sa", "st", "sg", "dx0", "dx1", "du", "dv", "dw", "dn0", "dn1", "oy", "ol", "oq0", "oq1", "lsem", "ry0", "ry1", "rz0", "rz1", "rk"]
+              + ["ar%d%d" % (r, h) for r in (1, 2, 3) for h in (0, 1)] + ["kr%d" % r for r in (1, 2, 3)])
 
 
-AT, WID = (0, 160), (160, 160)
+AT, WID = (0, 192), (192, 128)
 
 
 def cols(h):
@@ -50,6 +48,14 @@ def quad(h, t=0, step=1):
 
 def part(h):
     return slice(AT[h] // 16, (AT[h] + WID[h]) // 16)
+
+
+def share(h):
+    return slice(AT[h] // 32, (AT[h] + WID[h]) // 32)
+
+
+def halfrow(h, at=0):
+    return slice(at + AT[h] // 2, at + (AT[h] + WID[h]) // 2)
 
 
 def bits_of(engines):
@@ -90,12 +96,6 @@ def relay_program(g, core, T, topo):
             g.remote_dma(T.ls2[:, a:a + w], T.rls[:, a:a + w], T.sem["ar2%d" % h], T.sem.lsem, pid, rid, m)
             sent += 2 * n
         g.wait_ge(T.sem.lsem, sent)
-
-
-def table_of(a, s):
-    if s < 6:
-        return ("l", s + 1) if s < 2 * a else ("r", 6 - s + 2 * a)
-    return ("r", 7) if (s == 6) == (a == 0) else ("l", 0)
 
 
 def rank_program(g, core, T, topo):
@@ -145,27 +145,28 @@ def rank_program(g, core, T, topo):
             op("v", lambda e: e.tensor_scalar(o, a, s1, s2, f1, f2), r, w, us(n, c, x))
 
     def lin(o, a, m, b, r, w, n=10, x=False):
-        ts(o, a, float(m), float(b), OP.mult, OP.add, r, w, n, x)
+        ts(o, a, float(m) if isinstance(m, int) else m, float(b) if isinstance(b, int) else b, OP.mult, OP.add, r, w, n, x)
 
     def cp(o, a, r, w, q="v", n=10, x=False, c=1):
         fns = {"v": lambda e: e.tensor_copy(o, a), "a": lambda e: e.activation(o, a, AF.Copy)}
         node({k: fns[k] for k in q}, {k: us(n, c if k == "v" else 1, x) for k in q}, 0.0, r, w, None, 1)
 
-    def scaled(o, a, m, r, w, q, n, c=1):
-        fns = {"v": lambda e: e.tensor_scalar(o, a, m, None, OP.mult), "a": lambda e: e.activation(o, a, AF.Copy, scale=m)}
-        node({k: fns[k] for k in q}, {k: us(n, c if k == "v" else 1, False) for k in q}, 0.0, r, w, None, 1)
+    def scaled(o, a, m, b, r, w, q, n, c=1, x=False):
+        fns = {"v": (lambda e: e.tensor_scalar(o, a, m, b, OP.mult, OP.add)) if b else (lambda e: e.tensor_scalar(o, a, m, None, OP.mult)),
+               "a": (lambda e: e.activation(o, a, AF.Copy, bias=b, scale=m)) if b else (lambda e: e.activation(o, a, AF.Copy, scale=m))}
+        node({k: fns[k] for k in q}, {k: us(n, c if k == "v" else 1, x) for k in q}, 0.0, r, w, None, 1)
 
     def tr(o, a, r, w, n, c=1):
         op("v", lambda e: e.transpose(o, a), r, w, us(n, c, False))
 
-    def scan(o, d0, d1, f0, f1, r, w, n=160):
-        op("v", lambda e: e.tensor_tensor_scan(o, d0, d1, BIG, f0, f1), r, w, us(n, 1, False))
+    def scan(o, d0, d1, first, f0, f1, r, w, n, c=1):
+        op("v", lambda e: e.tensor_tensor_scan(o, d0, d1, first, f0, f1), r, w, us(n, c, False))
 
     def mm(bank, n, lq, lsc, rq, rsc, r):
         op("t", lambda e: e.matmul_mx(T.ps[:, 512 * bank:512 * bank + n], lq, lsc, rq, rsc, True, True), r, ["b%d" % bank], (n + 16) * 0.0011)
 
     def fill(o, c, w, n=10):
-        op("v", lambda e: e.memset(o, c), [], w, us(n, 1, False))
+        op("v", lambda e: e.memset(o, c), [], w, us(n, 0.5, False))
 
     def quant(q, s, t, r, w, n=640):
         op("v", lambda e: e.quantize_mx(q, s, t), r, w, 0.012 + n * 0.00028)
@@ -243,25 +244,15 @@ def rank_program(g, core, T, topo):
     def bank(b, n):
         return T.ps[:, 512 * b:512 * b + n]
 
-    mask1, rst1 = T.mask[:, 0:160], T.rs[:, 0:160]
-
+    dma("s", [(T.ub[:], T.u[:])], [], ["ub"], "du")
+    for k, (q, tab) in enumerate((("a", T.lam), ("s", T.rho))):
+        dma(q, [(T.raw[16 * gr + 8 * k:16 * gr + 8 * k + 8, :], tab[:]) for gr in range(8)], [], ["raw%d" % k], "dn%d" % k)
     for h in (0, 1):
-        dma("s", [(T.x0[:, quad(h)], T.x[:, quad(h)])], [], ["x0%d" % h], "dx%d" % h)
-    dma("a", [(T.ub[:], T.u[:])], [], ["ub"], "du")
-    for k, s in enumerate((6, 0, 7, 1, 2, 3, 4, 5)):
-        pairs = []
-        for a in range(4):
-            side, gr = table_of(a, s)
-            src = (T.lam if side == "l" else T.rho)[16 * gr:16 * gr + 16, :]
-            for b in (0, 1):
-                p = 16 * (2 * a + b)
-                pairs.append((T.nl[p:p + 16, 40 * s:40 * s + 40], src))
-        dma("s" if k % 2 == 0 else "a", pairs, [], ["nl%d" % s], "dn%d" % s)
+        dma("sa"[h], [(T.x0[:, quad(h)], T.x[:, quad(h)])], [], ["x0%d" % h], "dx%d" % h)
     dma("s", [(T.wq[:].bitcast(dt.uint8), T.wc[:]), (T.wsp[:], T.ws[:])], [], ["wq"], "dw")
-    dma("s", [(T.lni[:, 0:40], T.lam[:]), (T.lni[:, 40:80], T.rho[:])], [], ["lni"], "dl")
     dma("s", [(T.vb[:], T.v[:])], [], ["vb"], "dv")
 
-    def iota(o, pattern, base, cm, w, fl=False):
+    def iota(o, pattern, base, cm, w, fl=True):
         n = 1
         for step, count in pattern:
             n *= count
@@ -270,78 +261,122 @@ def rank_program(g, core, T, topo):
         else:
             op("g", lambda e: e.iota(o, pattern, base, cm), [], w, 0.15 + 0.002 * n)
 
-    iota(T.qi[:, 0:4], [[0, 4]], 0, 1, ["qi"])
-    iota(T.uf[:, 0:4], [[2, 4]], 0, 0, ["ufa"], True)
-    iota(T.uf[:, 4:8], [[32, 4]], 96, 0, ["ufb"], True)
-    iota(T.ui[:, 0:48], [[-16, 6], [32, 4], [0, 2]], 97, 0, ["ui"])
-    iota(T.w4[:], [[4, 320]], 1280, 0, ["w4"], True)
-    iota(T.jj[:], [[1, 320]], 128, -1, ["jj"])
-    iota(T.jk[:], [[1, 320]], 0, 0, ["jk"])
+    iota(T.pi[:, 0:1], [[0, 1]], 0, 1, ["p"], False)
+    iota(T.kk[:, 0:20], [[1, 20]], 0, 0, ["kk"])
+    iota(T.pat[:, 0:10], [[64, 5], [16, 2]], 0, 0, ["pata"])
     for a in range(4):
-        iota(T.cid[32 * a:32 * a + 32, 0:10], [[128, 10]], 1280, 4, ["cid%d" % a], True)
-    CID = ["cid%d" % a for a in range(4)]
-    iota(T.cli[:, 0:10], [[1, 10]], 0, 0, ["cl16"])
-    iota(T.cli[:, 32:52], [[1, 10], [0, 2]], 0, 0, ["cl32"])
+        rows = slice(32 * a, 32 * a + 32)
+        if a > 0:
+            iota(T.sel[rows, 0:2 * a], [[161, 2 * a]], 160, 0, ["sel%da" % a])
+        if a < 3:
+            iota(T.sel[rows, 2 * a + 1:6], [[159, 5 - 2 * a]], 159 * (2 * a + 1) + 175 + 2 * a, 0, ["sel%db" % a])
+            fill(T.sel[rows, 2 * a:2 * a + 1], 175.0, ["sel%dc" % a])
+    SEL = ["sel%d%s" % (a, c) for a in range(4) for c in "abc"]
+    iota(T.pat[:, 10:30], [[64, 5], [16, 2], [32, 2]], 0, 0, ["patb"])
+    iota(T.w4[:], [[4, 320]], 1280, 0, ["w4"])
+    iota(T.jj[:], [[1, 320]], 128, -1, ["jj"], False)
+    iota(T.jk[:], [[1, 320]], 0, 0, ["jk"], False)
 
-    ts(T.qi[:, 4:8], T.qi[:, 0:4], 15, None, OP.bitwise_and, None, ["qi"], ["qa"])
-    q4 = T.qf[:, 0:4]
-    cp(q4, T.qi[:, 4:8], ["qa"], ["q4"])
-    qe = T.qf[:, 20:24]
-    ts(T.qf[:, 24:28], q4, 10.0, -10.0, OP.is_ge, OP.mult, ["q4"], ["q_t"])
-    tt(qe, q4, T.qf[:, 24:28], OP.add, ["q4", "q_t"], ["qe"])
-    tt(T.qf[:, 4:8], qe, T.uf[:, 0:4], OP.is_lt, ["qe", "ufa"], ["q_m"])
-    ts(T.qf[:, 8:12], qe, -16.0, None, OP.mult, None, ["qe"], ["q_r"])
-    tt(T.qf[:, 8:12], T.qf[:, 8:12], T.uf[:, 4:8], OP.add, ["q_r", "ufb"], ["q_r"])
-    lin(T.qf[:, 12:16], qe, 16, 16, ["qe"], ["q_l"])
-    tt(T.qf[:, 12:16], T.qf[:, 12:16], T.qf[:, 8:12], OP.subtract, ["q_l", "q_r"], ["q_l"])
-    tt(T.qf[:, 12:16], T.qf[:, 12:16], T.qf[:, 4:8], OP.mult, ["q_l", "q_m"], ["q_l"])
-    tt(T.qf[:, 8:12], T.qf[:, 8:12], T.qf[:, 12:16], OP.add, ["q_r", "q_l"], ["q_r"])
-    ts(T.qf[:, 16:20], qe, 6.0, None, OP.is_lt, None, ["qe"], ["q_6"])
-    tt(T.qf[:, 8:12], T.qf[:, 8:12], T.qf[:, 16:20], OP.mult, ["q_r", "q_6"], ["q_r"])
-    ts(T.qf[:, 28:32], q4, 10.0, None, OP.is_ge, None, ["q4"], ["q_10"])
-    tt(T.qf[:, 8:12], T.qf[:, 8:12], T.qf[:, 28:32], OP.add, ["q_r", "q_10"], ["q_r"])
-    for k, (c, spec) in enumerate(((4, ((7, 112.0), (8, 1.0), (9, 113.0))), (1, ((6, 112.0), (8, 113.0), (9, 1.0))))):
-        o = 32 + 32 * k
-        for j, (q, val) in enumerate(spec):
-            ts(T.qf[:, o + 4 * j:o + 4 * j + c], T.qf[:, 0:c], float(q), val, OP.is_equal, OP.mult, ["q4"], ["qs%d%d" % (k, j)])
-        tt(T.qf[:, o:o + c], T.qf[:, o:o + c], T.qf[:, o + 4:o + 4 + c], OP.add, ["qs%d0" % k, "qs%d1" % k], ["qs%d0" % k])
-        tt(T.qf[:, o:o + c], T.qf[:, o:o + c], T.qf[:, o + 8:o + 8 + c], OP.add, ["qs%d0" % k, "qs%d2" % k], ["qs%d0" % k])
-    cp(T.qf[:, 32:33], T.qf[:, 64:65], ["qs10", "qs00"], ["qs00"])
-    tt(T.qf[:, 8:12], T.qf[:, 8:12], T.qf[:, 32:36], OP.add, ["q_r", "qs00"], ["q_r"])
-    cp(T.uoff[:, 0:8:2], T.qf[:, 8:12], ["q_r"], ["uoff0"])
-    cp(T.uoff[:, 1:8:2], T.qf[:, 8:12], ["q_r"], ["uoff1"])
-    quant(T.uq[:, 0:128], T.us[:, 0:128], T.ub[:, 0:512], ["ub"], ["uq"])
-    cp(T.utq[:, 0:128].bitcast(dt.uint32), T.uq[:, 0:128].bitcast(dt.uint32).indirect(T.uoff[:, 0:8]), ["uq", "uoff0", "uoff1"], ["utq"], n=128, x=True)
-    cp(T.uts[:, 0:128], T.us[:, 0:128].indirect(T.uoff[:, 0:8]), ["uq", "uoff0", "uoff1"], ["uts"], "av", n=128, x=True)
+    digits = {"i": (0, 15), "q7": (0, 7), "q8": (3, 1), "p32": (0, 31), "b": (4, 1), "a": (5, 3), "ih": (1, 7), "y": (0, 1), "x": (1, 1)}
+    place = {}
+    for k, (name, (sh, m)) in enumerate(digits.items()):
+        ts(T.pi[:, k + 1:k + 2], T.pi[:, 0:1], sh, m, OP.arith_shift_right, OP.bitwise_and, ["p"], ["pi%d" % k])
+        place[name] = k
+    cp(T.pc[:, 0:9], T.pi[:, 1:10], ["pi%d" % k for k in range(9)], list(digits))
+
+    def col(name):
+        return T.pc[:, place[name]:place[name] + 1]
+
+    def new(name, a, s1, s2, f1, f2):
+        place[name] = len(place)
+        use = [a] + [s for s in (s1, s2) if isinstance(s, str)]
+        s1, s2 = [col(s) if isinstance(s, str) else s if s is None else float(s) for s in (s1, s2)]
+        ts(col(name), col(a), s1, s2, f1, f2, use, [name])
+
+    def last_pair(name, v):
+        k = place[name]
+        fill(T.pc[96:128, k:k + 1], float(v), [name])
+
+    mul, add = OP.mult, OP.add
+    fill(T.zz[:], 0.0, ["zz"])
+    new("q16", "q7", 16, None, mul, None)
+    new("n16", "q8", -32, 16, mul, add)
+    new("n", "q16", "n16", 112, add, OP.min)
+    ts(T.uoff[:, 0:8], T.zz[:], col("q16"), 1.0, add, add, ["zz", "q16"], ["uoff0"])
+    ts(T.uoff[:, 8:16], T.zz[:], col("q16"), None, add, None, ["zz", "q16"], ["uoff1"])
+    ts(T.uoff[:, 16:24], T.zz[:], col("n"), 0.0, add, OP.max, ["zz", "n"], ["uoff2"])
+    quant(T.uq[:], T.us[:], T.ub[:], ["ub"], ["uq"], 512)
+    for k in (1, 2, 0):
+        c, o = slice(128 * k, 128 * k + 128), T.uoff[:, 8 * k:8 * k + 8]
+        cp(T.upq[:, c].bitcast(dt.uint32), T.uq[:].bitcast(dt.uint32).indirect(o), ["uq", "uoff%d" % k], ["upq%d" % k], n=128, x=True)
+        cp(T.ups[:, c], T.us[:].indirect(o), ["uq", "uoff%d" % k], ["ups%d" % k], "av", n=128, x=True)
+    new("sf", "q8", -2, 1, mul, add)
+    new("i15", "i", -1, 15, mul, add)
+    new("ii", "i", "i15", None, mul, None)
+    new("sd", "ii", 0, -1, OP.is_equal, mul)
+    new("e0", "q7", 80, "q8", mul, add)
+    new("e1", "e0", 40, None, add, None)
+    for k in (0, 1):
+        lin(T.el[:, 24 * k:24 * k + 20], T.kk[:, 0:20], 2, col("e%d" % k), ["kk", "e%d" % k], ["el%d" % k])
+    new("d2", "p32", 4, 2, mul, add)
+    lin(T.dl[:, 0:10], T.kk[:, 0:10], 128, col("d2"), ["kk", "d2"], ["dl"])
+    new("px", "b", 16, "p32", mul, add)
+    lin(T.tmp[:, 0:10], T.kk[:, 0:10], 32, col("p32"), ["kk", "p32"], ["yf"])
+    ts(T.tmp[:, 16:26], T.pat[:, 0:10], col("px"), None, add, None, ["pata", "px"], ["xf"])
+    cp(T.yl[:, 0:10], T.tmp[:, 0:10], ["yf"], ["yl"])
+    cp(T.xl[:, 0:10], T.tmp[:, 16:26], ["xf"], ["xl"])
+    fill(T.tt[:, 0:160], 0.0, ["T0"], n=320)
+    lin(T.tt[:, 0:160:16], T.tmp[:, 0:10], 2, -320, ["yf", "T0"], ["T0a"])
+    lin(T.tt[:, 1:160:16], T.tmp[:, 16:26], 2, -320, ["xf", "T0"], ["T0b"])
+    for h in (0, 1):
+        new("c%d" % h, "i", WID[h] // 32 - 1, 16, OP.min, mul)
+        ts(T.cl[:, 2 * h:24:4], T.sel[:, 0:6], col("c%d" % h), float(AT[h] // 2), add, add, SEL + ["c%d" % h], ["cl%d" % h])
+    new("se", "a", 322, -1, mul, add)
+    new("se0", "se", 0, None, OP.max, None)
+    new("so", "a", 322, 160, mul, add)
+    last_pair("so", 1)
+    lin(T.tmp[:, 32:34], T.kk[:, 0:2], 8, col("ih"), ["kk", "ih"], ["ku"])
+    ts(T.tmp[:, 32:34], T.tmp[:, 32:34], 9.0, 16.0, OP.min, mul, ["ku"], ["ku"])
+    ts(T.sl[:, 0:2], T.tmp[:, 32:34], col("se0"), None, add, None, ["ku", "se0"], ["sl0"])
+    ts(T.sl[:, 2:4], T.tmp[:, 32:34], col("so"), None, add, None, ["ku", "so"], ["sl1"])
+    new("c9", "i", 9, 16, OP.min, mul)
+    new("me", "a", 2, 1129, mul, add)
+    last_pair("me", 175)
+    new("mo", "a", 2, 970, mul, add)
+    last_pair("mo", 1126)
+    ts(T.sl[:, 4:5], col("c9"), col("me"), None, add, None, ["c9", "me"], ["sl2"])
+    ts(T.sl[:, 6:7], col("c9"), col("mo"), None, add, None, ["c9", "mo"], ["sl3"])
+    new("nb", "b", -1, 1, mul, add)
+    last_pair("nb", 1)
+    new("yx", "y", "x", "nb", OP.subtract, mul)
+    new("iyx", "i", "yx", None, add, None)
+    lin(T.tmp[:, 40:42], T.kk[:, 0:2], 16, col("iyx"), ["kk", "iyx"], ["kf"])
+    ts(T.sl[:, 8:10], T.tmp[:, 40:42], 16.0, 304.0, mul, OP.min, ["kf"], ["sl4"])
+    ts(T.ul[:, 0:20], T.pat[:, 10:30], col("i"), None, add, None, ["patb", "i"], ["ul"])
+    fill(T.ue[:], 0.0, ["ue"], n=512)
+    fill(T.uo[:], 0.0, ["uo"], n=512)
 
     ts(T.jj[:], T.jj[:], 15, None, OP.bitwise_and, None, ["jj"], ["jj"], n=320)
     ts(T.mask[:], T.jj[:], 0.0, None, OP.is_equal, None, ["jj"], ["mask"], n=320)
     ts(T.jk[:], T.jk[:], 15, None, OP.bitwise_and, None, ["jk"], ["jk"], n=320)
     ts(T.rs[:], T.jk[:], 0.0, BIG, OP.is_gt, OP.mult, ["jk"], ["rs"], n=320)
 
-    def list_of(s):
-        cp(T.nlu[:, 40 * s:40 * s + 40], T.nl[:, 40 * s:40 * s + 40], ["nl%d" % s], ["nlu%d" % s])
+    for t, v in ((0, 0.0), (2, 1.0), (3, -1.0)):
+        fill(T.d0[:, t:1280:4], v, ["d0c"] if t != 2 else ["sf0", "sf1"], n=320)
+    RAW = ["raw0", "raw1"]
+    for h in (0, 1):
+        c, n = cols(h), WID[h]
+        le, lo = T.el[:, part(h)], T.el[:, 24 + AT[h] // 16:24 + (AT[h] + n) // 16]
+        cp(T.oa[:, c], T.raw[:].indirect(lo), RAW + ["el1"], ["oa%d" % h], n=n, x=True)
+        scaled(T.ob[:, c], T.oa[:, c], 1.0, -320.0, ["oa%d" % h], ["ob%d" % h], "av", n)
+        tt(T.d1[:, quad(h, 0, 4)], T.raw[:].indirect(le), T.oa[:, c], OP.subtract, RAW + ["el0", "oa%d" % h], ["dif%d" % h], n=n, x=True)
+        tt(T.d1[:, quad(h, 2, 4)], T.raw[:].indirect(le), T.ob[:, c], OP.add, RAW + ["el0", "ob%d" % h], ["sum%d" % h], n=n, x=True)
+        ts(T.d1[:, quad(h, 3, 4)], T.d1[:, quad(h, 2, 4)], 2.0, None, mul, None, ["sum%d" % h], ["two%d" % h], n=n, c=0.5)
+    ts(T.d1[:, 1:1280:4], T.d0[:, 0:1280:4], 0.0, None, mul, None, ["d0c"], ["d1c"], n=320, c=0.5)
 
-    def window(s):
-        cp(T.tw[:, 640 * s:640 * s + 640], T.w4[:].indirect(T.nlu[:, 40 * s:40 * s + 40]), ["w4", "nlu%d" % s], ["tw%d" % s], "av", n=640, x=True)
-
-    for s in (6, 0, 7, 1, 2, 3, 4, 5):
-        list_of(s)
-        window(s)
-    iota(T.cw[:], [[0, 6], [32, 20]], 0, 0, ["cw"], True)
-    ts(T.qf[:, 96:97], T.qf[:, 0:1], 2.0, None, OP.mult, None, ["q4"], ["q2"])
-    ts(T.cw[:], T.cw[:], T.qf[:, 96:97], None, OP.add, None, ["cw", "q2"], ["cw"], n=120)
-    lin(T.cx[:], T.cw[:], 1, 1, ["cw"], ["cx"], n=120)
     for h in (0, 1):
         quant(T.qx0[:, cols(h)], T.sx0[:, cols(h)], T.x0[:, quad(h)], ["x0%d" % h], ["qx0%d" % h], 4 * WID[h])
-    for k in range(3):
-        w = 320 if k < 2 else 160
-        cp(T.rb[:, 320 * k:320 * k + w], T.rs[:, 0:w], ["rs"], ["rb%d" % s for s in ((1, 2), (3, 4), (5,))[k]], "av", n=w)
-    cp(T.clu[:, 0:10], T.cli[:, 0:10], ["cl16"], ["c16"])
-    cp(T.clu[:, 32:52], T.cli[:, 32:52], ["cl32"], ["c32"])
-    cp(T.lt0[0:32, 0:10], T.cid[0:32, 0:10], CID, ["lt0_0"])
-    cp(T.lt1[96:128, 0:10], T.cid[96:128, 0:10], CID, ["lt1_3"])
-    fill(T.ones[:], 1.0, ["ones"], n=256)
+    iota(T.ones[:], [[0, 512]], 1, 0, ["ones"])
 
     def one_in(b):
         op("g", lambda e: e.affine_select(T.et[:, 512 * b:512 * b + 512], T.ones[:], [[1, 512]], OP.is_equal, 0.0, -b, -4), ["ones"], ["et%d" % b], 1.2)
@@ -349,196 +384,93 @@ def rank_program(g, core, T, topo):
     for b in range(4):
         one_in(b)
 
+    def state_parts(k, h):
+        return ["x0%d" % h] if k == 0 else ["xn%d%d%d" % (k, h, t) for t in range(4)]
+
     def half_x(k, h):
         x = T["x%d" % k]
         for t in range(4):
-            scaled(T.xh[:, 320 * t + AT[h]:320 * t + AT[h] + WID[h]], x[:, quad(h, t, 4)], 0.5, state_parts(k, h)[t % len(state_parts(k, h)):][:1],
+            scaled(T.xh[:, 320 * t + AT[h]:320 * t + AT[h] + WID[h]], x[:, quad(h, t, 4)], 0.5, 0.0, state_parts(k, h)[t % len(state_parts(k, h)):][:1],
                    ["xh%d%d" % (h, t)], "av", WID[h], 0.5)
-        scaled(T.xg[:, quad(h)], x[:, quad(h)], 0.5, state_parts(k, h), ["xg%d" % h], "av", 4 * WID[h], 0.5)
-
-    def state_parts(k, h):
-        return ["x0%d" % h] if k == 0 else ["xn%d%d%d" % (k, h, t) for t in range(4)]
+            scaled(T.xg[:, quad(h, t, 4)], x[:, quad(h, t, 4)], 0.5, 0.0, state_parts(k, h)[t % len(state_parts(k, h)):][:1], ["xg%d%d" % (h, t)], "av", WID[h], 0.5)
 
     half_x(0, 0)
     half_x(0, 1)
 
-    def scores(k, h):
-        mm(h, WID[h], T.utq[:], T.uts[:], T["qx%d" % k][:, cols(h)], T["sx%d" % k][:, cols(h)], ["utq", "uts", "qx%d%d" % (k, h)])
-        tr(T.st[:, cols(h)], bank(h, WID[h]), ["b%d" % h], ["st%d" % h], WID[h])
+    def signs(k, h):
+        n = WID[h]
+        kinds = [(0, T.d0[:, quad(h, 2, 4)], col("sf"), EPS, "sf"), (1, T.d0[:, quad(h, 1, 4)], col("sd"), EPS, "sb"), (2, T.nr[:, cols(h)], 1.0, -EPS, "nr")]
+        for j, o, sc, eps, name in kinds[k == 0:1 if k == 3 else 3]:
+            c, b = slice(128 * j, 128 * j + 128), 3 * h + j
+            mm(b, n, T.upq[:, c], T.ups[:, c], T["qx%d" % k][:, cols(h)], T["sx%d" % k][:, cols(h)], ["upq%d" % j, "ups%d" % j, "qx%d%d" % (k, h)])
+            sign(o, bank(b, n), sc, eps, ["b%d" % b, "sf", "sd"], ["%s%d" % (name, h)], n)
+        scan(T.win[:, quad(h)], T.d0[:, quad(h)], T.d1[:, quad(h)], 0.0, mul, add,
+             ["d0c", "d1c"] + ["%s%d" % (s, h) for s in ("sf", "sb", "dif", "sum", "two")], ["win%d" % h], 4 * n, 0.5)
+        if k < 3:
+            for name, lst in (("by", T.yl), ("bx", T.xl)):
+                scaled(T[name][:, halfrow(h)], T.nr[:, 0:AT[h] + n].indirect(lst[:, share(h)]), 0.25, 0.25,
+                       ["nr%d" % j for j in range(h + 1)] + ["yl", "xl"], ["%s%d" % (name, h)], "a", n // 2, x=True)
 
-    ST = ["st0", "st1"]
+    def sign(o, i, sc, eps, r, w, n):
+        op("a", lambda e: e.activation(o, i, AF.Sign, bias=eps, scale=sc), r, w, us(n, 1, False))
 
-    def row(q):
-        return T.st[:, q:320:32]
+    def turned(h):
+        tt(T.d1[:, quad(h, 0, 4)], T.d1[:, quad(h, 0, 4)], T.d0[:, quad(h, 2, 4)], mul, ["dif%d" % h, "sf%d" % h], ["dif%d" % h], n=WID[h])
 
-    def tmp(k):
-        return T.tmp[:, 16 * k:16 * k + 10]
-
-    def rstart(s):
-        return T.rb[:, 160 * (s - 1):160 * s:16]
-
-    def sign(s, j):
-        o, i, sg = T.nw[:, 640 * s + 320 * j:640 * s + 320 * j + 320], bank(2 + s, 320), (T.sgn, T.sgc)[j][:, s:s + 1]
-        eps = EPS if j else -EPS
-        op("a", lambda e: e.activation(o, i, AF.Sign, bias=eps, scale=sg), ["b%d" % (2 + s), "sgc"], ["nw%d%d" % (s, j)], 0.33)
-
-    def flips(k):
-        for s in range(6):
-            mm(2 + s, 320, T.ufq[:, 128 * s:128 * s + 128], T.ufs[:, 128 * s:128 * s + 128], T["qx%d" % k][:], T["sx%d" % k][:], ["ufq", "ufs", "qx%d0" % k, "qx%d1" % k])
-        for s in range(6):
-            sign(s, 0)
-            sign(s, 1)
-
-    def turn_windows():
-        for s in range(6):
-            ts(T.fb[:, 10 * s:10 * s + 10], row(10 + s), T.sgc[:, s:s + 1], 0.0, OP.mult, OP.is_lt, ST + ["sgc"], ["fb%d" % s])
-        pairs = []
-        for a in range(4):
-            for b in (0, 1):
-                for c in (0, 1):
-                    p, q = 32 * a + 16 * b, 32 * a + 16 * c
-                    pairs.append((T.fx[q:q + 16, 60 * b:60 * b + 60], T.fb[p:p + 16, :]))
-        dma("s", pairs, ["fb%d" % s for s in range(6)], ["fx"], "dfx")
-        for k, (base, f) in enumerate(((T.cw, OP.add), (T.cx, OP.subtract))):
-            for b in (0, 1):
-                tt(T.fl[:, 120 * k + b:120 * k + 120:2], base[:, b:120:2], T.fx[:, 60 * b:60 * b + 60], f, ["fx", "cw", "cx"], ["fl%d%d" % (k, b)], n=60)
-            cp(T.flu[:, 128 * k:128 * k + 120], T.fl[:, 120 * k:120 * k + 120], ["fl%d0" % k, "fl%d1" % k], ["flu%d" % k], n=120)
-        for s in range(6):
-            for k in (0, 1):
-                cp(T.tx[:, 640 * s + k:640 * s + 640:2], T.tw[:, 640 * s:640 * s + 640].indirect(T.flu[:, 128 * k + 20 * s:128 * k + 20 * s + 20]),
-                   ["flu%d" % k, "tw%d" % s], ["tx%d%d" % (s, k)], "av", n=320, x=True)
-
-    def direct(n, rd):
-        dv = (T.dva, T.dvb)[n][:, 0:10]
-        name = ("dva", "dvb")[n]
-        o = 5 * n
-        if rd == 1:
-            ts(tmp(o), row(6 + n), 0.0, 2.0, OP.is_gt, OP.mult, ST, ["t%d" % o])
-            tt(tmp(o), tmp(o), T.cid[:, 0:10], OP.add, ["t%d" % o] + CID, ["t%d" % o])
-            lin(T.nu[:, 96 + 16 * n:106 + 16 * n], tmp(o), 0.5, -640, ["t%d" % o], ["nu%d" % (6 + n)])
-            tt(T.ye[:, 160 * n:160 * n + 160], T.tw[:, 640 * (6 + n):640 * (7 + n)].indirect(T.nu[:, 96 + 16 * n:106 + 16 * n]), mask1, OP.mult,
-               ["tw%d" % (6 + n), "nu%d" % (6 + n), "mask"], ["ye%d" % n], n=160, x=True)
-            scan(T.yes[:, 160 * n:160 * n + 160], rst1, T.ye[:, 160 * n:160 * n + 160], OP.min, OP.add, ["rs", "ye%d" % n], ["yes%d" % n])
-            cp(dv, T.yes[:, 160 * n + 15:160 * n + 160:16], ["yes%d" % n], [name])
-        else:
-            e, d = (T.ea, T.eb)[n][:, 0:10], (T.da, T.db)[n][:, 0:10]
-            ts(tmp(o), row(6 + n), 0.0, None, OP.is_gt, None, ST, ["t%d" % o])
-            ts(tmp(o + 1), row(8 + n), T.sgc[:, 6 + n:7 + n], 0.0, OP.mult, OP.is_lt, ST + ["sgc"], ["t%d" % (o + 1)])
-            tt(tmp(o + 2), tmp(o), tmp(o + 1), OP.not_equal, ["t%d" % o, "t%d" % (o + 1)], ["t%d" % (o + 2)])
-            tt(tmp(o + 2), tmp(o + 2), d, OP.mult, ["t%d" % (o + 2), "d%d" % n], ["t%d" % (o + 2)])
-            tt(dv, e, tmp(o + 2), OP.add, ["e%d" % n, "t%d" % (o + 2)], [name])
-
-    def turn_direct(n):
-        o = 5 * n
-        e, d = (T.ea, T.eb)[n][:, 0:10], (T.da, T.db)[n][:, 0:10]
-        tt(tmp(o + 3), tmp(o + 1), d, OP.mult, ["t%d" % (o + 1), "d%d" % n], ["t%d" % (o + 3)])
-        tt(e, e, tmp(o + 3), OP.add, ["e%d" % n, "t%d" % (o + 3)], ["e%d" % n])
-        tt(d, d, tmp(o + 3), OP.subtract, ["d%d" % n, "t%d" % (o + 3)], ["d%d" % n])
-        tt(d, d, tmp(o + 3), OP.subtract, ["d%d" % n, "t%d" % (o + 3)], ["d%d" % n])
-
-    def spread(j):
-        o, win, lst = (T.bc0, T.bc1)[j][:], (T.lt0, T.lt1)[j][:, 0:10], T.clu[:, 32:52]
-        node({"v": lambda e: e.tensor_scalar(o, win.indirect(lst), 0.25, -480.0, OP.mult, OP.add),
-              "a": lambda e: e.activation(o, win.indirect(lst), AF.Copy, bias=-480.0, scale=0.25)},
-             {"v": us(320, 1, True), "a": us(320, 1, True)}, 0.0, ["c32"] + ["lt%d_%d" % (j, a) for a in range(4)], ["bc%d" % j], None, 1)
-        tr(T.lw[:, 320 * j:320 * j + 320], o, ["bc%d" % j], ["lw%d" % j], 320, 0.5)
-
-    def lu(s):
-        return T.lu[:, 16 * s:16 * s + 10]
+    def upto(s, h):
+        names = ["T0a", "T0b"] + ["T%d%d" % (k, j) for k in range(1, s + 1) for j in (0, 1) if (k, j) <= (s, h)]
+        return T.tt[:, 0:halfrow(h, 160 * s).stop], names
 
     def walk(rd):
-        fl = rd > 1
-        rsc, cm, cb = (1280.0, 0.25, -320) if fl else (2.0, 0.5, -640)
-
-        def bits(s):
-            ts(rstart(s), row(s), 0.0, rsc, OP.is_gt, OP.mult, ST, ["rb%d" % s])
-
-        direct(0, rd)
-        ts(tmp(10), row(0), 0.0, rsc, OP.is_gt, OP.mult, ST, ["t10"])
-        tt(tmp(10), tmp(10), T.dva[:, 0:10], OP.add, ["t10", "dva"], ["t10"])
-        lin(lu(0), tmp(10), cm, cb, ["t10"], ["lu0a"])
-        if fl:
-            tt(T.y2i[:], T.dva[:, 0:10].indirect(T.clu[:, 0:10]), mask1, OP.mult, ["dva", "c16", "mask"], ["y2i"], n=160, x=True)
-        tabs = T.tx if rd == 3 else T.tw
-        for s in range(6):
-            L = ["lu%d%s" % (s, c) for c in "abc"]
-            prev = "y2i" if s == 0 else "y2%d" % (s - 1)
-            if fl:
-                pv = T.y2i[:] if s == 0 else T.y2[:, 160 * (s - 1):160 * s]
-                tt(T.y1[:], T.nw[:, 640 * s:640 * s + 640].indirect(lu(s)), pv, OP.add, L + ["nw%d0" % s, "nw%d1" % s, prev, prev + "x"], ["y1"], n=160, x=True)
-            if s < 5:
-                bits(s + 1)
-            if fl:
-                scan(T.y1s[:], rst1, T.y1[:], OP.min, OP.max, ["rs", "y1"], ["y1s"])
-                nu = T.nu[:, 16 * s:16 * s + 10]
-                lin(nu, T.y1s[:, 15:160:16], 0.5, -639.5, ["y1s"], ["nu%d" % s])
-                L, lst = ["nu%d" % s], nu
-            else:
-                lst = lu(s)
-            y2, y2s = T.y2[:, 160 * s:160 * s + 160], T.y2s[:, 160 * s:160 * s + 160]
-            tt(y2, tabs[:, 640 * s:640 * s + 640].indirect(lst), mask1, OP.mult, L + (["tx%d0" % s, "tx%d1" % s] if rd == 3 else ["tw%d" % s]) + ["mask"],
-               ["y2%d" % s, "y2%dx" % s], n=160, x=True)
-            rs = T.rb[:, 160 * s:160 * s + 160] if s < 5 else rst1
-            scan(y2s, rs, y2, OP.min, OP.add, ["y2%d" % s, "y2%dx" % s, "rb%d" % (s + 1), "rs"], ["y2s%d" % s])
-
-            def last(lo, hi):
-                return T.y2s[lo:hi, 160 * s + 15:160 * s + 160:16]
-
-            def rst(lo, hi):
-                return T.rb[lo:hi, 160 * s:160 * s + 160:16]
-
-            if s < 5:
-                n = 16 * (s + 1)
-                for k, (lo, hi) in enumerate({1: ((0, 32), (64, 128)), 3: ((0, 64), (96, 128))}.get(s, ((0, 128),))):
-                    lin(T.lu[lo:hi, n:n + 10], last(lo, hi), cm, cb, ["y2s%d" % s], ["lu%d%s" % (s + 1, "ab"[k])])
-            if s in (1, 3) and fl:
-                lo = 32 if s == 1 else 64
-                cp(T.y2[lo:lo + 32, 160 * s:160 * s + 160], T.y2b[lo:lo + 32, :], ["y2b", "y2%d" % s], ["y2%dx" % s], n=160)
-            lo = 32 * (1 + s // 2)
-            lt = (T.lt0, T.lt1)[s % 2]
-            if s < 5:
-                tt(lt[lo:lo + 32, 0:10], last(lo, lo + 32), rst(lo, lo + 32), OP.subtract, ["y2s%d" % s, "rb%d" % (s + 1)], ["lt%d_%d" % (s % 2, lo // 32)])
-            if s == 0:
-                direct(1, rd)
-                cp(T.lt1[0:32, 0:10], T.dvb[0:32, 0:10], ["dvb"], ["lt1_0"])
-                lin(T.mlu[96:128, 0:20:2], T.dvb[96:128, 0:10], 0.25, -320, ["dvb"], ["ml_e3"])
-                if fl:
-                    tt(T.y2b[:], T.dvb[:, 0:10].indirect(T.clu[:, 0:10]), mask1, OP.mult, ["dvb", "c16", "mask"], ["y2b"], n=160, x=True)
-            if s in (0, 2):
-                k = s + 2
-                lo = 16 * k
-                if k == 2:
-                    ts(tmp(11), row(2), 0.0, rsc, OP.is_gt, OP.mult, ST, ["t11"])
+        for s in range(1, 8):
+            for h in (0, 1):
+                n = WID[h] // 2
+                if s == 1:
+                    w, names, lst = T.win[:, 0:quad(h).stop], ["win%d" % j for j in range(h + 1)] + ["dl"], T.dl[:, share(h)]
                 else:
-                    ts(tmp(11), row(4), 0.0, rsc, OP.is_gt, OP.mult, ST, ["t11"])
-                tt(tmp(11), tmp(11), T.dvb[:, 0:10], OP.add, ["t11", "dvb"], ["t11"])
-                lin(T.lu[lo:lo + 32, 16 * k:16 * k + 10], T.tmp[lo:lo + 32, 176:186], cm, cb, ["t11"], ["lu%dc" % k])
-            if s == 4:
-                tt(T.tmp[0:96, 192:202], last(0, 96), rst(0, 96), OP.subtract, ["y2s4", "rb5"], ["t12"])
-                ts(T.mlu[0:96, 1:20:2], T.tmp[0:96, 192:202], 0.25, None, OP.mult, None, ["t12"], ["ml_o"])
-            if s in (3, 4):
-                spread(4 - s)
-            if s == 5:
-                ts(T.mlu[96:128, 1:20:2], last(96, 128), 0.25, None, OP.mult, None, ["y2s5"], ["ml_o3"])
-                lin(T.mlu[0:96, 0:20:2], last(0, 96), 0.25, -320, ["y2s5"], ["ml_e"])
-        cp(T.km[:], T.lw[:].indirect(T.mlu[:, 0:20]), ["lw0", "lw1", "ml_e", "ml_o", "ml_e3", "ml_o3"], ["km"], n=320, x=True)
-        tr(T.kt[:], T.km[:], ["km"], ["kt"], 320, 0.5)
-        lin(T["kl%d" % rd][:], T.kt[:, 0:320:16], 1, 160, ["kt"], ["kl%d" % rd])
+                    at = 32 * (s - 2) + 16 * h
+                    w, names, lst = T.win[:], ["win0", "win1", "lu%d%d" % (s, h)], T.lu[:, at:at + n // 16]
+                b = "by" if s % 2 else "bx"
+                tt(T.go[:, halfrow(h)], w.indirect(lst), T[b][:, halfrow(h)], add, names + ["%s%d" % (b, h)], ["go%d" % h], n=n, x=True)
+                tr(T.tt[:, halfrow(h, 160 * s)], T.go[:, halfrow(h)], ["go%d" % h], ["T%d%d" % (s, h)], n)
+                if s < 7:
+                    at = 32 * (s - 1) + 16 * h
+                    w, names = upto(s, h)
+                    k = 4 * (s - 1) + 2 * h
+                    lin(T.lu[:, at:at + 16], w.indirect(T.cl[:, k:k + 1]), 2, 642, names + ["cl%d" % h], ["lu%d%d" % (s + 1, h)], n=16, x=True)
+            if s in (5, 6):
+                w, names = upto(s, 1)
+                u, k = ("uo", 1) if s == 5 else ("ue", 0)
+                ts(T[u][:, 0:512:16], w.indirect(T.sl[:, 2 * k:2 * k + 2]), EVEN, -EVEN, add, add, names + ["sl%d" % k], [u], n=32, x=True)
+                if s == 5:
+                    tr(T.lp[:], T.uo[:, 0:320], ["uo"], ["lp"], 320, 0.5)
+                    cp(T.lw[:, 320:640], T.lp[:].indirect(T.ul[:, 0:20]), ["lp", "ul"], ["lw1"], "a", n=320, x=True)
+                else:
+                    tr(T.lw[:, 0:320], T.ue[:, 0:320], ["ue"], ["lw0"], 320, 0.5)
+        w, names = upto(7, 1)
+        for k in (0, 1):
+            lin(T.mlu[:, k:32:2], w.indirect(T.sl[:, 4 + 2 * k:5 + 2 * k]), 0.5, 160 + 320 * k, names + ["sl%d" % (2 + k)], ["ml%d" % k], n=16, x=True)
+        for h in (0, 1):
+            cp(T.km[:, cols(h)], T.lw[:].indirect(T.mlu[:, part(h)]), ["lw0", "lw1", "ml0", "ml1"], ["km%d" % h], "va"[h], n=WID[h], x=True)
+        tr(T.kt[:], T.km[:], ["km0", "km1"], ["kt"], 320, 0.5)
+        lin(T["kl%d" % rd][:], T.kt[:].indirect(T.sl[:, 8:10]), 0.5, 160, ["kt", "sl4"], ["kl%d" % rd], n=32, x=True)
 
     sent = [0]
 
     def send(rd, what, h):
         dst = T.cores[rank ^ STEP[rd - 1]]
+
         def put(fn, cost, late, land, sem, inc, own):
             sent[0] += own
             node({"g": fn}, {"g": cost}, late, ["kl%d" % rd if what == "k" else "qh%d%d" % (rd, h)], [land], sem, inc)
 
         q, s, lq, ls = T["qh%d" % rd], T["sh%d" % rd], T["lq%d" % rd], T["ls%d" % rd]
+        kl = T["kl%d" % rd][:, 0:20]
         if topo.may_write(core, dst):
             rid, pid = topo.addr(dst, core)
             m, n = topo.mask(core, dst), len(topo.engines(core, dst))
             if what == "k":
-                put(lambda e: e.remote_dma(T["kr%d" % rd][:], T["kl%d" % rd][:], T.sem["kr%d" % rd], T.sem.lsem, pid, rid, m), 1.0, 2.5, "kr%d" % rd, "kr%d" % rd, n, n)
+                put(lambda e: e.remote_dma(T["kr%d" % rd][:], kl, T.sem["kr%d" % rd], T.sem.lsem, pid, rid, m), 1.0, 2.5, "kr%d" % rd, "kr%d" % rd, n, n)
                 return
             c = cols(h)
             sem = T.sem["ar%d%d" % (rd, h)]
@@ -556,7 +488,7 @@ def rank_program(g, core, T, topo):
         masks = [bits_of(eng[:n]), bits_of(eng[n:])]
         far = len(topo.engines(rel[0], dst))
         if what == "k":
-            put(lambda e: e.remote_dma(T.rlk[:], T["kl%d" % rd][:], T.sem.rk, T.sem.lsem, ways[0][1], ways[0][0], masks[0]), 1.0, 5.0, "kr%d" % rd, "kr%d" % rd, far, n)
+            put(lambda e: e.remote_dma(T.rlk[:], kl, T.sem.rk, T.sem.lsem, ways[0][1], ways[0][0], masks[0]), 1.0, 5.0, "kr%d" % rd, "kr%d" % rd, far, n)
             return
 
         w = WID[h] // 2
@@ -578,7 +510,7 @@ def rank_program(g, core, T, topo):
     def meet(rd, h):
         for t in range(4):
             tt(T.vt[:, quad(h, t, 4)], T.xh[:, 320 * t:320 * t + 320].indirect(T["kl%d" % rd][:, part(h)]), T.xg[:, quad(h, t, 4)], OP.add,
-               ["xh0%d" % t, "xh1%d" % t, "xg%d" % h, "kl%d" % rd] + ["@v"] * h, ["vt%d%d" % (h, t)], n=WID[h], x=True)
+               ["xh0%d" % t, "xh1%d" % t, "xg%d%d" % (h, t), "kl%d" % rd] + ["@v"] * h, ["vt%d%d" % (h, t)], n=WID[h], x=True)
 
     def layer(h):
         c = cols(h)
@@ -586,7 +518,7 @@ def rank_program(g, core, T, topo):
             mm(4 * h + b, WID[h], T.wq[:, 128 * b:128 * b + 128], T.wsp[:, 128 * b:128 * b + 128], T.qv[:, c], T.qvs[:, c], ["wq", "qv%d" % h])
 
     def layer_out(h, b, q):
-        scaled(T.ht[:, quad(h, b, 4)], bank(4 * h + b, WID[h]), 0.03125, ["b%d" % (4 * h + b)], ["ht%d%d" % (h, b)], q, WID[h])
+        scaled(T.ht[:, quad(h, b, 4)], bank(4 * h + b, WID[h]), 0.03125, 0.0, ["b%d" % (4 * h + b)], ["ht%d%d" % (h, b)], q, WID[h])
 
     def quant_v(h):
         quant(T.qv[:, cols(h)], T.qvs[:, cols(h)], T.vt[:, quad(h)], ["vt%d%d" % (h, t) for t in range(4)], ["qv%d" % h] + ["@v"] * (1 - h), 4 * WID[h])
@@ -594,25 +526,8 @@ def rank_program(g, core, T, topo):
     def quant_h(rd, h):
         quant(T["qh%d" % rd][:, cols(h)], T["sh%d" % rd][:, cols(h)], T.ht[:, quad(h)], ["ht%d%d" % (h, b) for b in range(4)], ["qh%d%d" % (rd, h)], 4 * WID[h])
 
-    def natural(k, rd):
-        mm(0, 320, T.uq[:], T.us[:], T["qx%d" % k][:], T["sx%d" % k][:], ["uq", "qx%d0" % k, "qx%d1" % k])
-        cp(T.sn[:], bank(0, 320), ["b0"], ["sn"], "av", n=320)
-        dma("s", [(T.fn[:], T.sn[1:128:16, :])], ["sn"], ["fn"], "fn%d" % rd)
-
-    def turn_tables(final=False):
-        for k, (tab, f) in enumerate(((T.ltb, OP.is_lt), (T.rtb, OP.is_gt))):
-            n = "lr%d" % k
-            a, d, z = T.lt2[:, 32 * k:32 * k + 20], T.ld[:, 32 * k:32 * k + 20], T.lz[:, 32 * k:32 * k + 20]
-            e0, e1 = tab[:, 0:40:2], tab[:, 1:40:2]
-            o = T.lout[:, 40 * k:40 * k + 40] if final else tab
-            tt(d, e1, e0, OP.subtract, [n + "a", n + "b"], [n + "d"])
-            ts(a, T.fn[:], 0.0, None, f, None, ["fn"], [n + "t"])
-            tt(z, d, a, OP.mult, [n + "d", n + "t"], [n + "z"])
-            tt(o[:, 0:40:2], e0, z, OP.add, [n + "a", n + "z"], [("lo%da" % k) if final else n + "a"])
-            tt(o[:, 1:40:2], e1, z, OP.subtract, [n + "b", n + "z"], [("lo%db" % k) if final else n + "b"])
-
     for h in (0, 1):
-        scores(0, h)
+        signs(0, h)
     for rd in (1, 2, 3):
         walk(rd)
         send(rd, "k", 0)
@@ -632,48 +547,17 @@ def rank_program(g, core, T, topo):
         send(rd, "h", 1)
         if rd == 1:
             quant(T.eq[:], T.es[:], T.et[:], ["et%d" % b for b in range(4)], ["eq"], n=2048)
-            for s in range(6):
-                fill(T.ui[:, 8 * s + 2 * (s // 2 + 1):8 * s + 8], 16 * (s + 1) + 1, ["ui"])
-            cp(T.uoff[:, 8:56], T.ui[:, 0:48], ["ui"], ["uoff2"])
-            fill(T.sgc[:], 1.0, ["sgc"])
-            for hi, lo in ((32, 0), (64, 2), (96, 4)):
-                fill(T.sgc[0:hi, lo:6], -1.0, ["sgc"])
-            fill(T.sgc[0:32, 6:7], -1.0, ["sgc"])
-            fill(T.sgc[32:64, 7:8], -1.0, ["sgc"])
-            fill(T.sgc[64:128, 7:8], -1.0, ["sgc"])
-            ts(T.sgn[:], T.sgc[:], -1.0, None, OP.mult, None, ["sgc"], ["sgc"])
-            cp(T.ufq[:].bitcast(dt.uint32), T.uq[:, 0:128].bitcast(dt.uint32).indirect(T.uoff[:, 8:56]), ["uq", "uoff2"], ["ufq"], n=768, x=True)
-            cp(T.ufs[:], T.us[:, 0:128].indirect(T.uoff[:, 8:56]), ["uq", "uoff2"], ["ufs"], "av", n=768, x=True)
-            for n in (0, 1):
-                for c in (0, 1):
-                    k = 2 * n + c
-                    if n == 0:
-                        lin(T.lu[:, 96 + 16 * c:106 + 16 * c], T.cid[:, 0:10], 0.5, -640 + c, CID, ["lc%d" % c])
-                    tt(T.ye[:, 160 * k:160 * k + 160], T.tw[:, 640 * (6 + n):640 * (7 + n)].indirect(T.lu[:, 96 + 16 * c:106 + 16 * c]), mask1, OP.mult,
-                       ["tw%d" % (6 + n), "lc%d" % c, "mask"], ["ye%d" % k], n=160, x=True)
-                    scan(T.yes[:, 160 * k:160 * k + 160], rst1, T.ye[:, 160 * k:160 * k + 160], OP.min, OP.add, ["rs", "ye%d" % k], ["yes%d" % k])
-                e, d = (T.ea, T.eb)[n][:, 0:10], (T.da, T.db)[n][:, 0:10]
-                first, second = T.yes[:, 320 * n + 15:320 * n + 160:16], T.yes[:, 320 * n + 175:320 * n + 320:16]
-                cp(e, first, ["yes%d" % (2 * n)], ["e%d" % n])
-                tt(d, second, first, OP.subtract, ["yes%d" % (2 * n), "yes%d" % (2 * n + 1)], ["d%d" % n])
-            cp(T.lnu[:], T.lni[:], ["lni"], ["lnu"], n=80)
-        elif rd == 2:
-            turn_direct(0)
-            turn_direct(1)
+        else:
+            turned(0)
+            turned(1)
+        if rd == 3:
+            fill(T.d0[:, 1:1280:4], 1.0, ["sb0", "sb1"], n=320)
+            quant(T.vq[:], T.vs[:], T.vb[:], ["vb"], ["vq"], 512)
         kl, kr = T["kl%d" % rd], T["kr%d" % rd]
         cp(T.kw[:], T.w4[:].indirect(kr[:]), ["w4", "kr%d" % rd], ["kw"], "av", n=320, x=True)
-        tt(T.ky[:], T.kw[:].indirect(kl[:]), T.mask[:], OP.mult, ["kw", "kl%d" % rd, "mask"], ["ky"], n=320, x=True)
-        scan(T.kys[:], T.rs[:], T.ky[:], OP.min, OP.add, ["ky", "rs"], ["kys"], n=320)
-        lin(T.mo[:, 0:20], T.kys[:, 15:320:16], 0.25, -320, ["kys"], ["mo"])
-        if rd == 1:
-            for k, tgt in ((0, T.lrow), (1, T.rrow)):
-                cp(tgt[:], T.w4[:].indirect(T.lnu[:, 40 * k:40 * k + 40]), ["w4", "lnu"], ["row%d" % k], "av", n=640, x=True)
-                dma("s", [((T.ltb, T.rtb)[k][:], tgt[0:128:16, :])], ["row%d" % k], ["lr%d" % k], "dt%d" % k)
-                tab = (T.ltb, T.rtb)[k]
-                for c in (0, 1):
-                    lin(tab[:, c:40:2], tab[:, c:40:2], 0.25, -320, ["lr%d" % k], ["lr%d%s" % (k, "ab"[c])])
-        if rd == 3:
-            quant(T.vq[:], T.vs[:], T.vb[:], ["vb"], ["vq"])
+        tt(T.ky[:], T.kw[:].indirect(kl[:, 0:20]), T.mask[:], OP.mult, ["kw", "kl%d" % rd, "mask"], ["ky"], n=320, x=True)
+        scan(T.kys[:], T.rs[:], T.ky[:], BIG, OP.min, OP.add, ["ky", "rs"], ["kys"], 320)
+        lin(T.mo[:, 0:20], T.kys[:, 15:320:16], 0.25, -320, ["kys"], ["mo_"])
         for h in (0, 1):
             lq, ls = T["lq%d" % rd], T["ls%d" % rd]
             for b in range(4):
@@ -685,29 +569,23 @@ def rank_program(g, core, T, topo):
         for h in (0, 1):
             for t in range(4):
                 tt(xn[:, quad(h, t, 4)], T.dd[:, 320 * t:320 * t + 320].indirect(T.mo[:, part(h)]), T.vt[:, quad(h, t, 4)], OP.add,
-                   ["mo", "vt%d%d" % (h, t), "dd0%d" % t, "dd1%d" % t] + ["@x"] * h, ["xn%d%d%d" % (rd, h, t)], n=WID[h], x=True)
+                   ["mo_", "vt%d%d" % (h, t), "dd0%d" % t, "dd1%d" % t] + ["@x"] * h, ["xn%d%d%d" % (rd, h, t)], n=WID[h], x=True)
             quant(qn[:, cols(h)], sn[:, cols(h)], xn[:, quad(h)], state_parts(rd, h), ["qx%d%d" % (rd, h)] + ["@x"] * (1 - h), 4 * WID[h])
+            signs(rd, h)
             if rd == 3:
                 c = cols(h)
                 dma("s", [(T.oc[:, quad(h)], qn[:, c].bitcast(dt.uint8))] + [(T.osc[4 * k:4 * k + 4, c], sn[32 * k:32 * k + 4, c]) for k in range(4)],
                     ["qx3%d" % h], [], "oq%d" % h)
-            else:
-                scores(rd, h)
         if rd < 3:
-            flips(rd)
             half_x(rd, 0)
             half_x(rd, 1)
-            natural(rd, rd)
-            turn_tables()
-            if rd == 1:
-                turn_windows()
-    natural(3, 3)
-    mm(1, 320, T.vq[:], T.vs[:], T.qx3[:], T.sx3[:], ["vq", "qx30", "qx31"])
-    cp(T.yb[:], bank(1, 320), ["b1"], ["yb"], "av", n=320)
+    mm(6, 320, T.vq[:], T.vs[:], T.qx3[:], T.sx3[:], ["vq", "qx30", "qx31"])
+    cp(T.yb[:], bank(6, 320), ["b6"], ["yb"], "av", n=320)
     dma("s", [(T.y[:], T.yb[:])], ["yb"], [], "oy")
-    turn_tables(True)
-    for k in (0, 1):
-        dma("s", [(T.lr[:, 640 * k:640 * k + 640], T.lout[:, 40 * k:40 * k + 40])], ["lo%da" % k, "lo%db" % k], [], "ol")
+    for h in (0, 1):
+        for k in (0, 1):
+            scaled(T.lout[:, 2 * AT[h] + k:2 * (AT[h] + WID[h]):2], T.win[:, quad(h, 2 + k, 4)], 0.5, 160.0, ["win%d" % h], ["lo%d%d" % (h, k)], "av", WID[h])
+    dma("s", [(T.lr[:, 640 * k:640 * k + 640], T.lout[8 * k:8 * k + 8, :]) for k in (0, 1)], ["lo00", "lo01", "lo10", "lo11"], [], "ol")
     issue()
     need("g", dict(total))
     g.wait_ge(T.sem.lsem, sent[0])

@@ -5,10 +5,12 @@ import comms_topo
 OP = AluOpType
 AF = ActivationFunctionType
 STEP = [4, 1, 2]
-BIG = 1.0e6
-WAKE, SPARE, LOOK = 0.07, 0.5, 0.3
+FAR = 4096
+WAKE, SPARE, LOOK = 0.12, 0.3, 0.3
+DRQ = "vava"
+LATE = 2.0
+ACT = 0.05
 EPS = 2.0 ** -93
-EVEN = 1.5 * 2.0 ** 24
 
 F, B, H, I, U, C4, S8 = "float32", "bfloat16", "float16", "int32", "uint16", "float8_e4m3fn_x4", "uint8"
 SCRATCH = {"ps": ("psum", [128, 4096], F)}
@@ -20,19 +22,24 @@ for _n, _w, _d in [
     ("qx0", 320, C4), ("sx0", 320, S8), ("qx1", 320, C4), ("sx1", 320, S8), ("qx2", 320, C4), ("sx2", 320, S8), ("qx3", 320, C4), ("sx3", 320, S8),
     ("qv", 320, C4), ("qvs", 320, S8),
     ("qh1", 320, C4), ("sh1", 320, S8), ("qh2", 320, C4), ("sh2", 320, S8), ("qh3", 320, C4), ("sh3", 320, S8),
-    ("lq1", 320, C4), ("ls1", 320, S8), ("lq2", 320, C4), ("ls2", 320, S8), ("lq3", 320, C4), ("ls3", 320, S8), ("rlq", 320, C4), ("rls", 320, S8),
-    ("raw", 640, I), ("oa", 320, F), ("ob", 320, F), ("d0", 1280, B), ("d1", 1280, H), ("win", 1280, B), ("nr", 320, B), ("by", 160, F), ("bx", 160, F),
-    ("go", 160, F), ("tt", 1280, F), ("lu", 192, U), ("ue", 512, B), ("uo", 512, B), ("lp", 320, B), ("lw", 640, B), ("mlu", 32, U), ("km", 320, B), ("kt", 320, B),
-    ("kl1", 32, U), ("kl2", 32, U), ("kl3", 32, U), ("kr1", 20, U), ("kr2", 20, U), ("kr3", 20, U), ("rlk", 20, U),
-    ("w4", 320, F), ("jj", 320, I), ("jk", 320, I), ("mask", 320, F), ("rs", 320, F), ("kw", 320, F), ("ky", 320, F), ("kys", 320, F), ("mo", 32, U),
+    ("lq1", 320, C4), ("ls1", 320, S8), ("lq2", 320, C4), ("ls2", 320, S8), ("lq3", 320, C4), ("ls3", 320, S8), ("rlq", 320, C4), ("rls", 320, S8), ("rlt", 320, S8),
+    ("raw", 640, I), ("rb", 640, B), ("oa", 320, F), ("d0", 1280, B), ("d1", 1280, H), ("win", 1280, B), ("nr", 320, B), ("bb", 320, F),
+    ("go", 160, F), ("tt", 1280, F), ("lu", 192, U), ("ue", 512, B), ("uo", 512, B), ("lp", 320, B), ("lw", 640, B), ("mlu", 64, U), ("km", 320, B), ("kt", 320, B),
+    ("kl1", 32, U), ("kl2", 32, U), ("kl3", 32, U), ("kr1", 20, U), ("kr2", 24, U), ("kr3", 20, U), ("rlk", 8, U),
+    ("dr", 1280, B), ("w4", 320, F), ("mask", 320, F), ("rs", 320, F), ("kw", 320, F), ("ky", 320, F), ("kys", 320, F), ("mo", 32, U),
     ("lout", 640, F), ("yb", 320, F),
     ("pi", 16, I), ("pc", 48, F), ("kk", 32, F), ("zz", 8, F), ("sel", 16, F), ("pat", 32, F), ("tmp", 64, F),
-    ("uoff", 24, U), ("cl", 24, U), ("dl", 16, U), ("yl", 16, U), ("xl", 16, U), ("el", 48, U), ("ul", 32, U), ("sl", 16, U),
+    ("uoff", 24, U), ("cl", 24, U), ("dl", 16, U), ("bl", 32, U), ("el", 48, U), ("ul", 32, U), ("sl", 16, U),
 ]:
     SCRATCH[_n] = ("sbuf", [128, _w], _d)
 
-SEMAPHORES = (["sv", "sa", "st", "sg", "dx0", "dx1", "du", "dv", "dw", "dn0", "dn1", "oy", "ol", "oq0", "oq1", "lsem", "ry0", "ry1", "rz0", "rz1", "rk"]
+SEMAPHORES = (["sv", "sa", "st", "sg", "dx0", "dx1", "os", "og", "du", "dv", "dw", "dn0", "dn1", "oy", "ol", "oq0", "oq1", "lsem", "ry0", "ry1", "rk"]
               + ["ar%d%d" % (r, h) for r in (1, 2, 3) for h in (0, 1)] + ["kr%d" % r for r in (1, 2, 3)])
+VW = (160, 160)
+
+
+def out(h, n=1, t=0, step=1):
+    return slice(n * VW[0] * h + t, n * (VW[0] + VW[1] * h), step)
 
 
 AT, WID = (0, 192), (192, 128)
@@ -67,7 +74,8 @@ def bits_of(engines):
 
 def relays_of(core, dst, topo):
     c = [k for k in topo.cores_of(core) if k != core and topo.may_write(k, dst)]
-    return [[k for k in c if topo.die(k) == topo.die(core)][0], [k for k in c if topo.die(k) != topo.die(core)][0]]
+    near, far = [k for k in c if topo.die(k) == topo.die(core)], [k for k in c if topo.die(k) != topo.die(core)]
+    return [near[0], far[0], near[1]]
 
 
 def relay_program(g, core, T, topo):
@@ -81,21 +89,18 @@ def relay_program(g, core, T, topo):
         k = rel.index(core)
         rid, pid = topo.addr(dst, core)
         m, n = topo.mask(core, dst), len(topo.engines(core, dst))
-        half = len(topo.engines(src, core)) // 2
-        sent = 0
-        if k == 0:
-            g.wait_ge(T.sem.rk, half)
-            g.remote_dma(T.kr2[:], T.rlk[:], T.sem.kr2, T.sem.lsem, pid, rid, m)
-            sent += n
+        all_ = len(topo.engines(src, core))
+        g.wait_ge(T.sem.rk, all_ // (2 if k == 2 else 4))
+        g.remote_dma(T.kr2[:, 8 * k:8 * k + 8], T.rlk[:], T.sem.kr2, T.sem.lsem, pid, rid, m)
         for h in (0, 1):
-            w = WID[h] // 2
-            a = AT[h] + w * k
-            g.wait_ge(T.sem["ry%d" % h], half)
-            g.remote_dma(T.lq2[:, a:a + w].bitcast(dt.uint8), T.rlq[:, a:a + w].bitcast(dt.uint8), T.sem["ar2%d" % h], T.sem.lsem, pid, rid, m)
-            g.wait_ge(T.sem["rz%d" % h], half)
-            g.remote_dma(T.ls2[:, a:a + w], T.rls[:, a:a + w], T.sem["ar2%d" % h], T.sem.lsem, pid, rid, m)
-            sent += 2 * n
-        g.wait_ge(T.sem.lsem, sent)
+            if k < 2:
+                a, w = out(h).start + VW[h] // 2 * k, VW[h] // 2
+                g.wait_ge(T.sem["ry%d" % h], all_ // (2 + 2 * h))
+                g.remote_dma(T.lq2[:, a:a + w].bitcast(dt.uint8), T.rlq[:, a:a + w].bitcast(dt.uint8), T.sem["ar2%d" % h], T.sem.lsem, pid, rid, m)
+            else:
+                g.wait_ge(T.sem["ry%d" % h], all_ // (1 + h))
+                g.remote_dma(T.ls2[:, out(h)], (T.rls, T.rlt)[h][:, out(h)], T.sem["ar2%d" % h], T.sem.lsem, pid, rid, m)
+        g.wait_ge(T.sem.lsem, 3 * n)
 
 
 def rank_program(g, core, T, topo):
@@ -116,6 +121,8 @@ def rank_program(g, core, T, topo):
             if k[0] != "@":
                 pre.update(readers.get(k, ()))
         i = len(nodes)
+        if "a" in cost and sem is None:
+            cost["a"] += ACT
         nodes.append({"fns": fns, "cost": cost, "late": late, "pre": sorted(pre), "order": sorted(pre | after), "sem": sem, "inc": inc})
         for k in r:
             readers.setdefault(k, set()).add(i)
@@ -126,14 +133,14 @@ def rank_program(g, core, T, topo):
     def op(q, fn, r, w, us):
         node({q: fn}, {q: us}, 0.0, r, list(w) + (["gpsimd"] if q == "g" else []), None, 1)
 
-    def dma(q, pairs, r, w, sem):
+    def dma(q, pairs, r, w, sem, late=2.0):
         def go(e):
             for o, i in pairs:
                 e.dma_start(o, i).then_inc(T.sem[sem], 16)
-        node({q: go}, {q: 0.06 * len(pairs)}, 2.0, r, w, sem, 16 * len(pairs))
+        node({q: go}, {q: 0.1 * len(pairs)}, late, r, w, sem, 16 * len(pairs))
 
     def us(n, cycles, gather):
-        return 0.05 + n * 0.0015 if gather else max(64, n * cycles) * 0.001
+        return 0.05 + n * 0.0016 if gather else max(64, n * cycles) * 0.001
 
     def tt(o, a, b, f, r, w, n=10, x=False, c=2):
         op("v", lambda e: e.tensor_tensor(o, a, b, f), r, w, us(n, c, x))
@@ -162,8 +169,8 @@ def rank_program(g, core, T, topo):
     def scan(o, d0, d1, first, f0, f1, r, w, n, c=1):
         op("v", lambda e: e.tensor_tensor_scan(o, d0, d1, first, f0, f1), r, w, us(n, c, False))
 
-    def mm(bank, n, lq, lsc, rq, rsc, r):
-        op("t", lambda e: e.matmul_mx(T.ps[:, 512 * bank:512 * bank + n], lq, lsc, rq, rsc, True, True), r, ["b%d" % bank], (n + 16) * 0.0011)
+    def mm(bank, n, lq, lsc, rq, rsc, r, turn=()):
+        op("t", lambda e: e.matmul_mx(T.ps[:, 512 * bank:512 * bank + n], lq, lsc, rq, rsc, True, True), r, ["b%d" % bank] + list(turn), (n + 16) * 0.0011)
 
     def fill(o, c, w, n=10):
         op("v", lambda e: e.memset(o, c), [], w, us(n, 0.5, False))
@@ -212,7 +219,7 @@ def rank_program(g, core, T, topo):
             order.append((s, len(order), i, q))
             for k in out[i]:
                 left[k] -= 1
-                ready[k] = max(ready[k], free[q] + nodes[i]["late"] + WAKE)
+                ready[k] = max(ready[k], free[q] + (nodes[i]["late"] + WAKE if i in nodes[k]["pre"] else 0.0))
                 if left[k] == 0:
                     open_.append(k)
         return [(i, q) for s, m, i, q in order]
@@ -244,13 +251,15 @@ def rank_program(g, core, T, topo):
     def bank(b, n):
         return T.ps[:, 512 * b:512 * b + n]
 
-    dma("s", [(T.ub[:], T.u[:])], [], ["ub"], "du")
-    for k, (q, tab) in enumerate((("a", T.lam), ("s", T.rho))):
-        dma(q, [(T.raw[16 * gr + 8 * k:16 * gr + 8 * k + 8, :], tab[:]) for gr in range(8)], [], ["raw%d" % k], "dn%d" % k)
-    for h in (0, 1):
-        dma("sa"[h], [(T.x0[:, quad(h)], T.x[:, quad(h)])], [], ["x0%d" % h], "dx%d" % h)
-    dma("s", [(T.wq[:].bitcast(dt.uint8), T.wc[:]), (T.wsp[:], T.ws[:])], [], ["wq"], "dw")
-    dma("s", [(T.vb[:], T.v[:])], [], ["vb"], "dv")
+    for k, (q, tab) in enumerate((("s", T.lam), ("a", T.rho))):
+        if k:
+            dma("a", [(T.ub[:], T.u[:])], [], ["ub", "@d1"], "du", LATE)
+        else:
+            dma("s", [(T.x0[:, quad(0)], T.x[:, quad(0)])], [], ["x00", "@d0"], "dx0", LATE + 0.2)
+        dma(q, [(T.raw[16 * gr + k:16 * gr + 16:2, :], tab[:]) for gr in range(8)], [], ["raw%d" % k, "@d%d" % k], "dn%d" % k, LATE)
+    dma("s", [(T.x0[:, quad(1)], T.x[:, quad(1)])], ["@d0"], ["x01"], "dx1", LATE + 0.2)
+    dma("s", [(T.wq[:].bitcast(dt.uint8), T.wc[:]), (T.wsp[:], T.ws[:])], ["x00"], ["wq"], "dw", 3.5)
+    ts(T.rb[:], T.raw[:], -160.0, None, OP.add, None, ["raw0", "raw1"], ["rb0"], n=640)
 
     def iota(o, pattern, base, cm, w, fl=True):
         n = 1
@@ -267,15 +276,19 @@ def rank_program(g, core, T, topo):
     for a in range(4):
         rows = slice(32 * a, 32 * a + 32)
         if a > 0:
-            iota(T.sel[rows, 0:2 * a], [[161, 2 * a]], 160, 0, ["sel%da" % a])
+            iota(T.sel[rows, 0:2 * a], [[162, 2 * a]], 160, 0, ["sel%da" % a])
         if a < 3:
-            iota(T.sel[rows, 2 * a + 1:6], [[159, 5 - 2 * a]], 159 * (2 * a + 1) + 175 + 2 * a, 0, ["sel%db" % a])
-            fill(T.sel[rows, 2 * a:2 * a + 1], 175.0, ["sel%dc" % a])
+            lo = 2 * a + (a > 0)
+            iota(T.sel[rows, lo:6], [[158, 6 - lo]], 158 * lo + 175 + 4 * a, 0, ["sel%db" % a])
+        if 0 < a < 3:
+            iota(T.sel[rows, 2 * a:2 * a + 1], [[0, 1]], 175, 0, ["sel%dc" % a])
     SEL = ["sel%d%s" % (a, c) for a in range(4) for c in "abc"]
+    LAST = {"so": 1, "me": 175, "mo": 1132, "nb": 1}
+    for k, name in enumerate(LAST):
+        iota(T.pc[96:128, 40 + k:41 + k], [[0, 1]], LAST[name], 0, [name + "3"])
     iota(T.pat[:, 10:30], [[64, 5], [16, 2], [32, 2]], 0, 0, ["patb"])
     iota(T.w4[:], [[4, 320]], 1280, 0, ["w4"])
-    iota(T.jj[:], [[1, 320]], 128, -1, ["jj"], False)
-    iota(T.jk[:], [[1, 320]], 0, 0, ["jk"], False)
+    iota(T.rs[:], [[0, 20], [FAR, 16]], 0, 0, ["rs"])
 
     digits = {"i": (0, 15), "q7": (0, 7), "q8": (3, 1), "p32": (0, 31), "b": (4, 1), "a": (5, 3), "ih": (1, 7), "y": (0, 1), "x": (1, 1)}
     place = {}
@@ -288,91 +301,104 @@ def rank_program(g, core, T, topo):
         return T.pc[:, place[name]:place[name] + 1]
 
     def new(name, a, s1, s2, f1, f2):
-        place[name] = len(place)
+        place[name] = 40 + list(LAST).index(name) if name in LAST else len(place)
         use = [a] + [s for s in (s1, s2) if isinstance(s, str)]
         s1, s2 = [col(s) if isinstance(s, str) else s if s is None else float(s) for s in (s1, s2)]
-        ts(col(name), col(a), s1, s2, f1, f2, use, [name])
+        if name in LAST:
+            aff(T.pc[0:96, place[name]:place[name] + 1], T.pc[0:96, place[a]:place[a] + 1], s1, s2, use + [name + "3"], [name])
+        elif (f1, f2) == (mul, add):
+            aff(col(name), col(a), s1, s2, use, [name])
+        else:
+            ts(col(name), col(a), s1, s2, f1, f2, use, [name])
 
-    def last_pair(name, v):
-        k = place[name]
-        fill(T.pc[96:128, k:k + 1], float(v), [name])
+    def aff(o, a, m, b, r, w, n=10):
+        node({"a": lambda e: e.activation(o, a, AF.Identity, bias=b, scale=m), "v": lambda e: e.tensor_scalar(o, a, m, b, OP.mult, OP.add)},
+             {"a": us(n, 1, False), "v": us(n, 1, False)}, 0.0, r, w, None, 1)
 
     mul, add = OP.mult, OP.add
     fill(T.zz[:], 0.0, ["zz"])
-    new("q16", "q7", 16, None, mul, None)
-    new("n16", "q8", -32, 16, mul, add)
+    new("q16", "ih", 16, None, mul, None)
+    new("n16", "y", -32, 16, mul, add)
     new("n", "q16", "n16", 112, add, OP.min)
     ts(T.uoff[:, 0:8], T.zz[:], col("q16"), 1.0, add, add, ["zz", "q16"], ["uoff0"])
     ts(T.uoff[:, 8:16], T.zz[:], col("q16"), None, add, None, ["zz", "q16"], ["uoff1"])
     ts(T.uoff[:, 16:24], T.zz[:], col("n"), 0.0, add, OP.max, ["zz", "n"], ["uoff2"])
     quant(T.uq[:], T.us[:], T.ub[:], ["ub"], ["uq"], 512)
-    for k in (1, 2, 0):
+
+    def picked(k, after):
         c, o = slice(128 * k, 128 * k + 128), T.uoff[:, 8 * k:8 * k + 8]
-        cp(T.upq[:, c].bitcast(dt.uint32), T.uq[:].bitcast(dt.uint32).indirect(o), ["uq", "uoff%d" % k], ["upq%d" % k], n=128, x=True)
-        cp(T.ups[:, c], T.us[:].indirect(o), ["uq", "uoff%d" % k], ["ups%d" % k], "av", n=128, x=True)
-    new("sf", "q8", -2, 1, mul, add)
+        cp(T.upq[:, c].bitcast(dt.uint32), T.uq[:].bitcast(dt.uint32).indirect(o), ["uq", "uoff%d" % k] + after, ["upq%d" % k], n=128, x=True)
+        cp(T.ups[:, c], T.us[:].indirect(o), ["uq", "uoff%d" % k], ["ups%d" % k], "a", n=128, x=True)
+
+    picked(1, [])
+    picked(2, [])
+    new("sf", "y", -2, 1, mul, add)
     new("i15", "i", -1, 15, mul, add)
-    new("ii", "i", "i15", None, mul, None)
+    new("ii", "i", "i15", 0, mul, add)
     new("sd", "ii", 0, -1, OP.is_equal, mul)
     new("e0", "q7", 80, "q8", mul, add)
-    new("e1", "e0", 40, None, add, None)
+    new("e1", "e0", 1, 40, mul, add)
     for k in (0, 1):
         lin(T.el[:, 24 * k:24 * k + 20], T.kk[:, 0:20], 2, col("e%d" % k), ["kk", "e%d" % k], ["el%d" % k])
     new("d2", "p32", 4, 2, mul, add)
     lin(T.dl[:, 0:10], T.kk[:, 0:10], 128, col("d2"), ["kk", "d2"], ["dl"])
     new("px", "b", 16, "p32", mul, add)
-    lin(T.tmp[:, 0:10], T.kk[:, 0:10], 32, col("p32"), ["kk", "p32"], ["yf"])
-    ts(T.tmp[:, 16:26], T.pat[:, 0:10], col("px"), None, add, None, ["pata", "px"], ["xf"])
-    cp(T.yl[:, 0:10], T.tmp[:, 0:10], ["yf"], ["yl"])
-    cp(T.xl[:, 0:10], T.tmp[:, 16:26], ["xf"], ["xl"])
-    fill(T.tt[:, 0:160], 0.0, ["T0"], n=320)
-    lin(T.tt[:, 0:160:16], T.tmp[:, 0:10], 2, -320, ["yf", "T0"], ["T0a"])
-    lin(T.tt[:, 1:160:16], T.tmp[:, 16:26], 2, -320, ["xf", "T0"], ["T0b"])
+    for h in (0, 1):
+        at, n = AT[h] // 16, WID[h] // 32
+        lin(T.bl[:, at:at + n], T.kk[:, 0:n], 32, col("p32"), ["kk", "p32"], ["bl%d0" % h])
+        lin(T.bl[:, at + n:at + 2 * n], T.pat[:, 0:n], 1, col("px"), ["pata", "px"], ["bl%d1" % h])
+    new("sd2", "sd", 2, 0, mul, add)
+    fill(T.ue[:, 0:320], 0.0, ["ue"], n=320)
+    for t, v, names in ((0, 0.0, ["d0c"]), (1, 1.0, ["sb0", "sb1"]), (3, 0.0, ["d03"])):
+        scaled(T.d0[:, t:1280:4], T.ue[:, 0:320], 1.0, v, ["ue"], names, "a", 320)
+    scaled(T.uo[:, 0:320], T.ue[:, 0:320], 1.0, 0.0, ["ue"], ["uo"], "a", 320)
+    aff(T.tt[:, 0:160], T.ue[:, 0:160], 1.0, 0.0, ["ue"], ["T0"], 160)
+    new("ty", "p32", 2, -320, mul, add)
+    new("tx", "px", 2, -320, mul, add)
+    aff(T.tt[:, 0:160:16], T.kk[:, 0:10], 64.0, col("ty"), ["kk", "ty", "T0"], ["T0a"])
+    aff(T.tt[:, 1:160:16], T.pat[:, 0:10], 2.0, col("tx"), ["pata", "tx", "T0"], ["T0b"])
     for h in (0, 1):
         new("c%d" % h, "i", WID[h] // 32 - 1, 16, OP.min, mul)
         ts(T.cl[:, 2 * h:24:4], T.sel[:, 0:6], col("c%d" % h), float(AT[h] // 2), add, add, SEL + ["c%d" % h], ["cl%d" % h])
-    new("se", "a", 322, -1, mul, add)
+    new("se", "a", 324, -2, mul, add)
     new("se0", "se", 0, None, OP.max, None)
-    new("so", "a", 322, 160, mul, add)
-    last_pair("so", 1)
-    lin(T.tmp[:, 32:34], T.kk[:, 0:2], 8, col("ih"), ["kk", "ih"], ["ku"])
+    new("so", "a", 324, 160, mul, add)
+    aff(T.tmp[:, 32:34], T.kk[:, 0:2], 8.0, col("ih"), ["kk", "ih"], ["ku"])
     ts(T.tmp[:, 32:34], T.tmp[:, 32:34], 9.0, 16.0, OP.min, mul, ["ku"], ["ku"])
     ts(T.sl[:, 0:2], T.tmp[:, 32:34], col("se0"), None, add, None, ["ku", "se0"], ["sl0"])
     ts(T.sl[:, 2:4], T.tmp[:, 32:34], col("so"), None, add, None, ["ku", "so"], ["sl1"])
+    new("me", "a", 4, 1123, mul, add)
+    new("mo", "a", 4, 965, mul, add)
     new("c9", "i", 9, 16, OP.min, mul)
-    new("me", "a", 2, 1129, mul, add)
-    last_pair("me", 175)
-    new("mo", "a", 2, 970, mul, add)
-    last_pair("mo", 1126)
-    ts(T.sl[:, 4:5], col("c9"), col("me"), None, add, None, ["c9", "me"], ["sl2"])
-    ts(T.sl[:, 6:7], col("c9"), col("mo"), None, add, None, ["c9", "mo"], ["sl3"])
+    ts(T.sl[:, 4:8:2], T.pc[:, place["me"]:place["me"] + 2], col("c9"), None, add, None, ["c9", "me", "mo"], ["sm"])
     new("nb", "b", -1, 1, mul, add)
-    last_pair("nb", 1)
     new("yx", "y", "x", "nb", OP.subtract, mul)
-    new("iyx", "i", "yx", None, add, None)
-    lin(T.tmp[:, 40:42], T.kk[:, 0:2], 16, col("iyx"), ["kk", "iyx"], ["kf"])
-    ts(T.sl[:, 8:10], T.tmp[:, 40:42], 16.0, 304.0, mul, OP.min, ["kf"], ["sl4"])
+    new("iyx", "i", 1, "yx", mul, add)
+    aff(T.tmp[:, 40:42], T.kk[:, 0:2], 16.0, col("iyx"), ["kk", "iyx"], ["kf"])
+    ts(T.sl[:, 8:10], T.tmp[:, 40:42], 16.0, 304.0, mul, OP.min, ["kf"], ["sk"])
     ts(T.ul[:, 0:20], T.pat[:, 10:30], col("i"), None, add, None, ["patb", "i"], ["ul"])
-    fill(T.ue[:], 0.0, ["ue"], n=512)
-    fill(T.uo[:], 0.0, ["uo"], n=512)
+    new("far", "i", -FAR, 0, mul, add)
 
-    ts(T.jj[:], T.jj[:], 15, None, OP.bitwise_and, None, ["jj"], ["jj"], n=320)
-    ts(T.mask[:], T.jj[:], 0.0, None, OP.is_equal, None, ["jj"], ["mask"], n=320)
-    ts(T.jk[:], T.jk[:], 15, None, OP.bitwise_and, None, ["jk"], ["jk"], n=320)
-    ts(T.rs[:], T.jk[:], 0.0, BIG, OP.is_gt, OP.mult, ["jk"], ["rs"], n=320)
-
-    for t, v in ((0, 0.0), (2, 1.0), (3, -1.0)):
-        fill(T.d0[:, t:1280:4], v, ["d0c"] if t != 2 else ["sf0", "sf1"], n=320)
-    RAW = ["raw0", "raw1"]
+    RAW = ["rb0", "rb1", "rb2"]
     for h in (0, 1):
-        c, n = cols(h), WID[h]
-        le, lo = T.el[:, part(h)], T.el[:, 24 + AT[h] // 16:24 + (AT[h] + n) // 16]
-        cp(T.oa[:, c], T.raw[:].indirect(lo), RAW + ["el1"], ["oa%d" % h], n=n, x=True)
-        scaled(T.ob[:, c], T.oa[:, c], 1.0, -320.0, ["oa%d" % h], ["ob%d" % h], "av", n)
-        tt(T.d1[:, quad(h, 0, 4)], T.raw[:].indirect(le), T.oa[:, c], OP.subtract, RAW + ["el0", "oa%d" % h], ["dif%d" % h], n=n, x=True)
-        tt(T.d1[:, quad(h, 2, 4)], T.raw[:].indirect(le), T.ob[:, c], OP.add, RAW + ["el0", "ob%d" % h], ["sum%d" % h], n=n, x=True)
-        ts(T.d1[:, quad(h, 3, 4)], T.d1[:, quad(h, 2, 4)], 2.0, None, mul, None, ["sum%d" % h], ["two%d" % h], n=n, c=0.5)
-    ts(T.d1[:, 1:1280:4], T.d0[:, 0:1280:4], 0.0, None, mul, None, ["d0c"], ["d1c"], n=320, c=0.5)
+        n = WID[h]
+        for k in (1, 0):
+            scaled(T.dr[:, quad(h, 3 * k, 4)], T.rb[:].indirect(T.el[:, 24 * k + AT[h] // 16:24 * k + (AT[h] + n) // 16]), 2.0, 0.0,
+                   RAW + ["el%d" % k], ["dr%d%d" % (h, 3 * k)], DRQ[2 * h + k], n, x=True)
+        for t, m in ((1, -1.0), (2, 1.0)):
+            scaled(T.dr[:, quad(h, t, 4)], T.dr[:, quad(h, 3, 4)], m, 0.0, ["dr%d3" % h], ["dr%d%d" % (h, t)], "av", n, 0.5)
+
+    def twice(after):
+        cp(T.d1[:, quad(1, 1, 4)], T.d1[:, quad(1, 0, 4)], ["dif1", after], ["d1d"], n=WID[1], c=0.5)
+
+    def differences():
+        scaled(T.oa[:], T.dr[:, 3:1280:4], 0.5, 0.0, ["dr03", "dr13"], ["oa"], "a", 320)
+        tt(T.d1[:, 0:1280:4], T.rb[:].indirect(T.el[:, 0:20]), T.oa[:], OP.subtract, RAW + ["el0", "oa", "@s1"], ["dif0", "dif1"], n=320, x=True)
+        tt(T.d1[:, 2:1280:4], T.rb[:].indirect(T.el[:, 0:20]), T.oa[:], OP.add, RAW + ["el0", "oa", "@s1"], ["sum"], n=320, x=True)
+        ts(T.d1[:, 3:1280:4], T.d1[:, 2:1280:4], 2.0, None, mul, None, ["sum"], ["two"], n=320, c=0.5)
+        ts(T.d1[:, quad(0, 1, 4)], T.d0[:, quad(0, 0, 4)], 0.0, None, mul, None, ["d0c", "@s1"], ["d1c"], n=WID[0], c=0.5)
+        twice("@s1")
+        scaled(T.d0[:, 3:1280:4], T.d0[:, 0:1280:4], 1.0, -1.0, ["d0c", "kl10"], ["d03"], "a", 320)
 
     for h in (0, 1):
         quant(T.qx0[:, cols(h)], T.sx0[:, cols(h)], T.x0[:, quad(h)], ["x0%d" % h], ["qx0%d" % h], 4 * WID[h])
@@ -391,69 +417,83 @@ def rank_program(g, core, T, topo):
         x = T["x%d" % k]
         for t in range(4):
             scaled(T.xh[:, 320 * t + AT[h]:320 * t + AT[h] + WID[h]], x[:, quad(h, t, 4)], 0.5, 0.0, state_parts(k, h)[t % len(state_parts(k, h)):][:1],
-                   ["xh%d%d" % (h, t)], "av", WID[h], 0.5)
-            scaled(T.xg[:, quad(h, t, 4)], x[:, quad(h, t, 4)], 0.5, 0.0, state_parts(k, h)[t % len(state_parts(k, h)):][:1], ["xg%d%d" % (h, t)], "av", WID[h], 0.5)
-
-    half_x(0, 0)
-    half_x(0, 1)
+                   ["xh%d%d" % (h, t)], "a", WID[h], 0.5)
+        scaled(T.xg[:, quad(h)], x[:, quad(h)], 0.5, 0.0, state_parts(k, h) + ["bb1"], ["xg%d" % h], "a", 4 * WID[h], 0.5)
 
     def signs(k, h):
         n = WID[h]
         kinds = [(0, T.d0[:, quad(h, 2, 4)], col("sf"), EPS, "sf"), (1, T.d0[:, quad(h, 1, 4)], col("sd"), EPS, "sb"), (2, T.nr[:, cols(h)], 1.0, -EPS, "nr")]
-        for j, o, sc, eps, name in kinds[k == 0:1 if k == 3 else 3]:
+        if k == 0:
+            kinds = [(1, T.d0[:, quad(h, 2, 4)], col("sd"), EPS, "sf"), kinds[2]]
+        for j, o, sc, eps, name in kinds[:1 if k == 3 else 3]:
             c, b = slice(128 * j, 128 * j + 128), 3 * h + j
-            mm(b, n, T.upq[:, c], T.ups[:, c], T["qx%d" % k][:, cols(h)], T["sx%d" % k][:, cols(h)], ["upq%d" % j, "ups%d" % j, "qx%d%d" % (k, h)])
-            sign(o, bank(b, n), sc, eps, ["b%d" % b, "sf", "sd"], ["%s%d" % (name, h)], n)
-        scan(T.win[:, quad(h)], T.d0[:, quad(h)], T.d1[:, quad(h)], 0.0, mul, add,
-             ["d0c", "d1c"] + ["%s%d" % (s, h) for s in ("sf", "sb", "dif", "sum", "two")], ["win%d" % h], 4 * n, 0.5)
+            mm(b, n, T.upq[:, c], T.ups[:, c], T["qx%d" % k][:, cols(h)], T["sx%d" % k][:, cols(h)], ["upq%d" % j, "ups%d" % j, "qx%d%d" % (k, h)],
+               ["@n"] * (1 - h))
+            r, w = ["b%d" % b, "sf", "sd", "sd2", "d0c"], ["%s%d" % (name, h)]
+            if h == 0 or j == 0:
+                sign(o, bank(b, n), AF.Sign, sc, eps, r, w, n)
+                if k == 0 and j == 1:
+                    sign(o, o, AF.Relu, 1.0, 0.0, w, w, n)
+            elif j == 2:
+                ts(o, bank(b, n), 0.0, 0.5, OP.is_gt, mul, r, w, n)
+            elif k == 0:
+                ts(o, bank(b, n), sc, 0.0, mul, OP.is_ge, r, w, n)
+            else:
+                ts(o, bank(b, n), 0.0, col("sd2"), OP.is_gt, mul, r, w, n)
+        d1, names = (T.d1, [("d1c", "d1d")[h], "dif%d" % h, "sum", "two"]) if k else (T.dr, ["dr%d%d" % (h, t) for t in range(4)])
+        scan(T.win[:, quad(h)], T.d0[:, quad(h)], d1[:, quad(h)], 0.0, mul, add,
+             names + ["d0c", "d03", "sf%d" % h, "sb%d" % h, "@q%d" % k], ["win%d" % h], 4 * n, 0.5)
         if k < 3:
-            for name, lst in (("by", T.yl), ("bx", T.xl)):
-                scaled(T[name][:, halfrow(h)], T.nr[:, 0:AT[h] + n].indirect(lst[:, share(h)]), 0.25, 0.25,
-                       ["nr%d" % j for j in range(h + 1)] + ["yl", "xl"], ["%s%d" % (name, h)], "a", n // 2, x=True)
+            scaled(T.bb[:, cols(h)], T.nr[:, cols(h)].indirect(T.bl[:, part(h)]), (0.25, 1.0)[h], (0.25, 0.0)[h],
+                   ["nr%d" % h, "bl%d0" % h, "bl%d1" % h], ["bb%d" % h], "a", n, x=True)
 
-    def sign(o, i, sc, eps, r, w, n):
-        op("a", lambda e: e.activation(o, i, AF.Sign, bias=eps, scale=sc), r, w, us(n, 1, False))
+    def sign(o, i, f, sc, eps, r, w, n):
+        op("a", lambda e: e.activation(o, i, f, bias=eps, scale=sc), r, w, us(n, 1, False))
 
-    def turned(h):
-        tt(T.d1[:, quad(h, 0, 4)], T.d1[:, quad(h, 0, 4)], T.d0[:, quad(h, 2, 4)], mul, ["dif%d" % h, "sf%d" % h], ["dif%d" % h], n=WID[h])
+    def turned(rd):
+        tt(T.d1[:, 0:1280:4], T.d1[:, 0:1280:4], T.d0[:, 2:1280:4], mul, ["sf0", "sf1", "@g%d" % rd], ["dif0", "dif1", "@i"], n=320)
 
     def upto(s, h):
         names = ["T0a", "T0b"] + ["T%d%d" % (k, j) for k in range(1, s + 1) for j in (0, 1) if (k, j) <= (s, h)]
         return T.tt[:, 0:halfrow(h, 160 * s).stop], names
 
+    def step(s, h, after=()):
+        n = WID[h] // 2
+        if s == 1:
+            w, names, lst = T.win[:, 0:quad(h).stop], ["win%d" % j for j in range(h + 1)] + ["dl"], T.dl[:, share(h)]
+        else:
+            at = 32 * (s - 2) + 16 * h
+            w, names, lst = T.win[:], ["win0", "win1", "lu%d%d" % (s, h)], T.lu[:, at:at + n // 16]
+        at = AT[h] + n * (1 - s % 2)
+        tt(T.go[:, halfrow(h)], w.indirect(lst), T.bb[:, at:at + n], add, names + ["bb%d" % h] + list(after), ["go%d" % h], n=n, x=True)
+        tr(T.tt[:, halfrow(h, 160 * s)], T.go[:, halfrow(h)], ["go%d" % h], ["T%d%d" % (s, h)], n)
+        if s < 7:
+            at = 32 * (s - 1) + 16 * h
+            w, names = upto(s, h)
+            k = 4 * (s - 1) + 2 * h
+            lin(T.lu[:, at:at + 16], w.indirect(T.cl[:, k:k + 1]), 2, 642, names + ["cl%d" % h], ["lu%d%d" % (s + 1, h)], n=16, x=True)
+
     def walk(rd):
         for s in range(1, 8):
             for h in (0, 1):
-                n = WID[h] // 2
-                if s == 1:
-                    w, names, lst = T.win[:, 0:quad(h).stop], ["win%d" % j for j in range(h + 1)] + ["dl"], T.dl[:, share(h)]
-                else:
-                    at = 32 * (s - 2) + 16 * h
-                    w, names, lst = T.win[:], ["win0", "win1", "lu%d%d" % (s, h)], T.lu[:, at:at + n // 16]
-                b = "by" if s % 2 else "bx"
-                tt(T.go[:, halfrow(h)], w.indirect(lst), T[b][:, halfrow(h)], add, names + ["%s%d" % (b, h)], ["go%d" % h], n=n, x=True)
-                tr(T.tt[:, halfrow(h, 160 * s)], T.go[:, halfrow(h)], ["go%d" % h], ["T%d%d" % (s, h)], n)
-                if s < 7:
-                    at = 32 * (s - 1) + 16 * h
-                    w, names = upto(s, h)
-                    k = 4 * (s - 1) + 2 * h
-                    lin(T.lu[:, at:at + 16], w.indirect(T.cl[:, k:k + 1]), 2, 642, names + ["cl%d" % h], ["lu%d%d" % (s + 1, h)], n=16, x=True)
+                step(s, h, ["sk", "sm", "sl0", "sl1", "ul"] * (s == 4))
             if s in (5, 6):
                 w, names = upto(s, 1)
                 u, k = ("uo", 1) if s == 5 else ("ue", 0)
-                ts(T[u][:, 0:512:16], w.indirect(T.sl[:, 2 * k:2 * k + 2]), EVEN, -EVEN, add, add, names + ["sl%d" % k], [u], n=32, x=True)
+                cp(T[u][:, 0:512:16], w.indirect(T.sl[:, 2 * k:2 * k + 2]), names + ["sl%d" % k], [u], "a", n=32, x=True)
                 if s == 5:
                     tr(T.lp[:], T.uo[:, 0:320], ["uo"], ["lp"], 320, 0.5)
                     cp(T.lw[:, 320:640], T.lp[:].indirect(T.ul[:, 0:20]), ["lp", "ul"], ["lw1"], "a", n=320, x=True)
                 else:
                     tr(T.lw[:, 0:320], T.ue[:, 0:320], ["ue"], ["lw0"], 320, 0.5)
+
         w, names = upto(7, 1)
         for k in (0, 1):
-            lin(T.mlu[:, k:32:2], w.indirect(T.sl[:, 4 + 2 * k:5 + 2 * k]), 0.5, 160 + 320 * k, names + ["sl%d" % (2 + k)], ["ml%d" % k], n=16, x=True)
+            lin(T.mlu[:, k:32:2], w.indirect(T.sl[:, 4 + 2 * k:5 + 2 * k]), 0.5, 160 + 320 * k, names + ["sm"], ["ml%d" % k], n=16, x=True)
         for h in (0, 1):
             cp(T.km[:, cols(h)], T.lw[:].indirect(T.mlu[:, part(h)]), ["lw0", "lw1", "ml0", "ml1"], ["km%d" % h], "va"[h], n=WID[h], x=True)
         tr(T.kt[:], T.km[:], ["km0", "km1"], ["kt"], 320, 0.5)
-        lin(T["kl%d" % rd][:], T.kt[:].indirect(T.sl[:, 8:10]), 0.5, 160, ["kt", "sl4"], ["kl%d" % rd], n=32, x=True)
+        lin(T["kl%d" % rd][:], T.kt[:].indirect(T.sl[:, 8:10]), 0.5, 160, ["kt", "sk"], ["kl%d0" % rd, "kl%d1" % rd], n=32, x=True)
 
     sent = [0]
 
@@ -462,7 +502,7 @@ def rank_program(g, core, T, topo):
 
         def put(fn, cost, late, land, sem, inc, own):
             sent[0] += own
-            node({"g": fn}, {"g": cost}, late, ["kl%d" % rd if what == "k" else "qh%d%d" % (rd, h)], [land], sem, inc)
+            node({"g": fn}, {"g": cost}, late, ["kl%d0" % rd, "kl%d1" % rd] if what == "k" else ["qh%d%d" % (rd, j) for j in range(h + 1)], [land, "@sent"], sem, inc)
 
         q, s, lq, ls = T["qh%d" % rd], T["sh%d" % rd], T["lq%d" % rd], T["ls%d" % rd]
         kl = T["kl%d" % rd][:, 0:20]
@@ -472,62 +512,63 @@ def rank_program(g, core, T, topo):
             if what == "k":
                 put(lambda e: e.remote_dma(T["kr%d" % rd][:], kl, T.sem["kr%d" % rd], T.sem.lsem, pid, rid, m), 1.0, 2.5, "kr%d" % rd, "kr%d" % rd, n, n)
                 return
-            c = cols(h)
+            c = out(h)
             sem = T.sem["ar%d%d" % (rd, h)]
 
             def go(e):
                 e.remote_dma(lq[:, c].bitcast(dt.uint8), q[:, c].bitcast(dt.uint8), sem, T.sem.lsem, pid, rid, m)
                 e.remote_dma(ls[:, c], s[:, c], sem, T.sem.lsem, pid, rid, m)
 
-            put(go, 2.0, 4.0, "lq%d%d" % (rd, h), "ar%d%d" % (rd, h), 2 * n, 2 * n)
+            put(go, 1.2, 3.5, "lq%d%d" % (rd, h), "ar%d%d" % (rd, h), 2 * n, 2 * n)
             return
         rel = relays_of(core, dst, topo)
         ways = [topo.addr(k, core) for k in rel]
+        far = len(topo.engines(rel[0], dst))
         eng = topo.engines(core, rel[0])
         n = len(eng) // 2
-        masks = [bits_of(eng[:n]), bits_of(eng[n:])]
-        far = len(topo.engines(rel[0], dst))
+        three = [eng[:n // 2], eng[n // 2:n], eng[n:]]
         if what == "k":
-            put(lambda e: e.remote_dma(T.rlk[:], kl, T.sem.rk, T.sem.lsem, ways[0][1], ways[0][0], masks[0]), 1.0, 5.0, "kr%d" % rd, "kr%d" % rd, far, n)
+            put(lambda e: e.remote_dma_fused([RemoteDMATransfer(dst_ids=[DstId(rid=ways[k][0], pnc=ways[k][1])], dma_engine_mask=bits_of(three[k]), remote_sem=T.sem.rk,
+                                                                src=T.kl2[:, 8 * k:8 * k + 8], dst=T.rlk[:]) for k in range(3)], local_sem=T.sem.lsem),
+                0.6, 5.0, "kr%d" % rd, "kr%d" % rd, 3 * far, 2 * n)
             return
+        a, w = out(h).start, VW[h] // 2
 
-        w = WID[h] // 2
-
-        def both_ways(e, view, land, sem):
-            tr_ = []
-            for k in (0, 1):
-                a = AT[h] + w * k
-                tr_.append(RemoteDMATransfer(dst_ids=[DstId(rid=ways[k][0], pnc=ways[k][1])], dma_engine_mask=masks[k], remote_sem=sem,
-                                             src=view(a), dst=land(a)))
-            e.remote_dma_fused(tr_, local_sem=T.sem.lsem)
+        pieces = [(q[:, a + w * k:a + w * k + w].bitcast(dt.uint8), T.rlq[:, a + w * k:a + w * k + w].bitcast(dt.uint8)) for k in (0, 1)] + [(s[:], T.rlt[:])] * h
+        engs = three if h else [eng[:n], eng[n:]]
 
         def go2(e):
-            both_ways(e, lambda a: q[:, a:a + w].bitcast(dt.uint8), lambda a: T.rlq[:, a:a + w].bitcast(dt.uint8), T.sem["ry%d" % h])
-            both_ways(e, lambda a: s[:, a:a + w], lambda a: T.rls[:, a:a + w], T.sem["rz%d" % h])
+            e.remote_dma_fused([RemoteDMATransfer(dst_ids=[DstId(rid=ways[k][0], pnc=ways[k][1])], dma_engine_mask=bits_of(engs[k]),
+                                                  remote_sem=T.sem["ry%d" % h], src=src, dst=land) for k, (src, land) in enumerate(pieces)], local_sem=T.sem.lsem)
+            if h == 0:
+                e.remote_dma(T.rls[:, out(h)], s[:, out(h)], T.sem["ry%d" % h], T.sem.lsem, ways[2][1], ways[2][0], bits_of(eng))
 
-        put(go2, 2.0, 6.0, "lq%d%d" % (rd, h), "ar%d%d" % (rd, h), 4 * far, 4 * n)
+        put(go2, 1.2 - 0.6 * h, 6.0 - 0.5 * h, "lq%d%d" % (rd, h), "ar%d%d" % (rd, h), 3 * far, (4 - 2 * h) * n)
 
     def meet(rd, h):
         for t in range(4):
-            tt(T.vt[:, quad(h, t, 4)], T.xh[:, 320 * t:320 * t + 320].indirect(T["kl%d" % rd][:, part(h)]), T.xg[:, quad(h, t, 4)], OP.add,
-               ["xh0%d" % t, "xh1%d" % t, "xg%d%d" % (h, t), "kl%d" % rd] + ["@v"] * h, ["vt%d%d" % (h, t)], n=WID[h], x=True)
+            tt(T.vt[:, out(h, 4, t, 4)], T.xh[:, 320 * t:320 * t + 320].indirect(T["kl%d" % rd][:, out(h).start // 16:out(h).stop // 16]), T.xg[:, out(h, 4, t, 4)],
+               OP.add, ["xh0%d" % t, "xh1%d" % t, "xg0", "xg1", "kl%d%d" % (rd, h)] + ["@v"] * h, ["vt%d%d" % (h, t)], n=VW[h], x=True)
 
     def layer(h):
-        c = cols(h)
+        c = out(h)
         for b in range(4):
-            mm(4 * h + b, WID[h], T.wq[:, 128 * b:128 * b + 128], T.wsp[:, 128 * b:128 * b + 128], T.qv[:, c], T.qvs[:, c], ["wq", "qv%d" % h])
+            mm(4 * h + b, VW[h], T.wq[:, 128 * b:128 * b + 128], T.wsp[:, 128 * b:128 * b + 128], T.qv[:, c], T.qvs[:, c], ["wq", "qv%d" % h], ["@l"])
 
     def layer_out(h, b, q):
-        scaled(T.ht[:, quad(h, b, 4)], bank(4 * h + b, WID[h]), 0.03125, 0.0, ["b%d" % (4 * h + b)], ["ht%d%d" % (h, b)], q, WID[h])
+        scaled(T.ht[:, out(h, 4, b, 4)], bank(4 * h + b, VW[h]), 0.03125, 0.0, ["b%d" % (4 * h + b)] + ["@i"] * (q == "v"), ["ht%d%d" % (h, b)], q, VW[h])
 
     def quant_v(h):
-        quant(T.qv[:, cols(h)], T.qvs[:, cols(h)], T.vt[:, quad(h)], ["vt%d%d" % (h, t) for t in range(4)], ["qv%d" % h] + ["@v"] * (1 - h), 4 * WID[h])
+        quant(T.qv[:, out(h)], T.qvs[:, out(h)], T.vt[:, out(h, 4)], ["vt%d%d" % (h, t) for t in range(4)], ["qv%d" % h, ("@v", "@h")[h]], 4 * VW[h])
 
     def quant_h(rd, h):
-        quant(T["qh%d" % rd][:, cols(h)], T["sh%d" % rd][:, cols(h)], T.ht[:, quad(h)], ["ht%d%d" % (h, b) for b in range(4)], ["qh%d%d" % (rd, h)], 4 * WID[h])
+        quant(T["qh%d" % rd][:, out(h)], T["sh%d" % rd][:, out(h)], T.ht[:, out(h, 4)], ["ht%d%d" % (h, b) for b in range(4)] + ["@h"],
+              ["qh%d%d" % (rd, h), ("@g%d", "@s%d")[h] % rd], 4 * VW[h])
 
     for h in (0, 1):
         signs(0, h)
+    half_x(0, 0)
+    half_x(0, 1)
     for rd in (1, 2, 3):
         walk(rd)
         send(rd, "k", 0)
@@ -541,51 +582,61 @@ def rank_program(g, core, T, topo):
         layer(1)
         quant_h(rd, 0)
         send(rd, "h", 0)
+        if rd == 1:
+            quant(T.eq[:], T.es[:], T.et[:], ["et%d" % b for b in range(4)] + ["@g1"], ["eq", "@i"], n=2048)
+        else:
+            turned(rd)
         for b in range(4):
-            layer_out(1, b, "av")
+            layer_out(1, b, "av"[b == 3])
         quant_h(rd, 1)
         send(rd, "h", 1)
         if rd == 1:
-            quant(T.eq[:], T.es[:], T.et[:], ["et%d" % b for b in range(4)], ["eq"], n=2048)
+            sign(T.mask[:], T.rs[:], AF.Abs, 1.0, col("far"), ["rs", "far", "kl10"], ["mask"], 320)
+            sign(T.mask[:], T.mask[:], AF.Relu, -1.0, 1.0, ["mask"], ["mask"], 320)
+            differences()
+            picked(0, ["@s1"])
+            dma("g", [(T.vb[:], T.v[:])], ["@sent"], ["vb"], "dv", 2.5)
         else:
-            turned(0)
-            turned(1)
+            twice("@s%d" % rd)
+        if rd == 2:
+            quant(T.vq[:], T.vs[:], T.vb[:], ["vb", "@s2"], ["vq"], 512)
         if rd == 3:
-            fill(T.d0[:, 1:1280:4], 1.0, ["sb0", "sb1"], n=320)
-            quant(T.vq[:], T.vs[:], T.vb[:], ["vb"], ["vq"], 512)
+            for h in (0, 1):
+                scaled(T.d0[:, quad(h, 1, 4)], T.d0[:, quad(h, 0, 4)], 1.0, 1.0 - h, ["d0c", "@s3"], ["sb%d" % h], "a", WID[h])
         kl, kr = T["kl%d" % rd], T["kr%d" % rd]
-        cp(T.kw[:], T.w4[:].indirect(kr[:]), ["w4", "kr%d" % rd], ["kw"], "av", n=320, x=True)
-        tt(T.ky[:], T.kw[:].indirect(kl[:, 0:20]), T.mask[:], OP.mult, ["kw", "kl%d" % rd, "mask"], ["ky"], n=320, x=True)
-        scan(T.kys[:], T.rs[:], T.ky[:], BIG, OP.min, OP.add, ["ky", "rs"], ["kys"], 320)
+        cp(T.kw[:], T.w4[:].indirect(kr[:, 0:20]), ["w4", "kr%d" % rd, "@s%d" % rd], ["kw"], "a", n=320, x=True)
+        tt(T.ky[:], T.kw[:].indirect(kl[:, 0:20]), T.mask[:], OP.mult, ["kw", "kl%d0" % rd, "kl%d1" % rd, "mask"], ["ky"], n=320, x=True)
+        scan(T.kys[:], T.rs[:], T.ky[:], 0.0, OP.min, OP.add, ["ky", "rs"], ["kys"], 320)
         lin(T.mo[:, 0:20], T.kys[:, 15:320:16], 0.25, -320, ["kys"], ["mo_"])
+        lq, ls = T["lq%d" % rd], T["ls%d" % rd]
         for h in (0, 1):
-            lq, ls = T["lq%d" % rd], T["ls%d" % rd]
             for b in range(4):
-                mm(4 * h + b, WID[h], T.eq[:, 128 * b:128 * b + 128], T.es[:, 128 * b:128 * b + 128], lq[:, cols(h)], ls[:, cols(h)],
-                   ["eq", "lq%d%d" % (rd, h)])
-            for b in range(4):
-                cp(T.dd[:, 320 * b + AT[h]:320 * b + AT[h] + WID[h]], bank(4 * h + b, WID[h]), ["b%d" % (4 * h + b)], ["dd%d%d" % (h, b)], "av", n=WID[h])
+                c = out(h)
+                mm(4 * h + b, VW[h], T.eq[:, 128 * b:128 * b + 128], T.es[:, 128 * b:128 * b + 128], lq[:, c], ls[:, c], ["eq", "lq%d%d" % (rd, h)], ["@u"])
+                cp(T.dd[:, 320 * b + c.start:320 * b + c.stop], bank(4 * h + b, VW[h]), ["b%d" % (4 * h + b)], ["dd%d%d" % (h, b)],
+                   "v" if (b, h) == (0, 1) else "a", n=VW[h])
         xn, qn, sn = T["x%d" % rd], T["qx%d" % rd], T["sx%d" % rd]
         for h in (0, 1):
             for t in range(4):
                 tt(xn[:, quad(h, t, 4)], T.dd[:, 320 * t:320 * t + 320].indirect(T.mo[:, part(h)]), T.vt[:, quad(h, t, 4)], OP.add,
-                   ["mo_", "vt%d%d" % (h, t), "dd0%d" % t, "dd1%d" % t] + ["@x"] * h, ["xn%d%d%d" % (rd, h, t)], n=WID[h], x=True)
-            quant(qn[:, cols(h)], sn[:, cols(h)], xn[:, quad(h)], state_parts(rd, h), ["qx%d%d" % (rd, h)] + ["@x"] * (1 - h), 4 * WID[h])
+                   ["mo_", "vt0%d" % t, "vt1%d" % t, "dd0%d" % t, "dd1%d" % t] + ["@x"] * (h * t > 0), ["xn%d%d%d" % (rd, h, t)], n=WID[h], x=True)
+            quant(qn[:, cols(h)], sn[:, cols(h)], xn[:, quad(h)], state_parts(rd, h), ["qx%d%d" % (rd, h), ("@x", "@q%d" % rd)[h]], 4 * WID[h])
+        for h in (0, 1):
             signs(rd, h)
-            if rd == 3:
-                c = cols(h)
-                dma("s", [(T.oc[:, quad(h)], qn[:, c].bitcast(dt.uint8))] + [(T.osc[4 * k:4 * k + 4, c], sn[32 * k:32 * k + 4, c]) for k in range(4)],
-                    ["qx3%d" % h], [], "oq%d" % h)
         if rd < 3:
             half_x(rd, 0)
             half_x(rd, 1)
-    mm(6, 320, T.vq[:], T.vs[:], T.qx3[:], T.sx3[:], ["vq", "qx30", "qx31"])
-    cp(T.yb[:], bank(6, 320), ["b6"], ["yb"], "av", n=320)
-    dma("s", [(T.y[:], T.yb[:])], ["yb"], [], "oy")
     for h in (0, 1):
+        c = cols(h)
+        dma("s", [(T.oc[:, quad(h)], T.qx3[:, c].bitcast(dt.uint8))], ["qx3%d" % h], [], "oq%d" % h)
+        mm(6 + h, WID[h], T.vq[:], T.vs[:], T.qx3[:, c], T.sx3[:, c], ["vq", "qx3%d" % h])
+        cp(T.yb[:, c], bank(6 + h, WID[h]), ["b%d" % (6 + h)], ["yb%d" % h], "a", n=WID[h])
+        dma("s", [(T.y[:, c], T.yb[:, c])], ["yb%d" % h], [], "oy")
         for k in (0, 1):
-            scaled(T.lout[:, 2 * AT[h] + k:2 * (AT[h] + WID[h]):2], T.win[:, quad(h, 2 + k, 4)], 0.5, 160.0, ["win%d" % h], ["lo%d%d" % (h, k)], "av", WID[h])
-    dma("s", [(T.lr[:, 640 * k:640 * k + 640], T.lout[8 * k:8 * k + 8, :]) for k in (0, 1)], ["lo00", "lo01", "lo10", "lo11"], [], "ol")
+            scaled(T.lout[:, 2 * AT[h] + k:2 * (AT[h] + WID[h]):2], T.win[:, quad(h, 2 + k, 4)], 0.5, 160.0, ["win%d" % h], ["lo%d%d" % (h, k)], "va"[k], WID[h])
+    for q, ks, sem in (("s", (0, 1), "os"), ("g", (2, 3), "og")):
+        dma(q, [(T.osc[4 * k:4 * k + 4, :], T.sx3[32 * k:32 * k + 4, :]) for k in ks], ["qx30", "qx31"], [], sem)
+    dma("a", [(T.lr[:], T.lout[0:16, :])], ["lo00", "lo01", "lo10", "lo11"], [], "ol")
     issue()
     need("g", dict(total))
     g.wait_ge(T.sem.lsem, sent[0])

@@ -8,14 +8,17 @@ STEP = [4, 1, 2]
 FAR = 4096
 WAKE, SPARE, LOOK = 0.12, 0.3, 0.3
 DRQ = "vava"
-LATE = 2.0
+NRQ = "av"
+ROWQ = "aa"
+VA, XA = ((2, 3), (1, 2, 3)), ((), (0, 1, 2, 3))
+LATE = 3.0
 ACT = 0.05
 EPS = 2.0 ** -93
 
 F, B, H, I, U, C4, S8 = "float32", "bfloat16", "float16", "int32", "uint16", "float8_e4m3fn_x4", "uint8"
 SCRATCH = {"ps": ("psum", [128, 4096], F)}
 for _n, _w, _d in [
-    ("x0", 1280, B), ("x1", 1280, B), ("x2", 1280, B), ("x3", 1280, B), ("xh", 1280, B), ("xg", 1280, B), ("vt", 1280, B), ("ht", 1280, B), ("dd", 1280, B),
+    ("x0", 1280, B), ("x1", 1280, B), ("x2", 1280, B), ("x3", 1280, B), ("xh", 1280, B), ("xg", 1280, B), ("vg", 1280, B), ("dg", 1280, B), ("vt", 1280, B), ("ht", 1280, B), ("dd", 1280, B),
     ("ub", 512, B), ("vb", 512, B), ("et", 2048, B), ("ones", 512, B),
     ("uq", 128, C4), ("us", 128, S8), ("vq", 128, C4), ("vs", 128, S8), ("wq", 512, C4), ("wsp", 512, S8),
     ("upq", 384, C4), ("ups", 384, S8), ("eq", 512, C4), ("es", 512, S8),
@@ -23,17 +26,17 @@ for _n, _w, _d in [
     ("qv", 320, C4), ("qvs", 320, S8),
     ("qh1", 320, C4), ("sh1", 320, S8), ("qh2", 320, C4), ("sh2", 320, S8), ("qh3", 320, C4), ("sh3", 320, S8),
     ("lq1", 320, C4), ("ls1", 320, S8), ("lq2", 320, C4), ("ls2", 320, S8), ("lq3", 320, C4), ("ls3", 320, S8), ("rlq", 320, C4), ("rls", 320, S8), ("rlt", 320, S8),
-    ("raw", 640, I), ("rb", 640, B), ("oa", 320, F), ("d0", 1280, B), ("d1", 1280, H), ("win", 1280, B), ("nr", 320, B), ("bb", 320, F),
-    ("go", 160, F), ("tt", 1280, F), ("lu", 192, U), ("ue", 512, B), ("uo", 512, B), ("lp", 320, B), ("lw", 640, B), ("mlu", 64, U), ("km", 320, B), ("kt", 320, B),
+    ("raw", 640, I), ("rb", 640, B), ("oa", 320, F), ("d0", 1280, B), ("d1", 1280, H), ("win", 1600, B), ("nr", 320, B), ("bb", 320, F),
+    ("idn", 40, I), ("bc", 160, F), ("go", 352, F), ("tt", 1152, F), ("lu", 160, U), ("ue", 320, B), ("fl", 32, U), ("mlu", 32, U), ("km", 320, B), ("kt", 320, B),
     ("kl1", 32, U), ("kl2", 32, U), ("kl3", 32, U), ("kr1", 20, U), ("kr2", 24, U), ("kr3", 20, U), ("rlk", 8, U),
     ("dr", 1280, B), ("w4", 320, F), ("mask", 320, F), ("rs", 320, F), ("kw", 320, F), ("ky", 320, F), ("kys", 320, F), ("mo", 32, U),
     ("lout", 640, F), ("yb", 320, F),
-    ("pi", 16, I), ("pc", 48, F), ("kk", 32, F), ("zz", 8, F), ("sel", 16, F), ("pat", 32, F), ("tmp", 64, F),
-    ("uoff", 24, U), ("cl", 24, U), ("dl", 16, U), ("bl", 32, U), ("el", 48, U), ("ul", 32, U), ("sl", 16, U),
+    ("pi", 16, I), ("pc", 48, F), ("kk", 40, F), ("zz", 8, F), ("sel", 16, F), ("pat", 32, F), ("tmp", 64, F),
+    ("uoff", 24, U), ("cl", 24, U), ("dl", 16, U), ("bl", 32, U), ("blc", 16, U), ("el", 48, U), ("sl", 16, U),
 ]:
     SCRATCH[_n] = ("sbuf", [128, _w], _d)
 
-SEMAPHORES = (["sv", "sa", "st", "sg", "dx0", "dx1", "os", "og", "du", "dv", "dw", "dn0", "dn1", "oy", "ol", "oq0", "oq1", "lsem", "ry0", "ry1", "rk"]
+SEMAPHORES = (["sv", "sa", "st", "sg", "dx0", "dx1", "os", "og", "du", "dv", "dw", "dn0", "dn1", "dn2", "oy", "ol", "oq0", "oq1", "lsem", "ry0", "ry1", "rk"]
               + ["ar%d%d" % (r, h) for r in (1, 2, 3) for h in (0, 1)] + ["kr%d" % r for r in (1, 2, 3)])
 VW = (160, 160)
 
@@ -63,6 +66,19 @@ def share(h):
 
 def halfrow(h, at=0):
     return slice(at + AT[h] // 2, at + (AT[h] + WID[h]) // 2)
+
+
+WAY = [["R6", "R5", "R4", "R3", "R2"], ["R6", "R5", "R4", "L1", "R3"], ["L1", "L2", "R6", "L3", "R5"], ["L1", "L2", "L3", "L4", "L5"]]
+EVEN = [("R2", "R1"), ("R3", "L7"), ("R5", "L7"), ("R7", "L5")]
+ODD = [("R2", "L0"), ("R4", "L2"), ("R6", "L4"), ("L5", "L6")]
+
+
+def home(table):
+    return 2 * int(table[1]) + (table[0] == "R")
+
+
+def before(table):
+    return table[0] + str(int(table[1]) + (1 if table[0] == "R" else -1))
 
 
 def bits_of(engines):
@@ -256,10 +272,9 @@ def rank_program(g, core, T, topo):
             dma("a", [(T.ub[:], T.u[:])], [], ["ub", "@d1"], "du", LATE)
         else:
             dma("s", [(T.x0[:, quad(0)], T.x[:, quad(0)])], [], ["x00", "@d0"], "dx0", LATE + 0.2)
-        dma(q, [(T.raw[16 * gr + k:16 * gr + 16:2, :], tab[:]) for gr in range(8)], [], ["raw%d" % k, "@d%d" % k], "dn%d" % k, LATE)
-    dma("s", [(T.x0[:, quad(1)], T.x[:, quad(1)])], ["@d0"], ["x01"], "dx1", LATE + 0.2)
-    dma("s", [(T.wq[:].bitcast(dt.uint8), T.wc[:]), (T.wsp[:], T.ws[:])], ["x00"], ["wq"], "dw", 3.5)
-    ts(T.rb[:], T.raw[:], -160.0, None, OP.add, None, ["raw0", "raw1"], ["rb0"], n=640)
+        few = [8 - (k == 0 and 2 <= gr < 6) for gr in range(8)]
+        dma(q, [(T.raw[16 * gr + k:16 * gr + 2 * few[gr]:2, :], tab[0:16 * few[gr], :]) for gr in range(8)], [], ["raw%d" % k, "@d%d" % k], "dn%d" % k, LATE)
+    dma("s", [(T.x0[:, quad(1)], T.x[:, quad(1)])], ["@d0"], ["x01", "@d2"], "dx1", LATE + 0.2)
 
     def iota(o, pattern, base, cm, w, fl=True):
         n = 1
@@ -271,51 +286,59 @@ def rank_program(g, core, T, topo):
             op("g", lambda e: e.iota(o, pattern, base, cm), [], w, 0.15 + 0.002 * n)
 
     iota(T.pi[:, 0:1], [[0, 1]], 0, 1, ["p"], False)
-    iota(T.kk[:, 0:20], [[1, 20]], 0, 0, ["kk"])
+    iota(T.kk[:], [[1, 40]], 0, 0, ["kk"])
     iota(T.pat[:, 0:10], [[64, 5], [16, 2]], 0, 0, ["pata"])
-    for a in range(4):
-        rows = slice(32 * a, 32 * a + 32)
-        if a > 0:
-            iota(T.sel[rows, 0:2 * a], [[162, 2 * a]], 160, 0, ["sel%da" % a])
-        if a < 3:
-            lo = 2 * a + (a > 0)
-            iota(T.sel[rows, lo:6], [[158, 6 - lo]], 158 * lo + 175 + 4 * a, 0, ["sel%db" % a])
-        if 0 < a < 3:
-            iota(T.sel[rows, 2 * a:2 * a + 1], [[0, 1]], 175, 0, ["sel%dc" % a])
-    SEL = ["sel%d%s" % (a, c) for a in range(4) for c in "abc"]
-    LAST = {"so": 1, "me": 175, "mo": 1132, "nb": 1}
-    for k, name in enumerate(LAST):
-        iota(T.pc[96:128, 40 + k:41 + k], [[0, 1]], LAST[name], 0, [name + "3"])
-    iota(T.pat[:, 10:30], [[64, 5], [16, 2], [32, 2]], 0, 0, ["patb"])
+
+    def numbers(first, rows, name):
+        names = []
+        for a, row in enumerate(rows):
+            k = 0
+            while k < len(row):
+                n = min(2, len(row) - k)
+                while k + n < len(row) and row[k + n] - row[k + n - 1] == row[k + 1] - row[k]:
+                    n += 1
+                names.append("%s%d%d" % (name, a, k))
+                iota(T.sel[32 * a:32 * a + 32, first + k:first + k + n], [[row[k + n - 1] - row[k + max(n - 2, 0)], n]], row[k], 0, names[-1:])
+                k += n
+        return names
+
+    def spot(a, table):
+        s = 1 if table in ("L0", "R7") else 2 + WAY[a].index(table)
+        return 160 * (s % 6) + home(table)
+
+    SEL = numbers(0, [[spot(a, before(t)) - 160 for t in WAY[a]] for a in range(4)], "sel")
+    END = numbers(5, [[spot(a, ODD[a][0]), spot(a, EVEN[a][0]), home(WAY[a][3]), home(EVEN[a][1]), home(ODD[a][1]) - home(EVEN[a][1])] for a in range(4)], "end")
     iota(T.w4[:], [[4, 320]], 1280, 0, ["w4"])
     iota(T.rs[:], [[0, 20], [FAR, 16]], 0, 0, ["rs"])
 
-    digits = {"i": (0, 15), "q7": (0, 7), "q8": (3, 1), "p32": (0, 31), "b": (4, 1), "a": (5, 3), "ih": (1, 7), "y": (0, 1), "x": (1, 1)}
+    digits = {"i": (0, 15), "q7": (0, 7), "q8": (3, 1), "p32": (0, 31), "b": (4, 1), "a": (5, 3), "ih": (1, 7), "y": (0, 1), "x": (1, 1), "q4": (2, 3)}
     place = {}
     for k, (name, (sh, m)) in enumerate(digits.items()):
         ts(T.pi[:, k + 1:k + 2], T.pi[:, 0:1], sh, m, OP.arith_shift_right, OP.bitwise_and, ["p"], ["pi%d" % k])
         place[name] = k
-    cp(T.pc[:, 0:9], T.pi[:, 1:10], ["pi%d" % k for k in range(9)], list(digits))
+    cp(T.pc[:, 0:10], T.pi[:, 1:11], ["pi%d" % k for k in range(10)], list(digits))
 
     def col(name):
         return T.pc[:, place[name]:place[name] + 1]
 
     def new(name, a, s1, s2, f1, f2):
-        place[name] = 40 + list(LAST).index(name) if name in LAST else len(place)
+        place[name] = len(place)
         use = [a] + [s for s in (s1, s2) if isinstance(s, str)]
         s1, s2 = [col(s) if isinstance(s, str) else s if s is None else float(s) for s in (s1, s2)]
-        if name in LAST:
-            aff(T.pc[0:96, place[name]:place[name] + 1], T.pc[0:96, place[a]:place[a] + 1], s1, s2, use + [name + "3"], [name])
-        elif (f1, f2) == (mul, add):
+        if (f1, f2) == (mul, add):
             aff(col(name), col(a), s1, s2, use, [name])
         else:
             ts(col(name), col(a), s1, s2, f1, f2, use, [name])
 
-    def aff(o, a, m, b, r, w, n=10):
-        node({"a": lambda e: e.activation(o, a, AF.Identity, bias=b, scale=m), "v": lambda e: e.tensor_scalar(o, a, m, b, OP.mult, OP.add)},
-             {"a": us(n, 1, False), "v": us(n, 1, False)}, 0.0, r, w, None, 1)
+    def aff(o, a, m, b, r, w, n=10, q="av", c=1):
+        fns = {"a": lambda e: e.activation(o, a, AF.Identity, bias=b, scale=m), "v": lambda e: e.tensor_scalar(o, a, m, b, OP.mult, OP.add)}
+        node({k: fns[k] for k in q}, {k: us(n, c if k == "v" else 1, False) for k in q}, 0.0, r, w, None, 1)
 
     mul, add = OP.mult, OP.add
+    lin(T.idn[:], T.kk[:], 8, col("ih"), ["kk", "ih"], ["idn"], n=40)
+    dma("s", [(T.raw[32 + home("L7"):96:16, :], T.idn[0:64, :])], ["idn", "@d2"], ["raw2"], "dn2", LATE)
+    dma("s", [(T.wq[:].bitcast(dt.uint8), T.wc[:]), (T.wsp[:], T.ws[:])], ["x00"], ["wq"], "dw", 3.5)
+    ts(T.rb[:], T.raw[:], -160.0, None, OP.add, None, ["raw0", "raw1", "raw2"], ["rb0"], n=640)
     fill(T.zz[:], 0.0, ["zz"])
     new("q16", "ih", 16, None, mul, None)
     new("n16", "y", -32, 16, mul, add)
@@ -348,57 +371,69 @@ def rank_program(g, core, T, topo):
         lin(T.bl[:, at:at + n], T.kk[:, 0:n], 32, col("p32"), ["kk", "p32"], ["bl%d0" % h])
         lin(T.bl[:, at + n:at + 2 * n], T.pat[:, 0:n], 1, col("px"), ["pata", "px"], ["bl%d1" % h])
     new("sd2", "sd", 2, 0, mul, add)
-    fill(T.ue[:, 0:320], 0.0, ["ue"], n=320)
-    for t, v, names in ((0, 0.0, ["d0c"]), (1, 1.0, ["sb0", "sb1"]), (3, 0.0, ["d03"])):
-        scaled(T.d0[:, t:1280:4], T.ue[:, 0:320], 1.0, v, ["ue"], names, "a", 320)
-    scaled(T.uo[:, 0:320], T.ue[:, 0:320], 1.0, 0.0, ["ue"], ["uo"], "a", 320)
-    aff(T.tt[:, 0:160], T.ue[:, 0:160], 1.0, 0.0, ["ue"], ["T0"], 160)
-    new("ty", "p32", 2, -320, mul, add)
-    new("tx", "px", 2, -320, mul, add)
-    aff(T.tt[:, 0:160:16], T.kk[:, 0:10], 64.0, col("ty"), ["kk", "ty", "T0"], ["T0a"])
-    aff(T.tt[:, 1:160:16], T.pat[:, 0:10], 2.0, col("tx"), ["pata", "tx", "T0"], ["T0b"])
+    new("nd", "sd", -1, 0, mul, add)
+    new("nn", "sd", 1, 1, mul, add)
+    fill(T.ue[:], 0.0, ["ue"], n=320)
+    for t, v, names in ((0, 0.0, ["d0c"]), (1, 1.0, ["sb0", "sb1"])):
+        scaled(T.d0[:, t:1280:4], T.ue[:], 1.0, v, ["ue"], names, "a", 320)
+    aff(T.d0[:, 3:1280:4], T.ue[:], 1.0, col("nd"), ["ue", "nd"], ["d03"], 320, "a")
     for h in (0, 1):
         new("c%d" % h, "i", WID[h] // 32 - 1, 16, OP.min, mul)
-        ts(T.cl[:, 2 * h:24:4], T.sel[:, 0:6], col("c%d" % h), float(AT[h] // 2), add, add, SEL + ["c%d" % h], ["cl%d" % h])
-    new("se", "a", 324, -2, mul, add)
-    new("se0", "se", 0, None, OP.max, None)
-    new("so", "a", 324, 160, mul, add)
-    aff(T.tmp[:, 32:34], T.kk[:, 0:2], 8.0, col("ih"), ["kk", "ih"], ["ku"])
-    ts(T.tmp[:, 32:34], T.tmp[:, 32:34], 9.0, 16.0, OP.min, mul, ["ku"], ["ku"])
-    ts(T.sl[:, 0:2], T.tmp[:, 32:34], col("se0"), None, add, None, ["ku", "se0"], ["sl0"])
-    ts(T.sl[:, 2:4], T.tmp[:, 32:34], col("so"), None, add, None, ["ku", "so"], ["sl1"])
-    new("me", "a", 4, 1123, mul, add)
-    new("mo", "a", 4, 965, mul, add)
+        ts(T.cl[:, 2 * h:20:4], T.sel[:, 0:5], col("c%d" % h), float(AT[h] // 2), add, add, SEL + ["c%d" % h], ["cl%d" % h])
+    for a in range(4):
+        rows = slice(32 * a, 32 * a + 32)
+        src, m, p = (T.pat, 1, "px") if 0 < a < 3 else (T.kk, 32, "p32")
+        lin(T.blc[rows, 0:10], src[rows, 0:10], m, T.pc[rows, place[p]:place[p] + 1], ["kk", "pata", p], ["blc%d" % a])
+    for t in (0, 176):
+        fill(T.go[:, t:t + 16], 0.0, ["gom%d" % t])
+    new("m3", "a", 3, None, OP.is_equal, None)
+    new("xy", "x", "y", "m3", OP.subtract, mul)
+    new("ne", "xy", "y", "b", add, OP.not_equal)
+    new("bp", "x", "xy", 16, OP.subtract, mul)
+    new("sh", "b", -32, 192, mul, add)
+    aff(T.tmp[:, 30:31], col("ne"), col("sh"), T.sel[:, 7:8], ["ne", "sh"] + END, ["fa"])
+    aff(T.tmp[:, 31:32], T.tmp[:, 30:31], 1.0, col("bp"), ["fa", "bp"], ["fb"])
+    aff(T.tmp[:, 32:34], T.kk[:, 0:2], 4.0, col("q4"), ["kk", "q4"], ["ku"])
+    ts(T.tmp[:, 34:36], T.tmp[:, 32:34], 4.0, 32.0, OP.min, mul, ["ku"], ["kv"])
+    ts(T.sl[:, 0:2], T.tmp[:, 34:36], T.tmp[:, 31:32], None, add, None, ["kv", "fb"], ["sl0"])
     new("c9", "i", 9, 16, OP.min, mul)
-    ts(T.sl[:, 4:8:2], T.pc[:, place["me"]:place["me"] + 2], col("c9"), None, add, None, ["c9", "me", "mo"], ["sm"])
-    new("nb", "b", -1, 1, mul, add)
-    new("yx", "y", "x", "nb", OP.subtract, mul)
-    new("iyx", "i", 1, "yx", mul, add)
-    aff(T.tmp[:, 40:42], T.kk[:, 0:2], 16.0, col("iyx"), ["kk", "iyx"], ["kf"])
-    ts(T.sl[:, 8:10], T.tmp[:, 40:42], 16.0, 304.0, mul, OP.min, ["kf"], ["sk"])
-    ts(T.ul[:, 0:20], T.pat[:, 10:30], col("i"), None, add, None, ["patb", "i"], ["ul"])
+    ts(T.sl[:, 4:8:2], T.sel[:, 5:7], col("c9"), None, add, None, ["c9"] + END, ["sm"])
+    new("fe", "a", 0, None, OP.is_equal, None)
+    new("fo", "fe", 1, "m3", mul, add)
+    both = T.pc[:, place["fe"]:place["fe"] + 2]
+    aff(T.tmp[:, 36:38], both, 1.5, 0.5, ["fe", "fo"], ["fs"])
+    aff(T.tmp[:, 38:40], both, 642.0 - 1440.0, 1440.0, ["fe", "fo"], ["ft"])
+    new("fb1", "fe", "b", None, OP.max, None)
+    new("wx", "x", "y", "fb1", OP.subtract, mul)
+    new("i2", "y", "x", "i", OP.subtract, add)
+    new("i3", "i2", 1, "wx", mul, add)
+    aff(T.tmp[:, 40:42], T.kk[:, 0:2], 16.0, col("i3"), ["kk", "i3"], ["kf"])
+    ts(T.tmp[:, 42:44], T.tmp[:, 40:42], 19.0, 16.0, OP.min, mul, ["kf"], ["kg"])
+    aff(T.tmp[:, 44:45], T.sel[:, 9:10], col("b"), T.sel[:, 8:9], ["b"] + END, ["pos"])
+    ts(T.sl[:, 8:10], T.tmp[:, 42:44], T.tmp[:, 44:45], None, add, None, ["kg", "pos"], ["sk"])
     new("far", "i", -FAR, 0, mul, add)
+    new("nn2", "nn", 2, 0, mul, add)
+    new("n21", "nd", 2, -1, mul, add)
 
     RAW = ["rb0", "rb1", "rb2"]
     for h in (0, 1):
         n = WID[h]
         for k in (1, 0):
-            scaled(T.dr[:, quad(h, 3 * k, 4)], T.rb[:].indirect(T.el[:, 24 * k + AT[h] // 16:24 * k + (AT[h] + n) // 16]), 2.0, 0.0,
-                   RAW + ["el%d" % k], ["dr%d%d" % (h, 3 * k)], DRQ[2 * h + k], n, x=True)
-        for t, m in ((1, -1.0), (2, 1.0)):
-            scaled(T.dr[:, quad(h, t, 4)], T.dr[:, quad(h, 3, 4)], m, 0.0, ["dr%d3" % h], ["dr%d%d" % (h, t)], "av", n, 0.5)
+            scaled(T.dr[:, quad(h, 2 * k, 4)], T.rb[:].indirect(T.el[:, 24 * k + AT[h] // 16:24 * k + (AT[h] + n) // 16]), 2.0, 0.0,
+                   RAW + ["el%d" % k], ["dr%d%d" % (h, 2 * k)], DRQ[2 * h + k], n, x=True)
+        for t, m in ((1, -1.0), (3, col("nn"))):
+            aff(T.dr[:, quad(h, t, 4)], T.dr[:, quad(h, 2, 4)], m, 0.0, ["dr%d2" % h, "nn"], ["dr%d%d" % (h, t)], n, c=0.5)
 
     def twice(after):
-        cp(T.d1[:, quad(1, 1, 4)], T.d1[:, quad(1, 0, 4)], ["dif1", after], ["d1d"], n=WID[1], c=0.5)
+        cp(T.d1[:, 1:1280:4], T.d1[:, 0:1280:4], ["dif0", "dif1", after], ["d1d"], n=320, c=0.5)
 
     def differences():
-        scaled(T.oa[:], T.dr[:, 3:1280:4], 0.5, 0.0, ["dr03", "dr13"], ["oa"], "a", 320)
+        scaled(T.oa[:], T.dr[:, 2:1280:4], 0.5, 0.0, ["dr02", "dr12"], ["oa"], "a", 320)
         tt(T.d1[:, 0:1280:4], T.rb[:].indirect(T.el[:, 0:20]), T.oa[:], OP.subtract, RAW + ["el0", "oa", "@s1"], ["dif0", "dif1"], n=320, x=True)
         tt(T.d1[:, 2:1280:4], T.rb[:].indirect(T.el[:, 0:20]), T.oa[:], OP.add, RAW + ["el0", "oa", "@s1"], ["sum"], n=320, x=True)
-        ts(T.d1[:, 3:1280:4], T.d1[:, 2:1280:4], 2.0, None, mul, None, ["sum"], ["two"], n=320, c=0.5)
-        ts(T.d1[:, quad(0, 1, 4)], T.d0[:, quad(0, 0, 4)], 0.0, None, mul, None, ["d0c", "@s1"], ["d1c"], n=WID[0], c=0.5)
+        ts(T.d1[:, 3:1280:4], T.d1[:, 2:1280:4], col("nn2"), None, mul, None, ["sum", "nn2"], ["two"], n=320, c=0.5)
         twice("@s1")
-        scaled(T.d0[:, 3:1280:4], T.d0[:, 0:1280:4], 1.0, -1.0, ["d0c", "kl10"], ["d03"], "a", 320)
+        aff(T.d0[:, 3:1280:4], T.d0[:, 0:1280:4], 1.0, col("n21"), ["d0c", "kl10", "n21"], ["d03"], 320, "a")
 
     for h in (0, 1):
         quant(T.qx0[:, cols(h)], T.sx0[:, cols(h)], T.x0[:, quad(h)], ["x0%d" % h], ["qx0%d" % h], 4 * WID[h])
@@ -413,12 +448,14 @@ def rank_program(g, core, T, topo):
     def state_parts(k, h):
         return ["x0%d" % h] if k == 0 else ["xn%d%d%d" % (k, h, t) for t in range(4)]
 
-    def half_x(k, h):
+    def half_x(k):
         x = T["x%d" % k]
         for t in range(4):
-            scaled(T.xh[:, 320 * t + AT[h]:320 * t + AT[h] + WID[h]], x[:, quad(h, t, 4)], 0.5, 0.0, state_parts(k, h)[t % len(state_parts(k, h)):][:1],
-                   ["xh%d%d" % (h, t)], "a", WID[h], 0.5)
-        scaled(T.xg[:, quad(h)], x[:, quad(h)], 0.5, 0.0, state_parts(k, h) + ["bb1"], ["xg%d" % h], "a", 4 * WID[h], 0.5)
+            scaled(T.xh[:, 320 * t:320 * t + 320], x[:, t:1280:4], 0.5, 0.0, state_parts(k, 0) + state_parts(k, 1) + ["@bb"], ["xh%d" % t], "a", 320, 0.5)
+            runs = [h for h in (0, 1) if t not in VA[h]]
+            if runs:
+                a, z = out(runs[0]).start, out(runs[-1]).stop
+                scaled(T.xg[:, 320 * t + a:320 * t + z], x[:, 4 * a + t:4 * z:4], 0.5, 0.0, state_parts(k, 0) + state_parts(k, 1) + ["@bb"], ["xg%d" % t], "a", z - a, 0.5)
 
     def signs(k, h):
         n = WID[h]
@@ -430,22 +467,28 @@ def rank_program(g, core, T, topo):
             mm(b, n, T.upq[:, c], T.ups[:, c], T["qx%d" % k][:, cols(h)], T["sx%d" % k][:, cols(h)], ["upq%d" % j, "ups%d" % j, "qx%d%d" % (k, h)],
                ["@n"] * (1 - h))
             r, w = ["b%d" % b, "sf", "sd", "sd2", "d0c"], ["%s%d" % (name, h)]
-            if h == 0 or j == 0:
+            if j == 0 or j == 2 and NRQ[h] == "a":
                 sign(o, bank(b, n), AF.Sign, sc, eps, r, w, n)
-                if k == 0 and j == 1:
-                    sign(o, o, AF.Relu, 1.0, 0.0, w, w, n)
             elif j == 2:
                 ts(o, bank(b, n), 0.0, 0.5, OP.is_gt, mul, r, w, n)
             elif k == 0:
                 ts(o, bank(b, n), sc, 0.0, mul, OP.is_ge, r, w, n)
             else:
                 ts(o, bank(b, n), 0.0, col("sd2"), OP.is_gt, mul, r, w, n)
-        d1, names = (T.d1, [("d1c", "d1d")[h], "dif%d" % h, "sum", "two"]) if k else (T.dr, ["dr%d%d" % (h, t) for t in range(4)])
+        d1, names = (T.d1, ["d1d", "dif%d" % h, "sum", "two"]) if k else (T.dr, ["dr%d%d" % (h, t) for t in range(4)])
         scan(T.win[:, quad(h)], T.d0[:, quad(h)], d1[:, quad(h)], 0.0, mul, add,
              names + ["d0c", "d03", "sf%d" % h, "sb%d" % h, "@q%d" % k], ["win%d" % h], 4 * n, 0.5)
         if k < 3:
-            scaled(T.bb[:, cols(h)], T.nr[:, cols(h)].indirect(T.bl[:, part(h)]), (0.25, 1.0)[h], (0.25, 0.0)[h],
-                   ["nr%d" % h, "bl%d0" % h, "bl%d1" % h], ["bb%d" % h], "a", n, x=True)
+            for j in (0, 1):
+                at = AT[h] + j * n // 2
+                scaled(T.bb[:, at:at + n // 2], T.nr[:, cols(h)].indirect(T.bl[:, at // 16:(at + n // 2) // 16]), *HALF[NRQ[h]],
+                       ["nr%d" % h, "bl%d%d" % (h, j)], ["bb%d%d" % (h, j), "@bb"], "a", n // 2, x=True)
+
+    HALF = {"a": (0.25, 0.25), "v": (1.0, 0.0)}
+
+    def fifth(h):
+        scaled(T.bc[:, halfrow(h)], T.nr[:, 0:cols(h).stop].indirect(T.blc[:, share(h)]), *HALF[NRQ[h]],
+               ["nr%d" % j for j in range(h + 1)] + ["blc%d" % a for a in range(4)] + ["@bb"], ["bc%d" % h], "a", WID[h] // 2, x=True)
 
     def sign(o, i, f, sc, eps, r, w, n):
         op("a", lambda e: e.activation(o, i, f, bias=eps, scale=sc), r, w, us(n, 1, False))
@@ -454,8 +497,7 @@ def rank_program(g, core, T, topo):
         tt(T.d1[:, 0:1280:4], T.d1[:, 0:1280:4], T.d0[:, 2:1280:4], mul, ["sf0", "sf1", "@g%d" % rd], ["dif0", "dif1", "@i"], n=320)
 
     def upto(s, h):
-        names = ["T0a", "T0b"] + ["T%d%d" % (k, j) for k in range(1, s + 1) for j in (0, 1) if (k, j) <= (s, h)]
-        return T.tt[:, 0:halfrow(h, 160 * s).stop], names
+        return ["T%d%d" % (k, j) for k in range(1, s + 1) for j in (0, 1) if (k, j) <= (s, h)]
 
     def step(s, h, after=()):
         n = WID[h] // 2
@@ -463,35 +505,34 @@ def rank_program(g, core, T, topo):
             w, names, lst = T.win[:, 0:quad(h).stop], ["win%d" % j for j in range(h + 1)] + ["dl"], T.dl[:, share(h)]
         else:
             at = 32 * (s - 2) + 16 * h
-            w, names, lst = T.win[:], ["win0", "win1", "lu%d%d" % (s, h)], T.lu[:, at:at + n // 16]
+            w, names, lst = T.win[:, 0:1280], ["win0", "win1", "lu%d%d" % (s, h)], T.lu[:, at:at + n // 16]
         at = AT[h] + n * (1 - s % 2)
-        tt(T.go[:, halfrow(h)], w.indirect(lst), T.bb[:, at:at + n], add, names + ["bb%d" % h] + list(after), ["go%d" % h], n=n, x=True)
-        tr(T.tt[:, halfrow(h, 160 * s)], T.go[:, halfrow(h)], ["go%d" % h], ["T%d%d" % (s, h)], n)
-        if s < 7:
+        bits, go, name = (T.bc[:, halfrow(h)], T.go[:, halfrow(h, 16)], "5%d" % h) if s == 5 else (T.bb[:, at:at + n], T.go[:, halfrow(h, 192)], "%d" % h)
+        tt(go, w.indirect(lst), bits, add, names + ["bc%d" % h if s == 5 else "bb%d%d" % (h, 1 - s % 2)] + list(after), ["go" + name], n=n, x=True)
+        tr(T.tt[:, halfrow(h, 160 * (s % 6))], go, ["go" + name], ["T%d%d" % (s, h)], n)
+        if s < 6:
             at = 32 * (s - 1) + 16 * h
-            w, names = upto(s, h)
             k = 4 * (s - 1) + 2 * h
-            lin(T.lu[:, at:at + 16], w.indirect(T.cl[:, k:k + 1]), 2, 642, names + ["cl%d" % h], ["lu%d%d" % (s + 1, h)], n=16, x=True)
+            lin(T.lu[:, at:at + 16], T.tt[:, 160:halfrow(h, 160 * s).stop].indirect(T.cl[:, k:k + 1]), 2, 642, upto(s, h) + ["cl%d" % h],
+                ["lu%d%d" % (s + 1, h)], n=16, x=True)
 
     def walk(rd):
-        for s in range(1, 8):
-            for h in (0, 1):
-                step(s, h, ["sk", "sm", "sl0", "sl1", "ul"] * (s == 4))
-            if s in (5, 6):
-                w, names = upto(s, 1)
-                u, k = ("uo", 1) if s == 5 else ("ue", 0)
-                cp(T[u][:, 0:512:16], w.indirect(T.sl[:, 2 * k:2 * k + 2]), names + ["sl%d" % k], [u], "a", n=32, x=True)
-                if s == 5:
-                    tr(T.lp[:], T.uo[:, 0:320], ["uo"], ["lp"], 320, 0.5)
-                    cp(T.lw[:, 320:640], T.lp[:].indirect(T.ul[:, 0:20]), ["lp", "ul"], ["lw1"], "a", n=320, x=True)
-                else:
-                    tr(T.lw[:, 0:320], T.ue[:, 0:320], ["ue"], ["lw0"], 320, 0.5)
-
-        w, names = upto(7, 1)
-        for k in (0, 1):
-            lin(T.mlu[:, k:32:2], w.indirect(T.sl[:, 4 + 2 * k:5 + 2 * k]), 0.5, 160 + 320 * k, names + ["sm"], ["ml%d" % k], n=16, x=True)
         for h in (0, 1):
-            cp(T.km[:, cols(h)], T.lw[:].indirect(T.mlu[:, part(h)]), ["lw0", "lw1", "ml0", "ml1"], ["km%d" % h], "va"[h], n=WID[h], x=True)
+            fifth(h)
+        for s in range(1, 7):
+            for h in (0, 1):
+                step(s, h, ["sk", "sm", "sl0", "fs", "ft", "gom0", "gom176"] * (s == 3))
+            if s == 5:
+                tr(T.tt[:, 960:1152], T.go[:, 0:192], ["go50", "go51", "gom0", "gom176"], ["TS"], 192)
+                lin(T.fl[:], T.tt[:, 800:1152].indirect(T.sl[:, 0:2]), 2, 642, ["T50", "T51", "TS", "sl0"], ["fl"], n=32, x=True)
+                for h in (0, 1):
+                    cp(T.win[:, 1280 + 160 * h:1440 + 160 * h], T.win[:, 0:1280].indirect(T.fl[:, 10 * h:10 * h + 10]), ["win0", "win1", "fl"], ["row%d" % h],
+                       ROWQ[h], n=160, x=True)
+        for k in (0, 1):
+            lin(T.mlu[:, k:32:2], T.tt[:, 0:960].indirect(T.sl[:, 6 - 2 * k:7 - 2 * k]), T.tmp[:, 36 + k:37 + k], T.tmp[:, 38 + k:39 + k],
+                upto(6, 1) + ["sm", "fs", "ft"], ["ml%d" % k], n=16, x=True)
+        for h in (0, 1):
+            cp(T.km[:, out(h)], T.win[:].indirect(T.mlu[:, 10 * h:10 * h + 10]), ["win0", "win1", "row0", "row1", "ml0", "ml1"], ["km%d" % h], "va"[h], n=160, x=True)
         tr(T.kt[:], T.km[:], ["km0", "km1"], ["kt"], 320, 0.5)
         lin(T["kl%d" % rd][:], T.kt[:].indirect(T.sl[:, 8:10]), 0.5, 160, ["kt", "sk"], ["kl%d0" % rd, "kl%d1" % rd], n=32, x=True)
 
@@ -547,8 +588,14 @@ def rank_program(g, core, T, topo):
 
     def meet(rd, h):
         for t in range(4):
-            tt(T.vt[:, out(h, 4, t, 4)], T.xh[:, 320 * t:320 * t + 320].indirect(T["kl%d" % rd][:, out(h).start // 16:out(h).stop // 16]), T.xg[:, out(h, 4, t, 4)],
-               OP.add, ["xh0%d" % t, "xh1%d" % t, "xg0", "xg1", "kl%d%d" % (rd, h)] + ["@v"] * h, ["vt%d%d" % (h, t)], n=VW[h], x=True)
+            c = slice(320 * t + out(h).start, 320 * t + out(h).stop)
+            far = T.xh[:, 320 * t:320 * t + 320].indirect(T["kl%d" % rd][:, out(h).start // 16:out(h).stop // 16])
+            r, w = ["xh%d" % t, "kl%d%d" % (rd, h)], ["vt%d%d" % (h, t)]
+            if t in VA[h]:
+                cp(T.vg[:, c], far, r, ["vg%d%d" % (h, t)], "a", n=VW[h], x=True)
+                tt(T.vt[:, out(h, 4, t, 4)], T.vg[:, c], T.xh[:, c], OP.add, ["xh%d" % t, "vg%d%d" % (h, t)] + ["@v"] * h, w, n=VW[h], c=1)
+            else:
+                tt(T.vt[:, out(h, 4, t, 4)], far, T.xg[:, c], OP.add, r + ["xg%d" % t] + ["@v"] * h, w, n=VW[h], x=True)
 
     def layer(h):
         c = out(h)
@@ -567,8 +614,7 @@ def rank_program(g, core, T, topo):
 
     for h in (0, 1):
         signs(0, h)
-    half_x(0, 0)
-    half_x(0, 1)
+    half_x(0)
     for rd in (1, 2, 3):
         walk(rd)
         send(rd, "k", 0)
@@ -601,8 +647,9 @@ def rank_program(g, core, T, topo):
         if rd == 2:
             quant(T.vq[:], T.vs[:], T.vb[:], ["vb", "@s2"], ["vq"], 512)
         if rd == 3:
-            for h in (0, 1):
-                scaled(T.d0[:, quad(h, 1, 4)], T.d0[:, quad(h, 0, 4)], 1.0, 1.0 - h, ["d0c", "@s3"], ["sb%d" % h], "a", WID[h])
+            cp(T.d0[:, 1:1280:4], T.d0[:, 0:1280:4], ["d0c", "@s3"], ["sb0", "sb1"], "a", 320)
+            scaled(T.d0[:, 3:1280:4], T.d0[:, 0:1280:4], 1.0, -1.0, ["d0c", "@s3"], ["d03"], "a", 320)
+            ts(T.d1[:, 3:1280:4], T.d1[:, 2:1280:4], 2.0, None, mul, None, ["sum", "@s3"], ["two"], n=320, c=0.5)
         kl, kr = T["kl%d" % rd], T["kr%d" % rd]
         cp(T.kw[:], T.w4[:].indirect(kr[:, 0:20]), ["w4", "kr%d" % rd, "@s%d" % rd], ["kw"], "a", n=320, x=True)
         tt(T.ky[:], T.kw[:].indirect(kl[:, 0:20]), T.mask[:], OP.mult, ["kw", "kl%d0" % rd, "kl%d1" % rd, "mask"], ["ky"], n=320, x=True)
@@ -618,14 +665,19 @@ def rank_program(g, core, T, topo):
         xn, qn, sn = T["x%d" % rd], T["qx%d" % rd], T["sx%d" % rd]
         for h in (0, 1):
             for t in range(4):
-                tt(xn[:, quad(h, t, 4)], T.dd[:, 320 * t:320 * t + 320].indirect(T.mo[:, part(h)]), T.vt[:, quad(h, t, 4)], OP.add,
-                   ["mo_", "vt0%d" % t, "vt1%d" % t, "dd0%d" % t, "dd1%d" % t] + ["@x"] * (h * t > 0), ["xn%d%d%d" % (rd, h, t)], n=WID[h], x=True)
+                far, r = T.dd[:, 320 * t:320 * t + 320].indirect(T.mo[:, part(h)]), ["mo_", "dd0%d" % t, "dd1%d" % t]
+                near, w = ["vt0%d" % t, "vt1%d" % t] + ["@x"] * (h * t > 0), ["xn%d%d%d" % (rd, h, t)]
+                if t in XA[h]:
+                    c = slice(320 * t + AT[h], 320 * t + AT[h] + WID[h])
+                    cp(T.dg[:, c], far, r, ["dg%d%d" % (h, t)], "a", n=WID[h], x=True)
+                    tt(xn[:, quad(h, t, 4)], T.dg[:, c], T.vt[:, quad(h, t, 4)], OP.add, ["dg%d%d" % (h, t)] + near, w, n=WID[h], c=1)
+                else:
+                    tt(xn[:, quad(h, t, 4)], far, T.vt[:, quad(h, t, 4)], OP.add, r + near, w, n=WID[h], x=True)
             quant(qn[:, cols(h)], sn[:, cols(h)], xn[:, quad(h)], state_parts(rd, h), ["qx%d%d" % (rd, h), ("@x", "@q%d" % rd)[h]], 4 * WID[h])
         for h in (0, 1):
             signs(rd, h)
         if rd < 3:
-            half_x(rd, 0)
-            half_x(rd, 1)
+            half_x(rd)
     for h in (0, 1):
         c = cols(h)
         dma("s", [(T.oc[:, quad(h)], T.qx3[:, c].bitcast(dt.uint8))], ["qx3%d" % h], [], "oq%d" % h)

@@ -1,3 +1,4 @@
+import numpy as np
 from concourse.bass import DstId, RemoteDMATransfer
 from concourse.mybir import dt, AluOpType, ActivationFunctionType
 import comms_topo
@@ -7,37 +8,46 @@ AF = ActivationFunctionType
 STEP = [4, 1, 2]
 FAR = 4096
 WAKE, SPARE, LOOK = 0.12, 0.3, 0.3
-DRQ = "vava"
+NEWQ = "av"
 NRQ = "av"
 ROWQ = "aa"
 VA, XA = ((2, 3), (1, 2, 3)), ((), (0, 1, 2, 3))
-LATE = 3.0
-ACT = 0.05
+LATE = 2.2
+XL = (0.3, 0.5)
+AHEAD = {}
+HOLD = ("@x", "@v", "@q1", "@q2", "@q3", "@h", "@i")
+WARM, SEED = 0.03, 4
+TRIES, SWAPS, ORDER = 500, 500, {}
+CASES = np.array([[0.95, 1.5, 1.3, 1, 0.11, 0.06, 1, 1], [0.95, 1.1, 1.3, 1, 0.11, 0.06, 1, 0.75], [0.95, 2.0, 1.3, 1, 0.11, 0.06, 1.2, 1], [0.85, 1.5, 0.6, 1, 0.15, 0.06, 1, 0.75],
+                  [1.2, 1.5, 1.3, 1, 0.06, 0.06, 0.8, 1], [0.95, 1.5, 0.6, 2, 0.11, 0.12, 1, 1.2], [0.95, 1.3, 1.8, 1, 0.08, 0.03, 1.2, 0.75]])
+CYC, GAT, PE, TWO, WAKES, ACT, SLOW, QUICK = CASES.T * np.array([0.001] + [1] * 7)[:, None]
 EPS = 2.0 ** -93
 
 F, B, H, I, U, C4, S8 = "float32", "bfloat16", "float16", "int32", "uint16", "float8_e4m3fn_x4", "uint8"
 SCRATCH = {"ps": ("psum", [128, 4096], F)}
 for _n, _w, _d in [
     ("x0", 1280, B), ("x1", 1280, B), ("x2", 1280, B), ("x3", 1280, B), ("xh", 1280, B), ("xg", 1280, B), ("vg", 1280, B), ("dg", 1280, B), ("vt", 1280, B), ("ht", 1280, B), ("dd", 1280, B),
-    ("ub", 512, B), ("vb", 512, B), ("et", 2048, B), ("ones", 512, B),
+    ("ub", 512, B), ("vb", 512, B), ("et", 2048, B), ("ones", 128, B),
     ("uq", 128, C4), ("us", 128, S8), ("vq", 128, C4), ("vs", 128, S8), ("wq", 512, C4), ("wsp", 512, S8),
     ("upq", 384, C4), ("ups", 384, S8), ("eq", 512, C4), ("es", 512, S8),
     ("qx0", 320, C4), ("sx0", 320, S8), ("qx1", 320, C4), ("sx1", 320, S8), ("qx2", 320, C4), ("sx2", 320, S8), ("qx3", 320, C4), ("sx3", 320, S8),
     ("qv", 320, C4), ("qvs", 320, S8),
     ("qh1", 320, C4), ("sh1", 320, S8), ("qh2", 320, C4), ("sh2", 320, S8), ("qh3", 320, C4), ("sh3", 320, S8),
     ("lq1", 320, C4), ("ls1", 320, S8), ("lq2", 320, C4), ("ls2", 320, S8), ("lq3", 320, C4), ("ls3", 320, S8), ("rlq", 320, C4), ("rls", 320, S8), ("rlt", 320, S8),
-    ("raw", 640, I), ("rb", 640, B), ("oa", 320, F), ("d0", 1280, B), ("d1", 1280, H), ("win", 1600, B), ("nr", 320, B), ("bb", 320, F),
-    ("idn", 40, I), ("bc", 160, F), ("go", 352, F), ("tt", 1152, F), ("lu", 160, U), ("ue", 320, B), ("fl", 32, U), ("mlu", 32, U), ("km", 320, B), ("kt", 320, B),
+    ("raw", 640, I), ("oa", 640, B), ("d0", 1280, B), ("d1", 1280, H), ("win", 1600, B), ("nr", 320, B), ("bb", 320, F),
+    ("idn", 80, I), ("bc", 160, F), ("go", 352, F), ("tt", 1152, F), ("lu", 160, U), ("ue", 512, B), ("fl", 32, U), ("mlu", 32, U), ("km", 320, B), ("kt", 320, B),
     ("kl1", 32, U), ("kl2", 32, U), ("kl3", 32, U), ("kr1", 20, U), ("kr2", 24, U), ("kr3", 20, U), ("rlk", 8, U),
     ("dr", 1280, B), ("w4", 320, F), ("mask", 320, F), ("rs", 320, F), ("kw", 320, F), ("ky", 320, F), ("kys", 320, F), ("mo", 32, U),
     ("lout", 640, F), ("yb", 320, F),
-    ("pi", 16, I), ("pc", 48, F), ("kk", 40, F), ("zz", 8, F), ("sel", 16, F), ("pat", 32, F), ("tmp", 64, F),
+    ("pi", 80, I), ("pj", 16, I), ("pc", 64, F), ("kk", 40, F), ("zz", 8, F), ("sel", 16, F), ("pat", 32, F), ("tmp", 64, F),
     ("uoff", 24, U), ("cl", 24, U), ("dl", 16, U), ("bl", 32, U), ("blc", 16, U), ("el", 48, U), ("sl", 16, U),
 ]:
     SCRATCH[_n] = ("sbuf", [128, _w], _d)
 
-SEMAPHORES = (["sv", "sa", "st", "sg", "dx0", "dx1", "os", "og", "du", "dv", "dw", "dn0", "dn1", "dn2", "oy", "ol", "oq0", "oq1", "lsem", "ry0", "ry1", "rk"]
+SEMAPHORES = (["sv", "sa", "st", "sg", "dx0", "dx1", "os", "du", "dv", "dw", "dn0", "dn1", "dn2", "de", "oy", "ol", "oq0", "oq1", "lsem", "ry0", "ry1", "rk"]
               + ["ar%d%d" % (r, h) for r in (1, 2, 3) for h in (0, 1)] + ["kr%d" % r for r in (1, 2, 3)])
+ONE = 0
+WHOLE = (False, False)
 VW = (160, 160)
 
 
@@ -71,6 +81,14 @@ def halfrow(h, at=0):
 WAY = [["R6", "R5", "R4", "R3", "R2"], ["R6", "R5", "R4", "L1", "R3"], ["L1", "L2", "R6", "L3", "R5"], ["L1", "L2", "L3", "L4", "L5"]]
 EVEN = [("R2", "R1"), ("R3", "L7"), ("R5", "L7"), ("R7", "L5")]
 ODD = [("R2", "L0"), ("R4", "L2"), ("R6", "L4"), ("L5", "L6")]
+
+
+KM = ([(0, 96, "v"), (96, 96, "a")], [(0, 128, "a")])
+FIXQ, DDQ, DRQ, DIRQ, LRQ = "v", "v", "vvvv", "vv", "a"
+XB = ((), (0, 1, 2, 3))
+HQ = ["av"] * 4 + list("aaav")
+TURN = ()
+PLACE = [None, 0, 160, 320, 480, 800, 640]
 
 
 def home(table):
@@ -109,14 +127,19 @@ def relay_program(g, core, T, topo):
         g.wait_ge(T.sem.rk, all_ // (2 if k == 2 else 4))
         g.remote_dma(T.kr2[:, 8 * k:8 * k + 8], T.rlk[:], T.sem.kr2, T.sem.lsem, pid, rid, m)
         for h in (0, 1):
-            if k < 2:
+            if WHOLE[h]:
+                if k == 2 or k == 1 - h:
+                    g.wait_ge(T.sem["ry%d" % h], all_)
+                    o, i = (T.ls2[:, out(h)], T.rls[:, out(h)]) if k == 2 else (T.lq2[:, out(h)].bitcast(dt.uint8), T.rlq[:, out(h)].bitcast(dt.uint8))
+                    g.remote_dma(o, i, T.sem["ar2%d" % h], T.sem.lsem, pid, rid, m)
+            elif k < 2:
                 a, w = out(h).start + VW[h] // 2 * k, VW[h] // 2
-                g.wait_ge(T.sem["ry%d" % h], all_ // (2 + 2 * h))
+                g.wait_ge(T.sem["ry%d" % h], all_ // (2 + 2 * h * ONE))
                 g.remote_dma(T.lq2[:, a:a + w].bitcast(dt.uint8), T.rlq[:, a:a + w].bitcast(dt.uint8), T.sem["ar2%d" % h], T.sem.lsem, pid, rid, m)
             else:
-                g.wait_ge(T.sem["ry%d" % h], all_ // (1 + h))
-                g.remote_dma(T.ls2[:, out(h)], (T.rls, T.rlt)[h][:, out(h)], T.sem["ar2%d" % h], T.sem.lsem, pid, rid, m)
-        g.wait_ge(T.sem.lsem, 3 * n)
+                g.wait_ge(T.sem["ry%d" % h], all_ // (1 + h * ONE))
+                g.remote_dma(T.ls2[:, out(h)], (T.rls, T.rlt)[h * ONE][:, out(h)], T.sem["ar2%d" % h], T.sem.lsem, pid, rid, m)
+        g.wait_ge(T.sem.lsem, n * (1 + sum(k in (2, 1 - h) or not WHOLE[h] for h in (0, 1))))
 
 
 def rank_program(g, core, T, topo):
@@ -129,6 +152,7 @@ def rank_program(g, core, T, topo):
     nodes, writer, readers = [], {}, {}
 
     def node(fns, cost, late, r, w, sem, inc):
+        r = [k for k in r if k in HOLD or k not in ("@x", "@v", "@q1", "@q2", "@q3", "@h", "@i")]
         pre, after = set(), set()
         for k in list(r) + list(w):
             if k in writer:
@@ -138,8 +162,9 @@ def rank_program(g, core, T, topo):
                 pre.update(readers.get(k, ()))
         i = len(nodes)
         if "a" in cost and sem is None:
-            cost["a"] += ACT
-        nodes.append({"fns": fns, "cost": cost, "late": late, "pre": sorted(pre), "order": sorted(pre | after), "sem": sem, "inc": inc})
+            cost["a"] = cost["a"] + ACT
+        cost, late = {q: cost[q] + 0.0 * CYC for q in cost}, late * (SLOW if "g" in cost else QUICK)
+        nodes.append({"fns": fns, "cost": {q: float(cost[q][0]) for q in cost}, "late": float(late[0]), "all": cost, "slow": late, "pre": sorted(pre), "order": sorted(pre | after), "sem": sem, "inc": inc})
         for k in r:
             readers.setdefault(k, set()).add(i)
         for k in w:
@@ -156,10 +181,10 @@ def rank_program(g, core, T, topo):
         node({q: go}, {q: 0.1 * len(pairs)}, late, r, w, sem, 16 * len(pairs))
 
     def us(n, cycles, gather):
-        return 0.05 + n * 0.0016 if gather else max(64, n * cycles) * 0.001
+        return 0.05 + n * GAT * CYC if gather else np.maximum(64, n * cycles) * CYC
 
     def tt(o, a, b, f, r, w, n=10, x=False, c=2):
-        op("v", lambda e: e.tensor_tensor(o, a, b, f), r, w, us(n, c, x))
+        op("v", lambda e: e.tensor_tensor(o, a, b, f), r, w, us(n, c * TWO if c == 1 else c, x))
 
     def ts(o, a, s1, s2, f1, f2, r, w, n=10, x=False, c=1):
         if f2 is None:
@@ -179,6 +204,9 @@ def rank_program(g, core, T, topo):
                "a": (lambda e: e.activation(o, a, AF.Copy, bias=b, scale=m)) if b else (lambda e: e.activation(o, a, AF.Copy, scale=m))}
         node({k: fns[k] for k in q}, {k: us(n, c if k == "v" else 1, x) for k in q}, 0.0, r, w, None, 1)
 
+    def sign(o, i, f, sc, eps, r, w, n):
+        op("a", lambda e: e.activation(o, i, f, bias=eps, scale=sc), r, w, us(n, 1, False))
+
     def tr(o, a, r, w, n, c=1):
         op("v", lambda e: e.transpose(o, a), r, w, us(n, c, False))
 
@@ -186,24 +214,96 @@ def rank_program(g, core, T, topo):
         op("v", lambda e: e.tensor_tensor_scan(o, d0, d1, first, f0, f1), r, w, us(n, c, False))
 
     def mm(bank, n, lq, lsc, rq, rsc, r, turn=()):
-        op("t", lambda e: e.matmul_mx(T.ps[:, 512 * bank:512 * bank + n], lq, lsc, rq, rsc, True, True), r, ["b%d" % bank] + list(turn), (n + 16) * 0.0011)
+        op("t", lambda e: e.matmul_mx(T.ps[:, 512 * bank:512 * bank + n], lq, lsc, rq, rsc, True, True), r, ["b%d" % bank] + list(turn), (n + 16) * PE * CYC)
 
     def fill(o, c, w, n=10):
         op("v", lambda e: e.memset(o, c), [], w, us(n, 0.5, False))
 
     def quant(q, s, t, r, w, n=640):
-        op("v", lambda e: e.quantize_mx(q, s, t), r, w, 0.012 + n * 0.00028)
+        op("v", lambda e: e.quantize_mx(q, s, t), r, w, (14.0 + n * 0.265) * CYC)
+
+    def length(order):
+        free, done = {}, {}
+        for i, q in order:
+            d = nodes[i]
+            s = free.get(q, 0.0 * CYC)
+            for p in d["pre"]:
+                s = np.maximum(s, done[p])
+            free[q] = s + d["all"][q]
+            done[i] = free[q] + d["slow"] + WAKES
+        return float(np.mean(np.max(list(done.values()), axis=0)))
+
+    def waiting(order, c):
+        free, done, why, last = {}, {}, {}, {}
+        for i, q in order:
+            d = nodes[i]
+            s, why[i] = free.get(q, 0.0), (last.get(q), True)
+            for p in d["pre"]:
+                if done[p] > s:
+                    s, why[i] = done[p], (p, False)
+            free[q], last[q] = s + d["all"][q][c], i
+            done[i] = free[q] + d["slow"][c] + WAKES[c]
+        i, held = max(done, key=done.get), []
+        while i is not None:
+            if why[i][1] and why[i][0] is not None:
+                held.append(i)
+            i = why[i][0]
+        return held
 
     def arrange():
         n = len(nodes)
-        tail = [0.0] * n
-        out = [[] for _ in range(n)]
-        for i, d in enumerate(nodes):
-            for p in d["order"]:
-                out[p].append(i)
-        for i in range(n - 1, -1, -1):
-            d = nodes[i]
-            tail[i] = min(d["cost"].values()) + d["late"] + max([tail[k] + WAKE for k in out[i]] + [0.0])
+        if n not in ORDER:
+            tail = [0.0] * n
+            out = [[] for _ in range(n)]
+            for i, d in enumerate(nodes):
+                for p in d["order"]:
+                    out[p].append(i)
+            for i in range(n - 1, -1, -1):
+                d = nodes[i]
+                tail[i] = min(d["cost"].values()) + d["late"] + max([tail[k] + WAKE for k in out[i]] + [0.0])
+            rng = np.random.RandomState(SEED)
+            move, best = np.zeros(n), listed(tail, out)
+            least = length(best)
+            for _ in range(TRIES):
+                a = rng.randint(n)
+                other = move.copy()
+                other[a:a + 40] += rng.normal(0.0, 0.15, n)[a:a + 40]
+                order = listed(list(tail + other), out)
+                t = length(order)
+                if t < least:
+                    move, best, least = other, order, t
+            now, cur = best, least
+            for _ in range(SWAPS):
+                if _ % 20 == 0:
+                    held = waiting(now, rng.randint(len(CYC)))
+                i = held[rng.randint(len(held))]
+                a = [k for k, q in now].index(i)
+                q = now[a][1]
+                if len(nodes[i]["cost"]) > 1 and rng.rand() < 0.3:
+                    order = now[:a] + [(i, [k for k in nodes[i]["cost"] if k != q][0])] + now[a + 1:]
+                else:
+                    b, hops, along = a, rng.randint(1, 3), {i}
+                    while b > 0 and hops:
+                        b -= 1
+                        if now[b][1] == q:
+                            hops -= 1
+                    for k in range(a - 1, b - 1, -1):
+                        if any(now[k][0] in nodes[j]["order"] for j in along):
+                            along.add(now[k][0])
+                    if now[b][0] in along:
+                        continue
+                    order = now[:b] + [k for k in now[b:a + 1] if k[0] in along] + [k for k in now[b:a + 1] if k[0] not in along] + now[a + 1:]
+                t = length(order)
+                if t <= cur + WARM * rng.rand() * (1 - _ / SWAPS):
+                    now, cur = order, t
+                    if t < least:
+                        best, least = order, t
+            ORDER["least"] = least
+            ORDER[n] = best
+        return ORDER[n]
+
+    def listed(tail, out):
+        n = len(nodes)
         left = [len(d["order"]) for d in nodes]
         ready = [0.0] * n
         open_ = [i for i in range(n) if left[i] == 0]
@@ -271,10 +371,9 @@ def rank_program(g, core, T, topo):
         if k:
             dma("a", [(T.ub[:], T.u[:])], [], ["ub", "@d1"], "du", LATE)
         else:
-            dma("s", [(T.x0[:, quad(0)], T.x[:, quad(0)])], [], ["x00", "@d0"], "dx0", LATE + 0.2)
+            dma("s", [(T.x0[:, quad(0)], T.x[:, quad(0)])], [], ["x00", "@d0"], "dx0", LATE + XL[0])
         few = [8 - (k == 0 and 2 <= gr < 6) for gr in range(8)]
-        dma(q, [(T.raw[16 * gr + k:16 * gr + 2 * few[gr]:2, :], tab[0:16 * few[gr], :]) for gr in range(8)], [], ["raw%d" % k, "@d%d" % k], "dn%d" % k, LATE)
-    dma("s", [(T.x0[:, quad(1)], T.x[:, quad(1)])], ["@d0"], ["x01", "@d2"], "dx1", LATE + 0.2)
+        dma(q, [(T.raw[16 * gr + k:16 * gr + 2 * few[gr]:2, :], tab[0:16 * few[gr], :]) for gr in range(8)], [], ["raw%d" % k, "@d%d" % k], "dn%d" % k, LATE + XL[0])
 
     def iota(o, pattern, base, cm, w, fl=True):
         n = 1
@@ -285,9 +384,10 @@ def rank_program(g, core, T, topo):
         else:
             op("g", lambda e: e.iota(o, pattern, base, cm), [], w, 0.15 + 0.002 * n)
 
-    iota(T.pi[:, 0:1], [[0, 1]], 0, 1, ["p"], False)
-    iota(T.kk[:], [[1, 40]], 0, 0, ["kk"])
-    iota(T.pat[:, 0:10], [[64, 5], [16, 2]], 0, 0, ["pata"])
+    iota(T.pi[:, 0:1], [[0, 1]], 32, 64, ["p"], False)
+    iota(T.idn[0:8, :], [[0, 2], [8, 40]], 0, 1, ["idn"], False)
+    iota(T.kk[:], [[40, 2], [2, 20]], 0, 0, ["kk"])
+    iota(T.pat[:, 10:20], [[64, 5], [16, 2]], 0, 0, ["pata"])
 
     def numbers(first, rows, name):
         names = []
@@ -304,29 +404,29 @@ def rank_program(g, core, T, topo):
 
     def spot(a, table):
         s = 1 if table in ("L0", "R7") else 2 + WAY[a].index(table)
-        return 160 * (s % 6) + home(table)
+        return PLACE[s] + home(table)
 
-    SEL = numbers(0, [[spot(a, before(t)) - 160 for t in WAY[a]] for a in range(4)], "sel")
-    END = numbers(5, [[spot(a, ODD[a][0]), spot(a, EVEN[a][0]), home(WAY[a][3]), home(EVEN[a][1]), home(ODD[a][1]) - home(EVEN[a][1])] for a in range(4)], "end")
-    iota(T.w4[:], [[4, 320]], 1280, 0, ["w4"])
-    iota(T.rs[:], [[0, 20], [FAR, 16]], 0, 0, ["rs"])
+    SEL = numbers(0, [[spot(a, before(t)) for t in WAY[a]] + [spot(a, ODD[a][0]), spot(a, EVEN[a][0])] for a in range(4)], "sel")
 
-    digits = {"i": (0, 15), "q7": (0, 7), "q8": (3, 1), "p32": (0, 31), "b": (4, 1), "a": (5, 3), "ih": (1, 7), "y": (0, 1), "x": (1, 1), "q4": (2, 3)}
     place = {}
-    for k, (name, (sh, m)) in enumerate(digits.items()):
-        ts(T.pi[:, k + 1:k + 2], T.pi[:, 0:1], sh, m, OP.arith_shift_right, OP.bitwise_and, ["p"], ["pi%d" % k])
-        place[name] = k
-    cp(T.pc[:, 0:10], T.pi[:, 1:11], ["pi%d" % k for k in range(10)], list(digits))
+    for digits, then in (({"q16": (3, 112), "y16": (2, 16), "q7": (6, 7), "q8": (9, 1), "i16": (2, 240)}, "c2"),
+                         ({"p32": (6, 31), "d2": (4, 126), "b16": (6, 16), "c1": (2, 48), "x16": (3, 16), "a4": (9, 12), "h0": (3, 96)}, "h1")):
+        at = len(place)
+        for name, (sh, m) in digits.items():
+            k = place[name] = len(place)
+            ts(T.pj[:, k:k + 1], T.pi[:, 0:1], sh, m, OP.arith_shift_right, OP.bitwise_and, ["p"], ["pi" + name])
+        cp(T.pc[:, at:len(place)], T.pj[:, at:len(place)], ["pi" + name for name in digits], list(digits))
+        place[then] = len(place)
 
     def col(name):
         return T.pc[:, place[name]:place[name] + 1]
 
     def new(name, a, s1, s2, f1, f2):
-        place[name] = len(place)
+        place.setdefault(name, len(place))
         use = [a] + [s for s in (s1, s2) if isinstance(s, str)]
         s1, s2 = [col(s) if isinstance(s, str) else s if s is None else float(s) for s in (s1, s2)]
         if (f1, f2) == (mul, add):
-            aff(col(name), col(a), s1, s2, use, [name])
+            aff(col(name), col(a), s1, s2, use, [name], q="av" if name in ("n", "e0", "i15", "sd", "nd", "nn") else NEWQ)
         else:
             ts(col(name), col(a), s1, s2, f1, f2, use, [name])
 
@@ -335,17 +435,12 @@ def rank_program(g, core, T, topo):
         node({k: fns[k] for k in q}, {k: us(n, c if k == "v" else 1, False) for k in q}, 0.0, r, w, None, 1)
 
     mul, add = OP.mult, OP.add
-    lin(T.idn[:], T.kk[:], 8, col("ih"), ["kk", "ih"], ["idn"], n=40)
-    dma("s", [(T.raw[32 + home("L7"):96:16, :], T.idn[0:64, :])], ["idn", "@d2"], ["raw2"], "dn2", LATE)
-    dma("s", [(T.wq[:].bitcast(dt.uint8), T.wc[:]), (T.wsp[:], T.ws[:])], ["x00"], ["wq"], "dw", 3.5)
-    ts(T.rb[:], T.raw[:], -160.0, None, OP.add, None, ["raw0", "raw1", "raw2"], ["rb0"], n=640)
-    fill(T.zz[:], 0.0, ["zz"])
-    new("q16", "ih", 16, None, mul, None)
-    new("n16", "y", -32, 16, mul, add)
-    new("n", "q16", "n16", 112, add, OP.min)
-    ts(T.uoff[:, 0:8], T.zz[:], col("q16"), 1.0, add, add, ["zz", "q16"], ["uoff0"])
-    ts(T.uoff[:, 8:16], T.zz[:], col("q16"), None, add, None, ["zz", "q16"], ["uoff1"])
-    ts(T.uoff[:, 16:24], T.zz[:], col("n"), 0.0, add, OP.max, ["zz", "n"], ["uoff2"])
+    dma("s", [(T.raw[k:k + 1, :], T.idn[0:8, :]) for k in range(32 + home("L7"), 96, 16)], ["idn", "@d0"], ["raw2", "@d2"], "dn2", LATE)
+    dma("s", [(T.x0[:, quad(1)], T.x[:, quad(1)])], ["@d2"], ["x01", "@d3"], "dx1", LATE + XL[1])
+    fill(T.zz[:], 16.0, ["zz"])
+    new("n", "y16", -2, "q16", mul, add)
+    ts(T.uoff[:, 8:16], T.zz[:], col("q16"), -16.0, add, add, ["zz", "q16"], ["uoff1"])
+    ts(T.uoff[:, 16:24], T.zz[:], col("n"), 112.0, add, OP.min, ["zz", "n"], ["uoff2"])
     quant(T.uq[:], T.us[:], T.ub[:], ["ub"], ["uq"], 512)
 
     def picked(k, after):
@@ -355,93 +450,114 @@ def rank_program(g, core, T, topo):
 
     picked(1, [])
     picked(2, [])
-    new("sf", "y", -2, 1, mul, add)
-    new("i15", "i", -1, 15, mul, add)
-    new("ii", "i", "i15", 0, mul, add)
-    new("sd", "ii", 0, -1, OP.is_equal, mul)
+    new("sf", "y16", -0.125, 1, mul, add)
+    new("i15", "i16", -1, 240, mul, add)
+    new("sd", "i15", "i16", 0, mul, OP.is_equal)
+    new("sd", "sd", -1, 0, mul, add)
     new("e0", "q7", 80, "q8", mul, add)
-    new("e1", "e0", 1, 40, mul, add)
-    for k in (0, 1):
-        lin(T.el[:, 24 * k:24 * k + 20], T.kk[:, 0:20], 2, col("e%d" % k), ["kk", "e%d" % k], ["el%d" % k])
-    new("d2", "p32", 4, 2, mul, add)
-    lin(T.dl[:, 0:10], T.kk[:, 0:10], 128, col("d2"), ["kk", "d2"], ["dl"])
-    new("px", "b", 16, "p32", mul, add)
-    for h in (0, 1):
-        at, n = AT[h] // 16, WID[h] // 32
-        lin(T.bl[:, at:at + n], T.kk[:, 0:n], 32, col("p32"), ["kk", "p32"], ["bl%d0" % h])
-        lin(T.bl[:, at + n:at + 2 * n], T.pat[:, 0:n], 1, col("px"), ["pata", "px"], ["bl%d1" % h])
+    ts(T.el[:, 0:40], T.kk[:], col("e0"), None, add, None, ["kk", "e0"], ["el"])
+    lin(T.dl[:, 0:10], T.kk[:, 0:10], 64, col("d2"), ["kk", "d2"], ["dl"])
+    lin(T.bl[:, 0:10], T.kk[:, 0:10], 16, col("p32"), ["kk", "p32"], ["bl0"])
+    ts(T.bl[:, 10:20], T.pat[:, 10:20], col("p32"), col("b16"), add, add, ["pata", "p32", "b16"], ["bl1"])
     new("sd2", "sd", 2, 0, mul, add)
     new("nd", "sd", -1, 0, mul, add)
     new("nn", "sd", 1, 1, mul, add)
-    fill(T.ue[:], 0.0, ["ue"], n=320)
+    fill(T.ue[:], 0.0, ["ue"], n=512)
     for t, v, names in ((0, 0.0, ["d0c"]), (1, 1.0, ["sb0", "sb1"])):
-        scaled(T.d0[:, t:1280:4], T.ue[:], 1.0, v, ["ue"], names, "a", 320)
-    aff(T.d0[:, 3:1280:4], T.ue[:], 1.0, col("nd"), ["ue", "nd"], ["d03"], 320, "a")
+        scaled(T.d0[:, t:1280:4], T.ue[:, 0:320], 1.0, v, ["ue"], names, "a", 320)
+    aff(T.d0[:, 3:1280:4], T.ue[:, 0:320], 1.0, col("nd"), ["ue", "nd"], ["d03"], 320, "a")
+    new("c0", "i16", 80, None, OP.min, None)
     for h in (0, 1):
-        new("c%d" % h, "i", WID[h] // 32 - 1, 16, OP.min, mul)
         ts(T.cl[:, 2 * h:20:4], T.sel[:, 0:5], col("c%d" % h), float(AT[h] // 2), add, add, SEL + ["c%d" % h], ["cl%d" % h])
+    new("px", "b16", 1, "p32", mul, add)
     for a in range(4):
         rows = slice(32 * a, 32 * a + 32)
-        src, m, p = (T.pat, 1, "px") if 0 < a < 3 else (T.kk, 32, "p32")
-        lin(T.blc[rows, 0:10], src[rows, 0:10], m, T.pc[rows, place[p]:place[p] + 1], ["kk", "pata", p], ["blc%d" % a])
+        src, m, p = (T.pat[rows, 10:20], 1.0, "px") if 0 < a < 3 else (T.kk[rows, 0:10], 16.0, "p32")
+        aff(T.pat[rows, 0:10], src, m, T.pc[rows, place[p]:place[p] + 1], ["kk", "pata", p], ["blc%d" % a], q=NEWQ)
+    cp(T.blc[:, 0:10], T.pat[:, 0:10], ["blc%d" % a for a in range(4)], ["blc"])
     for t in (0, 176):
-        fill(T.go[:, t:t + 16], 0.0, ["gom%d" % t])
-    new("m3", "a", 3, None, OP.is_equal, None)
-    new("xy", "x", "y", "m3", OP.subtract, mul)
-    new("ne", "xy", "y", "b", add, OP.not_equal)
-    new("bp", "x", "xy", 16, OP.subtract, mul)
-    new("sh", "b", -32, 192, mul, add)
-    aff(T.tmp[:, 30:31], col("ne"), col("sh"), T.sel[:, 7:8], ["ne", "sh"] + END, ["fa"])
-    aff(T.tmp[:, 31:32], T.tmp[:, 30:31], 1.0, col("bp"), ["fa", "bp"], ["fb"])
-    aff(T.tmp[:, 32:34], T.kk[:, 0:2], 4.0, col("q4"), ["kk", "q4"], ["ku"])
-    ts(T.tmp[:, 34:36], T.tmp[:, 32:34], 4.0, 32.0, OP.min, mul, ["ku"], ["kv"])
-    ts(T.sl[:, 0:2], T.tmp[:, 34:36], T.tmp[:, 31:32], None, add, None, ["kv", "fb"], ["sl0"])
-    new("c9", "i", 9, 16, OP.min, mul)
-    ts(T.sl[:, 4:8:2], T.sel[:, 5:7], col("c9"), None, add, None, ["c9"] + END, ["sm"])
-    new("fe", "a", 0, None, OP.is_equal, None)
+        cp(T.go[:, t:t + 16], T.ue[:, 0:16], ["ue"], ["gom%d" % t], NEWQ)
+    def bent(name, f, a, m, b):
+        place.setdefault(name, len(place))
+        sign(col(name), col(a), f, float(m), col(b) if isinstance(b, str) else float(b), [a] + [b] * isinstance(b, str), [name], 1)
+
+    bent("m3", AF.Relu, "a4", 0.25, -2)
+    bent("fe", AF.Relu, "a4", -0.25, 1)
     new("fo", "fe", 1, "m3", mul, add)
-    both = T.pc[:, place["fe"]:place["fe"] + 2]
-    aff(T.tmp[:, 36:38], both, 1.5, 0.5, ["fe", "fo"], ["fs"])
-    aff(T.tmp[:, 38:40], both, 642.0 - 1440.0, 1440.0, ["fe", "fo"], ["ft"])
-    new("fb1", "fe", "b", None, OP.max, None)
-    new("wx", "x", "y", "fb1", OP.subtract, mul)
-    new("i2", "y", "x", "i", OP.subtract, add)
-    new("i3", "i2", 1, "wx", mul, add)
-    aff(T.tmp[:, 40:42], T.kk[:, 0:2], 16.0, col("i3"), ["kk", "i3"], ["kf"])
-    ts(T.tmp[:, 42:44], T.tmp[:, 40:42], 19.0, 16.0, OP.min, mul, ["kf"], ["kg"])
-    aff(T.tmp[:, 44:45], T.sel[:, 9:10], col("b"), T.sel[:, 8:9], ["b"] + END, ["pos"])
-    ts(T.sl[:, 8:10], T.tmp[:, 42:44], T.tmp[:, 44:45], None, add, None, ["kg", "pos"], ["sk"])
-    new("far", "i", -FAR, 0, mul, add)
+    new("xmy", "y16", -1, "x16", mul, add)
+    new("xy", "xmy", "m3", 0, mul, add)
+    new("ne", "xy", "y16", "b16", add, OP.not_equal)
+    new("x14", "x16", 1, -2, mul, add)
+    new("bp", "xy", -1, "x14", mul, add)
+    new("sh", "b16", -2, 192, mul, add)
+    new("f5", "m3", -2, "a4", mul, add)
+    new("fa", "ne", "sh", "f5", mul, add)
+    new("h1", "a4", 0, 128, mul, add)
+    ts(T.sl[:, 0:2], T.pc[:, place["h0"]:place["h0"] + 2], col("fa"), col("bp"), add, add, ["h0", "h1", "fa", "bp"], ["sl0"])
+    new("y", "y16", 0.0625, 0, mul, add)
+    aff(T.tmp[:, 31:32], T.sel[:, 6:7], -1.0, T.sel[:, 5:6], SEL, ["odd"], q=NEWQ)
+    aff(T.tmp[:, 32:33], T.tmp[:, 31:32], col("y"), T.sel[:, 6:7], ["y", "odd"], ["src"], q=NEWQ)
+    new("t0", "q16", 80, None, OP.min, None)
+    new("t1", "q16", 48, 96, OP.min, add)
+    ts(T.sl[:, 4:8:2], T.pc[:, place["t0"]:place["t0"] + 2], T.tmp[:, 32:33], None, add, None, ["t0", "t1", "src"], ["sm"])
+    aff(T.tmp[:, 36:37], col("fo"), 1.5, 0.5, ["fo"], ["fs0"], q=NEWQ)
+    aff(T.tmp[:, 37:38], col("fo"), 642.0 - 1440.0, 1440.0, ["fo", "fs0"], ["fs"], q=NEWQ)
+    cp(T.tt[:, PLACE[6]:PLACE[6] + 160], T.ue[:, 0:160], ["ue"], ["T60", "T61"], NEWQ, 160)
+    new("nf", "b16", "fe", 0, add, OP.is_equal)
+    new("nf", "nf", -1, 0, mul, add)
+    new("wx", "xmy", "nf", 0, mul, add)
+    new("k0", "i16", "wx", 176, add, OP.min)
+    new("k1", "q7", 16, "wx", mul, add)
+    new("k1", "k1", 1, 192, mul, add)
+    new("b", "b16", 0.0625, 0, mul, add)
+    e = [home(EVEN[a][1]) for a in range(4)]
+    new("pe0", "fe", e[0] - e[1], e[1], mul, add)
+    new("pe", "m3", e[3] - e[1], "pe0", mul, add)
+    new("pos", "pe", -1, "a4", mul, add)
+    new("pos", "pos", "b", "pe", mul, add)
+    ts(T.sl[:, 8:12:2], T.pc[:, place["k0"]:place["k0"] + 2], col("pos"), None, add, None, ["k0", "k1", "pos"], ["sk"])
+    new("far", "i16", -FAR // 16, 0, mul, add)
     new("nn2", "nn", 2, 0, mul, add)
     new("n21", "nd", 2, -1, mul, add)
 
-    RAW = ["rb0", "rb1", "rb2"]
+    if "a" in DRQ:
+        ts(T.oa[:], T.raw[:], -160.0, None, add, None, ["raw0", "raw1", "raw2"], ["oa0", "oa1"], n=640)
     for h in (0, 1):
         n = WID[h]
         for k in (1, 0):
-            scaled(T.dr[:, quad(h, 2 * k, 4)], T.rb[:].indirect(T.el[:, 24 * k + AT[h] // 16:24 * k + (AT[h] + n) // 16]), 2.0, 0.0,
-                   RAW + ["el%d" % k], ["dr%d%d" % (h, 2 * k)], DRQ[2 * h + k], n, x=True)
+            lst = T.el[:, 20 * k + AT[h] // 16:20 * k + (AT[h] + n) // 16]
+            if DRQ[2 * h + k] == "v":
+                lin(T.dr[:, quad(h, 2 * k, 4)], T.raw[:].indirect(lst), 2, -320, ["raw0", "raw1", "raw2", "el"], ["dr%d%d" % (h, 2 * k)], n, x=True)
+            else:
+                scaled(T.dr[:, quad(h, 2 * k, 4)], T.oa[:].indirect(lst), 2.0, 0.0, ["oa0", "oa1", "el"], ["dr%d%d" % (h, 2 * k)], "a", n, x=True)
         for t, m in ((1, -1.0), (3, col("nn"))):
             aff(T.dr[:, quad(h, t, 4)], T.dr[:, quad(h, 2, 4)], m, 0.0, ["dr%d2" % h, "nn"], ["dr%d%d" % (h, t)], n, c=0.5)
 
     def twice(after):
-        cp(T.d1[:, 1:1280:4], T.d1[:, 0:1280:4], ["dif0", "dif1", after], ["d1d"], n=320, c=0.5)
+        for h in (0, 1):
+            if DIRQ[h] == "v" or after == "@s1":
+                ts(T.d1[:, quad(h, 1, 4)], T.d1[:, quad(h, 0, 4)], float(DIRQ[h] == "v"), None, mul, None, ["dif0", "dif1", after], ["d1d"], n=WID[h], c=0.5)
 
     def differences():
-        scaled(T.oa[:], T.dr[:, 2:1280:4], 0.5, 0.0, ["dr02", "dr12"], ["oa"], "a", 320)
-        tt(T.d1[:, 0:1280:4], T.rb[:].indirect(T.el[:, 0:20]), T.oa[:], OP.subtract, RAW + ["el0", "oa", "@s1"], ["dif0", "dif1"], n=320, x=True)
-        tt(T.d1[:, 2:1280:4], T.rb[:].indirect(T.el[:, 0:20]), T.oa[:], OP.add, RAW + ["el0", "oa", "@s1"], ["sum"], n=320, x=True)
+        for k in (0, 1):
+            scaled(T.oa[:, 320 * k:320 * k + 320], T.dr[:, 2 * k:1280:4], 0.5, 0.0, ["dr0%d" % (2 * k), "dr1%d" % (2 * k), "@bb"], ["oa%d" % k], "a", 320)
+        tt(T.d1[:, 0:1280:4], T.oa[:, 0:320], T.oa[:, 320:640], OP.subtract, ["oa0", "oa1", "@s1"], ["dif0", "dif1"], n=320, c=1)
+        tt(T.d1[:, 2:1280:4], T.oa[:, 0:320], T.oa[:, 320:640], OP.add, ["oa0", "oa1", "@s1"], ["sum"], n=320, c=1)
         ts(T.d1[:, 3:1280:4], T.d1[:, 2:1280:4], col("nn2"), None, mul, None, ["sum", "nn2"], ["two"], n=320, c=0.5)
         twice("@s1")
         aff(T.d0[:, 3:1280:4], T.d0[:, 0:1280:4], 1.0, col("n21"), ["d0c", "kl10", "n21"], ["d03"], 320, "a")
 
     for h in (0, 1):
         quant(T.qx0[:, cols(h)], T.sx0[:, cols(h)], T.x0[:, quad(h)], ["x0%d" % h], ["qx0%d" % h], 4 * WID[h])
-    iota(T.ones[:], [[0, 512]], 1, 0, ["ones"])
+    scaled(T.ones[:], T.ue[:, 0:128], 1.0, 1.0, ["ue", "d0c"], ["ones"], "a", 128)
+    dma("s", [(T.et[:, 512 * b:512 * b + 512], T.ue[:]) for b in range(4)], ["ue", "x01"], ["et%d" % b for b in range(4)] + ["@d3"], "de", LATE + 0.5)
+    dma("s", [(T.wq[:].bitcast(dt.uint8), T.wc[:]), (T.wsp[:], T.ws[:])], ["@d3"], ["wq"], "dw", 3.5)
 
     def one_in(b):
-        op("g", lambda e: e.affine_select(T.et[:, 512 * b:512 * b + 512], T.ones[:], [[1, 512]], OP.is_equal, 0.0, -b, -4), ["ones"], ["et%d" % b], 1.2)
+        op("g", lambda e: e.affine_select(T.et[:, 513 * b:512 * b + 512:4], T.ones[:], [[1, 128]], OP.is_equal, 0.0, 0, -1), ["ones"], ["et%d" % b, "@sent"], 0.45)
 
+    iota(T.w4[:], [[4, 320]], 1280, 0, ["w4", "@sent"])
+    iota(T.rs[:], [[0, 20], [FAR, 16]], 0, 0, ["rs", "@sent"])
     for b in range(4):
         one_in(b)
 
@@ -467,7 +583,9 @@ def rank_program(g, core, T, topo):
             mm(b, n, T.upq[:, c], T.ups[:, c], T["qx%d" % k][:, cols(h)], T["sx%d" % k][:, cols(h)], ["upq%d" % j, "ups%d" % j, "qx%d%d" % (k, h)],
                ["@n"] * (1 - h))
             r, w = ["b%d" % b, "sf", "sd", "sd2", "d0c"], ["%s%d" % (name, h)]
-            if j == 0 or j == 2 and NRQ[h] == "a":
+            if (k, h) == (3, 1):
+                ts(T.d0[:, quad(h, 1, 4)], bank(b, n), sc, 0.0, mul, OP.is_ge, r, ["sb1"], n)
+            elif j == 0 or j == 2 and NRQ[h] == "a" or j == 1 and k and DIRQ[h] == "a":
                 sign(o, bank(b, n), AF.Sign, sc, eps, r, w, n)
             elif j == 2:
                 ts(o, bank(b, n), 0.0, 0.5, OP.is_gt, mul, r, w, n)
@@ -480,18 +598,14 @@ def rank_program(g, core, T, topo):
              names + ["d0c", "d03", "sf%d" % h, "sb%d" % h, "@q%d" % k], ["win%d" % h], 4 * n, 0.5)
         if k < 3:
             for j in (0, 1):
-                at = AT[h] + j * n // 2
-                scaled(T.bb[:, at:at + n // 2], T.nr[:, cols(h)].indirect(T.bl[:, at // 16:(at + n // 2) // 16]), *HALF[NRQ[h]],
-                       ["nr%d" % h, "bl%d%d" % (h, j)], ["bb%d%d" % (h, j), "@bb"], "a", n // 2, x=True)
+                scaled(T.bb[:, halfrow(h, 160 * j)], T.nr[:, 0:cols(h).stop].indirect(T.bl[:, 10 * j + share(h).start:10 * j + share(h).stop]), *HALF[NRQ[h]],
+                       ["nr0", "nr%d" % h, "bl%d" % j], ["bb%d%d" % (h, j), "@bb"], "a", n // 2, x=True)
 
     HALF = {"a": (0.25, 0.25), "v": (1.0, 0.0)}
 
     def fifth(h):
         scaled(T.bc[:, halfrow(h)], T.nr[:, 0:cols(h).stop].indirect(T.blc[:, share(h)]), *HALF[NRQ[h]],
-               ["nr%d" % j for j in range(h + 1)] + ["blc%d" % a for a in range(4)] + ["@bb"], ["bc%d" % h], "a", WID[h] // 2, x=True)
-
-    def sign(o, i, f, sc, eps, r, w, n):
-        op("a", lambda e: e.activation(o, i, f, bias=eps, scale=sc), r, w, us(n, 1, False))
+               ["nr%d" % j for j in range(h + 1)] + ["blc", "@bb"], ["bc%d" % h], "a", WID[h] // 2, x=True)
 
     def turned(rd):
         tt(T.d1[:, 0:1280:4], T.d1[:, 0:1280:4], T.d0[:, 2:1280:4], mul, ["sf0", "sf1", "@g%d" % rd], ["dif0", "dif1", "@i"], n=320)
@@ -506,14 +620,14 @@ def rank_program(g, core, T, topo):
         else:
             at = 32 * (s - 2) + 16 * h
             w, names, lst = T.win[:, 0:1280], ["win0", "win1", "lu%d%d" % (s, h)], T.lu[:, at:at + n // 16]
-        at = AT[h] + n * (1 - s % 2)
-        bits, go, name = (T.bc[:, halfrow(h)], T.go[:, halfrow(h, 16)], "5%d" % h) if s == 5 else (T.bb[:, at:at + n], T.go[:, halfrow(h, 192)], "%d" % h)
-        tt(go, w.indirect(lst), bits, add, names + ["bc%d" % h if s == 5 else "bb%d%d" % (h, 1 - s % 2)] + list(after), ["go" + name], n=n, x=True)
-        tr(T.tt[:, halfrow(h, 160 * (s % 6))], go, ["go" + name], ["T%d%d" % (s, h)], n)
+        bits, go, name = (T.bc[:, halfrow(h)], T.go[:, halfrow(h, 16)], "5%d" % h) if s == 5 else (T.bb[:, halfrow(h, 160 * (1 - s % 2))], T.go[:, halfrow(h, 192)], "%d" % h)
+        tt(go, w.indirect(lst), bits, add, names + ["bc%d" % h if s == 5 else "bb%d%d" % (h, 1 - s % 2)] + list(after) + ["@t0"] * (h == 1 and s in TURN),
+           ["go" + name], n=n, x=True)
+        tr(T.tt[:, halfrow(h, PLACE[s])], go, ["go" + name], ["T%d%d" % (s, h), "@t%d" % h], n)
         if s < 6:
             at = 32 * (s - 1) + 16 * h
             k = 4 * (s - 1) + 2 * h
-            lin(T.lu[:, at:at + 16], T.tt[:, 160:halfrow(h, 160 * s).stop].indirect(T.cl[:, k:k + 1]), 2, 642, upto(s, h) + ["cl%d" % h],
+            lin(T.lu[:, at:at + 16], T.tt[:, 0:halfrow(h, PLACE[s]).stop].indirect(T.cl[:, k:k + 1]), 2, 642, upto(s, h) + ["cl%d" % h] + ["T60", "T61"] * (s == 5),
                 ["lu%d%d" % (s + 1, h)], n=16, x=True)
 
     def walk(rd):
@@ -521,20 +635,21 @@ def rank_program(g, core, T, topo):
             fifth(h)
         for s in range(1, 7):
             for h in (0, 1):
-                step(s, h, ["sk", "sm", "sl0", "fs", "ft", "gom0", "gom176"] * (s == 3))
+                step(s, h, ["sk", "sm", "sl0", "fs", "gom0", "gom176"] * (s == 4))
             if s == 5:
                 tr(T.tt[:, 960:1152], T.go[:, 0:192], ["go50", "go51", "gom0", "gom176"], ["TS"], 192)
                 lin(T.fl[:], T.tt[:, 800:1152].indirect(T.sl[:, 0:2]), 2, 642, ["T50", "T51", "TS", "sl0"], ["fl"], n=32, x=True)
-                for h in (0, 1):
-                    cp(T.win[:, 1280 + 160 * h:1440 + 160 * h], T.win[:, 0:1280].indirect(T.fl[:, 10 * h:10 * h + 10]), ["win0", "win1", "fl"], ["row%d" % h],
-                       ROWQ[h], n=160, x=True)
-        for k in (0, 1):
-            lin(T.mlu[:, k:32:2], T.tt[:, 0:960].indirect(T.sl[:, 6 - 2 * k:7 - 2 * k]), T.tmp[:, 36 + k:37 + k], T.tmp[:, 38 + k:39 + k],
-                upto(6, 1) + ["sm", "fs", "ft"], ["ml%d" % k], n=16, x=True)
+                cp(T.win[:, 1280:1600], T.win[:, 0:1280].indirect(T.fl[:, 0:20]), ["win0", "win1", "fl"], ["row0", "row1"], "a", n=320, x=True)
+                aff(T.tt[96:128, home("R7"):160:16], T.tt[96:128, home("R7"):160:16], 0.25, 399.0, ["T10", "T11"], ["T10", "T11"], q=FIXQ)
         for h in (0, 1):
-            cp(T.km[:, out(h)], T.win[:].indirect(T.mlu[:, 10 * h:10 * h + 10]), ["win0", "win1", "row0", "row1", "ml0", "ml1"], ["km%d" % h], "va"[h], n=160, x=True)
-        tr(T.kt[:], T.km[:], ["km0", "km1"], ["kt"], 320, 0.5)
-        lin(T["kl%d" % rd][:], T.kt[:].indirect(T.sl[:, 8:10]), 0.5, 160, ["kt", "sk"], ["kl%d0" % rd, "kl%d1" % rd], n=32, x=True)
+            lin(T.mlu[:, 16 * h:16 * h + 16], T.tt[:, 0:halfrow(h, PLACE[6]).stop].indirect(T.sl[:, 4 + 2 * h:5 + 2 * h]), T.tmp[:, 36:37], T.tmp[:, 37:38],
+                upto(4, 1) + ["T60", "T6%d" % h, "sm", "fs"], ["ml%d" % h], n=16, x=True)
+            for j, (a, n, q) in enumerate(KM[h]):
+                cp(T.km[:, AT[h] + a:AT[h] + a + n], T.win[:].indirect(T.mlu[:, 16 * h + a // 16:16 * h + (a + n) // 16]), ["win0", "win1", "row0", "row1", "ml%d" % h],
+                   ["km%d%d" % (h, j)], q, n=n, x=True)
+            tr(T.kt[:, cols(h)], T.km[:, cols(h)], ["km%d%d" % (h, j) for j in range(len(KM[h]))], ["kt%d" % h], WID[h], 0.5)
+            lin(T["kl%d" % rd][:, part(h).start:part(h).start + 16], T.kt[:, 0:cols(h).stop].indirect(T.sl[:, 8 + 2 * h:9 + 2 * h]), 0.5, 160,
+                ["kt0", "kt%d" % h, "sk"], ["kl%d%d" % (rd, h), "klx"], n=16, x=True)
 
     sent = [0]
 
@@ -551,7 +666,7 @@ def rank_program(g, core, T, topo):
             rid, pid = topo.addr(dst, core)
             m, n = topo.mask(core, dst), len(topo.engines(core, dst))
             if what == "k":
-                put(lambda e: e.remote_dma(T["kr%d" % rd][:], kl, T.sem["kr%d" % rd], T.sem.lsem, pid, rid, m), 1.0, 2.5, "kr%d" % rd, "kr%d" % rd, n, n)
+                put(lambda e: e.remote_dma(T["kr%d" % rd][:], kl, T.sem["kr%d" % rd], T.sem.lsem, pid, rid, m), 0.4, 2.2 + 1.9 * (rd == 1), "kr%d" % rd, "kr%d" % rd, n, n)
                 return
             c = out(h)
             sem = T.sem["ar%d%d" % (rd, h)]
@@ -560,7 +675,7 @@ def rank_program(g, core, T, topo):
                 e.remote_dma(lq[:, c].bitcast(dt.uint8), q[:, c].bitcast(dt.uint8), sem, T.sem.lsem, pid, rid, m)
                 e.remote_dma(ls[:, c], s[:, c], sem, T.sem.lsem, pid, rid, m)
 
-            put(go, 1.2, 3.5, "lq%d%d" % (rd, h), "ar%d%d" % (rd, h), 2 * n, 2 * n)
+            put(go, 0.7, 2.9 + 0.5 * h, "lq%d%d" % (rd, h), "ar%d%d" % (rd, h), 2 * n, 2 * n)
             return
         rel = relays_of(core, dst, topo)
         ways = [topo.addr(k, core) for k in rel]
@@ -571,26 +686,34 @@ def rank_program(g, core, T, topo):
         if what == "k":
             put(lambda e: e.remote_dma_fused([RemoteDMATransfer(dst_ids=[DstId(rid=ways[k][0], pnc=ways[k][1])], dma_engine_mask=bits_of(three[k]), remote_sem=T.sem.rk,
                                                                 src=T.kl2[:, 8 * k:8 * k + 8], dst=T.rlk[:]) for k in range(3)], local_sem=T.sem.lsem),
-                0.6, 5.0, "kr%d" % rd, "kr%d" % rd, 3 * far, 2 * n)
+                0.6, 7.0, "kr%d" % rd, "kr%d" % rd, 3 * far, 2 * n)
+            return
+        if WHOLE[h]:
+            def go3(e):
+                e.remote_dma(T.rlq[:, out(h)].bitcast(dt.uint8), q[:, out(h)].bitcast(dt.uint8), T.sem["ry%d" % h], T.sem.lsem, ways[1 - h][1], ways[1 - h][0], bits_of(eng))
+                e.remote_dma(T.rls[:, out(h)], s[:, out(h)], T.sem["ry%d" % h], T.sem.lsem, ways[2][1], ways[2][0], bits_of(eng))
+
+            put(go3, 0.7, 5.3, "lq%d%d" % (rd, h), "ar%d%d" % (rd, h), 2 * far, 4 * n)
             return
         a, w = out(h).start, VW[h] // 2
 
-        pieces = [(q[:, a + w * k:a + w * k + w].bitcast(dt.uint8), T.rlq[:, a + w * k:a + w * k + w].bitcast(dt.uint8)) for k in (0, 1)] + [(s[:], T.rlt[:])] * h
-        engs = three if h else [eng[:n], eng[n:]]
+        pieces = [(q[:, a + w * k:a + w * k + w].bitcast(dt.uint8), T.rlq[:, a + w * k:a + w * k + w].bitcast(dt.uint8)) for k in (0, 1)]
+        pieces += [(s[:, max(320 - 4 * w, 0):320], T.rlt[:, max(320 - 4 * w, 0):320])] * h * ONE
+        engs = three if h * ONE else [eng[:n], eng[n:]]
 
         def go2(e):
             e.remote_dma_fused([RemoteDMATransfer(dst_ids=[DstId(rid=ways[k][0], pnc=ways[k][1])], dma_engine_mask=bits_of(engs[k]),
                                                   remote_sem=T.sem["ry%d" % h], src=src, dst=land) for k, (src, land) in enumerate(pieces)], local_sem=T.sem.lsem)
-            if h == 0:
+            if h * ONE == 0:
                 e.remote_dma(T.rls[:, out(h)], s[:, out(h)], T.sem["ry%d" % h], T.sem.lsem, ways[2][1], ways[2][0], bits_of(eng))
 
-        put(go2, 1.2 - 0.6 * h, 6.0 - 0.5 * h, "lq%d%d" % (rd, h), "ar%d%d" % (rd, h), 3 * far, (4 - 2 * h) * n)
+        put(go2, 0.8 - 0.2 * h, 5.1 + 0.7 * h, "lq%d%d" % (rd, h), "ar%d%d" % (rd, h), 3 * far, (4 - 2 * h * ONE) * n)
 
     def meet(rd, h):
         for t in range(4):
             c = slice(320 * t + out(h).start, 320 * t + out(h).stop)
             far = T.xh[:, 320 * t:320 * t + 320].indirect(T["kl%d" % rd][:, out(h).start // 16:out(h).stop // 16])
-            r, w = ["xh%d" % t, "kl%d%d" % (rd, h)], ["vt%d%d" % (h, t)]
+            r, w = ["xh%d" % t, "kl%d0" % rd, "kl%d%d" % (rd, h)], ["vt%d%d" % (h, t)]
             if t in VA[h]:
                 cp(T.vg[:, c], far, r, ["vg%d%d" % (h, t)], "a", n=VW[h], x=True)
                 tt(T.vt[:, out(h, 4, t, 4)], T.vg[:, c], T.xh[:, c], OP.add, ["xh%d" % t, "vg%d%d" % (h, t)] + ["@v"] * h, w, n=VW[h], c=1)
@@ -622,7 +745,7 @@ def rank_program(g, core, T, topo):
         quant_v(0)
         layer(0)
         for b in range(4):
-            layer_out(0, b, "av")
+            layer_out(0, b, HQ[b])
         meet(rd, 1)
         quant_v(1)
         layer(1)
@@ -633,41 +756,48 @@ def rank_program(g, core, T, topo):
         else:
             turned(rd)
         for b in range(4):
-            layer_out(1, b, "av"[b == 3])
+            layer_out(1, b, HQ[4 + b])
         quant_h(rd, 1)
         send(rd, "h", 1)
         if rd == 1:
             sign(T.mask[:], T.rs[:], AF.Abs, 1.0, col("far"), ["rs", "far", "kl10"], ["mask"], 320)
             sign(T.mask[:], T.mask[:], AF.Relu, -1.0, 1.0, ["mask"], ["mask"], 320)
             differences()
+            ts(T.uoff[:, 0:8], T.zz[:], col("q16"), -15.0, add, add, ["zz", "q16", "@s1"], ["uoff0"])
             picked(0, ["@s1"])
-            dma("g", [(T.vb[:], T.v[:])], ["@sent"], ["vb"], "dv", 2.5)
+            dma("s", [(T.vb[:], T.v[:])], ["wq"], ["vb"], "dv", 2.5)
         else:
             twice("@s%d" % rd)
         if rd == 2:
             quant(T.vq[:], T.vs[:], T.vb[:], ["vb", "@s2"], ["vq"], 512)
         if rd == 3:
-            cp(T.d0[:, 1:1280:4], T.d0[:, 0:1280:4], ["d0c", "@s3"], ["sb0", "sb1"], "a", 320)
+            scaled(T.d0[:, quad(0, 1, 4)], T.d0[:, quad(0, 0, 4)], 1.0, float(DIRQ[0] == "a"), ["d0c", "@s3"], ["sb0"], "a", WID[0])
+            scaled(T.d0[:, quad(1, 2, 4)], T.d0[:, quad(1, 0, 4)], 1.0, 1.0, ["d0c", "@s3"], ["sf1"], "a", WID[1])
+            ts(T.d1[:, quad(1, 1, 4)], T.d1[:, quad(1, 0, 4)], -1.0, None, mul, None, ["dif1", "@s3"], ["d1d"], n=WID[1], c=0.5)
+            ts(T.d1[:, quad(1, 0, 4)], T.d1[:, quad(1, 1, 4)], -2.0, None, mul, None, ["d1d"], ["dif1"], n=WID[1], c=0.5)
             scaled(T.d0[:, 3:1280:4], T.d0[:, 0:1280:4], 1.0, -1.0, ["d0c", "@s3"], ["d03"], "a", 320)
             ts(T.d1[:, 3:1280:4], T.d1[:, 2:1280:4], 2.0, None, mul, None, ["sum", "@s3"], ["two"], n=320, c=0.5)
         kl, kr = T["kl%d" % rd], T["kr%d" % rd]
-        cp(T.kw[:], T.w4[:].indirect(kr[:, 0:20]), ["w4", "kr%d" % rd, "@s%d" % rd], ["kw"], "a", n=320, x=True)
-        tt(T.ky[:], T.kw[:].indirect(kl[:, 0:20]), T.mask[:], OP.mult, ["kw", "kl%d0" % rd, "kl%d1" % rd, "mask"], ["ky"], n=320, x=True)
-        scan(T.kys[:], T.rs[:], T.ky[:], 0.0, OP.min, OP.add, ["ky", "rs"], ["kys"], 320)
-        lin(T.mo[:, 0:20], T.kys[:, 15:320:16], 0.25, -320, ["kys"], ["mo_"])
+        for h in (0, 1):
+            cp(T.kw[:, 160 * h:160 * h + 160], T.w4[:].indirect(kr[:, 10 * h:10 * h + 10]), ["w4", "kr%d" % rd, "@s%d" % rd], ["kw%d" % h], "va"[h], n=160, x=True)
+        for h in (0, 1):
+            c = cols(h)
+            tt(T.ky[:, c], T.kw[:].indirect(kl[:, part(h)]), T.mask[:, c], OP.mult, ["kw0", "kw1", "kl%d0" % rd, "kl%d1" % rd, "mask"], ["ky%d" % h], n=WID[h], x=True)
+            scan(T.kys[:, c], T.rs[:, c], T.ky[:, c], 0.0, OP.min, OP.add, ["ky%d" % h, "rs"], ["kys%d" % h], WID[h])
+            lin(T.mo[:, part(h)], T.kys[:, c.start + 15:c.stop:16], 0.25, -320, ["kys%d" % h], ["mo%d" % h])
         lq, ls = T["lq%d" % rd], T["ls%d" % rd]
         for h in (0, 1):
             for b in range(4):
                 c = out(h)
                 mm(4 * h + b, VW[h], T.eq[:, 128 * b:128 * b + 128], T.es[:, 128 * b:128 * b + 128], lq[:, c], ls[:, c], ["eq", "lq%d%d" % (rd, h)], ["@u"])
                 cp(T.dd[:, 320 * b + c.start:320 * b + c.stop], bank(4 * h + b, VW[h]), ["b%d" % (4 * h + b)], ["dd%d%d" % (h, b)],
-                   "v" if (b, h) == (0, 1) else "a", n=VW[h])
+                   DDQ if (b, h) == (0, 1) else "a", n=VW[h])
         xn, qn, sn = T["x%d" % rd], T["qx%d" % rd], T["sx%d" % rd]
         for h in (0, 1):
             for t in range(4):
-                far, r = T.dd[:, 320 * t:320 * t + 320].indirect(T.mo[:, part(h)]), ["mo_", "dd0%d" % t, "dd1%d" % t]
+                far, r = T.dd[:, 320 * t:320 * t + 320].indirect(T.mo[:, part(h)]), ["mo%d" % h, "dd0%d" % t, "dd1%d" % t]
                 near, w = ["vt0%d" % t, "vt1%d" % t] + ["@x"] * (h * t > 0), ["xn%d%d%d" % (rd, h, t)]
-                if t in XA[h]:
+                if t in (XA, XB)[rd == 3][h]:
                     c = slice(320 * t + AT[h], 320 * t + AT[h] + WID[h])
                     cp(T.dg[:, c], far, r, ["dg%d%d" % (h, t)], "a", n=WID[h], x=True)
                     tt(xn[:, quad(h, t, 4)], T.dg[:, c], T.vt[:, quad(h, t, 4)], OP.add, ["dg%d%d" % (h, t)] + near, w, n=WID[h], c=1)
@@ -683,12 +813,11 @@ def rank_program(g, core, T, topo):
         dma("s", [(T.oc[:, quad(h)], T.qx3[:, c].bitcast(dt.uint8))], ["qx3%d" % h], [], "oq%d" % h)
         mm(6 + h, WID[h], T.vq[:], T.vs[:], T.qx3[:, c], T.sx3[:, c], ["vq", "qx3%d" % h])
         cp(T.yb[:, c], bank(6 + h, WID[h]), ["b%d" % (6 + h)], ["yb%d" % h], "a", n=WID[h])
-        dma("s", [(T.y[:, c], T.yb[:, c])], ["yb%d" % h], [], "oy")
         for k in (0, 1):
-            scaled(T.lout[:, 2 * AT[h] + k:2 * (AT[h] + WID[h]):2], T.win[:, quad(h, 2 + k, 4)], 0.5, 160.0, ["win%d" % h], ["lo%d%d" % (h, k)], "va"[k], WID[h])
-    for q, ks, sem in (("s", (0, 1), "os"), ("g", (2, 3), "og")):
-        dma(q, [(T.osc[4 * k:4 * k + 4, :], T.sx3[32 * k:32 * k + 4, :]) for k in ks], ["qx30", "qx31"], [], sem)
-    dma("a", [(T.lr[:], T.lout[0:16, :])], ["lo00", "lo01", "lo10", "lo11"], [], "ol")
+            scaled(T.lout[:, 2 * AT[h] + k:2 * (AT[h] + WID[h]):2], T.win[:, quad(h, 2 + k, 4)], 0.5, 160.0, ["win%d" % h], ["lo%d%d" % (h, k)], ("aa", "va")[h][k], WID[h])
+    dma("s", [(T.osc[4 * k:4 * k + 4, :], T.sx3[32 * k:32 * k + 4, :]) for k in range(4)], ["qx30", "qx31"], [], "os")
+    dma("s", [(T.y[:], T.yb[:])], ["yb0", "yb1"], [], "oy", 2.3)
+    dma(LRQ, [(T.lr[:], T.lout[0:16, :])], ["lo00", "lo01", "lo10", "lo11"], [], "ol")
     issue()
     need("g", dict(total))
     g.wait_ge(T.sem.lsem, sent[0])

@@ -6,16 +6,12 @@ import comms_topo
 OP = AluOpType
 AF = ActivationFunctionType
 STEP = [4, 1, 2]
-FAR = 4096
 WAKE, SPARE, LOOK = 0.12, 0.3, 0.3
 NEWQ = "av"
-NRQ = "av"
-ROWQ = "aa"
 VA, XA = ((2, 3), (1, 2, 3)), ((), (0, 1, 2, 3))
 LATE = 2.2
 XL = (0.3, 0.5)
-AHEAD = {}
-HOLD = ("@x", "@v", "@q1", "@q2", "@q3", "@h", "@i")
+HOLD = ("@x", "@v", "@h", "@i")
 WARM, SEED = 0.03, 4
 TRIES, SWAPS, ORDER = 500, 500, {}
 CASES = np.array([[0.95, 1.5, 1.3, 1, 0.11, 0.06, 1, 1], [0.95, 1.1, 1.3, 1, 0.11, 0.06, 1, 0.75], [0.95, 2.0, 1.3, 1, 0.11, 0.06, 1.2, 1], [0.85, 1.5, 0.6, 1, 0.15, 0.06, 1, 0.75],
@@ -29,25 +25,23 @@ for _n, _w, _d in [
     ("x0", 1280, B), ("x1", 1280, B), ("x2", 1280, B), ("x3", 1280, B), ("xh", 1280, B), ("xg", 1280, B), ("vg", 1280, B), ("dg", 1280, B), ("vt", 1280, B), ("ht", 1280, B), ("dd", 1280, B),
     ("ub", 512, B), ("vb", 512, B), ("et", 2048, B), ("ones", 128, B),
     ("uq", 128, C4), ("us", 128, S8), ("vq", 128, C4), ("vs", 128, S8), ("wq", 512, C4), ("wsp", 512, S8),
-    ("upq", 384, C4), ("ups", 384, S8), ("eq", 512, C4), ("es", 512, S8),
+    ("upq", 256, C4), ("ups", 256, S8), ("eq", 512, C4), ("es", 512, S8),
     ("qx0", 320, C4), ("sx0", 320, S8), ("qx1", 320, C4), ("sx1", 320, S8), ("qx2", 320, C4), ("sx2", 320, S8), ("qx3", 320, C4), ("sx3", 320, S8),
     ("qv", 320, C4), ("qvs", 320, S8),
     ("qh1", 320, C4), ("sh1", 320, S8), ("qh2", 320, C4), ("sh2", 320, S8), ("qh3", 320, C4), ("sh3", 320, S8),
-    ("lq1", 320, C4), ("ls1", 320, S8), ("lq2", 320, C4), ("ls2", 320, S8), ("lq3", 320, C4), ("ls3", 320, S8), ("rlq", 320, C4), ("rls", 320, S8), ("rlt", 320, S8),
-    ("raw", 640, I), ("oa", 640, B), ("d0", 1280, B), ("d1", 1280, H), ("win", 1600, B), ("nr", 320, B), ("bb", 320, F),
-    ("idn", 80, I), ("bc", 160, F), ("go", 352, F), ("tt", 1152, F), ("lu", 160, U), ("ue", 512, B), ("fl", 32, U), ("mlu", 32, U), ("km", 320, B), ("kt", 320, B),
+    ("lq1", 320, C4), ("ls1", 320, S8), ("lq2", 320, C4), ("ls2", 320, S8), ("lq3", 320, C4), ("ls3", 320, S8), ("rlq", 320, C4), ("rls", 320, S8),
+    ("raw", 640, I), ("d0", 960, B), ("d1", 960, H), ("win", 1600, B), ("nb", 320, B), ("nt", 320, B), ("dt1", 320, H), ("xt", 320, H), ("te", 640, B), ("zb", 320, B),
+    ("bb", 480, F), ("idn", 80, I), ("go", 352, F), ("tt", 1152, F), ("lu", 160, U), ("ue", 512, B), ("fl", 32, U), ("mlu", 64, U), ("km", 320, B), ("kt", 320, B),
     ("kl1", 32, U), ("kl2", 32, U), ("kl3", 32, U), ("kr1", 20, U), ("kr2", 24, U), ("kr3", 20, U), ("rlk", 8, U),
-    ("dr", 1280, B), ("w4", 320, F), ("mask", 320, F), ("rs", 320, F), ("kw", 320, F), ("ky", 320, F), ("kys", 320, F), ("mo", 32, U),
+    ("w4", 320, B), ("kw", 320, B), ("ky", 352, B), ("kys", 672, B), ("mo", 32, U), ("eye", 128, B), ("two", 16, F),
     ("lout", 640, F), ("yb", 320, F),
-    ("pi", 80, I), ("pj", 16, I), ("pc", 64, F), ("kk", 40, F), ("zz", 8, F), ("sel", 16, F), ("pat", 32, F), ("tmp", 64, F),
-    ("uoff", 24, U), ("cl", 24, U), ("dl", 16, U), ("bl", 32, U), ("blc", 16, U), ("el", 48, U), ("sl", 16, U),
+    ("pi", 8, I), ("pj", 24, I), ("pc", 80, F), ("kk", 40, F), ("zz", 8, F), ("sel", 16, F), ("pat", 16, F),
+    ("uoff", 16, U), ("cl", 24, U), ("bl", 48, U), ("el", 48, U), ("sl", 16, U),
 ]:
     SCRATCH[_n] = ("sbuf", [128, _w], _d)
 
-SEMAPHORES = (["sv", "sa", "st", "sg", "dx0", "dx1", "os", "du", "dv", "dw", "dn0", "dn1", "dn2", "de", "oy", "ol", "oq0", "oq1", "lsem", "ry0", "ry1", "rk"]
+SEMAPHORES = (["sv", "sa", "st", "sg", "dx0", "dx1", "os", "du", "dv", "dw", "dn0", "dn1", "dn2", "de", "dg", "oy", "ol0", "ol1", "oq0", "oq1", "lsem", "ry0", "ry1", "rk"]
               + ["ar%d%d" % (r, h) for r in (1, 2, 3) for h in (0, 1)] + ["kr%d" % r for r in (1, 2, 3)])
-ONE = 0
-WHOLE = (False, False)
 VW = (160, 160)
 
 
@@ -58,20 +52,24 @@ def out(h, n=1, t=0, step=1):
 AT, WID = (0, 192), (192, 128)
 
 
-def cols(h):
-    return slice(AT[h], AT[h] + WID[h])
+def cols(h, t=0, step=1, at=0):
+    return slice(at + AT[h] + t, at + AT[h] + WID[h], step)
 
 
-def quad(h, t=0, step=1):
-    return slice(4 * AT[h] + t, 4 * (AT[h] + WID[h]), step)
+def quad(h, t=0, step=1, n=4):
+    return slice(n * AT[h] + t, n * (AT[h] + WID[h]), step)
+
+
+def tri(h, t=0, step=1):
+    return quad(h, t, step, 3)
 
 
 def part(h):
     return slice(AT[h] // 16, (AT[h] + WID[h]) // 16)
 
 
-def share(h):
-    return slice(AT[h] // 32, (AT[h] + WID[h]) // 32)
+def share(h, at=0):
+    return slice(at + AT[h] // 32, at + (AT[h] + WID[h]) // 32)
 
 
 def halfrow(h, at=0):
@@ -79,20 +77,24 @@ def halfrow(h, at=0):
 
 
 WAY = [["R6", "R5", "R4", "R3", "R2"], ["R6", "R5", "R4", "L1", "R3"], ["L1", "L2", "R6", "L3", "R5"], ["L1", "L2", "L3", "L4", "L5"]]
-EVEN = [("R2", "R1"), ("R3", "L7"), ("R5", "L7"), ("R7", "L5")]
+EVEN = [("R2", "R1"), ("R3", "I8"), ("R5", "I8"), ("R7", "L5")]
 ODD = [("R2", "L0"), ("R4", "L2"), ("R6", "L4"), ("L5", "L6")]
-
+RIGHT = [1, 0, 1, 0, 0, 1, 0, 1]
+SEQ = 13
+TABLE, ROW = (0.75, 481.75), (0.25, 1120.25)
 
 KM = ([(0, 96, "v"), (96, 96, "a")], [(0, 128, "a")])
-FIXQ, DDQ, DRQ, DIRQ, LRQ = "v", "v", "vvvv", "vv", "a"
+DDQ, LRQ = "vaaa", "as"
+FQ = {1: "aa", 2: "aa", 3: "av"}
 XB = ((), (0, 1, 2, 3))
-HQ = ["av"] * 4 + list("aaav")
-TURN = ()
-PLACE = [None, 0, 160, 320, 480, 800, 640]
+EARLY = "@s1"
+KQ = {1: "aa", 2: "va", 3: "va"}
+HQ = ["av"] * 4 + list("avav")
+PLACE = [None, 0, 160, 320, 480, 640, 800]
 
 
 def home(table):
-    return 2 * int(table[1]) + (table[0] == "R")
+    return int(table[1]) + 7 * (table[0] != "R")
 
 
 def before(table):
@@ -127,19 +129,14 @@ def relay_program(g, core, T, topo):
         g.wait_ge(T.sem.rk, all_ // (2 if k == 2 else 4))
         g.remote_dma(T.kr2[:, 8 * k:8 * k + 8], T.rlk[:], T.sem.kr2, T.sem.lsem, pid, rid, m)
         for h in (0, 1):
-            if WHOLE[h]:
-                if k == 2 or k == 1 - h:
-                    g.wait_ge(T.sem["ry%d" % h], all_)
-                    o, i = (T.ls2[:, out(h)], T.rls[:, out(h)]) if k == 2 else (T.lq2[:, out(h)].bitcast(dt.uint8), T.rlq[:, out(h)].bitcast(dt.uint8))
-                    g.remote_dma(o, i, T.sem["ar2%d" % h], T.sem.lsem, pid, rid, m)
-            elif k < 2:
+            if k < 2:
                 a, w = out(h).start + VW[h] // 2 * k, VW[h] // 2
-                g.wait_ge(T.sem["ry%d" % h], all_ // (2 + 2 * h * ONE))
+                g.wait_ge(T.sem["ry%d" % h], all_ // 2)
                 g.remote_dma(T.lq2[:, a:a + w].bitcast(dt.uint8), T.rlq[:, a:a + w].bitcast(dt.uint8), T.sem["ar2%d" % h], T.sem.lsem, pid, rid, m)
             else:
-                g.wait_ge(T.sem["ry%d" % h], all_ // (1 + h * ONE))
-                g.remote_dma(T.ls2[:, out(h)], (T.rls, T.rlt)[h * ONE][:, out(h)], T.sem["ar2%d" % h], T.sem.lsem, pid, rid, m)
-        g.wait_ge(T.sem.lsem, n * (1 + sum(k in (2, 1 - h) or not WHOLE[h] for h in (0, 1))))
+                g.wait_ge(T.sem["ry%d" % h], all_)
+                g.remote_dma(T.ls2[:, out(h)], T.rls[:, out(h)], T.sem["ar2%d" % h], T.sem.lsem, pid, rid, m)
+        g.wait_ge(T.sem.lsem, 3 * n)
 
 
 def rank_program(g, core, T, topo):
@@ -152,7 +149,7 @@ def rank_program(g, core, T, topo):
     nodes, writer, readers = [], {}, {}
 
     def node(fns, cost, late, r, w, sem, inc):
-        r = [k for k in r if k in HOLD or k not in ("@x", "@v", "@q1", "@q2", "@q3", "@h", "@i")]
+        r = [k for k in r if k in HOLD or k not in ("@x", "@v", "@h", "@i")]
         pre, after = set(), set()
         for k in list(r) + list(w):
             if k in writer:
@@ -217,7 +214,7 @@ def rank_program(g, core, T, topo):
         op("t", lambda e: e.matmul_mx(T.ps[:, 512 * bank:512 * bank + n], lq, lsc, rq, rsc, True, True), r, ["b%d" % bank] + list(turn), (n + 16) * PE * CYC)
 
     def fill(o, c, w, n=10):
-        op("v", lambda e: e.memset(o, c), [], w, us(n, 0.5, False))
+        op("v", lambda e: e.memset(o, float(c)), [], w, us(n, 0.5, False))
 
     def quant(q, s, t, r, w, n=640):
         op("v", lambda e: e.quantize_mx(q, s, t), r, w, (14.0 + n * 0.265) * CYC)
@@ -367,27 +364,29 @@ def rank_program(g, core, T, topo):
     def bank(b, n):
         return T.ps[:, 512 * b:512 * b + n]
 
-    for k, (q, tab) in enumerate((("s", T.lam), ("a", T.rho))):
-        if k:
-            dma("a", [(T.ub[:], T.u[:])], [], ["ub", "@d1"], "du", LATE)
-        else:
-            dma("s", [(T.x0[:, quad(0)], T.x[:, quad(0)])], [], ["x00", "@d0"], "dx0", LATE + XL[0])
-        few = [8 - (k == 0 and 2 <= gr < 6) for gr in range(8)]
-        dma(q, [(T.raw[16 * gr + k:16 * gr + 2 * few[gr]:2, :], tab[0:16 * few[gr], :]) for gr in range(8)], [], ["raw%d" % k, "@d%d" % k], "dn%d" % k, LATE + XL[0])
+    dma("s", [(T.x0[:, quad(0)], T.x[:, quad(0)])], [], ["x00", "@d0"], "dx0", LATE + XL[0])
+    dma("s", [(T.raw[16 * gr + 7 + RIGHT[gr]:16 * gr + 15, :], T.lam[16 * RIGHT[gr]:128, :]) for gr in range(8)], [], ["raw0", "@d0"], "dn0", LATE + XL[0])
+    dma("a", [(T.ub[:], T.u[:])], [], ["ub", "@d1"], "du", LATE)
+    dma("a", [(T.raw[16 * gr:16 * gr + 7 + RIGHT[gr], :], T.rho[0:112 + 16 * RIGHT[gr], :]) for gr in range(8)], [], ["raw1", "@d1"], "dn1", LATE + XL[0])
 
     def iota(o, pattern, base, cm, w, fl=True):
         n = 1
         for step, count in pattern:
             n *= count
         if fl:
-            op("g", lambda e: e.iota(o, pattern, base, cm, allow_small_or_imprecise_dtypes=True), [], w, 0.15 + 0.002 * n)
+            op("g", lambda e: e.iota(o, pattern, base, cm, allow_small_or_imprecise_dtypes=True), [], w, 0.22 + 0.0022 * n)
         else:
-            op("g", lambda e: e.iota(o, pattern, base, cm), [], w, 0.15 + 0.002 * n)
+            op("g", lambda e: e.iota(o, pattern, base, cm), [], w, 0.22 + 0.0022 * n)
 
     iota(T.pi[:, 0:1], [[0, 1]], 32, 64, ["p"], False)
-    iota(T.idn[0:8, :], [[0, 2], [8, 40]], 0, 1, ["idn"], False)
+    iota(T.idn[0:64, :], [[0, 2], [8, 40]], 0, 1, ["idn"], False)
     iota(T.kk[:], [[40, 2], [2, 20]], 0, 0, ["kk"])
-    iota(T.pat[:, 10:20], [[64, 5], [16, 2]], 0, 0, ["pata"])
+    iota(T.pat[:, 0:10], [[64, 5], [16, 2]], 0, 0, ["pata"])
+    dma("s", [(T.raw[home("I8"):128:16, :], T.idn[0:64, :])], ["idn", "@d0"], ["raw2", "@d2"], "dn2", LATE)
+    dma("s", [(T.x0[:, quad(1)], T.x[:, quad(1)])], ["@d2"], ["x01", "@d3"], "dx1", LATE + XL[1])
+
+    def spot(a, table):
+        return PLACE[1] if table in ("L0", "R7") else PLACE[2 + WAY[a].index(table)] + home(table)
 
     def numbers(first, rows, name):
         names = []
@@ -402,15 +401,12 @@ def rank_program(g, core, T, topo):
                 k += n
         return names
 
-    def spot(a, table):
-        s = 1 if table in ("L0", "R7") else 2 + WAY[a].index(table)
-        return PLACE[s] + home(table)
-
-    SEL = numbers(0, [[spot(a, before(t)) for t in WAY[a]] + [spot(a, ODD[a][0]), spot(a, EVEN[a][0])] for a in range(4)], "sel")
+    SEL = numbers(0, [[spot(a, before(t)) - PLACE[2] * (t == WAY[a][1]) for t in WAY[a][1:]] for a in range(4)], "sel")
+    END = numbers(4, [[spot(a, ODD[a][0]), spot(a, EVEN[a][0])] for a in range(4)], "end")
 
     place = {}
-    for digits, then in (({"q16": (3, 112), "y16": (2, 16), "q7": (6, 7), "q8": (9, 1), "i16": (2, 240)}, "c2"),
-                         ({"p32": (6, 31), "d2": (4, 126), "b16": (6, 16), "c1": (2, 48), "x16": (3, 16), "a4": (9, 12), "h0": (3, 96)}, "h1")):
+    for digits, then in (({"q16": (2, 240), "g32": (5, 224), "p32": (6, 31)}, "c0"),
+                         ({"c1": (2, 48), "b16": (6, 16), "x16": (2, 16), "y16": (3, 16), "a": (11, 3), "k1": (2, 112), "h0": (3, 96)}, "h1")):
         at = len(place)
         for name, (sh, m) in digits.items():
             k = place[name] = len(place)
@@ -421,12 +417,14 @@ def rank_program(g, core, T, topo):
     def col(name):
         return T.pc[:, place[name]:place[name] + 1]
 
+    late = [[]]
+
     def new(name, a, s1, s2, f1, f2):
         place.setdefault(name, len(place))
-        use = [a] + [s for s in (s1, s2) if isinstance(s, str)]
+        use = [a] + [s for s in (s1, s2) if isinstance(s, str)] + late[0]
         s1, s2 = [col(s) if isinstance(s, str) else s if s is None else float(s) for s in (s1, s2)]
         if (f1, f2) == (mul, add):
-            aff(col(name), col(a), s1, s2, use, [name], q="av" if name in ("n", "e0", "i15", "sd", "nd", "nn") else NEWQ)
+            aff(col(name), col(a), s1, s2, use, [name], q=NEWQ)
         else:
             ts(col(name), col(a), s1, s2, f1, f2, use, [name])
 
@@ -435,12 +433,19 @@ def rank_program(g, core, T, topo):
         node({k: fns[k] for k in q}, {k: us(n, c if k == "v" else 1, False) for k in q}, 0.0, r, w, None, 1)
 
     mul, add = OP.mult, OP.add
-    dma("s", [(T.raw[k:k + 1, :], T.idn[0:8, :]) for k in range(32 + home("L7"), 96, 16)], ["idn", "@d0"], ["raw2", "@d2"], "dn2", LATE)
-    dma("s", [(T.x0[:, quad(1)], T.x[:, quad(1)])], ["@d2"], ["x01", "@d3"], "dx1", LATE + XL[1])
-    fill(T.zz[:], 16.0, ["zz"])
-    new("n", "y16", -2, "q16", mul, add)
-    ts(T.uoff[:, 8:16], T.zz[:], col("q16"), -16.0, add, add, ["zz", "q16"], ["uoff1"])
-    ts(T.uoff[:, 16:24], T.zz[:], col("n"), 112.0, add, OP.min, ["zz", "n"], ["uoff2"])
+    fill(T.zz[:], 0.0, ["zz"])
+    for c in (slice(0, 4, 2), slice(5, 8, 2)):
+        fill(T.zz[:, c], 1.0, ["zz"])
+    new("g7", "q16", 112, -80, OP.is_ge, mul)
+    new("t", "q16", "g7", -16, add, add)
+    new("lo", "q16", 16, 112, OP.is_le, mul)
+    new("t", "t", "lo", 96, OP.max, OP.min)
+    new("mid", "q16", 208, None, OP.is_le, None)
+    new("e14", "q16", 224, None, OP.is_equal, None)
+    new("ua", "t", "mid", "e14", mul, add)
+    new("hi", "mid", -112, 112, mul, add)
+    new("ub_", "lo", -80.0 / 112.0, "hi", mul, add)
+    ts(T.uoff[:, 8:16], T.zz[:], col("ub_"), col("ua"), mul, add, ["zz", "ua", "ub_"], ["uoff1"])
     quant(T.uq[:], T.us[:], T.ub[:], ["ub"], ["uq"], 512)
 
     def picked(k, after):
@@ -449,117 +454,119 @@ def rank_program(g, core, T, topo):
         cp(T.ups[:, c], T.us[:].indirect(o), ["uq", "uoff%d" % k], ["ups%d" % k], "a", n=128, x=True)
 
     picked(1, [])
-    picked(2, [])
-    new("sf", "y16", -0.125, 1, mul, add)
-    new("i15", "i16", -1, 240, mul, add)
-    new("sd", "i15", "i16", 0, mul, OP.is_equal)
-    new("sd", "sd", -1, 0, mul, add)
-    new("e0", "q7", 80, "q8", mul, add)
+    new("e15", "q16", 240, -1, OP.is_equal, mul)
+    new("sc0", "q16", 192, "e15", OP.is_le, add)
+    new("bi", "q16", -16 * SEQ, 1, add, OP.min)
+    new("bi", "bi", -1, EPS, OP.max, mul)
+    new("q8", "q16", 128, -639, OP.is_ge, mul)
+    new("e0", "q16", 5, "q8", mul, add)
     ts(T.el[:, 0:40], T.kk[:], col("e0"), None, add, None, ["kk", "e0"], ["el"])
-    lin(T.dl[:, 0:10], T.kk[:, 0:10], 64, col("d2"), ["kk", "d2"], ["dl"])
+    new("off", "e15", "g32", -640, mul, add)
     lin(T.bl[:, 0:10], T.kk[:, 0:10], 16, col("p32"), ["kk", "p32"], ["bl0"])
-    ts(T.bl[:, 10:20], T.pat[:, 10:20], col("p32"), col("b16"), add, add, ["pata", "p32", "b16"], ["bl1"])
-    new("sd2", "sd", 2, 0, mul, add)
-    new("nd", "sd", -1, 0, mul, add)
-    new("nn", "sd", 1, 1, mul, add)
+    ts(T.bl[:, 16:26], T.pat[:, 0:10], col("p32"), col("b16"), add, add, ["pata", "p32", "b16"], ["bl1"])
+    cp(T.bl[:, 32:42], T.bl[:, 16:26], ["bl1"], ["bl2"])
+    for a in (1, 2):
+        cp(T.bl[32 * a:32 * a + 32, 32:42], T.bl[32 * a:32 * a + 32, 0:10], ["bl0"], ["bl2"])
     fill(T.ue[:], 0.0, ["ue"], n=512)
-    for t, v, names in ((0, 0.0, ["d0c"]), (1, 1.0, ["sb0", "sb1"])):
-        scaled(T.d0[:, t:1280:4], T.ue[:, 0:320], 1.0, v, ["ue"], names, "a", 320)
-    aff(T.d0[:, 3:1280:4], T.ue[:, 0:320], 1.0, col("nd"), ["ue", "nd"], ["d03"], 320, "a")
-    new("c0", "i16", 80, None, OP.min, None)
+    cp(T.dt1[:], T.ue[:, 0:320], ["ue"], ["dt0", "dt1", "st0", "st1"], n=320, c=0.5)
+    ts(T.dt1[:, SEQ + 3:320:32], T.ue[:, 0:10], 1.0, None, add, None, ["ue", "dt0"], ["beta"])
+    cp(T.win[:, 0:960:3], T.ue[:, 0:320], ["ue"], ["winz"], "a", 320)
+    new("c0", "q16", 80, None, OP.min, None)
     for h in (0, 1):
-        ts(T.cl[:, 2 * h:20:4], T.sel[:, 0:5], col("c%d" % h), float(AT[h] // 2), add, add, SEL + ["c%d" % h], ["cl%d" % h])
-    new("px", "b16", 1, "p32", mul, add)
-    for a in range(4):
-        rows = slice(32 * a, 32 * a + 32)
-        src, m, p = (T.pat[rows, 10:20], 1.0, "px") if 0 < a < 3 else (T.kk[rows, 0:10], 16.0, "p32")
-        aff(T.pat[rows, 0:10], src, m, T.pc[rows, place[p]:place[p] + 1], ["kk", "pata", p], ["blc%d" % a], q=NEWQ)
-    cp(T.blc[:, 0:10], T.pat[:, 0:10], ["blc%d" % a for a in range(4)], ["blc"])
+        ts(T.cl[:, 2 * h:16:4], T.sel[:, 0:4], col("c%d" % h), float(AT[h] // 2), add, add, SEL + ["c%d" % h], ["cl%d" % h])
+    new("c9", "q16", 144, None, OP.min, None)
+    ts(T.cl[:, 16:20:2], T.sel[:, 4:6], col("c9"), None, add, None, END + ["c9"], ["cl2"])
     for t in (0, 176):
         cp(T.go[:, t:t + 16], T.ue[:, 0:16], ["ue"], ["gom%d" % t], NEWQ)
-    def bent(name, f, a, m, b):
-        place.setdefault(name, len(place))
-        sign(col(name), col(a), f, float(m), col(b) if isinstance(b, str) else float(b), [a] + [b] * isinstance(b, str), [name], 1)
-
-    bent("m3", AF.Relu, "a4", 0.25, -2)
-    bent("fe", AF.Relu, "a4", -0.25, 1)
-    new("fo", "fe", 1, "m3", mul, add)
+    cp(T.tt[:, PLACE[1]:PLACE[1] + 160], T.ue[:, 0:160], ["ue"], ["T10", "T11"], NEWQ, 160)
+    iota(T.tt[:, PLACE[6]:PLACE[6] + 160], [[0, 160]], 0, 0, ["T60", "T61"])
+    new("m3", "a", 3, None, OP.is_equal, None)
     new("xmy", "y16", -1, "x16", mul, add)
     new("xy", "xmy", "m3", 0, mul, add)
-    new("ne", "xy", "y16", "b16", add, OP.not_equal)
-    new("x14", "x16", 1, -2, mul, add)
-    new("bp", "xy", -1, "x14", mul, add)
-    new("sh", "b16", -2, 192, mul, add)
-    new("f5", "m3", -2, "a4", mul, add)
-    new("fa", "ne", "sh", "f5", mul, add)
-    new("h1", "a4", 0, 128, mul, add)
-    ts(T.sl[:, 0:2], T.pc[:, place["h0"]:place["h0"] + 2], col("fa"), col("bp"), add, add, ["h0", "h1", "fa", "bp"], ["sl0"])
-    new("y", "y16", 0.0625, 0, mul, add)
-    aff(T.tmp[:, 31:32], T.sel[:, 6:7], -1.0, T.sel[:, 5:6], SEL, ["odd"], q=NEWQ)
-    aff(T.tmp[:, 32:33], T.tmp[:, 31:32], col("y"), T.sel[:, 6:7], ["y", "odd"], ["src"], q=NEWQ)
-    new("t0", "q16", 80, None, OP.min, None)
-    new("t1", "q16", 48, 96, OP.min, add)
-    ts(T.sl[:, 4:8:2], T.pc[:, place["t0"]:place["t0"] + 2], T.tmp[:, 32:33], None, add, None, ["t0", "t1", "src"], ["sm"])
-    aff(T.tmp[:, 36:37], col("fo"), 1.5, 0.5, ["fo"], ["fs0"], q=NEWQ)
-    aff(T.tmp[:, 37:38], col("fo"), 642.0 - 1440.0, 1440.0, ["fo", "fs0"], ["fs"], q=NEWQ)
-    cp(T.tt[:, PLACE[6]:PLACE[6] + 160], T.ue[:, 0:160], ["ue"], ["T60", "T61"], NEWQ, 160)
-    new("nf", "b16", "fe", 0, add, OP.is_equal)
-    new("nf", "nf", -1, 0, mul, add)
-    new("wx", "xmy", "nf", 0, mul, add)
-    new("k0", "i16", "wx", 176, add, OP.min)
-    new("k1", "q7", 16, "wx", mul, add)
-    new("k1", "k1", 1, 192, mul, add)
+    new("v16", "xy", 1, "y16", mul, add)
+    new("sh", "b16", -42.0 / 16.0, 22, mul, add)
+    new("a2", "a", 2, 7, mul, add)
+    new("f5", "a2", -1, 11, add, OP.min)
+    new("fa", "v16", "sh", "f5", mul, add)
+    new("fb", "b16", 20, "x16", mul, add)
+    new("fb", "xy", -1, "fb", mul, add)
+    new("h1", "a", 0, 128, mul, add)
+    ts(T.sl[:, 0:2], T.pc[:, place["h0"]:place["h0"] + 2], col("fa"), col("fb"), add, add, ["h0", "h1", "fa", "fb"], ["sl0"])
     new("b", "b16", 0.0625, 0, mul, add)
+    new("lay", "a", 0, "b", OP.is_equal, OP.max)
+    new("wx", "xmy", "lay", 0, mul, add)
+    place["k0"] = len(place)
+    place["k2"] = len(place)
+    new("k0", "q16", "wx", 176, add, OP.min)
+    new("k2", "k1", "wx", 192, add, add)
+    new("m0", "a", 0, None, OP.is_equal, None)
     e = [home(EVEN[a][1]) for a in range(4)]
-    new("pe0", "fe", e[0] - e[1], e[1], mul, add)
-    new("pe", "m3", e[3] - e[1], "pe0", mul, add)
-    new("pos", "pe", -1, "a4", mul, add)
+    new("pe", "m0", e[0] - e[1], e[1], mul, add)
+    new("pe", "m3", e[3] - e[1], "pe", mul, add)
+    new("pos", "pe", -1, "a2", mul, add)
     new("pos", "pos", "b", "pe", mul, add)
-    ts(T.sl[:, 8:12:2], T.pc[:, place["k0"]:place["k0"] + 2], col("pos"), None, add, None, ["k0", "k1", "pos"], ["sk"])
-    new("far", "i16", -FAR // 16, 0, mul, add)
-    new("nn2", "nn", 2, 0, mul, add)
-    new("n21", "nd", 2, -1, mul, add)
+    ts(T.sl[:, 8:12:2], T.pc[:, place["k0"]:place["k0"] + 2], col("pos"), None, add, None, ["k0", "k2", "pos"], ["sk"])
+    for b, m in enumerate(("m0", "m3")):
+        new("by%d" % b, m, TABLE[0] - ROW[0], ROW[0], mul, add)
+        new("at%d" % b, m, TABLE[1] - ROW[1], ROW[1], mul, add)
+    new("at1", "m0", 320, "at1", mul, add)
 
-    if "a" in DRQ:
-        ts(T.oa[:], T.raw[:], -160.0, None, add, None, ["raw0", "raw1", "raw2"], ["oa0", "oa1"], n=640)
     for h in (0, 1):
         n = WID[h]
-        for k in (1, 0):
-            lst = T.el[:, 20 * k + AT[h] // 16:20 * k + (AT[h] + n) // 16]
-            if DRQ[2 * h + k] == "v":
-                lin(T.dr[:, quad(h, 2 * k, 4)], T.raw[:].indirect(lst), 2, -320, ["raw0", "raw1", "raw2", "el"], ["dr%d%d" % (h, 2 * k)], n, x=True)
-            else:
-                scaled(T.dr[:, quad(h, 2 * k, 4)], T.oa[:].indirect(lst), 2.0, 0.0, ["oa0", "oa1", "el"], ["dr%d%d" % (h, 2 * k)], "a", n, x=True)
-        for t, m in ((1, -1.0), (3, col("nn"))):
-            aff(T.dr[:, quad(h, t, 4)], T.dr[:, quad(h, 2, 4)], m, 0.0, ["dr%d2" % h, "nn"], ["dr%d%d" % (h, t)], n, c=0.5)
-
-    def twice(after):
-        for h in (0, 1):
-            if DIRQ[h] == "v" or after == "@s1":
-                ts(T.d1[:, quad(h, 1, 4)], T.d1[:, quad(h, 0, 4)], float(DIRQ[h] == "v"), None, mul, None, ["dif0", "dif1", after], ["d1d"], n=WID[h], c=0.5)
-
-    def differences():
         for k in (0, 1):
-            scaled(T.oa[:, 320 * k:320 * k + 320], T.dr[:, 2 * k:1280:4], 0.5, 0.0, ["dr0%d" % (2 * k), "dr1%d" % (2 * k), "@bb"], ["oa%d" % k], "a", 320)
-        tt(T.d1[:, 0:1280:4], T.oa[:, 0:320], T.oa[:, 320:640], OP.subtract, ["oa0", "oa1", "@s1"], ["dif0", "dif1"], n=320, c=1)
-        tt(T.d1[:, 2:1280:4], T.oa[:, 0:320], T.oa[:, 320:640], OP.add, ["oa0", "oa1", "@s1"], ["sum"], n=320, c=1)
-        ts(T.d1[:, 3:1280:4], T.d1[:, 2:1280:4], col("nn2"), None, mul, None, ["sum", "nn2"], ["two"], n=320, c=0.5)
-        twice("@s1")
-        aff(T.d0[:, 3:1280:4], T.d0[:, 0:1280:4], 1.0, col("n21"), ["d0c", "kl10", "n21"], ["d03"], 320, "a")
+            lst = T.el[:, 20 * k + AT[h] // 16:20 * k + (AT[h] + n) // 16]
+            lin(T.win[:, tri(h, 1 + k, 3)], T.raw[:].indirect(lst), 4.0, col("off"), ["raw0", "raw1", "raw2", "el", "off"], ["win%d%d" % (h, k)], n, x=True)
+            tr(T.te[:, cols(h, at=320 * k)], T.win[:, tri(h, 1 + k, 3)], ["win%d%d" % (h, k)], ["te%d%d" % (h, k)], n, 0.5)
+        for t, f, name in ((0, OP.subtract, "dt"), (2, add, "st")):
+            tt(T.dt1[:, cols(h, SEQ + t, 16)], T.te[:, cols(h, home("L0"), 16)], T.te[:, cols(h, home("L0"), 16, 320)], f, ["te%d0" % h, "te%d1" % h], ["%s%d" % (name, h)])
+
+    def tables(h):
+        return ["win%d0" % h, "win%d1" % h]
+
+    WIN = tables(0) + tables(1) + ["winz"]
+
+    def flips():
+        late[0] = [EARLY]
+        for t, v in ((0, 0), (2, -1)):
+            iota(T.d0[:, t:960:3], [[0, 320]], v, 0, ["d0c%d" % t, "@sent"])
+        new("t", "g7", 1.4, "q16", mul, add)
+        new("t", "t", 1.25, 127, add, OP.min)
+        new("e7", "q16", 112, 112, OP.is_equal, mul)
+        ts(T.uoff[:, 0:8], T.zz[:], col("e7"), col("t"), mul, add, ["zz", "e7", "t"], ["uoff0"])
+        picked(0, [EARLY])
+        new("a1", "a", 2, None, OP.is_ge, None)
+        new("sd", "b", "a1", 2, OP.not_equal, mul)
+        new("sg", "q8", -2.0 / 639.0, -1, mul, add)
+        new("sf", "e7", "sd", 0, mul, add)
+        new("sf", "sf", 1.0 / 112.0, "sg", mul, add)
+        new("sd", "sd", 1, -1, mul, add)
+        new("sc1", "e14", "sd", "sc0", mul, add)
+        tt(T.d1[:, 2:960:3], T.win[:, 1:960:3], T.win[:, 2:960:3], add, WIN + [EARLY], ["sum"], n=320, c=1)
+
+    def ahead(k):
+        for h in (0, 1):
+            after, dif, mid = "@s%d" % k if k > 1 else EARLY, T.d1[:, tri(h, 0, 3)], T.d1[:, tri(h, 1, 3)]
+            if FQ[k][h] == "a" and k > 1:
+                tt(dif, dif, T.d0[:, tri(h, 1, 3)], mul, ["sf%d" % h, after], ["dif%d" % h], n=WID[h], c=1)
+                continue
+            tt(dif, T.win[:, tri(h, 1, 3)], T.win[:, tri(h, 2, 3)], OP.subtract, tables(h) + [after], ["dif%d" % h], n=WID[h], c=1)
+            if FQ[k][h] == "a":
+                ts(dif, dif, 0.5, None, mul, None, [], ["dif%d" % h], n=WID[h], c=0.5)
+                ts(mid, T.d1[:, tri(h, 2, 3)], 0.5, None, mul, None, ["sum"], ["mid%d" % h], n=WID[h], c=0.5)
+            else:
+                cp(mid, T.win[:, tri(h, 2, 3)], tables(h) + [after], ["mid%d" % h], n=WID[h], c=0.5)
 
     for h in (0, 1):
         quant(T.qx0[:, cols(h)], T.sx0[:, cols(h)], T.x0[:, quad(h)], ["x0%d" % h], ["qx0%d" % h], 4 * WID[h])
-    scaled(T.ones[:], T.ue[:, 0:128], 1.0, 1.0, ["ue", "d0c"], ["ones"], "a", 128)
-    dma("s", [(T.et[:, 512 * b:512 * b + 512], T.ue[:]) for b in range(4)], ["ue", "x01"], ["et%d" % b for b in range(4)] + ["@d3"], "de", LATE + 0.5)
+    iota(T.ones[:], [[0, 128]], 1, 0, ["ones"])
+    dma("s", [(T.zb[:], T.ue[:, 0:320]), (T.ky[:], T.ue[:, 0:352])] + [(T.et[:, 512 * b:512 * b + 512], T.ue[:]) for b in range(4)], ["ue", "x01"],
+        ["zb0", "zb1", "ky0", "ky1"] + ["et%d" % b for b in range(4)] + ["@d3"], "de", LATE + 0.5)
     dma("s", [(T.wq[:].bitcast(dt.uint8), T.wc[:]), (T.wsp[:], T.ws[:])], ["@d3"], ["wq"], "dw", 3.5)
 
-    def one_in(b):
-        op("g", lambda e: e.affine_select(T.et[:, 513 * b:512 * b + 512:4], T.ones[:], [[1, 128]], OP.is_equal, 0.0, 0, -1), ["ones"], ["et%d" % b, "@sent"], 0.45)
-
-    iota(T.w4[:], [[4, 320]], 1280, 0, ["w4", "@sent"])
-    iota(T.rs[:], [[0, 20], [FAR, 16]], 0, 0, ["rs", "@sent"])
+    op("g", lambda e: e.affine_select(T.eye[:], T.ones[:], [[1, 128]], OP.is_equal, 0.0, 0, -1), ["ones"], ["eye", "@sent"], 0.55)
+    iota(T.w4[:], [[4, 320]], -640, 0, ["w4", "@sent"])
     for b in range(4):
-        one_in(b)
+        cp(T.et[:, 513 * b:512 * b + 512:4], T.eye[:], ["eye", "@bb"], ["et%d" % b], "a", 128)
 
     def state_parts(k, h):
         return ["x0%d" % h] if k == 0 else ["xn%d%d%d" % (k, h, t) for t in range(4)]
@@ -567,88 +574,79 @@ def rank_program(g, core, T, topo):
     def half_x(k):
         x = T["x%d" % k]
         for t in range(4):
-            scaled(T.xh[:, 320 * t:320 * t + 320], x[:, t:1280:4], 0.5, 0.0, state_parts(k, 0) + state_parts(k, 1) + ["@bb"], ["xh%d" % t], "a", 320, 0.5)
-            runs = [h for h in (0, 1) if t not in VA[h]]
-            if runs:
-                a, z = out(runs[0]).start, out(runs[-1]).stop
-                scaled(T.xg[:, 320 * t + a:320 * t + z], x[:, 4 * a + t:4 * z:4], 0.5, 0.0, state_parts(k, 0) + state_parts(k, 1) + ["@bb"], ["xg%d" % t], "a", z - a, 0.5)
+            scaled(T.xh[:, 320 * t:320 * t + 320], x[:, t:1280:4], 0.5, 0.0, state_parts(k, 0) + state_parts(k, 1) + ["@bb"], ["xh%d" % t] + ["@xh"] * (t < 2), "a", 320, 0.5)
+        both = [t for t in range(4) if t not in VA[0] or t not in VA[1]]
+        c = slice(320 * both[0], 320 * both[-1] + (320 if both[-1] not in VA[1] else VW[0]))
+        dma("s", [(T.xg[:, c], T.xh[:, c])], ["xh%d" % t for t in both], ["xg%d" % t for t in both], "dg", 3.3)
+
+    def bits(j, h):
+        scaled(T.bb[:, halfrow(h, 160 * j)], T.nb[:, 0:cols(h).stop].indirect(T.bl[:, share(h, 16 * j)]), 0.5, 0.0,
+               ["nb0", "nb%d" % h, "bl%d" % j, ("@none", "@bb", "@xh")[j]], ["bb%d%d" % (h, j)] + ["@bb"] * (j == 0), "a", WID[h] // 2, x=True)
 
     def signs(k, h):
-        n = WID[h]
-        kinds = [(0, T.d0[:, quad(h, 2, 4)], col("sf"), EPS, "sf"), (1, T.d0[:, quad(h, 1, 4)], col("sd"), EPS, "sb"), (2, T.nr[:, cols(h)], 1.0, -EPS, "nr")]
-        if k == 0:
-            kinds = [(1, T.d0[:, quad(h, 2, 4)], col("sd"), EPS, "sf"), kinds[2]]
-        for j, o, sc, eps, name in kinds[:1 if k == 3 else 3]:
-            c, b = slice(128 * j, 128 * j + 128), 3 * h + j
-            mm(b, n, T.upq[:, c], T.ups[:, c], T["qx%d" % k][:, cols(h)], T["sx%d" % k][:, cols(h)], ["upq%d" % j, "ups%d" % j, "qx%d%d" % (k, h)],
-               ["@n"] * (1 - h))
-            r, w = ["b%d" % b, "sf", "sd", "sd2", "d0c"], ["%s%d" % (name, h)]
-            if (k, h) == (3, 1):
-                ts(T.d0[:, quad(h, 1, 4)], bank(b, n), sc, 0.0, mul, OP.is_ge, r, ["sb1"], n)
-            elif j == 0 or j == 2 and NRQ[h] == "a" or j == 1 and k and DIRQ[h] == "a":
-                sign(o, bank(b, n), AF.Sign, sc, eps, r, w, n)
-            elif j == 2:
-                ts(o, bank(b, n), 0.0, 0.5, OP.is_gt, mul, r, w, n)
-            elif k == 0:
-                ts(o, bank(b, n), sc, 0.0, mul, OP.is_ge, r, w, n)
-            else:
-                ts(o, bank(b, n), 0.0, col("sd2"), OP.is_gt, mul, r, w, n)
-        d1, names = (T.d1, ["d1d", "dif%d" % h, "sum", "two"]) if k else (T.dr, ["dr%d%d" % (h, t) for t in range(4)])
-        scan(T.win[:, quad(h)], T.d0[:, quad(h)], d1[:, quad(h)], 0.0, mul, add,
-             names + ["d0c", "d03", "sf%d" % h, "sb%d" % h, "@q%d" % k], ["win%d" % h], 4 * n, 0.5)
+        n, c = WID[h], cols(h)
+
+        def product(j):
+            u = slice(128 * j, 128 * j + 128)
+            mm(2 * h + j, n, T.upq[:, u], T.ups[:, u], T["qx%d" % k][:, c], T["sx%d" % k][:, c], ["upq%d" % j, "ups%d" % j, "qx%d%d" % (k, h)])
+            return bank(2 * h + j, n), "b%d" % (2 * h + j)
+
         if k < 3:
-            for j in (0, 1):
-                scaled(T.bb[:, halfrow(h, 160 * j)], T.nr[:, 0:cols(h).stop].indirect(T.bl[:, 10 * j + share(h).start:10 * j + share(h).stop]), *HALF[NRQ[h]],
-                       ["nr0", "nr%d" % h, "bl%d" % j], ["bb%d%d" % (h, j), "@bb"], "a", n // 2, x=True)
+            s, name = product(1)
+            sc = "sc%d" % min(k, 1)
+            sign(T.nb[:, c], s, AF.Sign, col(sc), col("bi"), [name, sc, "bi"], ["nb%d" % h], n)
+            tr(T.nt[:, c], T.nb[:, c], ["nb%d" % h], ["nt%d" % h], n, 0.5)
+            scan(T.xt[:, c], T.nt[:, c], T.dt1[:, c], 0.0, mul, add, ["nt%d" % h, "dt%d" % h, "st%d" % h, "beta"], ["xt%d" % h], n, 0.5)
+            lin(T.lu[:, 16 * h:16 * h + n // 32], T.xt[:, cols(h, SEQ + 4, 32)], TABLE[0] / 2, TABLE[1], ["xt%d" % h], ["lu2%d" % h])
+            bits(0, h)
+        if k:
+            s, name = product(0)
+            if FQ[k][h] == "a":
+                sign(T.d0[:, tri(h, 1, 3)], s, AF.Sign, col("sf"), EPS, [name, "sf"], ["sf%d" % h], n)
+            else:
+                ts(T.d0[:, tri(h, 1, 3)], s, col("sf"), 0.0, mul, OP.is_ge, [name, "sf"], ["sf%d" % h], n)
+            scan(T.win[:, tri(h)], T.d0[:, tri(h)], T.d1[:, tri(h)], 0.0, mul, add, ["dif%d" % h, "mid%d" % h, "sum", "d0c0", "d0c2", "sf%d" % h], tables(h) + ["winz"] * h, 3 * n, 0.5)
 
-    HALF = {"a": (0.25, 0.25), "v": (1.0, 0.0)}
-
-    def fifth(h):
-        scaled(T.bc[:, halfrow(h)], T.nr[:, 0:cols(h).stop].indirect(T.blc[:, share(h)]), *HALF[NRQ[h]],
-               ["nr%d" % j for j in range(h + 1)] + ["blc", "@bb"], ["bc%d" % h], "a", WID[h] // 2, x=True)
-
-    def turned(rd):
-        tt(T.d1[:, 0:1280:4], T.d1[:, 0:1280:4], T.d0[:, 2:1280:4], mul, ["sf0", "sf1", "@g%d" % rd], ["dif0", "dif1", "@i"], n=320)
-
-    def upto(s, h):
-        return ["T%d%d" % (k, j) for k in range(1, s + 1) for j in (0, 1) if (k, j) <= (s, h)]
+    def upto(s, h, first=1):
+        return ["T%d%d" % (k, j) for k in range(first, s + 1) for j in (0, 1) if (k, j) <= (s, h)]
 
     def step(s, h, after=()):
-        n = WID[h] // 2
-        if s == 1:
-            w, names, lst = T.win[:, 0:quad(h).stop], ["win%d" % j for j in range(h + 1)] + ["dl"], T.dl[:, share(h)]
-        else:
-            at = 32 * (s - 2) + 16 * h
-            w, names, lst = T.win[:, 0:1280], ["win0", "win1", "lu%d%d" % (s, h)], T.lu[:, at:at + n // 16]
-        bits, go, name = (T.bc[:, halfrow(h)], T.go[:, halfrow(h, 16)], "5%d" % h) if s == 5 else (T.bb[:, halfrow(h, 160 * (1 - s % 2))], T.go[:, halfrow(h, 192)], "%d" % h)
-        tt(go, w.indirect(lst), bits, add, names + ["bc%d" % h if s == 5 else "bb%d%d" % (h, 1 - s % 2)] + list(after) + ["@t0"] * (h == 1 and s in TURN),
-           ["go" + name], n=n, x=True)
-        tr(T.tt[:, halfrow(h, PLACE[s])], go, ["go" + name], ["T%d%d" % (s, h), "@t%d" % h], n)
+        n, at, j = WID[h] // 2, 32 * (s - 2) + 16 * h, 2 if s == 5 else s % 2
+        go, name = (T.go[:, halfrow(h, 16)], "go5%d" % h) if s == 5 else (T.go[:, halfrow(h, 192)], "go%d" % h)
+        tt(go, T.win[:, 0:960].indirect(T.lu[:, at:at + n // 16]), T.bb[:, halfrow(h, 160 * j)], add, WIN + ["lu%d%d" % (s, h), "bb%d%d" % (h, j)] + list(after), [name], n=n, x=True)
+        tr(T.tt[:, halfrow(h, PLACE[s])], go, [name], ["T%d%d" % (s, h)], n)
         if s < 6:
-            at = 32 * (s - 1) + 16 * h
-            k = 4 * (s - 1) + 2 * h
-            lin(T.lu[:, at:at + 16], T.tt[:, 0:halfrow(h, PLACE[s]).stop].indirect(T.cl[:, k:k + 1]), 2, 642, upto(s, h) + ["cl%d" % h] + ["T60", "T61"] * (s == 5),
+            k, first = 4 * (s - 2) + 2 * h, 2 if s == 2 else 1
+            lin(T.lu[:, at + 32:at + 48], T.tt[:, PLACE[first]:halfrow(h, PLACE[s]).stop].indirect(T.cl[:, k:k + 1]), *TABLE, upto(s, h, first) + ["cl%d" % h],
                 ["lu%d%d" % (s + 1, h)], n=16, x=True)
 
     def walk(rd):
-        for h in (0, 1):
-            fifth(h)
-        for s in range(1, 7):
+        second = T.xt[:, SEQ + 18:320:32]
+        tt(T.two[:, 0:10], second, T.nt[:, 0:320:32], add, ["xt0", "xt1", "nt0", "nt1", "lu20", "lu21"], ["two"])
+        scaled(T.tt[:, 0:160:16], T.two[:, 0:10], 0.5, 0.0, ["two"], ["T10", "T11"], "a", 10)
+        for b in (0, 1):
+            scaled(T.zb[:, home("L0") + 16 * b:320:32], T.two[:, 0:10], 0.5, 0.0, ["two", "@xh"], ["zb%d" % b], "a", 10)
+        for j in (1, 2):
             for h in (0, 1):
-                step(s, h, ["sk", "sm", "sl0", "fs", "gom0", "gom176"] * (s == 4))
+                bits(j, h)
+        for s in range(2, 7):
+            for h in (0, 1):
+                step(s, h, ["sk", "sl0", "gom0", "gom176"] * (s == 4))
+            if s == 3:
+                tr(T.win[:, 1280:1600], T.zb[:], ["zb0", "zb1"], ["back"], 320, 0.5)
             if s == 5:
                 tr(T.tt[:, 960:1152], T.go[:, 0:192], ["go50", "go51", "gom0", "gom176"], ["TS"], 192)
-                lin(T.fl[:], T.tt[:, 800:1152].indirect(T.sl[:, 0:2]), 2, 642, ["T50", "T51", "TS", "sl0"], ["fl"], n=32, x=True)
-                cp(T.win[:, 1280:1600], T.win[:, 0:1280].indirect(T.fl[:, 0:20]), ["win0", "win1", "fl"], ["row0", "row1"], "a", n=320, x=True)
-                aff(T.tt[96:128, home("R7"):160:16], T.tt[96:128, home("R7"):160:16], 0.25, 399.0, ["T10", "T11"], ["T10", "T11"], q=FIXQ)
+                lin(T.fl[:], T.tt[:, PLACE[5]:1152].indirect(T.sl[:, 0:2]), *TABLE, ["T50", "T51", "T60", "T61", "TS", "sl0"], ["fl"], n=32, x=True)
+                cp(T.win[:, 960:1280], T.win[:, 0:960].indirect(T.fl[:, 0:20]), WIN + ["fl"], ["row"], "a", n=320, x=True)
         for h in (0, 1):
-            lin(T.mlu[:, 16 * h:16 * h + 16], T.tt[:, 0:halfrow(h, PLACE[6]).stop].indirect(T.sl[:, 4 + 2 * h:5 + 2 * h]), T.tmp[:, 36:37], T.tmp[:, 37:38],
-                upto(4, 1) + ["T60", "T6%d" % h, "sm", "fs"], ["ml%d" % h], n=16, x=True)
+            for b in (0, 1) * (1 - h):
+                lin(T.mlu[:, b:32:2], T.tt[:, 0:960].indirect(T.cl[:, 18 - 2 * b:19 - 2 * b]), col("by%d" % b), col("at%d" % b),
+                    upto(6, 1) + ["by%d" % b, "at%d" % b, "cl2"], ["ml%d" % b], n=16, x=True)
             for j, (a, n, q) in enumerate(KM[h]):
-                cp(T.km[:, AT[h] + a:AT[h] + a + n], T.win[:].indirect(T.mlu[:, 16 * h + a // 16:16 * h + (a + n) // 16]), ["win0", "win1", "row0", "row1", "ml%d" % h],
+                cp(T.km[:, AT[h] + a:AT[h] + a + n], T.win[:].indirect(T.mlu[:, (AT[h] + a) // 16:(AT[h] + a + n) // 16]), WIN + ["row", "back", "ml0", "ml1"],
                    ["km%d%d" % (h, j)], q, n=n, x=True)
             tr(T.kt[:, cols(h)], T.km[:, cols(h)], ["km%d%d" % (h, j) for j in range(len(KM[h]))], ["kt%d" % h], WID[h], 0.5)
-            lin(T["kl%d" % rd][:, part(h).start:part(h).start + 16], T.kt[:, 0:cols(h).stop].indirect(T.sl[:, 8 + 2 * h:9 + 2 * h]), 0.5, 160,
+            lin(T["kl%d" % rd][:, part(h).start:part(h).start + 16], T.kt[:, 0:cols(h).stop].indirect(T.sl[:, 8 + 2 * h:9 + 2 * h]), 0.25, 160.25,
                 ["kt0", "kt%d" % h, "sk"], ["kl%d%d" % (rd, h), "klx"], n=16, x=True)
 
     sent = [0]
@@ -658,7 +656,7 @@ def rank_program(g, core, T, topo):
 
         def put(fn, cost, late, land, sem, inc, own):
             sent[0] += own
-            node({"g": fn}, {"g": cost}, late, ["kl%d0" % rd, "kl%d1" % rd] if what == "k" else ["qh%d%d" % (rd, j) for j in range(h + 1)], [land, "@sent"], sem, inc)
+            node({"g": fn}, {"g": cost}, late, ["kl%d0" % rd, "kl%d1" % rd] if what == "k" else ["qh%d%d" % (rd, h)], [land, "@sent"], sem, inc)
 
         q, s, lq, ls = T["qh%d" % rd], T["sh%d" % rd], T["lq%d" % rd], T["ls%d" % rd]
         kl = T["kl%d" % rd][:, 0:20]
@@ -688,26 +686,16 @@ def rank_program(g, core, T, topo):
                                                                 src=T.kl2[:, 8 * k:8 * k + 8], dst=T.rlk[:]) for k in range(3)], local_sem=T.sem.lsem),
                 0.6, 7.0, "kr%d" % rd, "kr%d" % rd, 3 * far, 2 * n)
             return
-        if WHOLE[h]:
-            def go3(e):
-                e.remote_dma(T.rlq[:, out(h)].bitcast(dt.uint8), q[:, out(h)].bitcast(dt.uint8), T.sem["ry%d" % h], T.sem.lsem, ways[1 - h][1], ways[1 - h][0], bits_of(eng))
-                e.remote_dma(T.rls[:, out(h)], s[:, out(h)], T.sem["ry%d" % h], T.sem.lsem, ways[2][1], ways[2][0], bits_of(eng))
-
-            put(go3, 0.7, 5.3, "lq%d%d" % (rd, h), "ar%d%d" % (rd, h), 2 * far, 4 * n)
-            return
         a, w = out(h).start, VW[h] // 2
 
         pieces = [(q[:, a + w * k:a + w * k + w].bitcast(dt.uint8), T.rlq[:, a + w * k:a + w * k + w].bitcast(dt.uint8)) for k in (0, 1)]
-        pieces += [(s[:, max(320 - 4 * w, 0):320], T.rlt[:, max(320 - 4 * w, 0):320])] * h * ONE
-        engs = three if h * ONE else [eng[:n], eng[n:]]
 
         def go2(e):
-            e.remote_dma_fused([RemoteDMATransfer(dst_ids=[DstId(rid=ways[k][0], pnc=ways[k][1])], dma_engine_mask=bits_of(engs[k]),
+            e.remote_dma_fused([RemoteDMATransfer(dst_ids=[DstId(rid=ways[k][0], pnc=ways[k][1])], dma_engine_mask=bits_of([eng[:n], eng[n:]][k]),
                                                   remote_sem=T.sem["ry%d" % h], src=src, dst=land) for k, (src, land) in enumerate(pieces)], local_sem=T.sem.lsem)
-            if h * ONE == 0:
-                e.remote_dma(T.rls[:, out(h)], s[:, out(h)], T.sem["ry%d" % h], T.sem.lsem, ways[2][1], ways[2][0], bits_of(eng))
+            e.remote_dma(T.rls[:, out(h)], s[:, out(h)], T.sem["ry%d" % h], T.sem.lsem, ways[2][1], ways[2][0], bits_of(eng))
 
-        put(go2, 0.8 - 0.2 * h, 5.1 + 0.7 * h, "lq%d%d" % (rd, h), "ar%d%d" % (rd, h), 3 * far, (4 - 2 * h * ONE) * n)
+        put(go2, 0.8 - 0.2 * h, 5.1 + 0.7 * h, "lq%d%d" % (rd, h), "ar%d%d" % (rd, h), 3 * far, 4 * n)
 
     def meet(rd, h):
         for t in range(4):
@@ -751,59 +739,53 @@ def rank_program(g, core, T, topo):
         layer(1)
         quant_h(rd, 0)
         send(rd, "h", 0)
-        if rd == 1:
-            quant(T.eq[:], T.es[:], T.et[:], ["et%d" % b for b in range(4)] + ["@g1"], ["eq", "@i"], n=2048)
-        else:
-            turned(rd)
         for b in range(4):
             layer_out(1, b, HQ[4 + b])
         quant_h(rd, 1)
         send(rd, "h", 1)
         if rd == 1:
-            sign(T.mask[:], T.rs[:], AF.Abs, 1.0, col("far"), ["rs", "far", "kl10"], ["mask"], 320)
-            sign(T.mask[:], T.mask[:], AF.Relu, -1.0, 1.0, ["mask"], ["mask"], 320)
-            differences()
-            ts(T.uoff[:, 0:8], T.zz[:], col("q16"), -15.0, add, add, ["zz", "q16", "@s1"], ["uoff0"])
-            picked(0, ["@s1"])
+            for b in range(4):
+                quant(T.eq[:, 128 * b:128 * b + 128], T.es[:, 128 * b:128 * b + 128], T.et[:, 512 * b:512 * b + 512], ["et%d" % b, EARLY], ["eq%d" % b], n=512)
+            flips()
+            new("ne", "x16", "b16", 336, OP.not_equal, mul)
+            for k, name in enumerate(("q16", "c1")):
+                ts(T.sl[:, 4 + k:5 + k], col(name), col("ne"), float(256 * k), add, add, [name, "ne", EARLY], ["sm%d" % k])
             dma("s", [(T.vb[:], T.v[:])], ["wq"], ["vb"], "dv", 2.5)
-        else:
-            twice("@s%d" % rd)
+        ahead(rd)
         if rd == 2:
             quant(T.vq[:], T.vs[:], T.vb[:], ["vb", "@s2"], ["vq"], 512)
-        if rd == 3:
-            scaled(T.d0[:, quad(0, 1, 4)], T.d0[:, quad(0, 0, 4)], 1.0, float(DIRQ[0] == "a"), ["d0c", "@s3"], ["sb0"], "a", WID[0])
-            scaled(T.d0[:, quad(1, 2, 4)], T.d0[:, quad(1, 0, 4)], 1.0, 1.0, ["d0c", "@s3"], ["sf1"], "a", WID[1])
-            ts(T.d1[:, quad(1, 1, 4)], T.d1[:, quad(1, 0, 4)], -1.0, None, mul, None, ["dif1", "@s3"], ["d1d"], n=WID[1], c=0.5)
-            ts(T.d1[:, quad(1, 0, 4)], T.d1[:, quad(1, 1, 4)], -2.0, None, mul, None, ["d1d"], ["dif1"], n=WID[1], c=0.5)
-            scaled(T.d0[:, 3:1280:4], T.d0[:, 0:1280:4], 1.0, -1.0, ["d0c", "@s3"], ["d03"], "a", 320)
-            ts(T.d1[:, 3:1280:4], T.d1[:, 2:1280:4], 2.0, None, mul, None, ["sum", "@s3"], ["two"], n=320, c=0.5)
         kl, kr = T["kl%d" % rd], T["kr%d" % rd]
         for h in (0, 1):
-            cp(T.kw[:, 160 * h:160 * h + 160], T.w4[:].indirect(kr[:, 10 * h:10 * h + 10]), ["w4", "kr%d" % rd, "@s%d" % rd], ["kw%d" % h], "va"[h], n=160, x=True)
+            cp(T.kw[:, 160 * h:160 * h + 160], T.w4[:].indirect(kr[:, 10 * h:10 * h + 10]), ["w4", "kr%d" % rd, "@s%d" % rd], ["kw%d" % h], KQ[rd][h], n=160, x=True)
         for h in (0, 1):
-            c = cols(h)
-            tt(T.ky[:, c], T.kw[:].indirect(kl[:, part(h)]), T.mask[:, c], OP.mult, ["kw0", "kw1", "kl%d0" % rd, "kl%d1" % rd, "mask"], ["ky%d" % h], n=WID[h], x=True)
-            scan(T.kys[:, c], T.rs[:, c], T.ky[:, c], 0.0, OP.min, OP.add, ["ky%d" % h, "rs"], ["kys%d" % h], WID[h])
-            lin(T.mo[:, part(h)], T.kys[:, c.start + 15:c.stop:16], 0.25, -320, ["kys%d" % h], ["mo%d" % h])
+            cp(T.ky[:, 16 + 160 * h:176 + 160 * h], T.kw[:].indirect(kl[:, 10 * h:10 * h + 10]), ["kw0", "kw1", "kl%d0" % rd, "kl%d1" % rd], ["ky%d" % h], KQ[rd][h], n=160, x=True)
+        tr(T.kys[:, 0:320], T.ky[:, 16:336], ["ky0", "ky1"], ["kys0"], 320, 0.5)
+        tr(T.kys[:, 320:672], T.ky[:], ["ky0", "ky1"], ["kys1"], 352, 0.5)
+        lin(T.mo[:], T.kys[:].indirect(T.sl[:, 4:6]), 0.25, 160.25, ["kys0", "kys1", "sm0", "sm1"], ["mo0", "mo1", "mo2"], n=32, x=True)
+        ts(T.mo[:, 20:28], T.mo[:, part(1)], 320.0, None, add, None, ["mo1"], ["mo2"])
+        if rd < 3:
+            cp(T.dt1[:, SEQ:320:16], T.xt[:, SEQ + 1:320:16], ["xt0", "xt1", "@s%d" % rd], ["dt0", "dt1"])
         lq, ls = T["lq%d" % rd], T["ls%d" % rd]
         for h in (0, 1):
             for b in range(4):
                 c = out(h)
-                mm(4 * h + b, VW[h], T.eq[:, 128 * b:128 * b + 128], T.es[:, 128 * b:128 * b + 128], lq[:, c], ls[:, c], ["eq", "lq%d%d" % (rd, h)], ["@u"])
+                mm(4 * h + b, VW[h], T.eq[:, 128 * b:128 * b + 128], T.es[:, 128 * b:128 * b + 128], lq[:, c], ls[:, c], ["eq%d" % b, "lq%d%d" % (rd, h)], ["@u"])
                 cp(T.dd[:, 320 * b + c.start:320 * b + c.stop], bank(4 * h + b, VW[h]), ["b%d" % (4 * h + b)], ["dd%d%d" % (h, b)],
-                   DDQ if (b, h) == (0, 1) else "a", n=VW[h])
+                   DDQ[b] if h else "a", n=VW[h])
         xn, qn, sn = T["x%d" % rd], T["qx%d" % rd], T["sx%d" % rd]
         for h in (0, 1):
             for t in range(4):
                 far, r = T.dd[:, 320 * t:320 * t + 320].indirect(T.mo[:, part(h)]), ["mo%d" % h, "dd0%d" % t, "dd1%d" % t]
                 near, w = ["vt0%d" % t, "vt1%d" % t] + ["@x"] * (h * t > 0), ["xn%d%d%d" % (rd, h, t)]
-                if t in (XA, XB)[rd == 3][h]:
-                    c = slice(320 * t + AT[h], 320 * t + AT[h] + WID[h])
-                    cp(T.dg[:, c], far, r, ["dg%d%d" % (h, t)], "a", n=WID[h], x=True)
-                    tt(xn[:, quad(h, t, 4)], T.dg[:, c], T.vt[:, quad(h, t, 4)], OP.add, ["dg%d%d" % (h, t)] + near, w, n=WID[h], c=1)
+                if h:
+                    n = WID[h]
+                    if t % 2 == 0:
+                        cp(T.dg[:, n * t:n * t + 2 * n], T.dd[:, 320 * t:320 * t + 640].indirect(T.mo[:, part(h).start:part(h).start + n // 8]),
+                           r + ["mo2", "dd0%d" % (t + 1), "dd1%d" % (t + 1)], ["dg%d" % (t // 2)], "a", n=2 * n, x=True)
+                    tt(xn[:, quad(h, t, 4)], T.dg[:, n * t:n * t + n], T.vt[:, quad(h, t, 4)], OP.add, ["dg%d" % (t // 2)] + near, w, n=n, c=1)
                 else:
                     tt(xn[:, quad(h, t, 4)], far, T.vt[:, quad(h, t, 4)], OP.add, r + near, w, n=WID[h], x=True)
-            quant(qn[:, cols(h)], sn[:, cols(h)], xn[:, quad(h)], state_parts(rd, h), ["qx%d%d" % (rd, h), ("@x", "@q%d" % rd)[h]], 4 * WID[h])
+            quant(qn[:, cols(h)], sn[:, cols(h)], xn[:, quad(h)], state_parts(rd, h), ["qx%d%d" % (rd, h)] + ["@x"] * (1 - h), 4 * WID[h])
         for h in (0, 1):
             signs(rd, h)
         if rd < 3:
@@ -814,10 +796,12 @@ def rank_program(g, core, T, topo):
         mm(6 + h, WID[h], T.vq[:], T.vs[:], T.qx3[:, c], T.sx3[:, c], ["vq", "qx3%d" % h])
         cp(T.yb[:, c], bank(6 + h, WID[h]), ["b%d" % (6 + h)], ["yb%d" % h], "a", n=WID[h])
         for k in (0, 1):
-            scaled(T.lout[:, 2 * AT[h] + k:2 * (AT[h] + WID[h]):2], T.win[:, quad(h, 2 + k, 4)], 0.5, 160.0, ["win%d" % h], ["lo%d%d" % (h, k)], ("aa", "va")[h][k], WID[h])
+            scaled(T.lout[:, 2 * AT[h] + k:2 * (AT[h] + WID[h]):2], T.win[:, tri(h, 1 + k, 3)], 0.25, 160.0, tables(h), ["lo%d%d" % (h, k)], ("av", "va")[h][k], WID[h])
     dma("s", [(T.osc[4 * k:4 * k + 4, :], T.sx3[32 * k:32 * k + 4, :]) for k in range(4)], ["qx30", "qx31"], [], "os")
     dma("s", [(T.y[:], T.yb[:])], ["yb0", "yb1"], [], "oy", 2.3)
-    dma(LRQ, [(T.lr[:], T.lout[0:16, :])], ["lo00", "lo01", "lo10", "lo11"], [], "ol")
+    for k in (0, 1):
+        at = 16 * RIGHT.index(k) + home("L0") * (1 - k)
+        dma(LRQ[k], [(T.lr[:, 640 * k:640 * k + 640], T.lout[at:at + 8, :])], ["lo00", "lo01", "lo10", "lo11"], [], "ol%d" % k)
     issue()
     need("g", dict(total))
     g.wait_ge(T.sem.lsem, sent[0])

import numpy as np
from concourse.bass import DstId, RemoteDMATransfer
from concourse.mybir import dt, AluOpType, ActivationFunctionType
import comms_topo

OP = AluOpType
AF = ActivationFunctionType
STEP = [4, 1, 2]
WAKE, SPARE, LOOK = 0.12, 0.3, 0.3
NEWQ = "av"
VA, XA = ((2, 3), (1, 2, 3)), ((), (0, 1, 2, 3))
LATE = 2.2
XL = (0.3, 0.5)
HOLD = ("@x", "@v", "@h", "@i")
WARM, SEED = 0.03, 4
TRIES, SWAPS, ORDER = 500, 500, {}
CASES = np.array([[0.95, 1.5, 1.3, 1, 0.11, 0.06, 1, 1], [0.95, 1.1, 1.3, 1, 0.11, 0.06, 1, 0.75], [0.95, 2.0, 1.3, 1, 0.11, 0.06, 1.2, 1], [0.85, 1.5, 0.6, 1, 0.15, 0.06, 1, 0.75],
                  [1.2, 1.5, 1.3, 1, 0.06, 0.06, 0.8, 1], [0.95, 1.5, 0.6, 2, 0.11, 0.12, 1, 1.2], [0.95, 1.3, 1.8, 1, 0.08, 0.03, 1.2, 0.75]])
CYC, GAT, PE, TWO, WAKES, ACT, SLOW, QUICK = CASES.T * np.array([0.001] + [1] * 7)[:, None]
EPS = 2.0 ** -93

F, B, H, I, U, C4, S8 = "float32", "bfloat16", "float16", "int32", "uint16", "float8_e4m3fn_x4", "uint8"
SCRATCH = {"ps": ("psum", [128, 4096], F)}
for _n, _w, _d in [
    ("x0", 1280, B), ("x1", 1280, B), ("x2", 1280, B), ("x3", 1280, B), ("xh", 1280, B), ("xg", 1280, B), ("vg", 1280, B), ("dg", 1280, B), ("vt", 1280, B), ("ht", 1280, B), ("dd", 1280, B),
    ("ub", 512, B), ("vb", 512, B), ("et", 2048, B), ("ones", 128, B),
    ("uq", 128, C4), ("us", 128, S8), ("vq", 128, C4), ("vs", 128, S8), ("wq", 512, C4), ("wsp", 512, S8),
    ("upq", 256, C4), ("ups", 256, S8), ("eq", 512, C4), ("es", 512, S8),
    ("qx0", 320, C4), ("sx0", 320, S8), ("qx1", 320, C4), ("sx1", 320, S8), ("qx2", 320, C4), ("sx2", 320, S8), ("qx3", 320, C4), ("sx3", 320, S8),
    ("qv", 320, C4), ("qvs", 320, S8),
    ("qh1", 320, C4), ("sh1", 320, S8), ("qh2", 320, C4), ("sh2", 320, S8), ("qh3", 320, C4), ("sh3", 320, S8),
    ("lq1", 320, C4), ("ls1", 320, S8), ("lq2", 320, C4), ("ls2", 320, S8), ("lq3", 320, C4), ("ls3", 320, S8), ("rlq", 320, C4), ("rls", 320, S8),
    ("raw", 640, I), ("d0", 960, B), ("d1", 960, H), ("win", 1600, B), ("nb", 320, B), ("nt", 320, B), ("dt1", 320, H), ("xt", 320, H), ("te", 640, B), ("zb", 320, B),
    ("bb", 480, F), ("idn", 80, I), ("go", 352, F), ("tt", 1152, F), ("lu", 160, U), ("ue", 512, B), ("fl", 32, U), ("mlu", 64, U), ("km", 320, B), ("kt", 320, B),
    ("kl1", 32, U), ("kl2", 32, U), ("kl3", 32, U), ("kr1", 20, U), ("kr2", 24, U), ("kr3", 20, U), ("rlk", 8, U),
    ("w4", 320, B), ("kw", 320, B), ("ky", 352, B), ("kys", 672, B), ("mo", 32, U), ("eye", 128, B), ("two", 16, F),
    ("lout", 640, F), ("yb", 320, F),
    ("pi", 8, I), ("pj", 24, I), ("pc", 80, F), ("kk", 40, F), ("zz", 8, F), ("sel", 16, F), ("pat", 16, F),
    ("uoff", 16, U), ("cl", 24, U), ("bl", 48, U), ("el", 48, U), ("sl", 16, U),
]:
    SCRATCH[_n] = ("sbuf", [128, _w], _d)

SEMAPHORES = (["sv", "sa", "st", "sg", "dx0", "dx1", "os", "du", "dv", "dw", "dn0", "dn1", "dn2", "de", "dg", "oy", "ol0", "ol1", "oq0", "oq1", "lsem", "ry0", "ry1", "rk"]
              + ["ar%d%d" % (r, h) for r in (1, 2, 3) for h in (0, 1)] + ["kr%d" % r for r in (1, 2, 3)])
VW = (160, 160)


def out(h, n=1, t=0, step=1):
    return slice(n * VW[0] * h + t, n * (VW[0] + VW[1] * h), step)


AT, WID = (0, 192), (192, 128)


def cols(h, t=0, step=1, at=0):
    return slice(at + AT[h] + t, at + AT[h] + WID[h], step)


def quad(h, t=0, step=1, n=4):
    return slice(n * AT[h] + t, n * (AT[h] + WID[h]), step)


def tri(h, t=0, step=1):
    return quad(h, t, step, 3)


def part(h):
    return slice(AT[h] // 16, (AT[h] + WID[h]) // 16)


def share(h, at=0):
    return slice(at + AT[h] // 32, at + (AT[h] + WID[h]) // 32)


def halfrow(h, at=0):
    return slice(at + AT[h] // 2, at + (AT[h] + WID[h]) // 2)


WAY = [["R6", "R5", "R4", "R3", "R2"], ["R6", "R5", "R4", "L1", "R3"], ["L1", "L2", "R6", "L3", "R5"], ["L1", "L2", "L3", "L4", "L5"]]
EVEN = [("R2", "R1"), ("R3", "I8"), ("R5", "I8"), ("R7", "L5")]
ODD = [("R2", "L0"), ("R4", "L2"), ("R6", "L4"), ("L5", "L6")]
RIGHT = [1, 0, 1, 0, 0, 1, 0, 1]
SEQ = 13
TABLE, ROW = (0.75, 481.75), (0.25, 1120.25)

KM = ([(0, 96, "v"), (96, 96, "a")], [(0, 128, "a")])
DDQ, LRQ = "vaaa", "as"
FQ = {1: "aa", 2: "aa", 3: "av"}
XB = ((), (0, 1, 2, 3))
EARLY = "@s1"
KQ = {1: "aa", 2: "va", 3: "va"}
HQ = ["av"] * 4 + list("avav")
PLACE = [None, 0, 160, 320, 480, 640, 800]


def home(table):
    return int(table[1]) + 7 * (table[0] != "R")


def before(table):
    return table[0] + str(int(table[1]) + (1 if table[0] == "R" else -1))


def bits_of(engines):
    m = 0
    for e in engines:
        m |= 1 << e
    return m


def relays_of(core, dst, topo):
    c = [k for k in topo.cores_of(core) if k != core and topo.may_write(k, dst)]
    near, far = [k for k in c if topo.die(k) == topo.die(core)], [k for k in c if topo.die(k) != topo.die(core)]
    return [near[0], far[0], near[1]]


def relay_program(g, core, T, topo):
    for r, src in enumerate(T.cores):
        dst = T.cores[r ^ STEP[1]]
        if core not in topo.cores_of(src) or core == src:
            continue
        rel = relays_of(src, dst, topo)
        if core not in rel:
            continue
        k = rel.index(core)
        rid, pid = topo.addr(dst, core)
        m, n = topo.mask(core, dst), len(topo.engines(core, dst))
        all_ = len(topo.engines(src, core))
        g.wait_ge(T.sem.rk, all_ // (2 if k == 2 else 4))
        g.remote_dma(T.kr2[:, 8 * k:8 * k + 8], T.rlk[:], T.sem.kr2, T.sem.lsem, pid, rid, m)
        for h in (0, 1):
            if k < 2:
                a, w = out(h).start + VW[h] // 2 * k, VW[h] // 2
                g.wait_ge(T.sem["ry%d" % h], all_ // 2)
                g.remote_dma(T.lq2[:, a:a + w].bitcast(dt.uint8), T.rlq[:, a:a + w].bitcast(dt.uint8), T.sem["ar2%d" % h], T.sem.lsem, pid, rid, m)
            else:
                g.wait_ge(T.sem["ry%d" % h], all_)
                g.remote_dma(T.ls2[:, out(h)], T.rls[:, out(h)], T.sem["ar2%d" % h], T.sem.lsem, pid, rid, m)
        g.wait_ge(T.sem.lsem, 3 * n)


def rank_program(g, core, T, topo):
    rank = T.rank_of(core)
    if rank is None:
        relay_program(g, core, T, topo)
        return
    Q = {"g": g, "v": g.vector, "a": g.scalar, "t": g.tensor, "s": g.sync}
    SEM = {"g": "sg", "v": "sv", "a": "sa", "t": "st"}
    nodes, writer, readers = [], {}, {}

    def node(fns, cost, late, r, w, sem, inc):
        r = [k for k in r if k in HOLD or k not in ("@x", "@v", "@h", "@i")]
        pre, after = set(), set()
        for k in list(r) + list(w):
            if k in writer:
                (after if k[0] == "@" else pre).add(writer[k])
        for k in w:
            if k[0] != "@":
                pre.update(readers.get(k, ()))
        i = len(nodes)
        if "a" in cost and sem is None:
            cost["a"] = cost["a"] + ACT
        cost, late = {q: cost[q] + 0.0 * CYC for q in cost}, late * (SLOW if "g" in cost else QUICK)
        nodes.append({"fns": fns, "cost": {q: float(cost[q][0]) for q in cost}, "late": float(late[0]), "all": cost, "slow": late, "pre": sorted(pre), "order": sorted(pre | after), "sem": sem, "inc": inc})
        for k in r:
            readers.setdefault(k, set()).add(i)
        for k in w:
            writer[k] = i
            readers[k] = set()

    def op(q, fn, r, w, us):
        node({q: fn}, {q: us}, 0.0, r, list(w) + (["gpsimd"] if q == "g" else []), None, 1)

    def dma(q, pairs, r, w, sem, late=2.0):
        def go(e):
            for o, i in pairs:
                e.dma_start(o, i).then_inc(T.sem[sem], 16)
        node({q: go}, {q: 0.1 * len(pairs)}, late, r, w, sem, 16 * len(pairs))

    def us(n, cycles, gather):
        return 0.05 + n * GAT * CYC if gather else np.maximum(64, n * cycles) * CYC

    def tt(o, a, b, f, r, w, n=10, x=False, c=2):
        op("v", lambda e: e.tensor_tensor(o, a, b, f), r, w, us(n, c * TWO if c == 1 else c, x))

    def ts(o, a, s1, s2, f1, f2, r, w, n=10, x=False, c=1):
        if f2 is None:
            op("v", lambda e: e.tensor_scalar(o, a, s1, None, f1), r, w, us(n, c, x))
        else:
            op("v", lambda e: e.tensor_scalar(o, a, s1, s2, f1, f2), r, w, us(n, c, x))

    def lin(o, a, m, b, r, w, n=10, x=False):
        ts(o, a, float(m) if isinstance(m, int) else m, float(b) if isinstance(b, int) else b, OP.mult, OP.add, r, w, n, x)

    def cp(o, a, r, w, q="v", n=10, x=False, c=1):
        fns = {"v": lambda e: e.tensor_copy(o, a), "a": lambda e: e.activation(o, a, AF.Copy)}
        node({k: fns[k] for k in q}, {k: us(n, c if k == "v" else 1, x) for k in q}, 0.0, r, w, None, 1)

    def scaled(o, a, m, b, r, w, q, n, c=1, x=False):
        fns = {"v": (lambda e: e.tensor_scalar(o, a, m, b, OP.mult, OP.add)) if b else (lambda e: e.tensor_scalar(o, a, m, None, OP.mult)),
               "a": (lambda e: e.activation(o, a, AF.Copy, bias=b, scale=m)) if b else (lambda e: e.activation(o, a, AF.Copy, scale=m))}
        node({k: fns[k] for k in q}, {k: us(n, c if k == "v" else 1, x) for k in q}, 0.0, r, w, None, 1)

    def sign(o, i, f, sc, eps, r, w, n):
        op("a", lambda e: e.activation(o, i, f, bias=eps, scale=sc), r, w, us(n, 1, False))

    def tr(o, a, r, w, n, c=1):
        op("v", lambda e: e.transpose(o, a), r, w, us(n, c, False))

    def scan(o, d0, d1, first, f0, f1, r, w, n, c=1):
        op("v", lambda e: e.tensor_tensor_scan(o, d0, d1, first, f0, f1), r, w, us(n, c, False))

    def mm(bank, n, lq, lsc, rq, rsc, r, turn=()):
        op("t", lambda e: e.matmul_mx(T.ps[:, 512 * bank:512 * bank + n], lq, lsc, rq, rsc, True, True), r, ["b%d" % bank] + list(turn), (n + 16) * PE * CYC)

    def fill(o, c, w, n=10):
        op("v", lambda e: e.memset(o, float(c)), [], w, us(n, 0.5, False))

    def quant(q, s, t, r, w, n=640):
        op("v", lambda e: e.quantize_mx(q, s, t), r, w, (14.0 + n * 0.265) * CYC)

    def length(order):
        free, done = {}, {}
        for i, q in order:
            d = nodes[i]
            s = free.get(q, 0.0 * CYC)
            for p in d["pre"]:
                s = np.maximum(s, done[p])
            free[q] = s + d["all"][q]
            done[i] = free[q] + d["slow"] + WAKES
        return float(np.mean(np.max(list(done.values()), axis=0)))

    def waiting(order, c):
        free, done, why, last = {}, {}, {}, {}
        for i, q in order:
            d = nodes[i]
            s, why[i] = free.get(q, 0.0), (last.get(q), True)
            for p in d["pre"]:
                if done[p] > s:
                    s, why[i] = done[p], (p, False)
            free[q], last[q] = s + d["all"][q][c], i
            done[i] = free[q] + d["slow"][c] + WAKES[c]
        i, held = max(done, key=done.get), []
        while i is not None:
            if why[i][1] and why[i][0] is not None:
                held.append(i)
            i = why[i][0]
        return held

    def arrange():
        n = len(nodes)
        if n not in ORDER:
            tail = [0.0] * n
            out = [[] for _ in range(n)]
            for i, d in enumerate(nodes):
                for p in d["order"]:
                    out[p].append(i)
            for i in range(n - 1, -1, -1):
                d = nodes[i]
                tail[i] = min(d["cost"].values()) + d["late"] + max([tail[k] + WAKE for k in out[i]] + [0.0])
            rng = np.random.RandomState(SEED)
            move, best = np.zeros(n), listed(tail, out)
            least = length(best)
            for _ in range(TRIES):
                a = rng.randint(n)
                other = move.copy()
                other[a:a + 40] += rng.normal(0.0, 0.15, n)[a:a + 40]
                order = listed(list(tail + other), out)
                t = length(order)
                if t < least:
                    move, best, least = other, order, t
            now, cur = best, least
            for _ in range(SWAPS):
                if _ % 20 == 0:
                    held = waiting(now, rng.randint(len(CYC)))
                i = held[rng.randint(len(held))]
                a = [k for k, q in now].index(i)
                q = now[a][1]
                if len(nodes[i]["cost"]) > 1 and rng.rand() < 0.3:
                    order = now[:a] + [(i, [k for k in nodes[i]["cost"] if k != q][0])] + now[a + 1:]
                else:
                    b, hops, along = a, rng.randint(1, 3), {i}
                    while b > 0 and hops:
                        b -= 1
                        if now[b][1] == q:
                            hops -= 1
                    for k in range(a - 1, b - 1, -1):
                        if any(now[k][0] in nodes[j]["order"] for j in along):
                            along.add(now[k][0])
                    if now[b][0] in along:
                        continue
                    order = now[:b] + [k for k in now[b:a + 1] if k[0] in along] + [k for k in now[b:a + 1] if k[0] not in along] + now[a + 1:]
                t = length(order)
                if t <= cur + WARM * rng.rand() * (1 - _ / SWAPS):
                    now, cur = order, t
                    if t < least:
                        best, least = order, t
            ORDER["least"] = least
            ORDER[n] = best
        return ORDER[n]

    def listed(tail, out):
        n = len(nodes)
        left = [len(d["order"]) for d in nodes]
        ready = [0.0] * n
        open_ = [i for i in range(n) if left[i] == 0]
        free, order = {}, []
        while open_:
            cand = []
            for i in open_:
                d = nodes[i]
                for q in d["cost"]:
                    s = max(free.get(q, 0.0), ready[i])
                    extra = SPARE if q == "v" and len(d["cost"]) > 1 else 0.0
                    cand.append((s, i, q, extra))
            best = {}
            for s, i, q, extra in cand:
                e = s + nodes[i]["cost"][q] + extra
                if i not in best or e < best[i][0]:
                    best[i] = (e, s, q)
            s0, i0 = min((v[1], i) for i, v in best.items())
            q0 = best[i0][2]
            same = [(i, v[1]) for i, v in best.items() if v[2] == q0]
            i = max([k for k in same if k[1] <= s0 + 1e-9], key=lambda k: tail[k[0]])[0]
            c = nodes[i]["cost"][q0]
            soon = [k for k in same if k[1] < s0 + LOOK * c and tail[k[0]] > tail[i]]
            if soon:
                i = max(soon, key=lambda k: tail[k[0]])[0]
            e, s, q = best[i]
            open_.remove(i)
            free[q] = s + nodes[i]["cost"][q]
            order.append((s, len(order), i, q))
            for k in out[i]:
                left[k] -= 1
                ready[k] = max(ready[k], free[q] + (nodes[i]["late"] + WAKE if i in nodes[k]["pre"] else 0.0))
                if left[k] == 0:
                    open_.append(k)
        return [(i, q) for s, m, i, q in order]

    total, waited = {}, {}

    def need(q, deps):
        for sem in sorted(deps):
            if waited.get((q, sem), 0) < deps[sem]:
                waited[(q, sem)] = deps[sem]
                Q[q].wait_ge(T.sem[sem], deps[sem])

    def issue():
        done = {}
        for i, q in arrange():
            d = nodes[i]
            deps = {}
            for p in d["pre"]:
                sem, v = done[p]
                deps[sem] = max(deps.get(sem, 0), v)
            need(q, deps)
            inst = d["fns"][q](Q[q])
            sem = d["sem"] or SEM[q]
            if d["sem"] is None:
                inst.then_inc(T.sem[sem], 1)
            total[sem] = total.get(sem, 0) + d["inc"]
            done[i] = (sem, total[sem])

    def bank(b, n):
        return T.ps[:, 512 * b:512 * b + n]

    dma("s", [(T.x0[:, quad(0)], T.x[:, quad(0)])], [], ["x00", "@d0"], "dx0", LATE + XL[0])
    dma("s", [(T.raw[16 * gr + 7 + RIGHT[gr]:16 * gr + 15, :], T.lam[16 * RIGHT[gr]:128, :]) for gr in range(8)], [], ["raw0", "@d0"], "dn0", LATE + XL[0])
    dma("a", [(T.ub[:], T.u[:])], [], ["ub", "@d1"], "du", LATE)
    dma("a", [(T.raw[16 * gr:16 * gr + 7 + RIGHT[gr], :], T.rho[0:112 + 16 * RIGHT[gr], :]) for gr in range(8)], [], ["raw1", "@d1"], "dn1", LATE + XL[0])

    def iota(o, pattern, base, cm, w, fl=True):
        n = 1
        for step, count in pattern:
            n *= count
        if fl:
            op("g", lambda e: e.iota(o, pattern, base, cm, allow_small_or_imprecise_dtypes=True), [], w, 0.22 + 0.0022 * n)
        else:
            op("g", lambda e: e.iota(o, pattern, base, cm), [], w, 0.22 + 0.0022 * n)

    iota(T.pi[:, 0:1], [[0, 1]], 32, 64, ["p"], False)
    iota(T.idn[0:64, :], [[0, 2], [8, 40]], 0, 1, ["idn"], False)
    iota(T.kk[:], [[40, 2], [2, 20]], 0, 0, ["kk"])
    iota(T.pat[:, 0:10], [[64, 5], [16, 2]], 0, 0, ["pata"])
    dma("s", [(T.raw[home("I8"):128:16, :], T.idn[0:64, :])], ["idn", "@d0"], ["raw2", "@d2"], "dn2", LATE)
    dma("s", [(T.x0[:, quad(1)], T.x[:, quad(1)])], ["@d2"], ["x01", "@d3"], "dx1", LATE + XL[1])

    def spot(a, table):
        return PLACE[1] if table in ("L0", "R7") else PLACE[2 + WAY[a].index(table)] + home(table)

    def numbers(first, rows, name):
        names = []
        for a, row in enumerate(rows):
            k = 0
            while k < len(row):
                n = min(2, len(row) - k)
                while k + n < len(row) and row[k + n] - row[k + n - 1] == row[k + 1] - row[k]:
                    n += 1
                names.append("%s%d%d" % (name, a, k))
                iota(T.sel[32 * a:32 * a + 32, first + k:first + k + n], [[row[k + n - 1] - row[k + max(n - 2, 0)], n]], row[k], 0, names[-1:])
                k += n
        return names

    SEL = numbers(0, [[spot(a, before(t)) - PLACE[2] * (t == WAY[a][1]) for t in WAY[a][1:]] for a in range(4)], "sel")
    END = numbers(4, [[spot(a, ODD[a][0]), spot(a, EVEN[a][0])] for a in range(4)], "end")

    place = {}
    for digits, then in (({"q16": (2, 240), "g32": (5, 224), "p32": (6, 31)}, "c0"),
                         ({"c1": (2, 48), "b16": (6, 16), "x16": (2, 16), "y16": (3, 16), "a": (11, 3), "k1": (2, 112), "h0": (3, 96)}, "h1")):
        at = len(place)
        for name, (sh, m) in digits.items():
            k = place[name] = len(place)
            ts(T.pj[:, k:k + 1], T.pi[:, 0:1], sh, m, OP.arith_shift_right, OP.bitwise_and, ["p"], ["pi" + name])
        cp(T.pc[:, at:len(place)], T.pj[:, at:len(place)], ["pi" + name for name in digits], list(digits))
        place[then] = len(place)

    def col(name):
        return T.pc[:, place[name]:place[name] + 1]

    late = [[]]

    def new(name, a, s1, s2, f1, f2):
        place.setdefault(name, len(place))
        use = [a] + [s for s in (s1, s2) if isinstance(s, str)] + late[0]
        s1, s2 = [col(s) if isinstance(s, str) else s if s is None else float(s) for s in (s1, s2)]
        if (f1, f2) == (mul, add):
            aff(col(name), col(a), s1, s2, use, [name], q=NEWQ)
        else:
            ts(col(name), col(a), s1, s2, f1, f2, use, [name])

    def aff(o, a, m, b, r, w, n=10, q="av", c=1):
        fns = {"a": lambda e: e.activation(o, a, AF.Identity, bias=b, scale=m), "v": lambda e: e.tensor_scalar(o, a, m, b, OP.mult, OP.add)}
        node({k: fns[k] for k in q}, {k: us(n, c if k == "v" else 1, False) for k in q}, 0.0, r, w, None, 1)

    mul, add = OP.mult, OP.add
    fill(T.zz[:], 0.0, ["zz"])
    for c in (slice(0, 4, 2), slice(5, 8, 2)):
        fill(T.zz[:, c], 1.0, ["zz"])
    new("g7", "q16", 112, -80, OP.is_ge, mul)
    new("t", "q16", "g7", -16, add, add)
    new("lo", "q16", 16, 112, OP.is_le, mul)
    new("t", "t", "lo", 96, OP.max, OP.min)
    new("mid", "q16", 208, None, OP.is_le, None)
    new("e14", "q16", 224, None, OP.is_equal, None)
    new("ua", "t", "mid", "e14", mul, add)
    new("hi", "mid", -112, 112, mul, add)
    new("ub_", "lo", -80.0 / 112.0, "hi", mul, add)
    ts(T.uoff[:, 8:16], T.zz[:], col("ub_"), col("ua"), mul, add, ["zz", "ua", "ub_"], ["uoff1"])
    quant(T.uq[:], T.us[:], T.ub[:], ["ub"], ["uq"], 512)

    def picked(k, after):
        c, o = slice(128 * k, 128 * k + 128), T.uoff[:, 8 * k:8 * k + 8]
        cp(T.upq[:, c].bitcast(dt.uint32), T.uq[:].bitcast(dt.uint32).indirect(o), ["uq", "uoff%d" % k] + after, ["upq%d" % k], n=128, x=True)
        cp(T.ups[:, c], T.us[:].indirect(o), ["uq", "uoff%d" % k], ["ups%d" % k], "a", n=128, x=True)

    picked(1, [])
    new("e15", "q16", 240, -1, OP.is_equal, mul)
    new("sc0", "q16", 192, "e15", OP.is_le, add)
    new("bi", "q16", -16 * SEQ, 1, add, OP.min)
    new("bi", "bi", -1, EPS, OP.max, mul)
    new("q8", "q16", 128, -639, OP.is_ge, mul)
    new("e0", "q16", 5, "q8", mul, add)
    ts(T.el[:, 0:40], T.kk[:], col("e0"), None, add, None, ["kk", "e0"], ["el"])
    new("off", "e15", "g32", -640, mul, add)
    lin(T.bl[:, 0:10], T.kk[:, 0:10], 16, col("p32"), ["kk", "p32"], ["bl0"])
    ts(T.bl[:, 16:26], T.pat[:, 0:10], col("p32"), col("b16"), add, add, ["pata", "p32", "b16"], ["bl1"])
    cp(T.bl[:, 32:42], T.bl[:, 16:26], ["bl1"], ["bl2"])
    for a in (1, 2):
        cp(T.bl[32 * a:32 * a + 32, 32:42], T.bl[32 * a:32 * a + 32, 0:10], ["bl0"], ["bl2"])
    fill(T.ue[:], 0.0, ["ue"], n=512)
    cp(T.dt1[:], T.ue[:, 0:320], ["ue"], ["dt0", "dt1", "st0", "st1"], n=320, c=0.5)
    ts(T.dt1[:, SEQ + 3:320:32], T.ue[:, 0:10], 1.0, None, add, None, ["ue", "dt0"], ["beta"])
    cp(T.win[:, 0:960:3], T.ue[:, 0:320], ["ue"], ["winz"], "a", 320)
    new("c0", "q16", 80, None, OP.min, None)
    for h in (0, 1):
        ts(T.cl[:, 2 * h:16:4], T.sel[:, 0:4], col("c%d" % h), float(AT[h] // 2), add, add, SEL + ["c%d" % h], ["cl%d" % h])
    new("c9", "q16", 144, None, OP.min, None)
    ts(T.cl[:, 16:20:2], T.sel[:, 4:6], col("c9"), None, add, None, END + ["c9"], ["cl2"])
    for t in (0, 176):
        cp(T.go[:, t:t + 16], T.ue[:, 0:16], ["ue"], ["gom%d" % t], NEWQ)
    cp(T.tt[:, PLACE[1]:PLACE[1] + 160], T.ue[:, 0:160], ["ue"], ["T10", "T11"], NEWQ, 160)
    iota(T.tt[:, PLACE[6]:PLACE[6] + 160], [[0, 160]], 0, 0, ["T60", "T61"])
    new("m3", "a", 3, None, OP.is_equal, None)
    new("xmy", "y16", -1, "x16", mul, add)
    new("xy", "xmy", "m3", 0, mul, add)
    new("v16", "xy", 1, "y16", mul, add)
    new("sh", "b16", -42.0 / 16.0, 22, mul, add)
    new("a2", "a", 2, 7, mul, add)
    new("f5", "a2", -1, 11, add, OP.min)
    new("fa", "v16", "sh", "f5", mul, add)
    new("fb", "b16", 20, "x16", mul, add)
    new("fb", "xy", -1, "fb", mul, add)
    new("h1", "a", 0, 128, mul, add)
    ts(T.sl[:, 0:2], T.pc[:, place["h0"]:place["h0"] + 2], col("fa"), col("fb"), add, add, ["h0", "h1", "fa", "fb"], ["sl0"])
    new("b", "b16", 0.0625, 0, mul, add)
    new("lay", "a", 0, "b", OP.is_equal, OP.max)
    new("wx", "xmy", "lay", 0, mul, add)
    place["k0"] = len(place)
    place["k2"] = len(place)
    new("k0", "q16", "wx", 176, add, OP.min)
    new("k2", "k1", "wx", 192, add, add)
    new("m0", "a", 0, None, OP.is_equal, None)
    e = [home(EVEN[a][1]) for a in range(4)]
    new("pe", "m0", e[0] - e[1], e[1], mul, add)
    new("pe", "m3", e[3] - e[1], "pe", mul, add)
    new("pos", "pe", -1, "a2", mul, add)
    new("pos", "pos", "b", "pe", mul, add)
    ts(T.sl[:, 8:12:2], T.pc[:, place["k0"]:place["k0"] + 2], col("pos"), None, add, None, ["k0", "k2", "pos"], ["sk"])
    for b, m in enumerate(("m0", "m3")):
        new("by%d" % b, m, TABLE[0] - ROW[0], ROW[0], mul, add)
        new("at%d" % b, m, TABLE[1] - ROW[1], ROW[1], mul, add)
    new("at1", "m0", 320, "at1", mul, add)

    for h in (0, 1):
        n = WID[h]
        for k in (0, 1):
            lst = T.el[:, 20 * k + AT[h] // 16:20 * k + (AT[h] + n) // 16]
            lin(T.win[:, tri(h, 1 + k, 3)], T.raw[:].indirect(lst), 4.0, col("off"), ["raw0", "raw1", "raw2", "el", "off"], ["win%d%d" % (h, k)], n, x=True)
            tr(T.te[:, cols(h, at=320 * k)], T.win[:, tri(h, 1 + k, 3)], ["win%d%d" % (h, k)], ["te%d%d" % (h, k)], n, 0.5)
        for t, f, name in ((0, OP.subtract, "dt"), (2, add, "st")):
            tt(T.dt1[:, cols(h, SEQ + t, 16)], T.te[:, cols(h, home("L0"), 16)], T.te[:, cols(h, home("L0"), 16, 320)], f, ["te%d0" % h, "te%d1" % h], ["%s%d" % (name, h)])

    def tables(h):
        return ["win%d0" % h, "win%d1" % h]

    WIN = tables(0) + tables(1) + ["winz"]

    def flips():
        late[0] = [EARLY]
        for t, v in ((0, 0), (2, -1)):
            iota(T.d0[:, t:960:3], [[0, 320]], v, 0, ["d0c%d" % t, "@sent"])
        new("t", "g7", 1.4, "q16", mul, add)
        new("t", "t", 1.25, 127, add, OP.min)
        new("e7", "q16", 112, 112, OP.is_equal, mul)
        ts(T.uoff[:, 0:8], T.zz[:], col("e7"), col("t"), mul, add, ["zz", "e7", "t"], ["uoff0"])
        picked(0, [EARLY])
        new("a1", "a", 2, None, OP.is_ge, None)
        new("sd", "b", "a1", 2, OP.not_equal, mul)
        new("sg", "q8", -2.0 / 639.0, -1, mul, add)
        new("sf", "e7", "sd", 0, mul, add)
        new("sf", "sf", 1.0 / 112.0, "sg", mul, add)
        new("sd", "sd", 1, -1, mul, add)
        new("sc1", "e14", "sd", "sc0", mul, add)
        tt(T.d1[:, 2:960:3], T.win[:, 1:960:3], T.win[:, 2:960:3], add, WIN + [EARLY], ["sum"], n=320, c=1)

    def ahead(k):
        for h in (0, 1):
            after, dif, mid = "@s%d" % k if k > 1 else EARLY, T.d1[:, tri(h, 0, 3)], T.d1[:, tri(h, 1, 3)]
            if FQ[k][h] == "a" and k > 1:
                tt(dif, dif, T.d0[:, tri(h, 1, 3)], mul, ["sf%d" % h, after], ["dif%d" % h], n=WID[h], c=1)
                continue
            tt(dif, T.win[:, tri(h, 1, 3)], T.win[:, tri(h, 2, 3)], OP.subtract, tables(h) + [after], ["dif%d" % h], n=WID[h], c=1)
            if FQ[k][h] == "a":
                ts(dif, dif, 0.5, None, mul, None, [], ["dif%d" % h], n=WID[h], c=0.5)
                ts(mid, T.d1[:, tri(h, 2, 3)], 0.5, None, mul, None, ["sum"], ["mid%d" % h], n=WID[h], c=0.5)
            else:
                cp(mid, T.win[:, tri(h, 2, 3)], tables(h) + [after], ["mid%d" % h], n=WID[h], c=0.5)

    for h in (0, 1):
        quant(T.qx0[:, cols(h)], T.sx0[:, cols(h)], T.x0[:, quad(h)], ["x0%d" % h], ["qx0%d" % h], 4 * WID[h])
    iota(T.ones[:], [[0, 128]], 1, 0, ["ones"])
    dma("s", [(T.zb[:], T.ue[:, 0:320]), (T.ky[:], T.ue[:, 0:352])] + [(T.et[:, 512 * b:512 * b + 512], T.ue[:]) for b in range(4)], ["ue", "x01"],
        ["zb0", "zb1", "ky0", "ky1"] + ["et%d" % b for b in range(4)] + ["@d3"], "de", LATE + 0.5)
    dma("s", [(T.wq[:].bitcast(dt.uint8), T.wc[:]), (T.wsp[:], T.ws[:])], ["@d3"], ["wq"], "dw", 3.5)

    op("g", lambda e: e.affine_select(T.eye[:], T.ones[:], [[1, 128]], OP.is_equal, 0.0, 0, -1), ["ones"], ["eye", "@sent"], 0.55)
    iota(T.w4[:], [[4, 320]], -640, 0, ["w4", "@sent"])
    for b in range(4):
        cp(T.et[:, 513 * b:512 * b + 512:4], T.eye[:], ["eye", "@bb"], ["et%d" % b], "a", 128)

    def state_parts(k, h):
        return ["x0%d" % h] if k == 0 else ["xn%d%d%d" % (k, h, t) for t in range(4)]

    def half_x(k):
        x = T["x%d" % k]
        for t in range(4):
            scaled(T.xh[:, 320 * t:320 * t + 320], x[:, t:1280:4], 0.5, 0.0, state_parts(k, 0) + state_parts(k, 1) + ["@bb"], ["xh%d" % t] + ["@xh"] * (t < 2), "a", 320, 0.5)
        both = [t for t in range(4) if t not in VA[0] or t not in VA[1]]
        c = slice(320 * both[0], 320 * both[-1] + (320 if both[-1] not in VA[1] else VW[0]))
        dma("s", [(T.xg[:, c], T.xh[:, c])], ["xh%d" % t for t in both], ["xg%d" % t for t in both], "dg", 3.3)

    def bits(j, h):
        scaled(T.bb[:, halfrow(h, 160 * j)], T.nb[:, 0:cols(h).stop].indirect(T.bl[:, share(h, 16 * j)]), 0.5, 0.0,
               ["nb0", "nb%d" % h, "bl%d" % j, ("@none", "@bb", "@xh")[j]], ["bb%d%d" % (h, j)] + ["@bb"] * (j == 0), "a", WID[h] // 2, x=True)

    def signs(k, h):
        n, c = WID[h], cols(h)

        def product(j):
            u = slice(128 * j, 128 * j + 128)
            mm(2 * h + j, n, T.upq[:, u], T.ups[:, u], T["qx%d" % k][:, c], T["sx%d" % k][:, c], ["upq%d" % j, "ups%d" % j, "qx%d%d" % (k, h)])
            return bank(2 * h + j, n), "b%d" % (2 * h + j)

        if k < 3:
            s, name = product(1)
            sc = "sc%d" % min(k, 1)
            sign(T.nb[:, c], s, AF.Sign, col(sc), col("bi"), [name, sc, "bi"], ["nb%d" % h], n)
            tr(T.nt[:, c], T.nb[:, c], ["nb%d" % h], ["nt%d" % h], n, 0.5)
            scan(T.xt[:, c], T.nt[:, c], T.dt1[:, c], 0.0, mul, add, ["nt%d" % h, "dt%d" % h, "st%d" % h, "beta"], ["xt%d" % h], n, 0.5)
            lin(T.lu[:, 16 * h:16 * h + n // 32], T.xt[:, cols(h, SEQ + 4, 32)], TABLE[0] / 2, TABLE[1], ["xt%d" % h], ["lu2%d" % h])
            bits(0, h)
        if k:
            s, name = product(0)
            if FQ[k][h] == "a":
                sign(T.d0[:, tri(h, 1, 3)], s, AF.Sign, col("sf"), EPS, [name, "sf"], ["sf%d" % h], n)
            else:
                ts(T.d0[:, tri(h, 1, 3)], s, col("sf"), 0.0, mul, OP.is_ge, [name, "sf"], ["sf%d" % h], n)
            scan(T.win[:, tri(h)], T.d0[:, tri(h)], T.d1[:, tri(h)], 0.0, mul, add, ["dif%d" % h, "mid%d" % h, "sum", "d0c0", "d0c2", "sf%d" % h], tables(h) + ["winz"] * h, 3 * n, 0.5)

    def upto(s, h, first=1):
        return ["T%d%d" % (k, j) for k in range(first, s + 1) for j in (0, 1) if (k, j) <= (s, h)]

    def step(s, h, after=()):
        n, at, j = WID[h] // 2, 32 * (s - 2) + 16 * h, 2 if s == 5 else s % 2
        go, name = (T.go[:, halfrow(h, 16)], "go5%d" % h) if s == 5 else (T.go[:, halfrow(h, 192)], "go%d" % h)
        tt(go, T.win[:, 0:960].indirect(T.lu[:, at:at + n // 16]), T.bb[:, halfrow(h, 160 * j)], add, WIN + ["lu%d%d" % (s, h), "bb%d%d" % (h, j)] + list(after), [name], n=n, x=True)
        tr(T.tt[:, halfrow(h, PLACE[s])], go, [name], ["T%d%d" % (s, h)], n)
        if s < 6:
            k, first = 4 * (s - 2) + 2 * h, 2 if s == 2 else 1
            lin(T.lu[:, at + 32:at + 48], T.tt[:, PLACE[first]:halfrow(h, PLACE[s]).stop].indirect(T.cl[:, k:k + 1]), *TABLE, upto(s, h, first) + ["cl%d" % h],
                ["lu%d%d" % (s + 1, h)], n=16, x=True)

    def walk(rd):
        second = T.xt[:, SEQ + 18:320:32]
        tt(T.two[:, 0:10], second, T.nt[:, 0:320:32], add, ["xt0", "xt1", "nt0", "nt1", "lu20", "lu21"], ["two"])
        scaled(T.tt[:, 0:160:16], T.two[:, 0:10], 0.5, 0.0, ["two"], ["T10", "T11"], "a", 10)
        for b in (0, 1):
            scaled(T.zb[:, home("L0") + 16 * b:320:32], T.two[:, 0:10], 0.5, 0.0, ["two", "@xh"], ["zb%d" % b], "a", 10)
        for j in (1, 2):
            for h in (0, 1):
                bits(j, h)
        for s in range(2, 7):
            for h in (0, 1):
                step(s, h, ["sk", "sl0", "gom0", "gom176"] * (s == 4))
            if s == 3:
                tr(T.win[:, 1280:1600], T.zb[:], ["zb0", "zb1"], ["back"], 320, 0.5)
            if s == 5:
                tr(T.tt[:, 960:1152], T.go[:, 0:192], ["go50", "go51", "gom0", "gom176"], ["TS"], 192)
                lin(T.fl[:], T.tt[:, PLACE[5]:1152].indirect(T.sl[:, 0:2]), *TABLE, ["T50", "T51", "T60", "T61", "TS", "sl0"], ["fl"], n=32, x=True)
                cp(T.win[:, 960:1280], T.win[:, 0:960].indirect(T.fl[:, 0:20]), WIN + ["fl"], ["row"], "a", n=320, x=True)
        for h in (0, 1):
            for b in (0, 1) * (1 - h):
                lin(T.mlu[:, b:32:2], T.tt[:, 0:960].indirect(T.cl[:, 18 - 2 * b:19 - 2 * b]), col("by%d" % b), col("at%d" % b),
                    upto(6, 1) + ["by%d" % b, "at%d" % b, "cl2"], ["ml%d" % b], n=16, x=True)
            for j, (a, n, q) in enumerate(KM[h]):
                cp(T.km[:, AT[h] + a:AT[h] + a + n], T.win[:].indirect(T.mlu[:, (AT[h] + a) // 16:(AT[h] + a + n) // 16]), WIN + ["row", "back", "ml0", "ml1"],
                   ["km%d%d" % (h, j)], q, n=n, x=True)
            tr(T.kt[:, cols(h)], T.km[:, cols(h)], ["km%d%d" % (h, j) for j in range(len(KM[h]))], ["kt%d" % h], WID[h], 0.5)
            lin(T["kl%d" % rd][:, part(h).start:part(h).start + 16], T.kt[:, 0:cols(h).stop].indirect(T.sl[:, 8 + 2 * h:9 + 2 * h]), 0.25, 160.25,
                ["kt0", "kt%d" % h, "sk"], ["kl%d%d" % (rd, h), "klx"], n=16, x=True)

    sent = [0]

    def send(rd, what, h):
        dst = T.cores[rank ^ STEP[rd - 1]]

        def put(fn, cost, late, land, sem, inc, own):
            sent[0] += own
            node({"g": fn}, {"g": cost}, late, ["kl%d0" % rd, "kl%d1" % rd] if what == "k" else ["qh%d%d" % (rd, h)], [land, "@sent"], sem, inc)

        q, s, lq, ls = T["qh%d" % rd], T["sh%d" % rd], T["lq%d" % rd], T["ls%d" % rd]
        kl = T["kl%d" % rd][:, 0:20]
        if topo.may_write(core, dst):
            rid, pid = topo.addr(dst, core)
            m, n = topo.mask(core, dst), len(topo.engines(core, dst))
            if what == "k":
                put(lambda e: e.remote_dma(T["kr%d" % rd][:], kl, T.sem["kr%d" % rd], T.sem.lsem, pid, rid, m), 0.4, 2.2 + 1.9 * (rd == 1), "kr%d" % rd, "kr%d" % rd, n, n)
                return
            c = out(h)
            sem = T.sem["ar%d%d" % (rd, h)]

            def go(e):
                e.remote_dma(lq[:, c].bitcast(dt.uint8), q[:, c].bitcast(dt.uint8), sem, T.sem.lsem, pid, rid, m)
                e.remote_dma(ls[:, c], s[:, c], sem, T.sem.lsem, pid, rid, m)

            put(go, 0.7, 2.9 + 0.5 * h, "lq%d%d" % (rd, h), "ar%d%d" % (rd, h), 2 * n, 2 * n)
            return
        rel = relays_of(core, dst, topo)
        ways = [topo.addr(k, core) for k in rel]
        far = len(topo.engines(rel[0], dst))
        eng = topo.engines(core, rel[0])
        n = len(eng) // 2
        three = [eng[:n // 2], eng[n // 2:n], eng[n:]]
        if what == "k":
            put(lambda e: e.remote_dma_fused([RemoteDMATransfer(dst_ids=[DstId(rid=ways[k][0], pnc=ways[k][1])], dma_engine_mask=bits_of(three[k]), remote_sem=T.sem.rk,
                                                                src=T.kl2[:, 8 * k:8 * k + 8], dst=T.rlk[:]) for k in range(3)], local_sem=T.sem.lsem),
                0.6, 7.0, "kr%d" % rd, "kr%d" % rd, 3 * far, 2 * n)
            return
        a, w = out(h).start, VW[h] // 2

        pieces = [(q[:, a + w * k:a + w * k + w].bitcast(dt.uint8), T.rlq[:, a + w * k:a + w * k + w].bitcast(dt.uint8)) for k in (0, 1)]

        def go2(e):
            e.remote_dma_fused([RemoteDMATransfer(dst_ids=[DstId(rid=ways[k][0], pnc=ways[k][1])], dma_engine_mask=bits_of([eng[:n], eng[n:]][k]),
                                                  remote_sem=T.sem["ry%d" % h], src=src, dst=land) for k, (src, land) in enumerate(pieces)], local_sem=T.sem.lsem)
            e.remote_dma(T.rls[:, out(h)], s[:, out(h)], T.sem["ry%d" % h], T.sem.lsem, ways[2][1], ways[2][0], bits_of(eng))

        put(go2, 0.8 - 0.2 * h, 5.1 + 0.7 * h, "lq%d%d" % (rd, h), "ar%d%d" % (rd, h), 3 * far, 4 * n)

    def meet(rd, h):
        for t in range(4):
            c = slice(320 * t + out(h).start, 320 * t + out(h).stop)
            far = T.xh[:, 320 * t:320 * t + 320].indirect(T["kl%d" % rd][:, out(h).start // 16:out(h).stop // 16])
            r, w = ["xh%d" % t, "kl%d0" % rd, "kl%d%d" % (rd, h)], ["vt%d%d" % (h, t)]
            if t in VA[h]:
                cp(T.vg[:, c], far, r, ["vg%d%d" % (h, t)], "a", n=VW[h], x=True)
                tt(T.vt[:, out(h, 4, t, 4)], T.vg[:, c], T.xh[:, c], OP.add, ["xh%d" % t, "vg%d%d" % (h, t)] + ["@v"] * h, w, n=VW[h], c=1)
            else:
                tt(T.vt[:, out(h, 4, t, 4)], far, T.xg[:, c], OP.add, r + ["xg%d" % t] + ["@v"] * h, w, n=VW[h], x=True)

    def layer(h):
        c = out(h)
        for b in range(4):
            mm(4 * h + b, VW[h], T.wq[:, 128 * b:128 * b + 128], T.wsp[:, 128 * b:128 * b + 128], T.qv[:, c], T.qvs[:, c], ["wq", "qv%d" % h], ["@l"])

    def layer_out(h, b, q):
        scaled(T.ht[:, out(h, 4, b, 4)], bank(4 * h + b, VW[h]), 0.03125, 0.0, ["b%d" % (4 * h + b)] + ["@i"] * (q == "v"), ["ht%d%d" % (h, b)], q, VW[h])

    def quant_v(h):
        quant(T.qv[:, out(h)], T.qvs[:, out(h)], T.vt[:, out(h, 4)], ["vt%d%d" % (h, t) for t in range(4)], ["qv%d" % h, ("@v", "@h")[h]], 4 * VW[h])

    def quant_h(rd, h):
        quant(T["qh%d" % rd][:, out(h)], T["sh%d" % rd][:, out(h)], T.ht[:, out(h, 4)], ["ht%d%d" % (h, b) for b in range(4)] + ["@h"],
              ["qh%d%d" % (rd, h), ("@g%d", "@s%d")[h] % rd], 4 * VW[h])

    for h in (0, 1):
        signs(0, h)
    half_x(0)
    for rd in (1, 2, 3):
        walk(rd)
        send(rd, "k", 0)
        meet(rd, 0)
        quant_v(0)
        layer(0)
        for b in range(4):
            layer_out(0, b, HQ[b])
        meet(rd, 1)
        quant_v(1)
        layer(1)
        quant_h(rd, 0)
        send(rd, "h", 0)
        for b in range(4):
            layer_out(1, b, HQ[4 + b])
        quant_h(rd, 1)
        send(rd, "h", 1)
        if rd == 1:
            for b in range(4):
                quant(T.eq[:, 128 * b:128 * b + 128], T.es[:, 128 * b:128 * b + 128], T.et[:, 512 * b:512 * b + 512], ["et%d" % b, EARLY], ["eq%d" % b], n=512)
            flips()
            new("ne", "x16", "b16", 336, OP.not_equal, mul)
            for k, name in enumerate(("q16", "c1")):
                ts(T.sl[:, 4 + k:5 + k], col(name), col("ne"), float(256 * k), add, add, [name, "ne", EARLY], ["sm%d" % k])
            dma("s", [(T.vb[:], T.v[:])], ["wq"], ["vb"], "dv", 2.5)
        ahead(rd)
        if rd == 2:
            quant(T.vq[:], T.vs[:], T.vb[:], ["vb", "@s2"], ["vq"], 512)
        kl, kr = T["kl%d" % rd], T["kr%d" % rd]
        for h in (0, 1):
            cp(T.kw[:, 160 * h:160 * h + 160], T.w4[:].indirect(kr[:, 10 * h:10 * h + 10]), ["w4", "kr%d" % rd, "@s%d" % rd], ["kw%d" % h], KQ[rd][h], n=160, x=True)
        for h in (0, 1):
            cp(T.ky[:, 16 + 160 * h:176 + 160 * h], T.kw[:].indirect(kl[:, 10 * h:10 * h + 10]), ["kw0", "kw1", "kl%d0" % rd, "kl%d1" % rd], ["ky%d" % h], KQ[rd][h], n=160, x=True)
        tr(T.kys[:, 0:320], T.ky[:, 16:336], ["ky0", "ky1"], ["kys0"], 320, 0.5)
        tr(T.kys[:, 320:672], T.ky[:], ["ky0", "ky1"], ["kys1"], 352, 0.5)
        lin(T.mo[:], T.kys[:].indirect(T.sl[:, 4:6]), 0.25, 160.25, ["kys0", "kys1", "sm0", "sm1"], ["mo0", "mo1", "mo2"], n=32, x=True)
        ts(T.mo[:, 20:28], T.mo[:, part(1)], 320.0, None, add, None, ["mo1"], ["mo2"])
        if rd < 3:
            cp(T.dt1[:, SEQ:320:16], T.xt[:, SEQ + 1:320:16], ["xt0", "xt1", "@s%d" % rd], ["dt0", "dt1"])
        lq, ls = T["lq%d" % rd], T["ls%d" % rd]
        for h in (0, 1):
            for b in range(4):
                c = out(h)
                mm(4 * h + b, VW[h], T.eq[:, 128 * b:128 * b + 128], T.es[:, 128 * b:128 * b + 128], lq[:, c], ls[:, c], ["eq%d" % b, "lq%d%d" % (rd, h)], ["@u"])
                cp(T.dd[:, 320 * b + c.start:320 * b + c.stop], bank(4 * h + b, VW[h]), ["b%d" % (4 * h + b)], ["dd%d%d" % (h, b)],
                   DDQ[b] if h else "a", n=VW[h])
        xn, qn, sn = T["x%d" % rd], T["qx%d" % rd], T["sx%d" % rd]
        for h in (0, 1):
            for t in range(4):
                far, r = T.dd[:, 320 * t:320 * t + 320].indirect(T.mo[:, part(h)]), ["mo%d" % h, "dd0%d" % t, "dd1%d" % t]
                near, w = ["vt0%d" % t, "vt1%d" % t] + ["@x"] * (h * t > 0), ["xn%d%d%d" % (rd, h, t)]
                if h:
                    n = WID[h]
                    if t % 2 == 0:
                        cp(T.dg[:, n * t:n * t + 2 * n], T.dd[:, 320 * t:320 * t + 640].indirect(T.mo[:, part(h).start:part(h).start + n // 8]),
                           r + ["mo2", "dd0%d" % (t + 1), "dd1%d" % (t + 1)], ["dg%d" % (t // 2)], "a", n=2 * n, x=True)
                    tt(xn[:, quad(h, t, 4)], T.dg[:, n * t:n * t + n], T.vt[:, quad(h, t, 4)], OP.add, ["dg%d" % (t // 2)] + near, w, n=n, c=1)
                else:
                    tt(xn[:, quad(h, t, 4)], far, T.vt[:, quad(h, t, 4)], OP.add, r + near, w, n=WID[h], x=True)
            quant(qn[:, cols(h)], sn[:, cols(h)], xn[:, quad(h)], state_parts(rd, h), ["qx%d%d" % (rd, h)] + ["@x"] * (1 - h), 4 * WID[h])
        for h in (0, 1):
            signs(rd, h)
        if rd < 3:
            half_x(rd)
    for h in (0, 1):
        c = cols(h)
        dma("s", [(T.oc[:, quad(h)], T.qx3[:, c].bitcast(dt.uint8))], ["qx3%d" % h], [], "oq%d" % h)
        mm(6 + h, WID[h], T.vq[:], T.vs[:], T.qx3[:, c], T.sx3[:, c], ["vq", "qx3%d" % h])
        cp(T.yb[:, c], bank(6 + h, WID[h]), ["b%d" % (6 + h)], ["yb%d" % h], "a", n=WID[h])
        for k in (0, 1):
            scaled(T.lout[:, 2 * AT[h] + k:2 * (AT[h] + WID[h]):2], T.win[:, tri(h, 1 + k, 3)], 0.25, 160.0, tables(h), ["lo%d%d" % (h, k)], ("av", "va")[h][k], WID[h])
    dma("s", [(T.osc[4 * k:4 * k + 4, :], T.sx3[32 * k:32 * k + 4, :]) for k in range(4)], ["qx30", "qx31"], [], "os")
    dma("s", [(T.y[:], T.yb[:])], ["yb0", "yb1"], [], "oy", 2.3)
    for k in (0, 1):
        at = 16 * RIGHT.index(k) + home("L0") * (1 - k)
        dma(LRQ[k], [(T.lr[:, 640 * k:640 * k + 640], T.lout[at:at + 8, :])], ["lo00", "lo01", "lo10", "lo11"], [], "ol%d" % k)
    issue()
    need("g", dict(total))
    g.wait_ge(T.sem.lsem, sent[0])
